import numpy as np
import ml_dtypes


def mxq(x, axis, fmt="e4m3"):
    dtype, down = {"e4m3": (ml_dtypes.float8_e4m3fn, 7), "e5m2": (ml_dtypes.float8_e5m2, 14)}[fmt]
    v = np.moveaxis(np.asarray(x, np.float32).astype(ml_dtypes.bfloat16).astype(np.float64), axis, -1)
    blocks = v.reshape(v.shape[:-1] + (-1, 32))
    amax = np.abs(blocks).max(-1, keepdims=True)
    byte = np.maximum(np.where(amax > 0, np.frexp(amax)[1] - 1 + 127, 0) - down, 1)
    scale = np.exp2(byte - 127.0)
    codes = (blocks / scale).astype(np.float32).astype(dtype).astype(np.float64)
    return np.moveaxis((codes * scale).reshape(v.shape), -1, axis)


WIDE = False


def mx_kscale(k):
    if not WIDE:
        return np.ones(k)
    levels = np.array([10, -10, 5, -5, 0])
    if k % 512:
        return np.exp2(np.random.permutation(np.resize(levels, k // 32))).repeat(32)
    a = np.empty((k // 512, 16))
    for p in range(k // 512):
        a[p, :8] = np.random.permutation(np.resize(levels, 8))
        for g in range(8):
            far = levels[np.abs(levels - a[p, g]) >= 10]
            a[p, g + 8] = far[np.random.randint(len(far))]
    return np.exp2(a.ravel()).repeat(32)


BF16 = ml_dtypes.bfloat16


def bf(x):
    return np.asarray(x, np.float32).astype(BF16)


def f64(x):
    return np.asarray(x).astype(np.float64)


D, T, K, N, F = 2, 1024, 512, 1024, 1536


def draw0():
    s = mx_kscale(N)
    t = mx_kscale(T)
    return {
        "x": bf(np.random.standard_normal((D, T, K)) / np.sqrt(T) / t[:, None]),
        "dy": bf(np.random.standard_normal((D, T, N)) * s * t[:, None]),
        "w2": bf(np.random.standard_normal((F, N)) / np.sqrt(N) / s),
        "g": bf(np.random.uniform(0.1, 1.1, (D, T, F))),
        "c": bf(np.random.uniform(0.3, 0.8, (D,))),
    }


def core(x, dy, w2, g, c):
    x, dy, g, c = f64(x), f64(dy), f64(g), f64(c)
    w2q = mxq(f64(w2), 1, "e4m3")
    dw = np.zeros((K, F))
    for d in range(D):
        dh = (mxq(dy[d], 1, "e4m3") @ w2q.T) * g[d]
        part = mxq(x[d], 0, "e4m3").T @ mxq(dh, 0, "e4m3")
        dw = dw + c[d] * part
    return dw


def e4m3fn_bytes(y):
    return np.clip(np.asarray(y, np.float64), -448.0, 448.0).astype(np.float32).astype(ml_dtypes.float8_e4m3fn).view(np.uint8)


def e4m3fn_values(b):
    return np.asarray(b, np.uint8).view(ml_dtypes.float8_e4m3fn).astype(np.float64)


def setup_inputs():
    d = draw0()
    x0 = np.asarray(d['w2']).astype(np.float64)
    s = (np.max(np.abs(x0), axis=(0,), keepdims=True) / 448.0).astype(np.float32)
    out = {}
    for k, v in d.items():
        if k == 'w2':
            out['w2_bytes'] = e4m3fn_bytes(x0 / s.astype(np.float64))
            out['w2_scale'] = s
        else:
            out[k] = v
    return out


def reference(x, dy, w2_bytes, w2_scale, g, c):
    return core(x, dy, e4m3fn_values(w2_bytes) * w2_scale.astype(np.float64), g, c)

@@ -1,0 +1,577 @@
+from contextlib import ExitStack
+
+import concourse.mybir as mybir
+from concourse.masks import make_identity
+
+D, T, K, N, F = 2, 1024, 512, 1024, 1536
+FLOPS = 2 * D * T * N * F + 2 * D * T * K * F
+
+F32 = mybir.dt.float32
+BF16 = mybir.dt.bfloat16
+U32 = mybir.dt.uint32
+U8 = mybir.dt.uint8
+FP8 = mybir.dt.float8_e4m3fn
+FP8X4 = mybir.dt.float8_e4m3fn_x4
+MULT = mybir.AluOpType.mult
+ADD = mybir.AluOpType.add
+COPY = mybir.ActivationFunctionType.Copy
+
+P = 128
+HALVES = 2
+PAIRS = 6
+PF = 256
+RUN = 4
+SEQ = ((0,0),(0,1),(0,2),(0,3),(1,0),(0,4),(1,1),(0,5),(1,2),(1,3),(1,4),(1,5))
+
+
+def tile_shard_weight_grad_s7_kernel(tc, x, dy, w2_bytes, w2_scale, g, c, out):
+    nc = tc.nc
+    with ExitStack() as ctx:
+        keep = ctx.enter_context(tc.tile_pool(name="keep", bufs=1))
+        work = ctx.enter_context(tc.tile_pool(name="work", bufs=2))
+        psum = ctx.enter_context(tc.psum_pool(name="psum", bufs=2))
+        ctx.enter_context(tc.manual_schedule())
+
+        scale_col = keep.tile([P, 8], F32, name="scale_col")
+        nc.scalar.dma_start(out=scale_col[:], in_=w2_scale.rearrange("o (p c) -> p (o c)", c=8))
+        c_bf = keep.tile([P, D], BF16, name="c_bf")
+        nc.scalar.dma_start(out=c_bf[:], in_=c.partition_broadcast(P))
+
+        w_raw, y_raw, x_raw, g_raw = {}, {}, {}, {}
+        w_view = w2_bytes.rearrange("(j b p) n -> j p b n", b=2, p=P)
+        out_view = out.rearrange("(h kt p) f -> h p kt f", kt=2, p=P)
+
+        def load_w(j):
+            w_raw[j] = work.tile([P, 2, N], U8, name="w_raw", bufs=PAIRS)
+            nc.sync.dma_start(out=w_raw[j][:], in_=w_view[j])
+
+        def load_y(dd, q, tp):
+            y_raw[dd, q, tp] = work.tile([P, 2, N], BF16, name="y_raw", bufs=8, align_bytes=64)
+            nc.sync.dma_start(
+                out=y_raw[dd, q, tp][:],
+                in_=dy[dd].rearrange("(q p t) n -> q p t n", q=2, t=4)[q][:, 2 * tp : 2 * tp + 2, :],
+            )
+
+        def load_x(dd, q):
+            x_raw[dd, q] = work.tile([P, 4, K], BF16, name="x_raw", bufs=4, align_bytes=64)
+            nc.sync.dma_start(out=x_raw[dd, q][:], in_=x[dd].rearrange("(q p t) k -> q p t k", q=2, t=4)[q])
+
+        def load_g(dd, q, ch):
+            g_raw[dd, q, ch] = work.tile([P, 4, 512], BF16, name="g_raw", bufs=8, align_bytes=64)
+            nc.sync.dma_start(
+                out=g_raw[dd, q, ch][:],
+                in_=g[dd].rearrange("(q p t) f -> q p t f", q=2, t=4)[q][:, :, 512 * ch : 512 * (ch + 1)],
+            )
+
+        load_y(0, 0, 0)
+        load_w(0)
+        load_y(0, 0, 1)
+        load_w(1)
+        load_y(0, 1, 0)
+        load_w(2)
+        load_y(0, 1, 1)
+        load_g(0, 0, 0)
+        load_x(0, 0)
+        load_g(0, 1, 0)
+        load_x(0, 1)
+        load_w(3)
+        load_g(0, 0, 1)
+        load_g(0, 1, 1)
+        load_y(1, 0, 0)
+        load_y(1, 0, 1)
+        load_y(1, 1, 0)
+        load_y(1, 1, 1)
+        load_w(4)
+        load_x(1, 0)
+        load_g(1, 0, 0)
+        load_x(1, 1)
+        load_g(1, 1, 0)
+        load_g(0, 0, 2)
+        load_w(5)
+        load_g(0, 1, 2)
+
+        ident = keep.tile([P, P], F32, name="ident", align_bytes=64)
+        make_identity(nc, ident[:])
+        zeros = keep.tile([P, 512], BF16, name="zeros", align_bytes=64)
+        nc.vector.memset(zeros[:], 0.0)
+
+        def warm(n):
+            for i in range(n):
+                ps = psum.tile([P, 512], F32, name="p2", bufs=3)
+                nc.tensor.matmul(ps[:], lhsT=zeros[:, 0:P], rhs=zeros[:], start=True, stop=True)
+
+        warm(4)
+        scale_all = keep.tile([P, P, 8], F32, name="scale_all", align_bytes=64)
+        for h in range(2):
+            ps = psum.tile([P, 4, P], F32, name="tr", bufs=2)
+            for cc in range(4):
+                col = 4 * h + cc
+                nc.tensor.transpose(ps[:, cc, :], scale_col[:, col : col + 1].to_broadcast([P, P]), ident[:])
+            view = ps[:].rearrange("p c j -> p j c")
+            if h == 0:
+                nc.scalar.copy(out=scale_all[:, :, 0:4], in_=view)
+            else:
+                nc.vector.tensor_copy(out=scale_all[:, :, 4:8], in_=view)
+        c_all = keep.tile([P, D], F32, name="c_all")
+        nc.scalar.copy(out=c_all[:], in_=c_bf[:])
+
+        wb, gw, w_codes, w_scales = {}, {}, {}, {}
+        gy, y_codes, y_scales = {}, {}, {}
+        x_codes, x_scales, gx = {}, {}, {}
+        bank = {}
+        dh, d_codes, d_scales = {}, {}, {}
+        acc = {}
+
+        def prod(b):
+            wb[b] = work.tile([P, N], BF16, name="wb", bufs=8, align_bytes=64)
+            nc.vector.tensor_tensor(
+                out=wb[b][:],
+                in0=w_raw[b // 2][:, b % 2, :].bitcast(FP8),
+                in1=scale_all[:].rearrange("p j c -> p (j c)"),
+                op=MULT,
+            )
+
+        def word_transposes(words, ps):
+            for gi in range(2):
+                for u in range(2):
+                    nc.tensor.transpose(ps[:, gi, u, :], words[:, 256 * gi + u : 256 * (gi + 1) : 2], ident[:])
+
+        def wtr(b):
+            ps = psum.tile([P, 2, 2, P], F32, name="tr", bufs=2)
+            word_transposes(wb[b][:].bitcast(F32), ps)
+            bank["w", b] = ps
+
+        def wex(b):
+            j = b // 2
+            if j not in gw:
+                gw[j] = work.tile([P, 2, 2, P, 4], BF16, name="gw", bufs=3, align_bytes=64)
+            dst = gw[j][:, b % 2].rearrange("p g f t -> p (g f t)").bitcast(F32)
+            nc.scalar.copy(
+                out=dst.rearrange("p (g f u) -> p g f u", g=2, u=2),
+                in_=bank["w", b][:].rearrange("p g u f -> p g f u"),
+            )
+
+        def wq(j):
+            w_codes[j] = work.tile([P, 2, 2, P], U32, name="w_codes", bufs=PAIRS, align_bytes=64)
+            w_scales[j] = work.tile([P, 2, 2, P], U8, name="w_scales", bufs=PAIRS, align_bytes=64)
+            nc.vector.quantize_mx(
+                out=w_codes[j][:].rearrange("p b g f -> p (b g f)").bitcast(FP8X4),
+                scales=w_scales[j][:].rearrange("p b g f -> p (b g f)"),
+                in_=gw[j][:].rearrange("p b g f t -> p (b g f t)"),
+            )
+
+        def ytr(dd, q, t):
+            ps = psum.tile([P, 2, 2, P], F32, name="tr", bufs=2)
+            word_transposes(y_raw[dd, q, t // 2][:, t % 2, :].bitcast(F32), ps)
+            bank["y", dd, q, t] = ps
+
+        def yex(dd, q, t):
+            tp = t // 2
+            if (dd, q, tp) not in gy:
+                gy[dd, q, tp] = work.tile([P, 2, 2, P, 4], BF16, name="gy", bufs=4, align_bytes=64)
+            dst = gy[dd, q, tp][:, t % 2].rearrange("p g m t -> p (g m t)").bitcast(F32)
+            nc.scalar.copy(
+                out=dst.rearrange("p (g m u) -> p g m u", g=2, u=2),
+                in_=bank["y", dd, q, t][:].rearrange("p g u m -> p g m u"),
+            )
+
+        def yq(dd, q, tp):
+            y_codes[dd, q, tp] = work.tile([P, 2, 2, P], U32, name="y_codes", bufs=8, align_bytes=64)
+            y_scales[dd, q, tp] = work.tile([P, 2, 2, P], U8, name="y_scales", bufs=8, align_bytes=64)
+            nc.vector.quantize_mx(
+                out=y_codes[dd, q, tp][:].rearrange("p b g f -> p (b g f)").bitcast(FP8X4),
+                scales=y_scales[dd, q, tp][:].rearrange("p b g f -> p (b g f)"),
+                in_=gy[dd, q, tp][:].rearrange("p b g f t -> p (b g f t)"),
+            )
+
+        def xint(dd, q, kq):
+            if (dd, q) not in gx:
+                gx[dd, q] = work.tile([P, K, 4], BF16, name="gx", bufs=2, align_bytes=64)
+            ks = slice(128 * kq, 128 * (kq + 1))
+            nc.scalar.copy(
+                out=gx[dd, q][:, ks, :].rearrange("p (c i) t -> p c t i", i=RUN),
+                in_=x_raw[dd, q][:, :, ks].rearrange("p t (c i) -> p c t i", i=RUN),
+            )
+
+        def xq(dd, q):
+            x_codes[dd, q] = work.tile([P, K], U32, name="x_codes", bufs=4, align_bytes=64)
+            x_scales[dd, q] = work.tile([P, K], U8, name="x_scales", bufs=4, align_bytes=64)
+            nc.vector.quantize_mx(
+                out=x_codes[dd, q][:].bitcast(FP8X4),
+                scales=x_scales[dd, q][:],
+                in_=gx[dd, q][:].rearrange("p k t -> p (k t)"),
+            )
+
+        def unit(s, i):
+            dd, j = SEQ[s]
+            q, b = divmod(i, 2)
+            ps = psum.tile([P, 4, P], F32, name="unit", bufs=3)
+            for t in range(4):
+                for gi in range(2):
+                    nc.tensor.matmul_mx(
+                        out=ps[:, t, :],
+                        lhsT=y_codes[dd, q, t // 2][:, t % 2, gi, :].bitcast(FP8X4),
+                        lhsT_scale=y_scales[dd, q, t // 2][:, t % 2, gi, :],
+                        rhs=w_codes[j][:, b, gi, :].bitcast(FP8X4),
+                        rhs_scale=w_scales[j][:, b, gi, :],
+                        start=(gi == 0),
+                        stop=(gi == 1),
+                    )
+            bank["u", s, i] = ps
+
+        def dhg(s, i):
+            dd, j = SEQ[s]
+            q, b = divmod(i, 2)
+            if (s, q) not in dh:
+                dh[s, q] = work.tile([P, PF, 4], BF16, name="dh", bufs=4, align_bytes=64)
+            f0 = PF * (j % 2) + P * b
+            nc.vector.tensor_tensor(
+                out=dh[s, q][:, P * b : P * (b + 1), :].rearrange("p (c i) t -> p c t i", i=RUN),
+                in0=bank["u", s, i][:].rearrange("p t (c i) -> p c t i", i=RUN),
+                in1=g_raw[dd, q, j // 2][:, :, f0 : f0 + P].rearrange("p t (c i) -> p c t i", i=RUN),
+                op=MULT,
+            )
+
+        def qd(s, q):
+            d_codes[s, q] = work.tile([P, PF], U32, name="d_codes", bufs=4, align_bytes=64)
+            d_scales[s, q] = work.tile([P, PF], U8, name="d_scales", bufs=4, align_bytes=64)
+            nc.vector.quantize_mx(
+                out=d_codes[s, q][:].bitcast(FP8X4),
+                scales=d_scales[s, q][:],
+                in_=dh[s, q][:].rearrange("p f t -> p (f t)"),
+            )
+
+        def p2(s, h):
+            dd = SEQ[s][0]
+            ps = psum.tile([P, 2, PF], F32, name="p2", bufs=3)
+            for k2 in range(2):
+                kc = slice(P * (2 * h + k2), P * (2 * h + k2 + 1))
+                for q in range(2):
+                    nc.tensor.matmul_mx(
+                        out=ps[:, k2, :],
+                        lhsT=x_codes[dd, q][:, kc].bitcast(FP8X4),
+                        lhsT_scale=x_scales[dd, q][:, kc],
+                        rhs=d_codes[s, q][:].bitcast(FP8X4),
+                        rhs_scale=d_scales[s, q][:],
+                        start=(q == 0),
+                        stop=(q == 1),
+                    )
+            bank["p", s, h] = ps
+
+        def pex(s, h):
+            dd, j = SEQ[s]
+            ps = bank["p", s, h]
+            if dd == 0:
+                acc[j, h] = work.tile([P, 2, PF], F32, name="acc", bufs=12)
+                nc.scalar.activation(out=acc[j, h][:], in_=ps[:], func=COPY, scale=c_all[:, 0:1])
+            else:
+                nc.vector.scalar_tensor_tensor(
+                    out=acc[j, h][:], in0=ps[:], scalar=c_all[:, 1:2], in1=acc[j, h][:], op0=MULT, op1=ADD
+                )
+                nc.sync.dma_start(out=out_view[h][:, :, PF * j : PF * (j + 1)], in_=acc[j, h][:])
+
+        tail = {}
+
+        def tail_pass(q):
+            s = 2 * PAIRS - 1
+            for kt in range(4):
+                if q == 0:
+                    tail[kt] = psum.tile([P, PF], F32, name=("tr", "unit")[kt // 2], bufs=(2, 3)[kt // 2])
+                kc = slice(P * kt, P * (kt + 1))
+                nc.tensor.matmul_mx(
+                    out=tail[kt][:],
+                    lhsT=x_codes[1, q][:, kc].bitcast(FP8X4),
+                    lhsT_scale=x_scales[1, q][:, kc],
+                    rhs=d_codes[s, q][:].bitcast(FP8X4),
+                    rhs_scale=d_scales[s, q][:],
+                    start=(q == 0),
+                    stop=(q == 1),
+                )
+
+        def tail_out():
+            j = PAIRS - 1
+            for kt in range(4):
+                total = acc[j, kt // 2][:, kt % 2, :]
+                nc.vector.scalar_tensor_tensor(
+                    out=total, in0=tail[kt][:], scalar=c_all[:, 1:2], in1=total, op0=MULT, op1=ADD
+                )
+                nc.sync.dma_start(out=out[P * kt : P * (kt + 1), PF * j : PF * (j + 1)], in_=total)
+
+        warm(1)
+        ytr(0, 0, 0)
+        ytr(0, 0, 1)
+        prod(0)
+        yex(0, 0, 0)
+        yex(0, 0, 1)
+        warm(1)
+        ytr(0, 0, 2)
+        prod(1)
+        wtr(0)
+        yex(0, 0, 2)
+        prod(2)
+        warm(1)
+        ytr(0, 0, 3)
+        wex(0)
+        prod(3)
+        wtr(1)
+        yex(0, 0, 3)
+        warm(1)
+        ytr(0, 1, 0)
+        wex(1)
+        yq(0, 0, 0)
+        ytr(0, 1, 1)
+        wq(0)
+        yex(0, 1, 0)
+        yq(0, 0, 1)
+        warm(1)
+        ytr(0, 1, 2)
+        yex(0, 1, 1)
+        prod(4)
+        ytr(0, 1, 3)
+        yex(0, 1, 2)
+        unit(0, 0)
+        yq(0, 1, 0)
+        yex(0, 1, 3)
+        wtr(2)
+        prod(5)
+        xint(0, 0, 0)
+        wtr(3)
+        xint(0, 0, 2)
+        unit(0, 1)
+        dhg(0, 0)
+        wex(2)
+        yq(0, 1, 1)
+        wex(3)
+        wtr(4)
+        dhg(0, 1)
+        xint(0, 0, 1)
+        wtr(5)
+        wq(1)
+        xint(0, 0, 3)
+        unit(0, 2)
+        qd(0, 0)
+        xint(0, 1, 0)
+        xq(0, 0)
+        unit(0, 3)
+        xint(0, 1, 2)
+        dhg(0, 2)
+        unit(1, 0)
+        xint(0, 1, 1)
+        dhg(0, 3)
+        unit(1, 1)
+        xint(0, 1, 3)
+        dhg(1, 0)
+        unit(1, 2)
+        wex(4)
+        dhg(1, 1)
+        load_g(1, 0, 1)
+        unit(1, 3)
+        wex(5)
+        xq(0, 1)
+        ytr(1, 0, 0)
+        dhg(1, 2)
+        ytr(1, 0, 1)
+        qd(0, 1)
+        yex(1, 0, 0)
+        dhg(1, 3)
+        load_g(1, 1, 1)
+        p2(0, 0)
+        yex(1, 0, 1)
+        wq(2)
+        p2(0, 1)
+        qd(1, 0)
+        pex(0, 0)
+        unit(2, 0)
+        prod(6)
+        pex(0, 1)
+        unit(2, 1)
+        dhg(2, 0)
+        wtr(6)
+        dhg(2, 1)
+        ytr(1, 0, 2)
+        prod(7)
+        wex(6)
+        unit(2, 2)
+        yex(1, 0, 2)
+        unit(2, 3)
+        qd(1, 1)
+        xint(1, 0, 1)
+        dhg(2, 2)
+        p2(1, 0)
+        xint(1, 0, 3)
+        dhg(2, 3)
+        p2(1, 1)
+        pex(1, 0)
+        qd(2, 0)
+        wtr(7)
+        qd(2, 1)
+        pex(1, 1)
+        prod(8)
+        ytr(1, 0, 3)
+        wex(7)
+        p2(2, 0)
+        yex(1, 0, 3)
+        prod(9)
+        p2(2, 1)
+        pex(2, 0)
+        ytr(1, 1, 0)
+        wq(3)
+        pex(2, 1)
+        ytr(1, 1, 1)
+        yq(1, 0, 0)
+        yex(1, 1, 0)
+        unit(3, 0)
+        yq(1, 0, 1)
+        yex(1, 1, 1)
+        unit(3, 1)
+        prod(10)
+        xint(1, 0, 0)
+        unit(3, 2)
+        xint(1, 0, 2)
+        dhg(3, 0)
+        ytr(1, 1, 2)
+        xint(1, 1, 1)
+        dhg(3, 1)
+        load_g(1, 0, 2)
+        ytr(1, 1, 3)
+        xint(1, 1, 3)
+        dhg(3, 2)
+        unit(3, 3)
+        yex(1, 1, 2)
+        qd(3, 0)
+        yex(1, 1, 3)
+        yq(1, 1, 0)
+        unit(4, 0)
+        xint(1, 1, 0)
+        dhg(3, 3)
+        load_g(1, 1, 2)
+        wtr(8)
+        xint(1, 1, 2)
+        dhg(4, 0)
+        wtr(9)
+        wex(8)
+        qd(3, 1)
+        unit(4, 1)
+        yq(1, 1, 1)
+        wex(9)
+        p2(3, 0)
+        xq(1, 0)
+        p2(3, 1)
+        dhg(4, 1)
+        pex(3, 0)
+        unit(4, 2)
+        wq(4)
+        pex(3, 1)
+        unit(4, 3)
+        qd(4, 0)
+        dhg(4, 2)
+        unit(5, 0)
+        dhg(4, 3)
+        unit(5, 1)
+        dhg(5, 0)
+        unit(5, 2)
+        dhg(5, 1)
+        unit(5, 3)
+        xq(1, 1)
+        unit(6, 0)
+        dhg(5, 2)
+        wtr(10)
+        qd(4, 1)
+        dhg(5, 3)
+        p2(4, 0)
+        wex(10)
+        dhg(6, 0)
+        p2(4, 1)
+        qd(5, 0)
+        unit(6, 1)
+        prod(11)
+        unit(6, 2)
+        dhg(6, 1)
+        wtr(11)
+        dhg(6, 2)
+        unit(6, 3)
+        qd(5, 1)
+        wex(11)
+        pex(4, 0)
+        p2(5, 0)
+        dhg(6, 3)
+        p2(5, 1)
+        pex(5, 0)
+        wq(5)
+        unit(8, 0)
+        pex(5, 1)
+        qd(6, 0)
+        unit(7, 0)
+        pex(4, 1)
+        unit(7, 1)
+        qd(6, 1)
+        dhg(7, 0)
+        p2(6, 0)
+        dhg(7, 1)
+        p2(6, 1)
+        dhg(8, 0)
+        unit(7, 2)
+        qd(7, 0)
+        unit(7, 3)
+        pex(6, 0)
+        dhg(7, 2)
+        unit(8, 1)
+        dhg(7, 3)
+        unit(8, 2)
+        dhg(8, 1)
+        unit(8, 3)
+        dhg(8, 2)
+        unit(9, 0)
+        qd(7, 1)
+        dhg(8, 3)
+        unit(9, 1)
+        dhg(9, 0)
+        p2(7, 0)
+        qd(8, 0)
+        p2(7, 1)
+        pex(6, 1)
+        pex(7, 0)
+        unit(9, 2)
+        dhg(9, 1)
+        pex(7, 1)
+        unit(9, 3)
+        dhg(9, 2)
+        unit(10, 0)
+        qd(8, 1)
+        dhg(9, 3)
+        p2(8, 0)
+        dhg(10, 0)
+        p2(8, 1)
+        qd(9, 0)
+        unit(10, 1)
+        qd(9, 1)
+        pex(8, 0)
+        p2(9, 0)
+        dhg(10, 1)
+        p2(9, 1)
+        pex(8, 1)
+        unit(10, 2)
+        qd(10, 0)
+        unit(10, 3)
+        pex(9, 0)
+        dhg(10, 2)
+        unit(11, 0)
+        dhg(10, 3)
+        unit(11, 1)
+        dhg(11, 0)
+        unit(11, 2)
+        dhg(11, 1)
+        unit(11, 3)
+        dhg(11, 2)
+        qd(10, 1)
+        dhg(11, 3)
+        p2(10, 0)
+        qd(11, 0)
+        tail_pass(0)
+        p2(10, 1)
+        pex(9, 1)
+        pex(10, 0)
+        qd(11, 1)
+        tail_pass(1)
+        pex(10, 1)
+        tail_out()

@@ -17,11 +17,12 @@ ADD = mybir.AluOpType.add
 COPY = mybir.ActivationFunctionType.Copy
 
 P = 128
-HALVES = 2
 PAIRS = 6
 PF = 256
 RUN = 4
-SEQ = ((0,0),(0,1),(0,2),(0,3),(1,0),(0,4),(1,1),(0,5),(1,2),(1,3),(1,4),(1,5))
+GROUPS = 4
+WARM = 1
+G_PAIRS = ()
 
 
 def tile_shard_weight_grad_s7_kernel(tc, x, dy, w2_bytes, w2_scale, g, c, out):
@@ -32,8 +33,8 @@ def tile_shard_weight_grad_s7_kernel(tc, x, dy, w2_bytes, w2_scale, g, c, out):
         psum = ctx.enter_context(tc.psum_pool(name="psum", bufs=2))
         ctx.enter_context(tc.manual_schedule())
 
-        scale_col = keep.tile([P, 8], F32, name="scale_col")
-        nc.scalar.dma_start(out=scale_col[:], in_=w2_scale.rearrange("o (p c) -> p (o c)", c=8))
+        scale_col = keep.tile([P, 2, 4], F32, name="scale_col")
+        nc.scalar.dma_start(out=scale_col[:], in_=w2_scale.rearrange("o (g p t) -> p (o g) t", p=P, t=4))
         c_bf = keep.tile([P, D], BF16, name="c_bf")
         nc.scalar.dma_start(out=c_bf[:], in_=c.partition_broadcast(P))
 
@@ -41,54 +42,38 @@ def tile_shard_weight_grad_s7_kernel(tc, x, dy, w2_bytes, w2_scale, g, c, out):
         w_view = w2_bytes.rearrange("(j b p) n -> j p b n", b=2, p=P)
         out_view = out.rearrange("(h kt p) f -> h p kt f", kt=2, p=P)
 
+        def rows(t3, a):
+            return t3[a // 2].rearrange("(q p t) n -> q p t n", q=2, t=4)[a % 2]
+
         def load_w(j):
             w_raw[j] = work.tile([P, 2, N], U8, name="w_raw", bufs=PAIRS)
             nc.sync.dma_start(out=w_raw[j][:], in_=w_view[j])
 
-        def load_y(dd, q, tp):
-            y_raw[dd, q, tp] = work.tile([P, 2, N], BF16, name="y_raw", bufs=8, align_bytes=64)
-            nc.sync.dma_start(
-                out=y_raw[dd, q, tp][:],
-                in_=dy[dd].rearrange("(q p t) n -> q p t n", q=2, t=4)[q][:, 2 * tp : 2 * tp + 2, :],
-            )
+        def load_y(a, tp):
+            y_raw[a, tp] = work.tile([P, 2, N], BF16, name="y_raw", bufs=6, align_bytes=64)
+            nc.sync.dma_start(out=y_raw[a, tp][:], in_=rows(dy, a)[:, 2 * tp : 2 * tp + 2, :])
 
-        def load_x(dd, q):
-            x_raw[dd, q] = work.tile([P, 4, K], BF16, name="x_raw", bufs=4, align_bytes=64)
-            nc.sync.dma_start(out=x_raw[dd, q][:], in_=x[dd].rearrange("(q p t) k -> q p t k", q=2, t=4)[q])
+        def load_x(a):
+            x_raw[a] = work.tile([P, 4, K], BF16, name="x_raw", bufs=4, align_bytes=64)
+            nc.sync.dma_start(out=x_raw[a][:], in_=rows(x, a))
 
-        def load_g(dd, q, ch):
-            g_raw[dd, q, ch] = work.tile([P, 4, 512], BF16, name="g_raw", bufs=8, align_bytes=64)
-            nc.sync.dma_start(
-                out=g_raw[dd, q, ch][:],
-                in_=g[dd].rearrange("(q p t) f -> q p t f", q=2, t=4)[q][:, :, 512 * ch : 512 * (ch + 1)],
-            )
+        def load_g(a, ch):
+            g_raw[a, ch] = work.tile([P, 4, 512], BF16, name="g_raw", bufs=8, align_bytes=64)
+            nc.sync.dma_start(out=g_raw[a, ch][:], in_=rows(g, a)[:, :, 512 * ch : 512 * (ch + 1)])
 
-        load_y(0, 0, 0)
+        load_y(0, 0)
         load_w(0)
-        load_y(0, 0, 1)
+        load_y(0, 1)
         load_w(1)
-        load_y(0, 1, 0)
+        load_y(1, 0)
+        load_y(1, 1)
+        load_g(0, 0)
+        load_x(0)
+        load_y(2, 0)
+        load_y(2, 1)
         load_w(2)
-        load_y(0, 1, 1)
-        load_g(0, 0, 0)
-        load_x(0, 0)
-        load_g(0, 1, 0)
-        load_x(0, 1)
-        load_w(3)
-        load_g(0, 0, 1)
-        load_g(0, 1, 1)
-        load_y(1, 0, 0)
-        load_y(1, 0, 1)
-        load_y(1, 1, 0)
-        load_y(1, 1, 1)
-        load_w(4)
-        load_x(1, 0)
-        load_g(1, 0, 0)
-        load_x(1, 1)
-        load_g(1, 1, 0)
-        load_g(0, 0, 2)
-        load_w(5)
-        load_g(0, 1, 2)
+        load_g(1, 0)
+        load_x(1)
 
         ident = keep.tile([P, P], F32, name="ident", align_bytes=64)
         make_identity(nc, ident[:])
@@ -97,39 +82,46 @@ def tile_shard_weight_grad_s7_kernel(tc, x, dy, w2_bytes, w2_scale, g, c, out):
 
         def warm(n):
             for i in range(n):
-                ps = psum.tile([P, 512], F32, name="p2", bufs=3)
+                ps = psum.tile([P, 512], F32, name="side", bufs=5)
                 nc.tensor.matmul(ps[:], lhsT=zeros[:, 0:P], rhs=zeros[:], start=True, stop=True)
 
-        warm(4)
-        scale_all = keep.tile([P, P, 8], F32, name="scale_all", align_bytes=64)
-        for h in range(2):
-            ps = psum.tile([P, 4, P], F32, name="tr", bufs=2)
-            for cc in range(4):
-                col = 4 * h + cc
-                nc.tensor.transpose(ps[:, cc, :], scale_col[:, col : col + 1].to_broadcast([P, P]), ident[:])
-            view = ps[:].rearrange("p c j -> p j c")
-            if h == 0:
-                nc.scalar.copy(out=scale_all[:, :, 0:4], in_=view)
-            else:
-                nc.vector.tensor_copy(out=scale_all[:, :, 4:8], in_=view)
+        warm(4 * WARM)
         c_all = keep.tile([P, D], F32, name="c_all")
         nc.scalar.copy(out=c_all[:], in_=c_bf[:])
+        scale_all = keep.tile([P, 2, P, 4], F32, name="scale_all", align_bytes=64)
+        for gi in range(2):
+            ps = psum.tile([P, 4, P], F32, name="unit", bufs=3)
+            for t in range(4):
+                nc.tensor.transpose(ps[:, t, :], scale_col[:, gi, t : t + 1].to_broadcast([P, P]), ident[:])
+            view = ps[:].rearrange("p t j -> p j t")
+            if gi == 0:
+                nc.scalar.copy(out=scale_all[:, 0], in_=view)
+            else:
+                nc.vector.tensor_copy(out=scale_all[:, 1], in_=view)
 
-        wb, gw, w_codes, w_scales = {}, {}, {}, {}
+        wb, gw, planes, w_codes, w_scales = {}, {}, {}, {}, {}
         gy, y_codes, y_scales = {}, {}, {}
         x_codes, x_scales, gx = {}, {}, {}
         bank = {}
         dh, d_codes, d_scales = {}, {}, {}
         acc = {}
 
+        units = [(a, b) for a in range(GROUPS) for b in range(4)]
+        units = units + [(a, 2 * j + i) for j in range(2, PAIRS) for a in range(GROUPS) for i in range(2)]
+        where = {u: n for n, u in enumerate(units)}
+
         def prod(b):
-            wb[b] = work.tile([P, N], BF16, name="wb", bufs=8, align_bytes=64)
+            wb[b] = work.tile([P, N], BF16, name="wb", bufs=4, align_bytes=64)
             nc.vector.tensor_tensor(
                 out=wb[b][:],
                 in0=w_raw[b // 2][:, b % 2, :].bitcast(FP8),
-                in1=scale_all[:].rearrange("p j c -> p (j c)"),
+                in1=scale_all[:].rearrange("p g j t -> p (g j t)"),
                 op=MULT,
             )
+
+        def widen(b):
+            wb[b] = work.tile([P, N], BF16, name="wb", bufs=4, align_bytes=64)
+            nc.scalar.copy(out=wb[b][:], in_=w_raw[b // 2][:, b % 2, :].bitcast(FP8))
 
         def word_transposes(words, ps):
             for gi in range(2):
@@ -137,441 +129,344 @@ def tile_shard_weight_grad_s7_kernel(tc, x, dy, w2_bytes, w2_scale, g, c, out):
                     nc.tensor.transpose(ps[:, gi, u, :], words[:, 256 * gi + u : 256 * (gi + 1) : 2], ident[:])
 
         def wtr(b):
-            ps = psum.tile([P, 2, 2, P], F32, name="tr", bufs=2)
+            ps = psum.tile([P, 2, 2, P], F32, name="side", bufs=5)
             word_transposes(wb[b][:].bitcast(F32), ps)
             bank["w", b] = ps
 
         def wex(b):
             j = b // 2
             if j not in gw:
-                gw[j] = work.tile([P, 2, 2, P, 4], BF16, name="gw", bufs=3, align_bytes=64)
-            dst = gw[j][:, b % 2].rearrange("p g f t -> p (g f t)").bitcast(F32)
+                gw[j] = work.tile([P, 2, 2, P, 2], F32, name="gw", bufs=2, align_bytes=64)
+            nc.scalar.copy(out=gw[j][:, :, b % 2], in_=bank["w", b][:].rearrange("p g u f -> p g f u"))
+
+        def wtr_raw(j, gi):
+            ps = psum.tile([P, 2, 2, P], F32, name="side", bufs=5)
+            for u in range(2):
+                for i in range(2):
+                    words = wb[2 * j + i][:].bitcast(F32)
+                    nc.tensor.transpose(ps[:, u, i, :], words[:, 256 * gi + u : 256 * (gi + 1) : 2], ident[:])
+            bank["r", j, gi] = ps
+
+        def wscale(j, gi):
+            planes[j, gi] = work.tile([P, 4, PF], BF16, name="planes", bufs=2, align_bytes=64)
+            for t in range(4):
+                u, e = divmod(t, 2)
+                halves = bank["r", j, gi][:, u].rearrange("p i f -> p (i f)").bitcast(BF16)
+                nc.scalar.activation(
+                    out=planes[j, gi][:, t, :], in_=halves[:, e : 2 * PF : 2], func=COPY, scale=scale_col[:, gi, t : t + 1]
+                )
+
+        def wint(j, gi):
+            if j not in gw:
+                gw[j] = work.tile([P, 2, 2, P, 2], F32, name="gw", bufs=2, align_bytes=64)
+            dst = gw[j][:, gi].rearrange("p b f u -> p (b f u)").bitcast(BF16)
             nc.scalar.copy(
-                out=dst.rearrange("p (g f u) -> p g f u", g=2, u=2),
-                in_=bank["w", b][:].rearrange("p g u f -> p g f u"),
+                out=dst.rearrange("p (c i t) -> p c t i", i=RUN, t=4),
+                in_=planes[j, gi][:].rearrange("p t (c i) -> p c t i", i=RUN),
             )
 
         def wq(j):
             w_codes[j] = work.tile([P, 2, 2, P], U32, name="w_codes", bufs=PAIRS, align_bytes=64)
             w_scales[j] = work.tile([P, 2, 2, P], U8, name="w_scales", bufs=PAIRS, align_bytes=64)
             nc.vector.quantize_mx(
-                out=w_codes[j][:].rearrange("p b g f -> p (b g f)").bitcast(FP8X4),
-                scales=w_scales[j][:].rearrange("p b g f -> p (b g f)"),
-                in_=gw[j][:].rearrange("p b g f t -> p (b g f t)"),
+                out=w_codes[j][:].rearrange("p g b f -> p (g b f)").bitcast(FP8X4),
+                scales=w_scales[j][:].rearrange("p g b f -> p (g b f)"),
+                in_=gw[j][:].rearrange("p g b f u -> p (g b f u)").bitcast(BF16),
             )
 
-        def ytr(dd, q, t):
-            ps = psum.tile([P, 2, 2, P], F32, name="tr", bufs=2)
-            word_transposes(y_raw[dd, q, t // 2][:, t % 2, :].bitcast(F32), ps)
-            bank["y", dd, q, t] = ps
+        def ytr(a, t):
+            ps = psum.tile([P, 2, 2, P], F32, name="side", bufs=5)
+            word_transposes(y_raw[a, t // 2][:, t % 2, :].bitcast(F32), ps)
+            bank["y", a, t] = ps
 
-        def yex(dd, q, t):
+        def yex(a, t):
             tp = t // 2
-            if (dd, q, tp) not in gy:
-                gy[dd, q, tp] = work.tile([P, 2, 2, P, 4], BF16, name="gy", bufs=4, align_bytes=64)
-            dst = gy[dd, q, tp][:, t % 2].rearrange("p g m t -> p (g m t)").bitcast(F32)
-            nc.scalar.copy(
-                out=dst.rearrange("p (g m u) -> p g m u", g=2, u=2),
-                in_=bank["y", dd, q, t][:].rearrange("p g u m -> p g m u"),
-            )
+            if (a, tp) not in gy:
+                gy[a, tp] = work.tile([P, 2, 2, P, 2], F32, name="gy", bufs=3, align_bytes=64)
+            nc.scalar.copy(out=gy[a, tp][:, t % 2], in_=bank["y", a, t][:].rearrange("p g u m -> p g m u"))
 
-        def yq(dd, q, tp):
-            y_codes[dd, q, tp] = work.tile([P, 2, 2, P], U32, name="y_codes", bufs=8, align_bytes=64)
-            y_scales[dd, q, tp] = work.tile([P, 2, 2, P], U8, name="y_scales", bufs=8, align_bytes=64)
+        def yq(a, tp):
+            y_codes[a, tp] = work.tile([P, 2, 2, P], U32, name="y_codes", bufs=8, align_bytes=64)
+            y_scales[a, tp] = work.tile([P, 2, 2, P], U8, name="y_scales", bufs=8, align_bytes=64)
             nc.vector.quantize_mx(
-                out=y_codes[dd, q, tp][:].rearrange("p b g f -> p (b g f)").bitcast(FP8X4),
-                scales=y_scales[dd, q, tp][:].rearrange("p b g f -> p (b g f)"),
-                in_=gy[dd, q, tp][:].rearrange("p b g f t -> p (b g f t)"),
+                out=y_codes[a, tp][:].rearrange("p b g f -> p (b g f)").bitcast(FP8X4),
+                scales=y_scales[a, tp][:].rearrange("p b g f -> p (b g f)"),
+                in_=gy[a, tp][:].rearrange("p b g f u -> p (b g f u)").bitcast(BF16),
             )
 
-        def xint(dd, q, kq):
-            if (dd, q) not in gx:
-                gx[dd, q] = work.tile([P, K, 4], BF16, name="gx", bufs=2, align_bytes=64)
-            ks = slice(128 * kq, 128 * (kq + 1))
+        def xint(a, kh):
+            if a not in gx:
+                gx[a] = work.tile([P, K, 4], BF16, name="gx", bufs=2, align_bytes=64)
+            ks = slice(256 * kh, 256 * (kh + 1))
             nc.scalar.copy(
-                out=gx[dd, q][:, ks, :].rearrange("p (c i) t -> p c t i", i=RUN),
-                in_=x_raw[dd, q][:, :, ks].rearrange("p t (c i) -> p c t i", i=RUN),
+                out=gx[a][:, ks, :].rearrange("p (c i) t -> p c t i", i=RUN),
+                in_=x_raw[a][:, :, ks].rearrange("p t (c i) -> p c t i", i=RUN),
             )
 
-        def xq(dd, q):
-            x_codes[dd, q] = work.tile([P, K], U32, name="x_codes", bufs=4, align_bytes=64)
-            x_scales[dd, q] = work.tile([P, K], U8, name="x_scales", bufs=4, align_bytes=64)
+        def xq(a):
+            x_codes[a] = work.tile([P, K], U32, name="x_codes", bufs=4, align_bytes=64)
+            x_scales[a] = work.tile([P, K], U8, name="x_scales", bufs=4, align_bytes=64)
             nc.vector.quantize_mx(
-                out=x_codes[dd, q][:].bitcast(FP8X4),
-                scales=x_scales[dd, q][:],
-                in_=gx[dd, q][:].rearrange("p k t -> p (k t)"),
+                out=x_codes[a][:].bitcast(FP8X4),
+                scales=x_scales[a][:],
+                in_=gx[a][:].rearrange("p k t -> p (k t)"),
             )
 
-        def unit(s, i):
-            dd, j = SEQ[s]
-            q, b = divmod(i, 2)
+        def unit(n):
+            a, b = units[n]
             ps = psum.tile([P, 4, P], F32, name="unit", bufs=3)
             for t in range(4):
                 for gi in range(2):
                     nc.tensor.matmul_mx(
                         out=ps[:, t, :],
-                        lhsT=y_codes[dd, q, t // 2][:, t % 2, gi, :].bitcast(FP8X4),
-                        lhsT_scale=y_scales[dd, q, t // 2][:, t % 2, gi, :],
-                        rhs=w_codes[j][:, b, gi, :].bitcast(FP8X4),
-                        rhs_scale=w_scales[j][:, b, gi, :],
+                        lhsT=y_codes[a, t // 2][:, t % 2, gi, :].bitcast(FP8X4),
+                        lhsT_scale=y_scales[a, t // 2][:, t % 2, gi, :],
+                        rhs=w_codes[b // 2][:, gi, b % 2, :].bitcast(FP8X4),
+                        rhs_scale=w_scales[b // 2][:, gi, b % 2, :],
                         start=(gi == 0),
                         stop=(gi == 1),
                     )
-            bank["u", s, i] = ps
+            bank["u", n] = ps
 
-        def dhg(s, i):
-            dd, j = SEQ[s]
-            q, b = divmod(i, 2)
-            if (s, q) not in dh:
-                dh[s, q] = work.tile([P, PF, 4], BF16, name="dh", bufs=4, align_bytes=64)
-            f0 = PF * (j % 2) + P * b
+        def dhg(n):
+            a, b = units[n]
+            k, i = divmod(n, 4)
+            if k not in dh:
+                dh[k] = work.tile([P, 4 * P, 4], BF16, name="dh", bufs=3, align_bytes=64)
+            f0 = P * (b % 4)
             nc.vector.tensor_tensor(
-                out=dh[s, q][:, P * b : P * (b + 1), :].rearrange("p (c i) t -> p c t i", i=RUN),
-                in0=bank["u", s, i][:].rearrange("p t (c i) -> p c t i", i=RUN),
-                in1=g_raw[dd, q, j // 2][:, :, f0 : f0 + P].rearrange("p t (c i) -> p c t i", i=RUN),
+                out=dh[k][:, P * i : P * (i + 1), :].rearrange("p (c i) t -> p c t i", i=RUN),
+                in0=bank["u", n][:].rearrange("p t (c i) -> p c t i", i=RUN),
+                in1=g_raw[a, b // 4][:, :, f0 : f0 + P].rearrange("p t (c i) -> p c t i", i=RUN),
                 op=MULT,
             )
 
-        def qd(s, q):
-            d_codes[s, q] = work.tile([P, PF], U32, name="d_codes", bufs=4, align_bytes=64)
-            d_scales[s, q] = work.tile([P, PF], U8, name="d_scales", bufs=4, align_bytes=64)
+        def qd(k, f0=0, f1=4 * P):
+            if k not in d_codes:
+                d_codes[k] = work.tile([P, 4 * P], U32, name="d_codes", bufs=8, align_bytes=64)
+                d_scales[k] = work.tile([P, 4 * P], U8, name="d_scales", bufs=8, align_bytes=64)
             nc.vector.quantize_mx(
-                out=d_codes[s, q][:].bitcast(FP8X4),
-                scales=d_scales[s, q][:],
-                in_=dh[s, q][:].rearrange("p f t -> p (f t)"),
+                out=d_codes[k][:, f0:f1].bitcast(FP8X4),
+                scales=d_scales[k][:, f0:f1],
+                in_=dh[k][:, f0:f1, :].rearrange("p f t -> p (f t)"),
             )
 
-        def p2(s, h):
-            dd = SEQ[s][0]
-            ps = psum.tile([P, 2, PF], F32, name="p2", bufs=3)
+        def p2(dd, j, h):
+            ps = psum.tile([P, 2, PF], F32, name="side", bufs=5)
             for k2 in range(2):
                 kc = slice(P * (2 * h + k2), P * (2 * h + k2 + 1))
                 for q in range(2):
+                    a = 2 * dd + q
+                    k, i = divmod(where[a, 2 * j], 4)
+                    fs = slice(P * i, P * i + PF)
                     nc.tensor.matmul_mx(
                         out=ps[:, k2, :],
-                        lhsT=x_codes[dd, q][:, kc].bitcast(FP8X4),
-                        lhsT_scale=x_scales[dd, q][:, kc],
-                        rhs=d_codes[s, q][:].bitcast(FP8X4),
-                        rhs_scale=d_scales[s, q][:],
+                        lhsT=x_codes[a][:, kc].bitcast(FP8X4),
+                        lhsT_scale=x_scales[a][:, kc],
+                        rhs=d_codes[k][:, fs].bitcast(FP8X4),
+                        rhs_scale=d_scales[k][:, fs],
                         start=(q == 0),
                         stop=(q == 1),
                     )
-            bank["p", s, h] = ps
+            bank["p", dd, j, h] = ps
 
-        def pex(s, h):
-            dd, j = SEQ[s]
-            ps = bank["p", s, h]
+        def pex(dd, j, h):
+            ps = bank["p", dd, j, h]
             if dd == 0:
-                acc[j, h] = work.tile([P, 2, PF], F32, name="acc", bufs=12)
+                acc[j, h] = work.tile([P, 2, PF], F32, name="acc", bufs=8)
                 nc.scalar.activation(out=acc[j, h][:], in_=ps[:], func=COPY, scale=c_all[:, 0:1])
+                return
+            if j in G_PAIRS:
+                part = work.tile([P, 2, PF], F32, name="part", bufs=3)
+                nc.scalar.activation(out=part[:], in_=ps[:], func=COPY, scale=c_all[:, 1:2])
+                for k2 in range(2):
+                    nc.gpsimd.tensor_tensor(out=acc[j, h][:, k2], in0=acc[j, h][:, k2], in1=part[:, k2], op=ADD)
             else:
                 nc.vector.scalar_tensor_tensor(
                     out=acc[j, h][:], in0=ps[:], scalar=c_all[:, 1:2], in1=acc[j, h][:], op0=MULT, op1=ADD
                 )
-                nc.sync.dma_start(out=out_view[h][:, :, PF * j : PF * (j + 1)], in_=acc[j, h][:])
+            nc.sync.dma_start(out=out_view[h][:, :, PF * j : PF * (j + 1)], in_=acc[j, h][:])
 
         tail = {}
 
         def tail_pass(q):
-            s = 2 * PAIRS - 1
+            k = len(units) // 4 - 1
+            fs = slice(PF * q, PF * (q + 1))
             for kt in range(4):
                 if q == 0:
-                    tail[kt] = psum.tile([P, PF], F32, name=("tr", "unit")[kt // 2], bufs=(2, 3)[kt // 2])
+                    tail[kt] = psum.tile([P, PF], F32, name=("unit", "side")[kt // 2], bufs=(3, 5)[kt // 2])
                 kc = slice(P * kt, P * (kt + 1))
                 nc.tensor.matmul_mx(
                     out=tail[kt][:],
-                    lhsT=x_codes[1, q][:, kc].bitcast(FP8X4),
-                    lhsT_scale=x_scales[1, q][:, kc],
-                    rhs=d_codes[s, q][:].bitcast(FP8X4),
-                    rhs_scale=d_scales[s, q][:],
+                    lhsT=x_codes[2 + q][:, kc].bitcast(FP8X4),
+                    lhsT_scale=x_scales[2 + q][:, kc],
+                    rhs=d_codes[k][:, fs].bitcast(FP8X4),
+                    rhs_scale=d_scales[k][:, fs],
                     start=(q == 0),
                     stop=(q == 1),
                 )
 
-        def tail_out():
+        def tail_out(kt):
             j = PAIRS - 1
-            for kt in range(4):
-                total = acc[j, kt // 2][:, kt % 2, :]
-                nc.vector.scalar_tensor_tensor(
-                    out=total, in0=tail[kt][:], scalar=c_all[:, 1:2], in1=total, op0=MULT, op1=ADD
-                )
-                nc.sync.dma_start(out=out[P * kt : P * (kt + 1), PF * j : PF * (j + 1)], in_=total)
+            total = acc[j, kt // 2][:, kt % 2, :]
+            nc.vector.scalar_tensor_tensor(
+                out=total, in0=tail[kt][:], scalar=c_all[:, 1:2], in1=total, op0=MULT, op1=ADD
+            )
+            nc.sync.dma_start(out=out[P * kt : P * (kt + 1), PF * j : PF * (j + 1)], in_=total)
 
-        warm(1)
-        ytr(0, 0, 0)
-        ytr(0, 0, 1)
-        prod(0)
-        yex(0, 0, 0)
-        yex(0, 0, 1)
-        warm(1)
-        ytr(0, 0, 2)
-        prod(1)
-        wtr(0)
-        yex(0, 0, 2)
-        prod(2)
-        warm(1)
-        ytr(0, 0, 3)
-        wex(0)
-        prod(3)
-        wtr(1)
-        yex(0, 0, 3)
-        warm(1)
-        ytr(0, 1, 0)
-        wex(1)
-        yq(0, 0, 0)
-        ytr(0, 1, 1)
+        ytr(0, 0)
+        yex(0, 0)
+        for b in range(4):
+            prod(b)
+            a, t = divmod(b + 1, 4)
+            ytr(a, t)
+            yex(a, t)
+            warm(WARM)
+            wtr(b)
+            wex(b)
+        yq(0, 0)
+        yq(0, 1)
+        for t in range(1, 4):
+            ytr(1, t)
+            yex(1, t)
         wq(0)
-        yex(0, 1, 0)
-        yq(0, 0, 1)
-        warm(1)
-        ytr(0, 1, 2)
-        yex(0, 1, 1)
-        prod(4)
-        ytr(0, 1, 3)
-        yex(0, 1, 2)
-        unit(0, 0)
-        yq(0, 1, 0)
-        yex(0, 1, 3)
-        wtr(2)
-        prod(5)
-        xint(0, 0, 0)
-        wtr(3)
-        xint(0, 0, 2)
-        unit(0, 1)
-        dhg(0, 0)
-        wex(2)
-        yq(0, 1, 1)
-        wex(3)
-        wtr(4)
-        dhg(0, 1)
-        xint(0, 0, 1)
-        wtr(5)
         wq(1)
-        xint(0, 0, 3)
-        unit(0, 2)
-        qd(0, 0)
-        xint(0, 1, 0)
-        xq(0, 0)
-        unit(0, 3)
-        xint(0, 1, 2)
-        dhg(0, 2)
-        unit(1, 0)
-        xint(0, 1, 1)
-        dhg(0, 3)
-        unit(1, 1)
-        xint(0, 1, 3)
-        dhg(1, 0)
-        unit(1, 2)
-        wex(4)
-        dhg(1, 1)
-        load_g(1, 0, 1)
-        unit(1, 3)
-        wex(5)
-        xq(0, 1)
-        ytr(1, 0, 0)
-        dhg(1, 2)
-        ytr(1, 0, 1)
-        qd(0, 1)
-        yex(1, 0, 0)
-        dhg(1, 3)
-        load_g(1, 1, 1)
-        p2(0, 0)
-        yex(1, 0, 1)
+        yq(1, 0)
+        for e in ((load_y, 3, 0), (load_y, 3, 1), (load_g, 2, 0), (load_w, 3), (load_g, 3, 0), (load_x, 2), (load_x, 3), (load_g, 0, 1), (load_g, 1, 1), (load_w, 4), (load_g, 2, 1), (load_g, 3, 1), (load_w, 5)):
+            e[0](*e[1:])
+
+        def turn_y(a):
+            for t in range(4):
+                ytr(a, t)
+                yex(a, t)
+
+        def turn_w(j):
+            for b in (2 * j, 2 * j + 1):
+                wtr(b)
+                wex(b)
+
+        def turn_raw(j):
+            for gi in range(2):
+                wtr_raw(j, gi)
+                wscale(j, gi)
+
+        def x_all(a):
+            xint(a, 0)
+            xint(a, 1)
+
+        def widen2(j):
+            widen(2 * j)
+            widen(2 * j + 1)
+
+        def wint2(j):
+            wint(j, 0)
+            wint(j, 1)
+
+        def second(dd, j, h):
+            p2(dd, j, h)
+            pex(dd, j, h)
+
+        def quad(k):
+            for n in range(4 * k, 4 * k + 4):
+                unit(n)
+                dhg(n)
+
+        quad(0)
+        yq(1, 1)
+        prod(4)
+        qd(0)
+        x_all(0)
+        turn_y(2)
+        xq(0)
+        load_g(0, 2)
+        quad(1)
+        yq(2, 0)
+        yq(2, 1)
+        qd(1)
+        prod(5)
+        x_all(1)
+        turn_y(3)
+        load_g(1, 2)
+        quad(2)
+        yq(3, 0)
+        yq(3, 1)
+        qd(2)
+        widen2(3)
+        turn_w(2)
+        turn_raw(3)
         wq(2)
-        p2(0, 1)
-        qd(1, 0)
-        pex(0, 0)
-        unit(2, 0)
-        prod(6)
-        pex(0, 1)
-        unit(2, 1)
-        dhg(2, 0)
-        wtr(6)
-        dhg(2, 1)
-        ytr(1, 0, 2)
-        prod(7)
-        wex(6)
-        unit(2, 2)
-        yex(1, 0, 2)
-        unit(2, 3)
-        qd(1, 1)
-        xint(1, 0, 1)
-        dhg(2, 2)
-        p2(1, 0)
-        xint(1, 0, 3)
-        dhg(2, 3)
-        p2(1, 1)
-        pex(1, 0)
-        qd(2, 0)
-        wtr(7)
-        qd(2, 1)
-        pex(1, 1)
-        prod(8)
-        ytr(1, 0, 3)
-        wex(7)
-        p2(2, 0)
-        yex(1, 0, 3)
-        prod(9)
-        p2(2, 1)
-        pex(2, 0)
-        ytr(1, 1, 0)
+        load_g(2, 2)
+        quad(3)
+        xq(1)
+        qd(3)
+        x_all(2)
+        x_all(3)
+        widen2(4)
+        load_g(3, 2)
+        quad(4)
+        xq(2)
+        qd(4)
+        xq(3)
+        wint2(3)
+        second(0, 0, 0)
+        second(0, 0, 1)
+        quad(5)
+        qd(5)
         wq(3)
-        pex(2, 1)
-        ytr(1, 1, 1)
-        yq(1, 0, 0)
-        yex(1, 1, 0)
-        unit(3, 0)
-        yq(1, 0, 1)
-        yex(1, 1, 1)
-        unit(3, 1)
-        prod(10)
-        xint(1, 0, 0)
-        unit(3, 2)
-        xint(1, 0, 2)
-        dhg(3, 0)
-        ytr(1, 1, 2)
-        xint(1, 1, 1)
-        dhg(3, 1)
-        load_g(1, 0, 2)
-        ytr(1, 1, 3)
-        xint(1, 1, 3)
-        dhg(3, 2)
-        unit(3, 3)
-        yex(1, 1, 2)
-        qd(3, 0)
-        yex(1, 1, 3)
-        yq(1, 1, 0)
-        unit(4, 0)
-        xint(1, 1, 0)
-        dhg(3, 3)
-        load_g(1, 1, 2)
-        wtr(8)
-        xint(1, 1, 2)
-        dhg(4, 0)
-        wtr(9)
-        wex(8)
-        qd(3, 1)
-        unit(4, 1)
-        yq(1, 1, 1)
-        wex(9)
-        p2(3, 0)
-        xq(1, 0)
-        p2(3, 1)
-        dhg(4, 1)
-        pex(3, 0)
-        unit(4, 2)
+        turn_raw(4)
+        second(1, 0, 0)
+        second(1, 0, 1)
+        quad(6)
+        qd(6)
+        wint(4, 0)
+        second(0, 1, 0)
+        second(0, 1, 1)
+        second(1, 1, 0)
+        second(1, 1, 1)
+        wint(4, 1)
+        widen2(5)
+        quad(7)
         wq(4)
-        pex(3, 1)
-        unit(4, 3)
-        qd(4, 0)
-        dhg(4, 2)
-        unit(5, 0)
-        dhg(4, 3)
-        unit(5, 1)
-        dhg(5, 0)
-        unit(5, 2)
-        dhg(5, 1)
-        unit(5, 3)
-        xq(1, 1)
-        unit(6, 0)
-        dhg(5, 2)
-        wtr(10)
-        qd(4, 1)
-        dhg(5, 3)
-        p2(4, 0)
-        wex(10)
-        dhg(6, 0)
-        p2(4, 1)
-        qd(5, 0)
-        unit(6, 1)
-        prod(11)
-        unit(6, 2)
-        dhg(6, 1)
-        wtr(11)
-        dhg(6, 2)
-        unit(6, 3)
-        qd(5, 1)
-        wex(11)
-        pex(4, 0)
-        p2(5, 0)
-        dhg(6, 3)
-        p2(5, 1)
-        pex(5, 0)
+        qd(7)
+        second(0, 2, 0)
+        second(0, 2, 1)
+        turn_raw(5)
+        quad(8)
+        second(1, 2, 0)
+        qd(8)
+        second(1, 2, 1)
+        wint(5, 0)
+        second(0, 3, 0)
+        second(0, 3, 1)
+        wint(5, 1)
+        quad(9)
         wq(5)
-        unit(8, 0)
-        pex(5, 1)
-        qd(6, 0)
-        unit(7, 0)
-        pex(4, 1)
-        unit(7, 1)
-        qd(6, 1)
-        dhg(7, 0)
-        p2(6, 0)
-        dhg(7, 1)
-        p2(6, 1)
-        dhg(8, 0)
-        unit(7, 2)
-        qd(7, 0)
-        unit(7, 3)
-        pex(6, 0)
-        dhg(7, 2)
-        unit(8, 1)
-        dhg(7, 3)
-        unit(8, 2)
-        dhg(8, 1)
-        unit(8, 3)
-        dhg(8, 2)
-        unit(9, 0)
-        qd(7, 1)
-        dhg(8, 3)
-        unit(9, 1)
-        dhg(9, 0)
-        p2(7, 0)
-        qd(8, 0)
-        p2(7, 1)
-        pex(6, 1)
-        pex(7, 0)
-        unit(9, 2)
-        dhg(9, 1)
-        pex(7, 1)
-        unit(9, 3)
-        dhg(9, 2)
-        unit(10, 0)
-        qd(8, 1)
-        dhg(9, 3)
-        p2(8, 0)
-        dhg(10, 0)
-        p2(8, 1)
-        qd(9, 0)
-        unit(10, 1)
-        qd(9, 1)
-        pex(8, 0)
-        p2(9, 0)
-        dhg(10, 1)
-        p2(9, 1)
-        pex(8, 1)
-        unit(10, 2)
-        qd(10, 0)
-        unit(10, 3)
-        pex(9, 0)
-        dhg(10, 2)
-        unit(11, 0)
-        dhg(10, 3)
-        unit(11, 1)
-        dhg(11, 0)
-        unit(11, 2)
-        dhg(11, 1)
-        unit(11, 3)
-        dhg(11, 2)
-        qd(10, 1)
-        dhg(11, 3)
-        p2(10, 0)
-        qd(11, 0)
+        second(1, 3, 0)
+        qd(9)
+        second(1, 3, 1)
+        second(0, 4, 0)
+        second(0, 4, 1)
+        quad(10)
+        qd(10)
+        p2(1, 4, 0)
+        p2(1, 4, 1)
+        unit(44)
+        dhg(44)
+        unit(45)
+        dhg(45)
+        unit(46)
+        dhg(46)
+        qd(11, 0, 256)
+        unit(47)
+        dhg(47)
+        pex(1, 4, 0)
+        second(0, 5, 0)
+        second(0, 5, 1)
         tail_pass(0)
-        p2(10, 1)
-        pex(9, 1)
-        pex(10, 0)
-        qd(11, 1)
+        qd(11, 256, 512)
+        pex(1, 4, 1)
         tail_pass(1)
-        pex(10, 1)
-        tail_out()
+        tail_out(0)
+        tail_out(1)
+        tail_out(2)
+        tail_out(3)

@@ -21,7 +21,7 @@ PAIRS = 6
 PF = 256
 RUN = 4
 GROUPS = 4
-WARM = 1
+XG = 384
 G_PAIRS = ()
 
 
@@ -34,7 +34,7 @@ def tile_shard_weight_grad_s7_kernel(tc, x, dy, w2_bytes, w2_scale, g, c, out):
         ctx.enter_context(tc.manual_schedule())
 
         scale_col = keep.tile([P, 2, 4], F32, name="scale_col")
-        nc.scalar.dma_start(out=scale_col[:], in_=w2_scale.rearrange("o (g p t) -> p (o g) t", p=P, t=4))
+        nc.sync.dma_start(out=scale_col[:], in_=w2_scale.rearrange("o (g p t) -> p (o g) t", p=P, t=4))
         c_bf = keep.tile([P, D], BF16, name="c_bf")
         nc.scalar.dma_start(out=c_bf[:], in_=c.partition_broadcast(P))
 
@@ -49,6 +49,11 @@ def tile_shard_weight_grad_s7_kernel(tc, x, dy, w2_bytes, w2_scale, g, c, out):
             w_raw[j] = work.tile([P, 2, N], U8, name="w_raw", bufs=PAIRS)
             nc.sync.dma_start(out=w_raw[j][:], in_=w_view[j])
 
+        def load_strip(i):
+            if i == 0:
+                w_raw[0] = work.tile([P, 2, N], U8, name="w_raw", bufs=PAIRS)
+            nc.sync.dma_start(out=w_raw[0][:, i, :], in_=w_view[0][:, i, :])
+
         def load_y(a, tp):
             y_raw[a, tp] = work.tile([P, 2, N], BF16, name="y_raw", bufs=6, align_bytes=64)
             nc.sync.dma_start(out=y_raw[a, tp][:], in_=rows(dy, a)[:, 2 * tp : 2 * tp + 2, :])
@@ -61,43 +66,31 @@ def tile_shard_weight_grad_s7_kernel(tc, x, dy, w2_bytes, w2_scale, g, c, out):
             g_raw[a, ch] = work.tile([P, 4, 512], BF16, name="g_raw", bufs=8, align_bytes=64)
             nc.sync.dma_start(out=g_raw[a, ch][:], in_=rows(g, a)[:, :, 512 * ch : 512 * (ch + 1)])
 
+        load_strip(0)
         load_y(0, 0)
-        load_w(0)
+        load_strip(1)
         load_y(0, 1)
         load_w(1)
         load_y(1, 0)
         load_y(1, 1)
+        load_w(2)
         load_g(0, 0)
         load_x(0)
+        load_w(3)
         load_y(2, 0)
         load_y(2, 1)
-        load_w(2)
         load_g(1, 0)
         load_x(1)
 
         ident = keep.tile([P, P], F32, name="ident", align_bytes=64)
         make_identity(nc, ident[:])
-        zeros = keep.tile([P, 512], BF16, name="zeros", align_bytes=64)
-        nc.vector.memset(zeros[:], 0.0)
-
-        def warm(n):
-            for i in range(n):
-                ps = psum.tile([P, 512], F32, name="side", bufs=5)
-                nc.tensor.matmul(ps[:], lhsT=zeros[:, 0:P], rhs=zeros[:], start=True, stop=True)
-
-        warm(4 * WARM)
         c_all = keep.tile([P, D], F32, name="c_all")
-        nc.scalar.copy(out=c_all[:], in_=c_bf[:])
         scale_all = keep.tile([P, 2, P, 4], F32, name="scale_all", align_bytes=64)
         for gi in range(2):
             ps = psum.tile([P, 4, P], F32, name="unit", bufs=3)
             for t in range(4):
                 nc.tensor.transpose(ps[:, t, :], scale_col[:, gi, t : t + 1].to_broadcast([P, P]), ident[:])
-            view = ps[:].rearrange("p t j -> p j t")
-            if gi == 0:
-                nc.scalar.copy(out=scale_all[:, 0], in_=view)
-            else:
-                nc.vector.tensor_copy(out=scale_all[:, 1], in_=view)
+            nc.scalar.copy(out=scale_all[:, gi], in_=ps[:].rearrange("p t j -> p j t"))
 
         wb, gw, planes, w_codes, w_scales = {}, {}, {}, {}, {}
         gy, y_codes, y_scales = {}, {}, {}
@@ -110,17 +103,19 @@ def tile_shard_weight_grad_s7_kernel(tc, x, dy, w2_bytes, w2_scale, g, c, out):
         units = units + [(a, 2 * j + i) for j in range(2, PAIRS) for a in range(GROUPS) for i in range(2)]
         where = {u: n for n, u in enumerate(units)}
 
-        def prod(b):
-            wb[b] = work.tile([P, N], BF16, name="wb", bufs=4, align_bytes=64)
-            nc.vector.tensor_tensor(
-                out=wb[b][:],
-                in0=w_raw[b // 2][:, b % 2, :].bitcast(FP8),
-                in1=scale_all[:].rearrange("p g j t -> p (g j t)"),
-                op=MULT,
-            )
+        def prod(b, parts=1):
+            wb[b] = work.tile([P, N], BF16, name="wb", bufs=6, align_bytes=64)
+            for i in range(parts):
+                ns = slice(N // parts * i, N // parts * (i + 1))
+                nc.vector.tensor_tensor(
+                    out=wb[b][:, ns],
+                    in0=w_raw[b // 2][:, b % 2, ns].bitcast(FP8),
+                    in1=scale_all[:].rearrange("p g j t -> p (g j t)")[:, ns],
+                    op=MULT,
+                )
 
         def widen(b):
-            wb[b] = work.tile([P, N], BF16, name="wb", bufs=4, align_bytes=64)
+            wb[b] = work.tile([P, N], BF16, name="wb", bufs=6, align_bytes=64)
             nc.scalar.copy(out=wb[b][:], in_=w_raw[b // 2][:, b % 2, :].bitcast(FP8))
 
         def word_transposes(words, ps):
@@ -194,13 +189,21 @@ def tile_shard_weight_grad_s7_kernel(tc, x, dy, w2_bytes, w2_scale, g, c, out):
                 in_=gy[a, tp][:].rearrange("p b g f u -> p (b g f u)").bitcast(BF16),
             )
 
-        def xint(a, kh):
-            if a not in gx:
-                gx[a] = work.tile([P, K, 4], BF16, name="gx", bufs=2, align_bytes=64)
-            ks = slice(256 * kh, 256 * (kh + 1))
+        def xg(a):
+            gx[a] = work.tile([P, K, 4], BF16, name="dh%d" % (a % 2), bufs=1, align_bytes=64)
+            nc.gpsimd.tensor_scalar(
+                out=gx[a][:, 0:XG, :],
+                in0=x_raw[a][:, :, 0:XG].rearrange("p t k -> p k t"),
+                scalar1=1.0,
+                scalar2=0.0,
+                op0=MULT,
+                op1=ADD,
+            )
+
+        def xint(a):
             nc.scalar.copy(
-                out=gx[a][:, ks, :].rearrange("p (c i) t -> p c t i", i=RUN),
-                in_=x_raw[a][:, :, ks].rearrange("p t (c i) -> p c t i", i=RUN),
+                out=gx[a][:, XG:K, :].rearrange("p (c i) t -> p c t i", i=RUN),
+                in_=x_raw[a][:, :, XG:K].rearrange("p t (c i) -> p c t i", i=RUN),
             )
 
         def xq(a):
@@ -232,7 +235,7 @@ def tile_shard_weight_grad_s7_kernel(tc, x, dy, w2_bytes, w2_scale, g, c, out):
             a, b = units[n]
             k, i = divmod(n, 4)
             if k not in dh:
-                dh[k] = work.tile([P, 4 * P, 4], BF16, name="dh", bufs=3, align_bytes=64)
+                dh[k] = work.tile([P, 4 * P, 4], BF16, name="dh%d" % (k % 2), bufs=1, align_bytes=64)
             f0 = P * (b % 4)
             nc.vector.tensor_tensor(
                 out=dh[k][:, P * i : P * (i + 1), :].rearrange("p (c i) t -> p c t i", i=RUN),
@@ -279,8 +282,7 @@ def tile_shard_weight_grad_s7_kernel(tc, x, dy, w2_bytes, w2_scale, g, c, out):
             if j in G_PAIRS:
                 part = work.tile([P, 2, PF], F32, name="part", bufs=3)
                 nc.scalar.activation(out=part[:], in_=ps[:], func=COPY, scale=c_all[:, 1:2])
-                for k2 in range(2):
-                    nc.gpsimd.tensor_tensor(out=acc[j, h][:, k2], in0=acc[j, h][:, k2], in1=part[:, k2], op=ADD)
+                nc.gpsimd.tensor_tensor(out=acc[j, h][:], in0=acc[j, h][:], in1=part[:], op=ADD)
             else:
                 nc.vector.scalar_tensor_tensor(
                     out=acc[j, h][:], in0=ps[:], scalar=c_all[:, 1:2], in1=acc[j, h][:], op0=MULT, op1=ADD
@@ -317,11 +319,10 @@ def tile_shard_weight_grad_s7_kernel(tc, x, dy, w2_bytes, w2_scale, g, c, out):
         ytr(0, 0)
         yex(0, 0)
         for b in range(4):
-            prod(b)
+            prod(b, 2 if b == 0 else 1)
             a, t = divmod(b + 1, 4)
             ytr(a, t)
             yex(a, t)
-            warm(WARM)
             wtr(b)
             wex(b)
         yq(0, 0)
@@ -331,8 +332,10 @@ def tile_shard_weight_grad_s7_kernel(tc, x, dy, w2_bytes, w2_scale, g, c, out):
             yex(1, t)
         wq(0)
         wq(1)
+        prod(4)
         yq(1, 0)
-        for e in ((load_y, 3, 0), (load_y, 3, 1), (load_g, 2, 0), (load_w, 3), (load_g, 3, 0), (load_x, 2), (load_x, 3), (load_g, 0, 1), (load_g, 1, 1), (load_w, 4), (load_g, 2, 1), (load_g, 3, 1), (load_w, 5)):
+        nc.scalar.copy(out=c_all[:], in_=c_bf[:])
+        for e in ((load_y, 3, 0), (load_y, 3, 1), (load_g, 2, 0), (load_w, 4), (load_x, 2), (load_g, 3, 0), (load_x, 3), (load_g, 0, 1), (load_g, 1, 1), (load_g, 2, 1), (load_g, 3, 1), (load_w, 5)):
             e[0](*e[1:])
 
         def turn_y(a):
@@ -373,77 +376,79 @@ def tile_shard_weight_grad_s7_kernel(tc, x, dy, w2_bytes, w2_scale, g, c, out):
 
         quad(0)
         yq(1, 1)
-        prod(4)
+        prod(5)
         qd(0)
-        x_all(0)
+        xg(0)
+        widen2(3)
         turn_y(2)
-        xq(0)
+        xint(0)
         load_g(0, 2)
         quad(1)
         yq(2, 0)
         yq(2, 1)
+        xq(0)
         qd(1)
-        prod(5)
-        x_all(1)
+        xg(1)
         turn_y(3)
+        xint(1)
         load_g(1, 2)
         quad(2)
         yq(3, 0)
         yq(3, 1)
+        xq(1)
         qd(2)
-        widen2(3)
+        xg(2)
+        widen2(4)
         turn_w(2)
         turn_raw(3)
-        wq(2)
+        xint(2)
         load_g(2, 2)
         quad(3)
-        xq(1)
-        qd(3)
-        x_all(2)
-        x_all(3)
-        widen2(4)
-        load_g(3, 2)
-        quad(4)
+        wq(2)
         xq(2)
-        qd(4)
-        xq(3)
+        qd(3)
+        xg(3)
         wint2(3)
         second(0, 0, 0)
         second(0, 0, 1)
-        quad(5)
-        qd(5)
+        xint(3)
+        p2(0, 1, 0)
+        load_g(3, 2)
+        quad(4)
         wq(3)
-        turn_raw(4)
-        second(1, 0, 0)
-        second(1, 0, 1)
-        quad(6)
-        qd(6)
-        wint(4, 0)
-        second(0, 1, 0)
+        xq(3)
+        qd(4)
+        pex(0, 1, 0)
         second(0, 1, 1)
-        second(1, 1, 0)
-        second(1, 1, 1)
-        wint(4, 1)
+        turn_raw(4)
+        quad(5)
+        second(1, 0, 0)
+        qd(5)
+        second(1, 0, 1)
+        wint2(4)
         widen2(5)
-        quad(7)
-        wq(4)
-        qd(7)
         second(0, 2, 0)
-        second(0, 2, 1)
+        quad(6)
+        wq(4)
+        second(1, 1, 0)
+        qd(6)
+        second(1, 1, 1)
         turn_raw(5)
-        quad(8)
+        quad(7)
         second(1, 2, 0)
-        qd(8)
+        qd(7)
+        second(0, 2, 1)
         second(1, 2, 1)
-        wint(5, 0)
+        wint2(5)
+        quad(8)
+        qd(8)
         second(0, 3, 0)
         second(0, 3, 1)
-        wint(5, 1)
+        second(1, 3, 0)
         quad(9)
         wq(5)
-        second(1, 3, 0)
-        qd(9)
         second(1, 3, 1)
+        qd(9)
         second(0, 4, 0)
         second(0, 4, 1)
         quad(10)

@@ -58,6 +58,11 @@ def tile_shard_weight_grad_s7_kernel(tc, x, dy, w2_bytes, w2_scale, g, c, out):
             y_raw[a, tp] = work.tile([P, 2, N], BF16, name="y_raw", bufs=6, align_bytes=64)
             nc.sync.dma_start(out=y_raw[a, tp][:], in_=rows(dy, a)[:, 2 * tp : 2 * tp + 2, :])
 
+        def load_y_row(t):
+            if t % 2 == 0:
+                y_raw[0, t // 2] = work.tile([P, 2, N], BF16, name="y_raw", bufs=6, align_bytes=64)
+            nc.sync.dma_start(out=y_raw[0, t // 2][:, t % 2, :], in_=rows(dy, 0)[:, t, :])
+
         def load_x(a):
             x_raw[a] = work.tile([P, 4, K], BF16, name="x_raw", bufs=4, align_bytes=64)
             nc.sync.dma_start(out=x_raw[a][:], in_=rows(x, a))
@@ -67,16 +72,18 @@ def tile_shard_weight_grad_s7_kernel(tc, x, dy, w2_bytes, w2_scale, g, c, out):
             nc.sync.dma_start(out=g_raw[a, ch][:], in_=rows(g, a)[:, :, 512 * ch : 512 * (ch + 1)])
 
         load_strip(0)
-        load_y(0, 0)
+        load_y_row(0)
+        load_y_row(1)
         load_strip(1)
-        load_y(0, 1)
+        load_y_row(2)
+        load_y_row(3)
         load_w(1)
         load_y(1, 0)
         load_y(1, 1)
         load_w(2)
+        load_w(3)
         load_g(0, 0)
         load_x(0)
-        load_w(3)
         load_y(2, 0)
         load_y(2, 1)
         load_g(1, 0)
@@ -84,6 +91,8 @@ def tile_shard_weight_grad_s7_kernel(tc, x, dy, w2_bytes, w2_scale, g, c, out):
 
         ident = keep.tile([P, P], F32, name="ident", align_bytes=64)
         make_identity(nc, ident[:])
+        one = keep.tile([P, 1], F32, name="one")
+        nc.vector.memset(one[:], 1.0)
         c_all = keep.tile([P, D], F32, name="c_all")
         scale_all = keep.tile([P, 2, P, 4], F32, name="scale_all", align_bytes=64)
         for gi in range(2):
@@ -98,9 +107,12 @@ def tile_shard_weight_grad_s7_kernel(tc, x, dy, w2_bytes, w2_scale, g, c, out):
         bank = {}
         dh, d_codes, d_scales = {}, {}, {}
         acc = {}
+        plain = set()
+        y_split = {}
 
         units = [(a, b) for a in range(GROUPS) for b in range(4)]
         units = units + [(a, 2 * j + i) for j in range(2, PAIRS) for a in range(GROUPS) for i in range(2)]
+        units = units[:-4] + [(a, b) for b in (10, 11) for a in (2, 3)]
         where = {u: n for n, u in enumerate(units)}
 
         def prod(b, parts=1):
@@ -116,7 +128,25 @@ def tile_shard_weight_grad_s7_kernel(tc, x, dy, w2_bytes, w2_scale, g, c, out):
 
         def widen(b):
             wb[b] = work.tile([P, N], BF16, name="wb", bufs=6, align_bytes=64)
+            nc.vector.tensor_scalar(
+                out=wb[b][:].rearrange("p (u w e) -> p w u e", u=2, e=2),
+                in0=w_raw[b // 2][:, b % 2, :].bitcast(FP8).rearrange("p (w u e) -> p w u e", u=2, e=2),
+                scalar1=one[:],
+                scalar2=None,
+                op0=MULT,
+            )
+
+        def swiden(b):
+            wb[b] = work.tile([P, N], BF16, name="wb", bufs=6, align_bytes=64)
             nc.scalar.copy(out=wb[b][:], in_=w_raw[b // 2][:, b % 2, :].bitcast(FP8))
+            plain.add(b)
+
+        def split_y(a, tp):
+            y_split[a, tp] = work.tile([P, 2, 2, 256], F32, name="y_split", bufs=2, align_bytes=64)
+            nc.scalar.copy(
+                out=y_split[a, tp][:],
+                in_=y_raw[a, tp][:].bitcast(F32).rearrange("p r (w u) -> p r u w", u=2),
+            )
 
         def word_transposes(words, ps):
             for gi in range(2):
@@ -139,11 +169,15 @@ def tile_shard_weight_grad_s7_kernel(tc, x, dy, w2_bytes, w2_scale, g, c, out):
             for u in range(2):
                 for i in range(2):
                     words = wb[2 * j + i][:].bitcast(F32)
-                    nc.tensor.transpose(ps[:, u, i, :], words[:, 256 * gi + u : 256 * (gi + 1) : 2], ident[:])
+                    if 2 * j + i in plain:
+                        cols = slice(256 * gi + u, 256 * (gi + 1), 2)
+                    else:
+                        cols = slice(256 * u + P * gi, 256 * u + P * (gi + 1))
+                    nc.tensor.transpose(ps[:, u, i, :], words[:, cols], ident[:])
             bank["r", j, gi] = ps
 
         def wscale(j, gi):
-            planes[j, gi] = work.tile([P, 4, PF], BF16, name="planes", bufs=2, align_bytes=64)
+            planes[j, gi] = work.tile([P, 4, PF], BF16, name="planes", bufs=4, align_bytes=64)
             for t in range(4):
                 u, e = divmod(t, 2)
                 halves = bank["r", j, gi][:, u].rearrange("p i f -> p (i f)").bitcast(BF16)
@@ -171,13 +205,18 @@ def tile_shard_weight_grad_s7_kernel(tc, x, dy, w2_bytes, w2_scale, g, c, out):
 
         def ytr(a, t):
             ps = psum.tile([P, 2, 2, P], F32, name="side", bufs=5)
-            word_transposes(y_raw[a, t // 2][:, t % 2, :].bitcast(F32), ps)
+            if (a, t // 2) in y_split:
+                for gi in range(2):
+                    for u in range(2):
+                        nc.tensor.transpose(ps[:, gi, u, :], y_split[a, t // 2][:, t % 2, u, P * gi : P * (gi + 1)], ident[:])
+            else:
+                word_transposes(y_raw[a, t // 2][:, t % 2, :].bitcast(F32), ps)
             bank["y", a, t] = ps
 
         def yex(a, t):
             tp = t // 2
             if (a, tp) not in gy:
-                gy[a, tp] = work.tile([P, 2, 2, P, 2], F32, name="gy", bufs=3, align_bytes=64)
+                gy[a, tp] = work.tile([P, 2, 2, P, 2], F32, name="gy%d" % ((2 * a + tp) % 4), bufs=1, align_bytes=64)
             nc.scalar.copy(out=gy[a, tp][:, t % 2], in_=bank["y", a, t][:].rearrange("p g u m -> p g m u"))
 
         def yq(a, tp):
@@ -190,7 +229,7 @@ def tile_shard_weight_grad_s7_kernel(tc, x, dy, w2_bytes, w2_scale, g, c, out):
             )
 
         def xg(a):
-            gx[a] = work.tile([P, K, 4], BF16, name="dh%d" % (a % 2), bufs=1, align_bytes=64)
+            gx[a] = work.tile([P, K, 4], BF16, name="gy2" if a == 0 else "dh%d" % ((a - 1) % 3), bufs=1, align_bytes=64)
             nc.gpsimd.tensor_scalar(
                 out=gx[a][:, 0:XG, :],
                 in0=x_raw[a][:, :, 0:XG].rearrange("p t k -> p k t"),
@@ -235,7 +274,7 @@ def tile_shard_weight_grad_s7_kernel(tc, x, dy, w2_bytes, w2_scale, g, c, out):
             a, b = units[n]
             k, i = divmod(n, 4)
             if k not in dh:
-                dh[k] = work.tile([P, 4 * P, 4], BF16, name="dh%d" % (k % 2), bufs=1, align_bytes=64)
+                dh[k] = work.tile([P, 4 * P, 4], BF16, name="dh%d" % (k % 3), bufs=1, align_bytes=64)
             f0 = P * (b % 4)
             nc.vector.tensor_tensor(
                 out=dh[k][:, P * i : P * (i + 1), :].rearrange("p (c i) t -> p c t i", i=RUN),
@@ -246,8 +285,8 @@ def tile_shard_weight_grad_s7_kernel(tc, x, dy, w2_bytes, w2_scale, g, c, out):
 
         def qd(k, f0=0, f1=4 * P):
             if k not in d_codes:
-                d_codes[k] = work.tile([P, 4 * P], U32, name="d_codes", bufs=8, align_bytes=64)
-                d_scales[k] = work.tile([P, 4 * P], U8, name="d_scales", bufs=8, align_bytes=64)
+                d_codes[k] = work.tile([P, 4 * P], U32, name="d_codes", bufs=6, align_bytes=64)
+                d_scales[k] = work.tile([P, 4 * P], U8, name="d_scales", bufs=6, align_bytes=64)
             nc.vector.quantize_mx(
                 out=d_codes[k][:, f0:f1].bitcast(FP8X4),
                 scales=d_scales[k][:, f0:f1],
@@ -279,52 +318,64 @@ def tile_shard_weight_grad_s7_kernel(tc, x, dy, w2_bytes, w2_scale, g, c, out):
                 acc[j, h] = work.tile([P, 2, PF], F32, name="acc", bufs=8)
                 nc.scalar.activation(out=acc[j, h][:], in_=ps[:], func=COPY, scale=c_all[:, 0:1])
                 return
-            if j in G_PAIRS:
-                part = work.tile([P, 2, PF], F32, name="part", bufs=3)
-                nc.scalar.activation(out=part[:], in_=ps[:], func=COPY, scale=c_all[:, 1:2])
-                nc.gpsimd.tensor_tensor(out=acc[j, h][:], in0=acc[j, h][:], in1=part[:], op=ADD)
-            else:
-                nc.vector.scalar_tensor_tensor(
-                    out=acc[j, h][:], in0=ps[:], scalar=c_all[:, 1:2], in1=acc[j, h][:], op0=MULT, op1=ADD
-                )
+            nc.vector.scalar_tensor_tensor(
+                out=acc[j, h][:], in0=ps[:], scalar=c_all[:, 1:2], in1=acc[j, h][:], op0=MULT, op1=ADD
+            )
             nc.sync.dma_start(out=out_view[h][:, :, PF * j : PF * (j + 1)], in_=acc[j, h][:])
+
+        part = {}
+
+        def pex1(j, h):
+            part[j, h] = work.tile([P, 2, PF], F32, name="part", bufs=4)
+            nc.scalar.activation(out=part[j, h][:], in_=bank["p", 1, j, h][:], func=COPY, scale=c_all[:, 1:2])
+
+        def gadd(j, h, k):
+            total = work.tile([P, 2, PF], F32, name="dh%d" % (k % 3), bufs=1, align_bytes=64)
+            nc.gpsimd.tensor_tensor(out=total[:], in0=acc[j, h][:], in1=part[j, h][:], op=ADD)
+            nc.sync.dma_start(out=out_view[h][:, :, PF * j : PF * (j + 1)], in_=total[:])
 
         tail = {}
 
-        def tail_pass(q):
+        def tail_pass(i, h):
             k = len(units) // 4 - 1
-            fs = slice(PF * q, PF * (q + 1))
-            for kt in range(4):
-                if q == 0:
-                    tail[kt] = psum.tile([P, PF], F32, name=("unit", "side")[kt // 2], bufs=(3, 5)[kt // 2])
-                kc = slice(P * kt, P * (kt + 1))
-                nc.tensor.matmul_mx(
-                    out=tail[kt][:],
-                    lhsT=x_codes[2 + q][:, kc].bitcast(FP8X4),
-                    lhsT_scale=x_scales[2 + q][:, kc],
-                    rhs=d_codes[k][:, fs].bitcast(FP8X4),
-                    rhs_scale=d_scales[k][:, fs],
-                    start=(q == 0),
-                    stop=(q == 1),
-                )
+            ps = psum.tile([P, 2, P], F32, name="side", bufs=5)
+            for k2 in range(2):
+                kc = slice(P * (2 * h + k2), P * (2 * h + k2 + 1))
+                for q in range(2):
+                    fs = slice(P * (2 * i + q), P * (2 * i + q + 1))
+                    nc.tensor.matmul_mx(
+                        out=ps[:, k2, :],
+                        lhsT=x_codes[2 + q][:, kc].bitcast(FP8X4),
+                        lhsT_scale=x_scales[2 + q][:, kc],
+                        rhs=d_codes[k][:, fs].bitcast(FP8X4),
+                        rhs_scale=d_scales[k][:, fs],
+                        start=(q == 0),
+                        stop=(q == 1),
+                    )
+            tail[i, h] = ps
 
-        def tail_out(kt):
+        def tail_out(i, h):
             j = PAIRS - 1
-            total = acc[j, kt // 2][:, kt % 2, :]
+            total = acc[j, h][:, :, P * i : P * (i + 1)]
             nc.vector.scalar_tensor_tensor(
-                out=total, in0=tail[kt][:], scalar=c_all[:, 1:2], in1=total, op0=MULT, op1=ADD
+                out=total, in0=tail[i, h][:], scalar=c_all[:, 1:2], in1=total, op0=MULT, op1=ADD
             )
-            nc.sync.dma_start(out=out[P * kt : P * (kt + 1), PF * j : PF * (j + 1)], in_=total)
+            f0 = PF * j + P * i
+            nc.sync.dma_start(out=out_view[h][:, :, f0 : f0 + P], in_=total)
 
-        ytr(0, 0)
-        yex(0, 0)
+        for t in range(2):
+            ytr(0, t)
+            yex(0, t)
         for b in range(4):
             prod(b, 2 if b == 0 else 1)
-            a, t = divmod(b + 1, 4)
-            ytr(a, t)
-            yex(a, t)
+            if b < 2:
+                ytr(0, b + 2)
+                yex(0, b + 2)
             wtr(b)
             wex(b)
+            if b == 2:
+                ytr(1, 0)
+                yex(1, 0)
         yq(0, 0)
         yq(0, 1)
         for t in range(1, 4):
@@ -334,8 +385,12 @@ def tile_shard_weight_grad_s7_kernel(tc, x, dy, w2_bytes, w2_scale, g, c, out):
         wq(1)
         prod(4)
         yq(1, 0)
+        xg(0)
+        swiden(6)
+        swiden(7)
+        xint(0)
         nc.scalar.copy(out=c_all[:], in_=c_bf[:])
-        for e in ((load_y, 3, 0), (load_y, 3, 1), (load_g, 2, 0), (load_w, 4), (load_x, 2), (load_g, 3, 0), (load_x, 3), (load_g, 0, 1), (load_g, 1, 1), (load_g, 2, 1), (load_g, 3, 1), (load_w, 5)):
+        for e in ((load_y, 3, 0), (load_y, 3, 1), (load_g, 2, 0), (load_w, 4), (load_x, 2), (load_g, 3, 0), (load_x, 3), (load_w, 5), (load_g, 0, 1), (load_g, 1, 1), (load_g, 2, 1), (load_g, 3, 1)):
             e[0](*e[1:])
 
         def turn_y(a):
@@ -377,84 +432,100 @@ def tile_shard_weight_grad_s7_kernel(tc, x, dy, w2_bytes, w2_scale, g, c, out):
         quad(0)
         yq(1, 1)
         prod(5)
+        xq(0)
         qd(0)
-        xg(0)
-        widen2(3)
+        xg(1)
         turn_y(2)
-        xint(0)
+        wtr_raw(3, 0)
+        wscale(3, 0)
+        xint(1)
         load_g(0, 2)
         quad(1)
         yq(2, 0)
         yq(2, 1)
-        xq(0)
+        xq(1)
         qd(1)
-        xg(1)
+        xg(2)
+        wtr_raw(3, 1)
+        wscale(3, 1)
         turn_y(3)
-        xint(1)
+        xint(2)
         load_g(1, 2)
         quad(2)
         yq(3, 0)
         yq(3, 1)
-        xq(1)
-        qd(2)
-        xg(2)
-        widen2(4)
-        turn_w(2)
-        turn_raw(3)
-        xint(2)
-        load_g(2, 2)
-        quad(3)
-        wq(2)
         xq(2)
-        qd(3)
+        qd(2)
         xg(3)
-        wint2(3)
+        swiden(8)
+        swiden(9)
+        turn_w(2)
         second(0, 0, 0)
         second(0, 0, 1)
         xint(3)
-        p2(0, 1, 0)
+        load_g(2, 2)
+        quad(3)
+        wq(2)
+        xq(3)
+        widen(10)
+        qd(3)
+        wint2(3)
+        second(0, 1, 0)
+        second(0, 1, 1)
+        turn_raw(4)
         load_g(3, 2)
         quad(4)
         wq(3)
-        xq(3)
-        qd(4)
-        pex(0, 1, 0)
-        second(0, 1, 1)
-        turn_raw(4)
-        quad(5)
         second(1, 0, 0)
+        widen(11)
+        qd(4)
+        p2(1, 0, 1)
+        pex1(0, 1)
+        gadd(0, 1, 4)
+        p2(1, 1, 0)
+        pex1(1, 0)
+        p2(1, 1, 1)
+        quad(5)
+        pex(1, 1, 1)
         qd(5)
-        second(1, 0, 1)
+        gadd(1, 0, 5)
         wint2(4)
-        widen2(5)
         second(0, 2, 0)
+        second(0, 2, 1)
+        turn_raw(5)
         quad(6)
         wq(4)
-        second(1, 1, 0)
         qd(6)
-        second(1, 1, 1)
-        turn_raw(5)
+        p2(1, 2, 0)
+        pex1(2, 0)
+        gadd(2, 0, 6)
+        p2(1, 2, 1)
+        pex1(2, 1)
         quad(7)
-        second(1, 2, 0)
         qd(7)
-        second(0, 2, 1)
-        second(1, 2, 1)
+        gadd(2, 1, 7)
         wint2(5)
-        quad(8)
-        qd(8)
         second(0, 3, 0)
         second(0, 3, 1)
-        second(1, 3, 0)
-        quad(9)
+        quad(8)
         wq(5)
-        second(1, 3, 1)
+        qd(8)
+        p2(1, 3, 0)
+        pex1(3, 0)
+        gadd(3, 0, 8)
+        p2(1, 3, 1)
+        pex1(3, 1)
+        quad(9)
         qd(9)
+        gadd(3, 1, 9)
         second(0, 4, 0)
         second(0, 4, 1)
         quad(10)
+        second(1, 4, 0)
         qd(10)
-        p2(1, 4, 0)
         p2(1, 4, 1)
+        pex1(4, 1)
+        gadd(4, 1, 10)
         unit(44)
         dhg(44)
         unit(45)
@@ -464,14 +535,15 @@ def tile_shard_weight_grad_s7_kernel(tc, x, dy, w2_bytes, w2_scale, g, c, out):
         qd(11, 0, 256)
         unit(47)
         dhg(47)
-        pex(1, 4, 0)
         second(0, 5, 0)
         second(0, 5, 1)
-        tail_pass(0)
-        qd(11, 256, 512)
-        pex(1, 4, 1)
-        tail_pass(1)
-        tail_out(0)
-        tail_out(1)
-        tail_out(2)
-        tail_out(3)
+        qd(11, 256, 384)
+        qd(11, 384, 512)
+        tail_pass(0, 0)
+        tail_pass(0, 1)
+        tail_pass(1, 0)
+        tail_pass(1, 1)
+        tail_out(0, 0)
+        tail_out(0, 1)
+        tail_out(1, 0)
+        tail_out(1, 1)

@@ -17,12 +17,19 @@ ADD = mybir.AluOpType.add
 COPY = mybir.ActivationFunctionType.Copy
 
 P = 128
-PAIRS = 6
-PF = 256
+PACK = 4
+GROUPS = D * T // (P * PACK)
+PAIR = 2 * P
+PAIRS = F // PAIR
+BEAT = 4
+G_COLS = BEAT * P
 RUN = 4
-GROUPS = 4
-XG = 384
-G_PAIRS = ()
+VECTOR_PAIRS = 3
+X_GPSIMD = 384
+UNIT_BANKS = 3
+SIDE_BANKS = 5
+DH_SLOTS = 3
+Y_SLOTS = 4
 
 
 def tile_shard_weight_grad_s7_kernel(tc, x, dy, w2_bytes, w2_scale, g, c, out):
@@ -33,517 +40,399 @@ def tile_shard_weight_grad_s7_kernel(tc, x, dy, w2_bytes, w2_scale, g, c, out):
         psum = ctx.enter_context(tc.psum_pool(name="psum", bufs=2))
         ctx.enter_context(tc.manual_schedule())
 
-        scale_col = keep.tile([P, 2, 4], F32, name="scale_col")
-        nc.sync.dma_start(out=scale_col[:], in_=w2_scale.rearrange("o (g p t) -> p (o g) t", p=P, t=4))
+        w_raw, y_raw, x_raw, g_raw = {}, {}, {}, {}
+        w_view = w2_bytes.rearrange("(j i p) n -> j p i n", i=2, p=P)
+        out_view = out.rearrange("(h k2 p) f -> h p k2 f", k2=2, p=P)
+
+        def samples(tensor, a):
+            return tensor[a // 2].rearrange("(q p t) n -> q p t n", q=2, t=PACK)[a % 2]
+
+        def load_w(j, strips=(0, 1)):
+            if j not in w_raw:
+                w_raw[j] = work.tile([P, 2, N], U8, name="w_raw", bufs=PAIRS)
+            part = slice(strips[0], strips[-1] + 1)
+            nc.sync.dma_start(out=w_raw[j][:, part, :], in_=w_view[j][:, part, :])
+
+        def load_y(a, rows):
+            tp = rows[0] // 2
+            if (a, tp) not in y_raw:
+                y_raw[a, tp] = work.tile([P, 2, N], BF16, name="y_raw", bufs=6, align_bytes=64)
+            nc.sync.dma_start(
+                out=y_raw[a, tp][:, rows[0] % 2 : rows[-1] % 2 + 1, :], in_=samples(dy, a)[:, rows[0] : rows[-1] + 1, :]
+            )
+
+        def load_y_group(a):
+            load_y(a, (0, 1))
+            load_y(a, (2, 3))
+
+        def load_x(a):
+            x_raw[a] = work.tile([P, PACK, K], BF16, name="x_raw", bufs=GROUPS, align_bytes=64)
+            nc.sync.dma_start(out=x_raw[a][:], in_=samples(x, a))
+
+        def load_g(a, chunk):
+            g_raw[a, chunk] = work.tile([P, PACK, G_COLS], BF16, name="g_raw", bufs=2 * GROUPS, align_bytes=64)
+            nc.sync.dma_start(out=g_raw[a, chunk][:], in_=samples(g, a)[:, :, G_COLS * chunk : G_COLS * (chunk + 1)])
+
+        scale_col = keep.tile([P, 2, PACK], F32, name="scale_col")
+        nc.sync.dma_start(out=scale_col[:], in_=w2_scale.rearrange("o (g p t) -> p (o g) t", p=P, t=PACK))
         c_bf = keep.tile([P, D], BF16, name="c_bf")
         nc.scalar.dma_start(out=c_bf[:], in_=c.partition_broadcast(P))
 
-        w_raw, y_raw, x_raw, g_raw = {}, {}, {}, {}
-        w_view = w2_bytes.rearrange("(j b p) n -> j p b n", b=2, p=P)
-        out_view = out.rearrange("(h kt p) f -> h p kt f", kt=2, p=P)
-
-        def rows(t3, a):
-            return t3[a // 2].rearrange("(q p t) n -> q p t n", q=2, t=4)[a % 2]
-
-        def load_w(j):
-            w_raw[j] = work.tile([P, 2, N], U8, name="w_raw", bufs=PAIRS)
-            nc.sync.dma_start(out=w_raw[j][:], in_=w_view[j])
-
-        def load_strip(i):
-            if i == 0:
-                w_raw[0] = work.tile([P, 2, N], U8, name="w_raw", bufs=PAIRS)
-            nc.sync.dma_start(out=w_raw[0][:, i, :], in_=w_view[0][:, i, :])
-
-        def load_y(a, tp):
-            y_raw[a, tp] = work.tile([P, 2, N], BF16, name="y_raw", bufs=6, align_bytes=64)
-            nc.sync.dma_start(out=y_raw[a, tp][:], in_=rows(dy, a)[:, 2 * tp : 2 * tp + 2, :])
-
-        def load_y_row(t):
-            if t % 2 == 0:
-                y_raw[0, t // 2] = work.tile([P, 2, N], BF16, name="y_raw", bufs=6, align_bytes=64)
-            nc.sync.dma_start(out=y_raw[0, t // 2][:, t % 2, :], in_=rows(dy, 0)[:, t, :])
-
-        def load_x(a):
-            x_raw[a] = work.tile([P, 4, K], BF16, name="x_raw", bufs=4, align_bytes=64)
-            nc.sync.dma_start(out=x_raw[a][:], in_=rows(x, a))
-
-        def load_g(a, ch):
-            g_raw[a, ch] = work.tile([P, 4, 512], BF16, name="g_raw", bufs=8, align_bytes=64)
-            nc.sync.dma_start(out=g_raw[a, ch][:], in_=rows(g, a)[:, :, 512 * ch : 512 * (ch + 1)])
-
-        load_strip(0)
-        load_y_row(0)
-        load_y_row(1)
-        load_strip(1)
-        load_y_row(2)
-        load_y_row(3)
+        load_w(0, (0,))
+        load_y(0, (0,))
+        load_y(0, (1,))
+        load_w(0, (1,))
+        load_y(0, (2,))
+        load_y(0, (3,))
         load_w(1)
-        load_y(1, 0)
-        load_y(1, 1)
+        load_y_group(1)
         load_w(2)
         load_w(3)
         load_g(0, 0)
         load_x(0)
-        load_y(2, 0)
-        load_y(2, 1)
+        load_y_group(2)
         load_g(1, 0)
         load_x(1)
 
         ident = keep.tile([P, P], F32, name="ident", align_bytes=64)
         make_identity(nc, ident[:])
-        one = keep.tile([P, 1], F32, name="one")
-        nc.vector.memset(one[:], 1.0)
         c_all = keep.tile([P, D], F32, name="c_all")
-        scale_all = keep.tile([P, 2, P, 4], F32, name="scale_all", align_bytes=64)
+        scale_all = keep.tile([P, 2, P, PACK], F32, name="scale_all", align_bytes=64)
         for gi in range(2):
-            ps = psum.tile([P, 4, P], F32, name="unit", bufs=3)
-            for t in range(4):
+            ps = psum.tile([P, PACK, P], F32, name="unit", bufs=UNIT_BANKS)
+            for t in range(PACK):
                 nc.tensor.transpose(ps[:, t, :], scale_col[:, gi, t : t + 1].to_broadcast([P, P]), ident[:])
             nc.scalar.copy(out=scale_all[:, gi], in_=ps[:].rearrange("p t j -> p j t"))
 
-        wb, gw, planes, w_codes, w_scales = {}, {}, {}, {}, {}
-        gy, y_codes, y_scales = {}, {}, {}
-        x_codes, x_scales, gx = {}, {}, {}
-        bank = {}
-        dh, d_codes, d_scales = {}, {}, {}
-        acc = {}
-        plain = set()
-        y_split = {}
+        w_wide, w_planes, w_turned, w_codes, w_scales = {}, {}, {}, {}, {}
+        y_turned, y_codes, y_scales = {}, {}, {}
+        x_mixed, x_codes, x_scales = {}, {}, {}
+        dh, dh_codes, dh_scales = {}, {}, {}
+        bank, first_term, second_term = {}, {}, {}
 
-        units = [(a, b) for a in range(GROUPS) for b in range(4)]
-        units = units + [(a, 2 * j + i) for j in range(2, PAIRS) for a in range(GROUPS) for i in range(2)]
-        units = units[:-4] + [(a, b) for b in (10, 11) for a in (2, 3)]
-        where = {u: n for n, u in enumerate(units)}
+        def side_bank(shape):
+            return psum.tile(shape, F32, name="side", bufs=SIDE_BANKS)
 
-        def prod(b, parts=1):
-            wb[b] = work.tile([P, N], BF16, name="wb", bufs=6, align_bytes=64)
+        def quantise(name, bufs, source):
+            words = source.shape[1] // PACK
+            codes = work.tile([P, words], U32, name=name + "_codes", bufs=bufs, align_bytes=64)
+            scales = work.tile([P, words], U8, name=name + "_scales", bufs=bufs, align_bytes=64)
+            nc.vector.quantize_mx(out=codes[:].bitcast(FP8X4), scales=scales[:], in_=source)
+            return codes, scales
+
+        def multiply(ps, lhs, lhs_cols, rhs, rhs_cols, start, stop):
+            nc.tensor.matmul_mx(
+                out=ps,
+                lhsT=lhs[0][:, lhs_cols].bitcast(FP8X4),
+                lhsT_scale=lhs[1][:, lhs_cols],
+                rhs=rhs[0][:, rhs_cols].bitcast(FP8X4),
+                rhs_scale=rhs[1][:, rhs_cols],
+                start=start,
+                stop=stop,
+            )
+
+        def in_runs(rows):
+            return rows.rearrange("p t (c i) -> p c t i", i=RUN)
+
+        def mixed_runs(mixed):
+            return mixed.rearrange("p (c i) t -> p c t i", i=RUN)
+
+        def turn(ps, row, gi, u):
+            nc.tensor.transpose(ps, row.bitcast(F32)[:, PAIR * gi + u : PAIR * (gi + 1) : 2], ident[:])
+
+        def turn_row(row, turned):
+            ps = side_bank([P, 2, 2, P])
+            for gi in range(2):
+                for u in range(2):
+                    turn(ps[:, gi, u, :], row, gi, u)
+            nc.scalar.copy(out=turned, in_=ps[:].rearrange("p g u m -> p g m u"))
+
+        def turn_y(a, t):
+            tp = t // 2
+            if (a, tp) not in y_turned:
+                slot = "y_turned%d" % ((2 * a + tp) % Y_SLOTS)
+                y_turned[a, tp] = work.tile([P, 2, 2, P, 2], F32, name=slot, bufs=1, align_bytes=64)
+            turn_row(y_raw[a, tp][:, t % 2, :], y_turned[a, tp][:, t % 2])
+
+        def quantise_y(a, tp):
+            source = y_turned[a, tp][:].rearrange("p r g m u -> p (r g m u)").bitcast(BF16)
+            y_codes[a, tp] = quantise("y", 2 * GROUPS, source)
+
+        def wide_tile(b):
+            w_wide[b] = work.tile([P, N], BF16, name="w_wide", bufs=6, align_bytes=64)
+            return w_wide[b]
+
+        def pair_tile(j):
+            if j not in w_turned:
+                w_turned[j] = work.tile([P, 2, 2, P, 2], F32, name="w_turned", bufs=2, align_bytes=64)
+            return w_turned[j]
+
+        def scale_strip(b, parts=1):
+            wide = wide_tile(b)
             for i in range(parts):
                 ns = slice(N // parts * i, N // parts * (i + 1))
                 nc.vector.tensor_tensor(
-                    out=wb[b][:, ns],
+                    out=wide[:, ns],
                     in0=w_raw[b // 2][:, b % 2, ns].bitcast(FP8),
                     in1=scale_all[:].rearrange("p g j t -> p (g j t)")[:, ns],
                     op=MULT,
                 )
 
-        def widen(b):
-            wb[b] = work.tile([P, N], BF16, name="wb", bufs=6, align_bytes=64)
-            nc.vector.tensor_scalar(
-                out=wb[b][:].rearrange("p (u w e) -> p w u e", u=2, e=2),
-                in0=w_raw[b // 2][:, b % 2, :].bitcast(FP8).rearrange("p (w u e) -> p w u e", u=2, e=2),
-                scalar1=one[:],
-                scalar2=None,
-                op0=MULT,
-            )
+        def turn_strip(b):
+            turn_row(w_wide[b][:], pair_tile(b // 2)[:, :, b % 2])
 
-        def swiden(b):
-            wb[b] = work.tile([P, N], BF16, name="wb", bufs=6, align_bytes=64)
-            nc.scalar.copy(out=wb[b][:], in_=w_raw[b // 2][:, b % 2, :].bitcast(FP8))
-            plain.add(b)
+        def widen_pair(j):
+            for i in range(2):
+                nc.scalar.copy(out=wide_tile(2 * j + i)[:], in_=w_raw[j][:, i, :].bitcast(FP8))
 
-        def split_y(a, tp):
-            y_split[a, tp] = work.tile([P, 2, 2, 256], F32, name="y_split", bufs=2, align_bytes=64)
-            nc.scalar.copy(
-                out=y_split[a, tp][:],
-                in_=y_raw[a, tp][:].bitcast(F32).rearrange("p r (w u) -> p r u w", u=2),
-            )
-
-        def word_transposes(words, ps):
-            for gi in range(2):
-                for u in range(2):
-                    nc.tensor.transpose(ps[:, gi, u, :], words[:, 256 * gi + u : 256 * (gi + 1) : 2], ident[:])
-
-        def wtr(b):
-            ps = psum.tile([P, 2, 2, P], F32, name="side", bufs=5)
-            word_transposes(wb[b][:].bitcast(F32), ps)
-            bank["w", b] = ps
-
-        def wex(b):
-            j = b // 2
-            if j not in gw:
-                gw[j] = work.tile([P, 2, 2, P, 2], F32, name="gw", bufs=2, align_bytes=64)
-            nc.scalar.copy(out=gw[j][:, :, b % 2], in_=bank["w", b][:].rearrange("p g u f -> p g f u"))
-
-        def wtr_raw(j, gi):
-            ps = psum.tile([P, 2, 2, P], F32, name="side", bufs=5)
+        def turn_pair(j, gi):
+            ps = side_bank([P, 2, 2, P])
             for u in range(2):
                 for i in range(2):
-                    words = wb[2 * j + i][:].bitcast(F32)
-                    if 2 * j + i in plain:
-                        cols = slice(256 * gi + u, 256 * (gi + 1), 2)
-                    else:
-                        cols = slice(256 * u + P * gi, 256 * u + P * (gi + 1))
-                    nc.tensor.transpose(ps[:, u, i, :], words[:, cols], ident[:])
-            bank["r", j, gi] = ps
+                    turn(ps[:, u, i, :], w_wide[2 * j + i][:], gi, u)
+            bank["pair", j, gi] = ps
 
-        def wscale(j, gi):
-            planes[j, gi] = work.tile([P, 4, PF], BF16, name="planes", bufs=4, align_bytes=64)
-            for t in range(4):
+        def scale_pair(j, gi):
+            w_planes[j, gi] = work.tile([P, PACK, PAIR], BF16, name="w_planes", bufs=4, align_bytes=64)
+            for t in range(PACK):
                 u, e = divmod(t, 2)
-                halves = bank["r", j, gi][:, u].rearrange("p i f -> p (i f)").bitcast(BF16)
+                elements = bank["pair", j, gi][:, u].rearrange("p i f -> p (i f)").bitcast(BF16)
                 nc.scalar.activation(
-                    out=planes[j, gi][:, t, :], in_=halves[:, e : 2 * PF : 2], func=COPY, scale=scale_col[:, gi, t : t + 1]
+                    out=w_planes[j, gi][:, t, :],
+                    in_=elements[:, e : 2 * PAIR : 2],
+                    func=COPY,
+                    scale=scale_col[:, gi, t : t + 1],
                 )
 
-        def wint(j, gi):
-            if j not in gw:
-                gw[j] = work.tile([P, 2, 2, P, 2], F32, name="gw", bufs=2, align_bytes=64)
-            dst = gw[j][:, gi].rearrange("p b f u -> p (b f u)").bitcast(BF16)
-            nc.scalar.copy(
-                out=dst.rearrange("p (c i t) -> p c t i", i=RUN, t=4),
-                in_=planes[j, gi][:].rearrange("p t (c i) -> p c t i", i=RUN),
-            )
+        def turn_and_scale_pair(j):
+            for gi in range(2):
+                turn_pair(j, gi)
+                scale_pair(j, gi)
 
-        def wq(j):
-            w_codes[j] = work.tile([P, 2, 2, P], U32, name="w_codes", bufs=PAIRS, align_bytes=64)
-            w_scales[j] = work.tile([P, 2, 2, P], U8, name="w_scales", bufs=PAIRS, align_bytes=64)
-            nc.vector.quantize_mx(
-                out=w_codes[j][:].rearrange("p g b f -> p (g b f)").bitcast(FP8X4),
-                scales=w_scales[j][:].rearrange("p g b f -> p (g b f)"),
-                in_=gw[j][:].rearrange("p g b f u -> p (g b f u)").bitcast(BF16),
-            )
+        def mix_pair(j):
+            for gi in range(2):
+                mixed = pair_tile(j)[:, gi].rearrange("p i f u -> p (i f u)").bitcast(BF16)
+                nc.scalar.copy(
+                    out=mixed_runs(mixed.rearrange("p (f t) -> p f t", t=PACK)), in_=in_runs(w_planes[j, gi][:])
+                )
 
-        def ytr(a, t):
-            ps = psum.tile([P, 2, 2, P], F32, name="side", bufs=5)
-            if (a, t // 2) in y_split:
-                for gi in range(2):
-                    for u in range(2):
-                        nc.tensor.transpose(ps[:, gi, u, :], y_split[a, t // 2][:, t % 2, u, P * gi : P * (gi + 1)], ident[:])
-            else:
-                word_transposes(y_raw[a, t // 2][:, t % 2, :].bitcast(F32), ps)
-            bank["y", a, t] = ps
+        def quantise_w(j):
+            source = w_turned[j][:].rearrange("p g i f u -> p (g i f u)").bitcast(BF16)
+            w_codes[j] = quantise("w", PAIRS, source)
 
-        def yex(a, t):
-            tp = t // 2
-            if (a, tp) not in gy:
-                gy[a, tp] = work.tile([P, 2, 2, P, 2], F32, name="gy%d" % ((2 * a + tp) % 4), bufs=1, align_bytes=64)
-            nc.scalar.copy(out=gy[a, tp][:, t % 2], in_=bank["y", a, t][:].rearrange("p g u m -> p g m u"))
+        def slot_after(k):
+            return "dh%d" % (k % DH_SLOTS)
 
-        def yq(a, tp):
-            y_codes[a, tp] = work.tile([P, 2, 2, P], U32, name="y_codes", bufs=8, align_bytes=64)
-            y_scales[a, tp] = work.tile([P, 2, 2, P], U8, name="y_scales", bufs=8, align_bytes=64)
-            nc.vector.quantize_mx(
-                out=y_codes[a, tp][:].rearrange("p b g f -> p (b g f)").bitcast(FP8X4),
-                scales=y_scales[a, tp][:].rearrange("p b g f -> p (b g f)"),
-                in_=gy[a, tp][:].rearrange("p b g f u -> p (b g f u)").bitcast(BF16),
-            )
-
-        def xg(a):
-            gx[a] = work.tile([P, K, 4], BF16, name="gy2" if a == 0 else "dh%d" % ((a - 1) % 3), bufs=1, align_bytes=64)
+        def mix_x_gpsimd(a, slot):
+            x_mixed[a] = work.tile([P, K, PACK], BF16, name=slot, bufs=1, align_bytes=64)
             nc.gpsimd.tensor_scalar(
-                out=gx[a][:, 0:XG, :],
-                in0=x_raw[a][:, :, 0:XG].rearrange("p t k -> p k t"),
+                out=x_mixed[a][:, 0:X_GPSIMD, :],
+                in0=x_raw[a][:, :, 0:X_GPSIMD].rearrange("p t k -> p k t"),
                 scalar1=1.0,
                 scalar2=0.0,
                 op0=MULT,
                 op1=ADD,
             )
 
-        def xint(a):
-            nc.scalar.copy(
-                out=gx[a][:, XG:K, :].rearrange("p (c i) t -> p c t i", i=RUN),
-                in_=x_raw[a][:, :, XG:K].rearrange("p t (c i) -> p c t i", i=RUN),
-            )
+        def mix_x_scalar(a):
+            nc.scalar.copy(out=mixed_runs(x_mixed[a][:, X_GPSIMD:K, :]), in_=in_runs(x_raw[a][:, :, X_GPSIMD:K]))
 
-        def xq(a):
-            x_codes[a] = work.tile([P, K], U32, name="x_codes", bufs=4, align_bytes=64)
-            x_scales[a] = work.tile([P, K], U8, name="x_scales", bufs=4, align_bytes=64)
-            nc.vector.quantize_mx(
-                out=x_codes[a][:].bitcast(FP8X4),
-                scales=x_scales[a][:],
-                in_=gx[a][:].rearrange("p k t -> p (k t)"),
-            )
+        def quantise_x(a):
+            x_codes[a] = quantise("x", GROUPS, x_mixed[a][:].rearrange("p k t -> p (k t)"))
+
+        units = [(a, b) for a in range(GROUPS) for b in range(BEAT)]
+        units = units + [(a, 2 * j + i) for j in range(2, PAIRS) for a in range(GROUPS) for i in range(2)]
+        units = units[:-BEAT] + [(a, 2 * (PAIRS - 1) + i) for i in range(2) for a in (2, 3)]
+        place = {u: n for n, u in enumerate(units)}
+        last_beat = len(units) // BEAT - 1
 
         def unit(n):
             a, b = units[n]
-            ps = psum.tile([P, 4, P], F32, name="unit", bufs=3)
-            for t in range(4):
+            k, i = divmod(n, BEAT)
+            ps = psum.tile([P, PACK, P], F32, name="unit", bufs=UNIT_BANKS)
+            for t in range(PACK):
                 for gi in range(2):
-                    nc.tensor.matmul_mx(
-                        out=ps[:, t, :],
-                        lhsT=y_codes[a, t // 2][:, t % 2, gi, :].bitcast(FP8X4),
-                        lhsT_scale=y_scales[a, t // 2][:, t % 2, gi, :],
-                        rhs=w_codes[b // 2][:, gi, b % 2, :].bitcast(FP8X4),
-                        rhs_scale=w_scales[b // 2][:, gi, b % 2, :],
-                        start=(gi == 0),
-                        stop=(gi == 1),
+                    y0 = PAIR * (t % 2) + P * gi
+                    w0 = PAIR * gi + P * (b % 2)
+                    multiply(
+                        ps[:, t, :], y_codes[a, t // 2], slice(y0, y0 + P), w_codes[b // 2], slice(w0, w0 + P), gi == 0, gi == 1
                     )
-            bank["u", n] = ps
-
-        def dhg(n):
-            a, b = units[n]
-            k, i = divmod(n, 4)
             if k not in dh:
-                dh[k] = work.tile([P, 4 * P, 4], BF16, name="dh%d" % (k % 3), bufs=1, align_bytes=64)
-            f0 = P * (b % 4)
+                dh[k] = work.tile([P, BEAT * P, PACK], BF16, name=slot_after(k), bufs=1, align_bytes=64)
+            f0 = P * (b % BEAT)
             nc.vector.tensor_tensor(
-                out=dh[k][:, P * i : P * (i + 1), :].rearrange("p (c i) t -> p c t i", i=RUN),
-                in0=bank["u", n][:].rearrange("p t (c i) -> p c t i", i=RUN),
-                in1=g_raw[a, b // 4][:, :, f0 : f0 + P].rearrange("p t (c i) -> p c t i", i=RUN),
+                out=mixed_runs(dh[k][:, P * i : P * (i + 1), :]),
+                in0=in_runs(ps[:]),
+                in1=in_runs(g_raw[a, b // BEAT][:, :, f0 : f0 + P]),
                 op=MULT,
             )
 
-        def qd(k, f0=0, f1=4 * P):
-            if k not in d_codes:
-                d_codes[k] = work.tile([P, 4 * P], U32, name="d_codes", bufs=6, align_bytes=64)
-                d_scales[k] = work.tile([P, 4 * P], U8, name="d_scales", bufs=6, align_bytes=64)
-            nc.vector.quantize_mx(
-                out=d_codes[k][:, f0:f1].bitcast(FP8X4),
-                scales=d_scales[k][:, f0:f1],
-                in_=dh[k][:, f0:f1, :].rearrange("p f t -> p (f t)"),
-            )
-
-        def p2(dd, j, h):
-            ps = psum.tile([P, 2, PF], F32, name="side", bufs=5)
-            for k2 in range(2):
-                kc = slice(P * (2 * h + k2), P * (2 * h + k2 + 1))
-                for q in range(2):
-                    a = 2 * dd + q
-                    k, i = divmod(where[a, 2 * j], 4)
-                    fs = slice(P * i, P * i + PF)
-                    nc.tensor.matmul_mx(
-                        out=ps[:, k2, :],
-                        lhsT=x_codes[a][:, kc].bitcast(FP8X4),
-                        lhsT_scale=x_scales[a][:, kc],
-                        rhs=d_codes[k][:, fs].bitcast(FP8X4),
-                        rhs_scale=d_scales[k][:, fs],
-                        start=(q == 0),
-                        stop=(q == 1),
-                    )
-            bank["p", dd, j, h] = ps
-
-        def pex(dd, j, h):
-            ps = bank["p", dd, j, h]
-            if dd == 0:
-                acc[j, h] = work.tile([P, 2, PF], F32, name="acc", bufs=8)
-                nc.scalar.activation(out=acc[j, h][:], in_=ps[:], func=COPY, scale=c_all[:, 0:1])
-                return
-            nc.vector.scalar_tensor_tensor(
-                out=acc[j, h][:], in0=ps[:], scalar=c_all[:, 1:2], in1=acc[j, h][:], op0=MULT, op1=ADD
-            )
-            nc.sync.dma_start(out=out_view[h][:, :, PF * j : PF * (j + 1)], in_=acc[j, h][:])
-
-        part = {}
-
-        def pex1(j, h):
-            part[j, h] = work.tile([P, 2, PF], F32, name="part", bufs=4)
-            nc.scalar.activation(out=part[j, h][:], in_=bank["p", 1, j, h][:], func=COPY, scale=c_all[:, 1:2])
-
-        def gadd(j, h, k):
-            total = work.tile([P, 2, PF], F32, name="dh%d" % (k % 3), bufs=1, align_bytes=64)
-            nc.gpsimd.tensor_tensor(out=total[:], in0=acc[j, h][:], in1=part[j, h][:], op=ADD)
-            nc.sync.dma_start(out=out_view[h][:, :, PF * j : PF * (j + 1)], in_=total[:])
-
-        tail = {}
-
-        def tail_pass(i, h):
-            k = len(units) // 4 - 1
-            ps = psum.tile([P, 2, P], F32, name="side", bufs=5)
-            for k2 in range(2):
-                kc = slice(P * (2 * h + k2), P * (2 * h + k2 + 1))
-                for q in range(2):
-                    fs = slice(P * (2 * i + q), P * (2 * i + q + 1))
-                    nc.tensor.matmul_mx(
-                        out=ps[:, k2, :],
-                        lhsT=x_codes[2 + q][:, kc].bitcast(FP8X4),
-                        lhsT_scale=x_scales[2 + q][:, kc],
-                        rhs=d_codes[k][:, fs].bitcast(FP8X4),
-                        rhs_scale=d_scales[k][:, fs],
-                        start=(q == 0),
-                        stop=(q == 1),
-                    )
-            tail[i, h] = ps
-
-        def tail_out(i, h):
-            j = PAIRS - 1
-            total = acc[j, h][:, :, P * i : P * (i + 1)]
-            nc.vector.scalar_tensor_tensor(
-                out=total, in0=tail[i, h][:], scalar=c_all[:, 1:2], in1=total, op0=MULT, op1=ADD
-            )
-            f0 = PF * j + P * i
-            nc.sync.dma_start(out=out_view[h][:, :, f0 : f0 + P], in_=total)
-
-        for t in range(2):
-            ytr(0, t)
-            yex(0, t)
-        for b in range(4):
-            prod(b, 2 if b == 0 else 1)
-            if b < 2:
-                ytr(0, b + 2)
-                yex(0, b + 2)
-            wtr(b)
-            wex(b)
-            if b == 2:
-                ytr(1, 0)
-                yex(1, 0)
-        yq(0, 0)
-        yq(0, 1)
-        for t in range(1, 4):
-            ytr(1, t)
-            yex(1, t)
-        wq(0)
-        wq(1)
-        prod(4)
-        yq(1, 0)
-        xg(0)
-        swiden(6)
-        swiden(7)
-        xint(0)
-        nc.scalar.copy(out=c_all[:], in_=c_bf[:])
-        for e in ((load_y, 3, 0), (load_y, 3, 1), (load_g, 2, 0), (load_w, 4), (load_x, 2), (load_g, 3, 0), (load_x, 3), (load_w, 5), (load_g, 0, 1), (load_g, 1, 1), (load_g, 2, 1), (load_g, 3, 1)):
-            e[0](*e[1:])
-
-        def turn_y(a):
-            for t in range(4):
-                ytr(a, t)
-                yex(a, t)
-
-        def turn_w(j):
-            for b in (2 * j, 2 * j + 1):
-                wtr(b)
-                wex(b)
-
-        def turn_raw(j):
-            for gi in range(2):
-                wtr_raw(j, gi)
-                wscale(j, gi)
-
-        def x_all(a):
-            xint(a, 0)
-            xint(a, 1)
-
-        def widen2(j):
-            widen(2 * j)
-            widen(2 * j + 1)
-
-        def wint2(j):
-            wint(j, 0)
-            wint(j, 1)
-
-        def second(dd, j, h):
-            p2(dd, j, h)
-            pex(dd, j, h)
-
-        def quad(k):
-            for n in range(4 * k, 4 * k + 4):
+        def beat(k):
+            for n in range(BEAT * k, BEAT * (k + 1)):
                 unit(n)
-                dhg(n)
 
-        quad(0)
-        yq(1, 1)
-        prod(5)
-        xq(0)
-        qd(0)
-        xg(1)
-        turn_y(2)
-        wtr_raw(3, 0)
-        wscale(3, 0)
-        xint(1)
-        load_g(0, 2)
-        quad(1)
-        yq(2, 0)
-        yq(2, 1)
-        xq(1)
-        qd(1)
-        xg(2)
-        wtr_raw(3, 1)
-        wscale(3, 1)
-        turn_y(3)
-        xint(2)
-        load_g(1, 2)
-        quad(2)
-        yq(3, 0)
-        yq(3, 1)
-        xq(2)
-        qd(2)
-        xg(3)
-        swiden(8)
-        swiden(9)
-        turn_w(2)
-        second(0, 0, 0)
-        second(0, 0, 1)
-        xint(3)
-        load_g(2, 2)
-        quad(3)
-        wq(2)
-        xq(3)
-        widen(10)
-        qd(3)
-        wint2(3)
-        second(0, 1, 0)
-        second(0, 1, 1)
-        turn_raw(4)
-        load_g(3, 2)
-        quad(4)
-        wq(3)
-        second(1, 0, 0)
-        widen(11)
-        qd(4)
-        p2(1, 0, 1)
-        pex1(0, 1)
-        gadd(0, 1, 4)
-        p2(1, 1, 0)
-        pex1(1, 0)
-        p2(1, 1, 1)
-        quad(5)
-        pex(1, 1, 1)
-        qd(5)
-        gadd(1, 0, 5)
-        wint2(4)
-        second(0, 2, 0)
-        second(0, 2, 1)
-        turn_raw(5)
-        quad(6)
-        wq(4)
-        qd(6)
-        p2(1, 2, 0)
-        pex1(2, 0)
-        gadd(2, 0, 6)
-        p2(1, 2, 1)
-        pex1(2, 1)
-        quad(7)
-        qd(7)
-        gadd(2, 1, 7)
-        wint2(5)
-        second(0, 3, 0)
-        second(0, 3, 1)
-        quad(8)
-        wq(5)
-        qd(8)
-        p2(1, 3, 0)
-        pex1(3, 0)
-        gadd(3, 0, 8)
-        p2(1, 3, 1)
-        pex1(3, 1)
-        quad(9)
-        qd(9)
-        gadd(3, 1, 9)
-        second(0, 4, 0)
-        second(0, 4, 1)
-        quad(10)
-        second(1, 4, 0)
-        qd(10)
-        p2(1, 4, 1)
-        pex1(4, 1)
-        gadd(4, 1, 10)
-        unit(44)
-        dhg(44)
-        unit(45)
-        dhg(45)
-        unit(46)
-        dhg(46)
-        qd(11, 0, 256)
+        def quantise_dh(k, first=0, count=BEAT):
+            source = dh[k][:, P * first : P * (first + count), :].rearrange("p f t -> p (f t)")
+            quantised = quantise("dh", 6, source)
+            for i in range(count):
+                dh_codes[BEAT * k + first + i] = (quantised, P * i)
+
+        def half(d, j, h, strip=0, width=PAIR):
+            ps = side_bank([P, 2, width])
+            for k2 in range(2):
+                k0 = P * (2 * h + k2)
+                for q in range(2):
+                    quantised, f0 = dh_codes[place[2 * d + q, 2 * j + strip]]
+                    multiply(
+                        ps[:, k2, :], x_codes[2 * d + q], slice(k0, k0 + P), quantised, slice(f0, f0 + width), q == 0, q == 1
+                    )
+            bank["half", d, j, h, strip] = ps
+
+        def shard0(j):
+            for h in range(2):
+                half(0, j, h)
+                first_term[j, h] = work.tile([P, 2, PAIR], F32, name="first_term", bufs=8)
+                nc.scalar.activation(out=first_term[j, h][:], in_=bank["half", 0, j, h, 0][:], func=COPY, scale=c_all[:, 0:1])
+
+        def sum_on_vector(j, h, strip=0, width=PAIR):
+            total = first_term[j, h][:, :, P * strip : P * strip + width]
+            nc.vector.scalar_tensor_tensor(
+                out=total, in0=bank["half", 1, j, h, strip][:], scalar=c_all[:, 1:2], in1=total, op0=MULT, op1=ADD
+            )
+            f0 = PAIR * j + P * strip
+            nc.sync.dma_start(out=out_view[h][:, :, f0 : f0 + width], in_=total)
+
+        def shard1_on_scalar(j, h):
+            half(1, j, h)
+            second_term[j, h] = work.tile([P, 2, PAIR], F32, name="second_term", bufs=4)
+            nc.scalar.activation(out=second_term[j, h][:], in_=bank["half", 1, j, h, 0][:], func=COPY, scale=c_all[:, 1:2])
+
+        def sum_on_gpsimd(j, h, k):
+            total = work.tile([P, 2, PAIR], F32, name=slot_after(k), bufs=1, align_bytes=64)
+            nc.gpsimd.tensor_tensor(out=total[:], in0=first_term[j, h][:], in1=second_term[j, h][:], op=ADD)
+            nc.sync.dma_start(out=out_view[h][:, :, PAIR * j : PAIR * (j + 1)], in_=total[:])
+
+        turn_y(0, 0)
+        turn_y(0, 1)
+        for b in range(BEAT):
+            scale_strip(b, parts=2 if b == 0 else 1)
+            if b < 2:
+                turn_y(0, b + 2)
+            turn_strip(b)
+            if b == 2:
+                turn_y(1, 0)
+        quantise_y(0, 0)
+        quantise_y(0, 1)
+        for t in range(1, PACK):
+            turn_y(1, t)
+        quantise_w(0)
+        quantise_w(1)
+        scale_strip(4)
+        quantise_y(1, 0)
+        mix_x_gpsimd(0, "y_turned2")
+        widen_pair(3)
+        mix_x_scalar(0)
+        nc.scalar.copy(out=c_all[:], in_=c_bf[:])
+        load_y_group(3)
+        load_g(2, 0)
+        load_w(4)
+        load_x(2)
+        load_g(3, 0)
+        load_x(3)
+        load_w(5)
+        for a in range(GROUPS):
+            load_g(a, 1)
+
+        def scalar_road(k):
+            return {lead: (k + lead) // 2 for lead in (7, 5, 3) if k % 2 == 1 and VECTOR_PAIRS <= (k + lead) // 2 < PAIRS}
+
+        for k in range(GROUPS):
+            road = scalar_road(k)
+            for n in range(BEAT * k, BEAT * (k + 1)):
+                if k == 1 and n % BEAT == BEAT - 1:
+                    turn_and_scale_pair(road[5])
+                unit(n)
+            if k == 0:
+                quantise_y(1, 1)
+                scale_strip(5)
+            elif k + 1 < GROUPS:
+                quantise_y(k + 1, 0)
+                quantise_y(k + 1, 1)
+            else:
+                quantise_w(2)
+            quantise_x(k)
+            quantise_dh(k)
+            if k + 1 < GROUPS:
+                mix_x_gpsimd(k + 1, slot_after(k))
+            if k < 2:
+                for t in range(PACK):
+                    turn_y(k + 2, t)
+            if k == 2:
+                turn_strip(4)
+                turn_strip(5)
+            if 3 in road:
+                mix_pair(road[3])
+            if k >= 2:
+                shard0(k - 2)
+            if k + 1 < GROUPS:
+                mix_x_scalar(k + 1)
+            if k == 3:
+                turn_and_scale_pair(road[5])
+            if 7 in road:
+                widen_pair(road[7])
+            load_g(k, 2)
+
+        for j in range(2, PAIRS):
+            k = 2 * j
+            beat(k)
+            if j + 1 < PAIRS:
+                quantise_w(j + 1)
+            if j == 2:
+                for early in range(2):
+                    half(1, early, 0)
+                    half(1, early, 1)
+                sum_on_vector(0, 0)
+                quantise_dh(k)
+                sum_on_vector(0, 1)
+            elif j + 1 < PAIRS:
+                quantise_dh(k)
+                shard1_on_scalar(j - 1, 0)
+                sum_on_gpsimd(j - 1, 0, k)
+                shard1_on_scalar(j - 1, 1)
+            else:
+                half(1, j - 1, 1)
+                sum_on_vector(j - 1, 1)
+                quantise_dh(k)
+                shard1_on_scalar(j - 1, 0)
+                sum_on_gpsimd(j - 1, 0, k)
+                break
+
+            k = 2 * j + 1
+            road = scalar_road(k)
+            beat(k)
+            if j == 2:
+                sum_on_vector(1, 0)
+                quantise_dh(k)
+                sum_on_vector(1, 1)
+            else:
+                quantise_dh(k)
+                sum_on_gpsimd(j - 1, 1, k)
+            if 3 in road:
+                mix_pair(road[3])
+            shard0(j)
+            if 5 in road:
+                turn_and_scale_pair(road[5])
+
+        for n in (44, 45, 46):
+            unit(n)
+        quantise_dh(11, 0, 2)
         unit(47)
-        dhg(47)
-        second(0, 5, 0)
-        second(0, 5, 1)
-        qd(11, 256, 384)
-        qd(11, 384, 512)
-        tail_pass(0, 0)
-        tail_pass(0, 1)
-        tail_pass(1, 0)
-        tail_pass(1, 1)
-        tail_out(0, 0)
-        tail_out(0, 1)
-        tail_out(1, 0)
-        tail_out(1, 1)
+        shard0(5)
+        quantise_dh(11, 2, 1)
+        quantise_dh(11, 3, 1)
+        for strip in range(2):
+            for h in range(2):
+                half(1, 5, h, strip, P)
+        for strip in range(2):
+            for h in range(2):
+                sum_on_vector(5, h, strip, P)

@@ -26,8 +26,7 @@ G_COLS = BEAT * P
 RUN = 4
 VECTOR_PAIRS = 3
 X_GPSIMD = 384
-UNIT_BANKS = 3
-SIDE_BANKS = 5
+BANKS = 8
 DH_SLOTS = 3
 Y_SLOTS = 4
 
@@ -99,7 +98,7 @@ def tile_shard_weight_grad_s7_kernel(tc, x, dy, w2_bytes, w2_scale, g, c, out):
         c_all = keep.tile([P, D], F32, name="c_all")
         scale_all = keep.tile([P, 2, P, PACK], F32, name="scale_all", align_bytes=64)
         for gi in range(2):
-            ps = psum.tile([P, PACK, P], F32, name="unit", bufs=UNIT_BANKS)
+            ps = psum.tile([P, PACK, P], F32, name="bank", bufs=BANKS)
             for t in range(PACK):
                 nc.tensor.transpose(ps[:, t, :], scale_col[:, gi, t : t + 1].to_broadcast([P, P]), ident[:])
             nc.scalar.copy(out=scale_all[:, gi], in_=ps[:].rearrange("p t j -> p j t"))
@@ -111,7 +110,7 @@ def tile_shard_weight_grad_s7_kernel(tc, x, dy, w2_bytes, w2_scale, g, c, out):
         bank, first_term, second_term = {}, {}, {}
 
         def side_bank(shape):
-            return psum.tile(shape, F32, name="side", bufs=SIDE_BANKS)
+            return psum.tile(shape, F32, name="bank", bufs=BANKS)
 
         def quantise(name, bufs, source):
             words = source.shape[1] // PACK
@@ -249,7 +248,7 @@ def tile_shard_weight_grad_s7_kernel(tc, x, dy, w2_bytes, w2_scale, g, c, out):
         def unit(n):
             a, b = units[n]
             k, i = divmod(n, BEAT)
-            ps = psum.tile([P, PACK, P], F32, name="unit", bufs=UNIT_BANKS)
+            ps = psum.tile([P, PACK, P], F32, name="bank", bufs=BANKS)
             for t in range(PACK):
                 for gi in range(2):
                     y0 = PAIR * (t % 2) + P * gi
@@ -388,9 +387,8 @@ def tile_shard_weight_grad_s7_kernel(tc, x, dy, w2_bytes, w2_scale, g, c, out):
             if j + 1 < PAIRS:
                 quantise_w(j + 1)
             if j == 2:
-                for early in range(2):
-                    half(1, early, 0)
-                    half(1, early, 1)
+                half(1, 0, 0)
+                half(1, 0, 1)
                 sum_on_vector(0, 0)
                 quantise_dh(k)
                 sum_on_vector(0, 1)
@@ -411,6 +409,8 @@ def tile_shard_weight_grad_s7_kernel(tc, x, dy, w2_bytes, w2_scale, g, c, out):
             road = scalar_road(k)
             beat(k)
             if j == 2:
+                half(1, 1, 0)
+                half(1, 1, 1)
                 sum_on_vector(1, 0)
                 quantise_dh(k)
                 sum_on_vector(1, 1)

@@ -77,13 +77,13 @@ def tile_shard_weight_grad_s7_kernel(tc, x, dy, w2_bytes, w2_scale, g, c, out):
         c_bf = keep.tile([P, D], BF16, name="c_bf")
         nc.scalar.dma_start(out=c_bf[:], in_=c.partition_broadcast(P))
 
-        load_w(0, (0,))
         load_y(0, (0,))
+        load_w(0, (0,))
         load_y(0, (1,))
-        load_w(0, (1,))
         load_y(0, (2,))
-        load_y(0, (3,))
+        load_w(0, (1,))
         load_w(1)
+        load_y(0, (3,))
         load_y_group(1)
         load_w(2)
         load_w(3)
@@ -93,24 +93,22 @@ def tile_shard_weight_grad_s7_kernel(tc, x, dy, w2_bytes, w2_scale, g, c, out):
         load_g(1, 0)
         load_x(1)
 
+        def psum_bank(shape):
+            return psum.tile(shape, F32, name="bank", bufs=BANKS)
+
         ident = keep.tile([P, P], F32, name="ident", align_bytes=64)
         make_identity(nc, ident[:])
         c_all = keep.tile([P, D], F32, name="c_all")
         scale_all = keep.tile([P, 2, P, PACK], F32, name="scale_all", align_bytes=64)
         for gi in range(2):
-            ps = psum.tile([P, PACK, P], F32, name="bank", bufs=BANKS)
+            ps = psum_bank([P, PACK, P])
             for t in range(PACK):
                 nc.tensor.transpose(ps[:, t, :], scale_col[:, gi, t : t + 1].to_broadcast([P, P]), ident[:])
             nc.scalar.copy(out=scale_all[:, gi], in_=ps[:].rearrange("p t j -> p j t"))
 
-        w_wide, w_planes, w_turned, w_codes, w_scales = {}, {}, {}, {}, {}
-        y_turned, y_codes, y_scales = {}, {}, {}
-        x_mixed, x_codes, x_scales = {}, {}, {}
-        dh, dh_codes, dh_scales = {}, {}, {}
+        w_wide, w_split, w_planes, w_turned, w_mx = {}, {}, {}, {}, {}
+        y_turned, y_mx, x_mixed, x_mx, dh, dh_mx = {}, {}, {}, {}, {}, {}
         bank, first_term, second_term = {}, {}, {}
-
-        def side_bank(shape):
-            return psum.tile(shape, F32, name="bank", bufs=BANKS)
 
         def quantise(name, bufs, source):
             words = source.shape[1] // PACK
@@ -140,22 +138,24 @@ def tile_shard_weight_grad_s7_kernel(tc, x, dy, w2_bytes, w2_scale, g, c, out):
             nc.tensor.transpose(ps, row.bitcast(F32)[:, PAIR * gi + u : PAIR * (gi + 1) : 2], ident[:])
 
         def turn_row(row, turned):
-            ps = side_bank([P, 2, 2, P])
+            ps = psum_bank([P, 2, 2, P])
             for gi in range(2):
                 for u in range(2):
                     turn(ps[:, gi, u, :], row, gi, u)
             nc.scalar.copy(out=turned, in_=ps[:].rearrange("p g u m -> p g m u"))
 
+        def y_slot(a, tp):
+            return "y_turned%d" % ((2 * a + tp) % Y_SLOTS)
+
         def turn_y(a, t):
             tp = t // 2
             if (a, tp) not in y_turned:
-                slot = "y_turned%d" % ((2 * a + tp) % Y_SLOTS)
-                y_turned[a, tp] = work.tile([P, 2, 2, P, 2], F32, name=slot, bufs=1, align_bytes=64)
+                y_turned[a, tp] = work.tile([P, 2, 2, P, 2], F32, name=y_slot(a, tp), bufs=1, align_bytes=64)
             turn_row(y_raw[a, tp][:, t % 2, :], y_turned[a, tp][:, t % 2])
 
         def quantise_y(a, tp):
             source = y_turned[a, tp][:].rearrange("p r g m u -> p (r g m u)").bitcast(BF16)
-            y_codes[a, tp] = quantise("y", 2 * GROUPS, source)
+            y_mx[a, tp] = quantise("y", 2 * GROUPS, source)
 
         def wide_tile(b):
             w_wide[b] = work.tile([P, N], BF16, name="w_wide", bufs=6, align_bytes=64)
@@ -184,11 +184,19 @@ def tile_shard_weight_grad_s7_kernel(tc, x, dy, w2_bytes, w2_scale, g, c, out):
             for i in range(2):
                 nc.scalar.copy(out=wide_tile(2 * j + i)[:], in_=w_raw[j][:, i, :].bitcast(FP8))
 
+        def split_pair(j):
+            for b in (2 * j, 2 * j + 1):
+                w_split[b] = work.tile([P, 2, PAIR], F32, name="w_split", bufs=2, align_bytes=64)
+                nc.scalar.copy(out=w_split[b][:], in_=w_wide[b][:].bitcast(F32).rearrange("p (w u) -> p u w", u=2))
+
         def turn_pair(j, gi):
-            ps = side_bank([P, 2, 2, P])
+            ps = psum_bank([P, 2, 2, P])
             for u in range(2):
                 for i in range(2):
-                    turn(ps[:, u, i, :], w_wide[2 * j + i][:], gi, u)
+                    if 2 * j + i in w_split:
+                        nc.tensor.transpose(ps[:, u, i, :], w_split[2 * j + i][:, u, P * gi : P * (gi + 1)], ident[:])
+                    else:
+                        turn(ps[:, u, i, :], w_wide[2 * j + i][:], gi, u)
             bank["pair", j, gi] = ps
 
         def scale_pair(j, gi):
@@ -217,7 +225,7 @@ def tile_shard_weight_grad_s7_kernel(tc, x, dy, w2_bytes, w2_scale, g, c, out):
 
         def quantise_w(j):
             source = w_turned[j][:].rearrange("p g i f u -> p (g i f u)").bitcast(BF16)
-            w_codes[j] = quantise("w", PAIRS, source)
+            w_mx[j] = quantise("w", PAIRS, source)
 
         def slot_after(k):
             return "dh%d" % (k % DH_SLOTS)
@@ -237,24 +245,24 @@ def tile_shard_weight_grad_s7_kernel(tc, x, dy, w2_bytes, w2_scale, g, c, out):
             nc.scalar.copy(out=mixed_runs(x_mixed[a][:, X_GPSIMD:K, :]), in_=in_runs(x_raw[a][:, :, X_GPSIMD:K]))
 
         def quantise_x(a):
-            x_codes[a] = quantise("x", GROUPS, x_mixed[a][:].rearrange("p k t -> p (k t)"))
+            x_mx[a] = quantise("x", GROUPS, x_mixed[a][:].rearrange("p k t -> p (k t)"))
 
         units = [(a, b) for a in range(GROUPS) for b in range(BEAT)]
         units = units + [(a, 2 * j + i) for j in range(2, PAIRS) for a in range(GROUPS) for i in range(2)]
-        units = units[:-BEAT] + [(a, 2 * (PAIRS - 1) + i) for i in range(2) for a in (2, 3)]
+        units = units[:-BEAT] + [(a, 2 * (PAIRS - 1) + i) for i in range(2) for a in range(GROUPS - 2, GROUPS)]
         place = {u: n for n, u in enumerate(units)}
         last_beat = len(units) // BEAT - 1
 
         def unit(n):
             a, b = units[n]
             k, i = divmod(n, BEAT)
-            ps = psum.tile([P, PACK, P], F32, name="bank", bufs=BANKS)
+            ps = psum_bank([P, PACK, P])
             for t in range(PACK):
                 for gi in range(2):
                     y0 = PAIR * (t % 2) + P * gi
                     w0 = PAIR * gi + P * (b % 2)
                     multiply(
-                        ps[:, t, :], y_codes[a, t // 2], slice(y0, y0 + P), w_codes[b // 2], slice(w0, w0 + P), gi == 0, gi == 1
+                        ps[:, t, :], y_mx[a, t // 2], slice(y0, y0 + P), w_mx[b // 2], slice(w0, w0 + P), gi == 0, gi == 1
                     )
             if k not in dh:
                 dh[k] = work.tile([P, BEAT * P, PACK], BF16, name=slot_after(k), bufs=1, align_bytes=64)
@@ -274,16 +282,16 @@ def tile_shard_weight_grad_s7_kernel(tc, x, dy, w2_bytes, w2_scale, g, c, out):
             source = dh[k][:, P * first : P * (first + count), :].rearrange("p f t -> p (f t)")
             quantised = quantise("dh", 6, source)
             for i in range(count):
-                dh_codes[BEAT * k + first + i] = (quantised, P * i)
+                dh_mx[BEAT * k + first + i] = (quantised, P * i)
 
         def half(d, j, h, strip=0, width=PAIR):
-            ps = side_bank([P, 2, width])
+            ps = psum_bank([P, 2, width])
             for k2 in range(2):
                 k0 = P * (2 * h + k2)
                 for q in range(2):
-                    quantised, f0 = dh_codes[place[2 * d + q, 2 * j + strip]]
+                    quantised, f0 = dh_mx[place[2 * d + q, 2 * j + strip]]
                     multiply(
-                        ps[:, k2, :], x_codes[2 * d + q], slice(k0, k0 + P), quantised, slice(f0, f0 + width), q == 0, q == 1
+                        ps[:, k2, :], x_mx[2 * d + q], slice(k0, k0 + P), quantised, slice(f0, f0 + width), q == 0, q == 1
                     )
             bank["half", d, j, h, strip] = ps
 
@@ -311,14 +319,14 @@ def tile_shard_weight_grad_s7_kernel(tc, x, dy, w2_bytes, w2_scale, g, c, out):
             nc.gpsimd.tensor_tensor(out=total[:], in0=first_term[j, h][:], in1=second_term[j, h][:], op=ADD)
             nc.sync.dma_start(out=out_view[h][:, :, PAIR * j : PAIR * (j + 1)], in_=total[:])
 
-        turn_y(0, 0)
-        turn_y(0, 1)
+        for t in range(PACK - 1):
+            turn_y(0, t)
         for b in range(BEAT):
             scale_strip(b, parts=2 if b == 0 else 1)
-            if b < 2:
-                turn_y(0, b + 2)
             turn_strip(b)
-            if b == 2:
+            if b == 0:
+                turn_y(0, PACK - 1)
+            if b == 1:
                 turn_y(1, 0)
         quantise_y(0, 0)
         quantise_y(0, 1)
@@ -326,10 +334,10 @@ def tile_shard_weight_grad_s7_kernel(tc, x, dy, w2_bytes, w2_scale, g, c, out):
             turn_y(1, t)
         quantise_w(0)
         quantise_w(1)
-        scale_strip(4)
+        scale_strip(BEAT)
         quantise_y(1, 0)
-        mix_x_gpsimd(0, "y_turned2")
-        widen_pair(3)
+        mix_x_gpsimd(0, y_slot(1, 0))
+        widen_pair(VECTOR_PAIRS)
         mix_x_scalar(0)
         nc.scalar.copy(out=c_all[:], in_=c_bf[:])
         load_y_group(3)
@@ -342,57 +350,62 @@ def tile_shard_weight_grad_s7_kernel(tc, x, dy, w2_bytes, w2_scale, g, c, out):
         for a in range(GROUPS):
             load_g(a, 1)
 
-        def scalar_road(k):
-            return {lead: (k + lead) // 2 for lead in (7, 5, 3) if k % 2 == 1 and VECTOR_PAIRS <= (k + lead) // 2 < PAIRS}
+        last_pair = PAIRS - 1
+
+        def on_road(k, lead):
+            j, odd = divmod(k + lead, 2)
+            return j if not odd and VECTOR_PAIRS <= j < PAIRS else None
 
         for k in range(GROUPS):
-            road = scalar_road(k)
             for n in range(BEAT * k, BEAT * (k + 1)):
                 if k == 1 and n % BEAT == BEAT - 1:
-                    turn_and_scale_pair(road[5])
+                    turn_strip(BEAT)
+                    turn_strip(BEAT + 1)
                 unit(n)
             if k == 0:
                 quantise_y(1, 1)
-                scale_strip(5)
+                scale_strip(BEAT + 1)
             elif k + 1 < GROUPS:
                 quantise_y(k + 1, 0)
                 quantise_y(k + 1, 1)
-            else:
-                quantise_w(2)
+            if k == 2:
+                quantise_w(VECTOR_PAIRS - 1)
             quantise_x(k)
             quantise_dh(k)
             if k + 1 < GROUPS:
                 mix_x_gpsimd(k + 1, slot_after(k))
-            if k < 2:
+            if k + 2 < GROUPS:
                 for t in range(PACK):
                     turn_y(k + 2, t)
-            if k == 2:
-                turn_strip(4)
-                turn_strip(5)
-            if 3 in road:
-                mix_pair(road[3])
+            if k == 0:
+                split_pair(VECTOR_PAIRS)
+            if on_road(k, 4):
+                turn_and_scale_pair(on_road(k, 4))
+            if on_road(k, 3):
+                mix_pair(on_road(k, 3))
             if k >= 2:
                 shard0(k - 2)
+            if on_road(k, 7):
+                widen_pair(on_road(k, 7))
             if k + 1 < GROUPS:
                 mix_x_scalar(k + 1)
-            if k == 3:
-                turn_and_scale_pair(road[5])
-            if 7 in road:
-                widen_pair(road[7])
             load_g(k, 2)
 
-        for j in range(2, PAIRS):
-            k = 2 * j
+        for k in range(GROUPS, last_beat):
+            j, d = divmod(k, 2)
             beat(k)
-            if j + 1 < PAIRS:
-                quantise_w(j + 1)
+            if on_road(k, 2):
+                quantise_w(on_road(k, 2))
             if j == 2:
-                half(1, 0, 0)
-                half(1, 0, 1)
-                sum_on_vector(0, 0)
+                half(1, d, 0)
+                half(1, d, 1)
+                sum_on_vector(d, 0)
                 quantise_dh(k)
-                sum_on_vector(0, 1)
-            elif j + 1 < PAIRS:
+                sum_on_vector(d, 1)
+            elif d == 1:
+                quantise_dh(k)
+                sum_on_gpsimd(j - 1, 1, k)
+            elif j < last_pair:
                 quantise_dh(k)
                 shard1_on_scalar(j - 1, 0)
                 sum_on_gpsimd(j - 1, 0, k)
@@ -403,36 +416,26 @@ def tile_shard_weight_grad_s7_kernel(tc, x, dy, w2_bytes, w2_scale, g, c, out):
                 quantise_dh(k)
                 shard1_on_scalar(j - 1, 0)
                 sum_on_gpsimd(j - 1, 0, k)
-                break
+            if on_road(k, 3):
+                mix_pair(on_road(k, 3))
+            if d == 1:
+                shard0(j)
+            if on_road(k, 5) == last_pair:
+                split_pair(last_pair)
+            if on_road(k, 4):
+                turn_and_scale_pair(on_road(k, 4))
 
-            k = 2 * j + 1
-            road = scalar_road(k)
-            beat(k)
-            if j == 2:
-                half(1, 1, 0)
-                half(1, 1, 1)
-                sum_on_vector(1, 0)
-                quantise_dh(k)
-                sum_on_vector(1, 1)
-            else:
-                quantise_dh(k)
-                sum_on_gpsimd(j - 1, 1, k)
-            if 3 in road:
-                mix_pair(road[3])
-            shard0(j)
-            if 5 in road:
-                turn_and_scale_pair(road[5])
-
-        for n in (44, 45, 46):
+        first = BEAT * last_beat
+        for n in range(first, first + BEAT - 1):
             unit(n)
-        quantise_dh(11, 0, 2)
-        unit(47)
-        shard0(5)
-        quantise_dh(11, 2, 1)
-        quantise_dh(11, 3, 1)
+        quantise_dh(last_beat, 0, 2)
+        unit(first + BEAT - 1)
+        shard0(last_pair)
+        quantise_dh(last_beat, 2, 1)
+        quantise_dh(last_beat, 3, 1)
         for strip in range(2):
             for h in range(2):
-                half(1, 5, h, strip, P)
+                half(1, last_pair, h, strip, P)
         for strip in range(2):
             for h in range(2):
-                sum_on_vector(5, h, strip, P)
+                sum_on_vector(last_pair, h, strip, P)

@@ -26,8 +26,13 @@ G_COLS = BEAT * P
 RUN = 4
 VECTOR_PAIRS = 3
 X_GPSIMD = 384
+BAR = 2 * BEAT
+BARS = 3
+STAGES = 5
+READS = 1
 BANKS = 8
 DH_SLOTS = 3
+SPLITS = 2
 Y_SLOTS = 4
 
 
@@ -48,7 +53,7 @@ def tile_shard_weight_grad_s7_kernel(tc, x, dy, w2_bytes, w2_scale, g, c, out):
 
         def load_w(j, strips=(0, 1)):
             if j not in w_raw:
-                w_raw[j] = work.tile([P, 2, N], U8, name="w_raw", bufs=PAIRS)
+                w_raw[j] = work.tile([P, 2, N], U8, name="w_raw", bufs=4)
             part = slice(strips[0], strips[-1] + 1)
             nc.sync.dma_start(out=w_raw[j][:, part, :], in_=w_view[j][:, part, :])
 
@@ -65,7 +70,7 @@ def tile_shard_weight_grad_s7_kernel(tc, x, dy, w2_bytes, w2_scale, g, c, out):
             load_y(a, (2, 3))
 
         def load_x(a):
-            x_raw[a] = work.tile([P, PACK, K], BF16, name="x_raw", bufs=GROUPS, align_bytes=64)
+            x_raw[a] = work.tile([P, PACK, K], BF16, name="x_raw", bufs=3, align_bytes=64)
             nc.sync.dma_start(out=x_raw[a][:], in_=samples(x, a))
 
         def load_g(a, chunk):
@@ -82,16 +87,16 @@ def tile_shard_weight_grad_s7_kernel(tc, x, dy, w2_bytes, w2_scale, g, c, out):
         load_y(0, (1,))
         load_y(0, (2,))
         load_w(0, (1,))
-        load_w(1)
         load_y(0, (3,))
+        load_w(1)
         load_y_group(1)
         load_w(2)
-        load_w(3)
-        load_g(0, 0)
+        load_y(2, (0, 1))
         load_x(0)
-        load_y_group(2)
-        load_g(1, 0)
+        load_g(0, 0)
+        load_y(2, (2, 3))
         load_x(1)
+        load_g(1, 0)
 
         def psum_bank(shape):
             return psum.tile(shape, F32, name="bank", bufs=BANKS)
@@ -108,7 +113,7 @@ def tile_shard_weight_grad_s7_kernel(tc, x, dy, w2_bytes, w2_scale, g, c, out):
 
         w_wide, w_split, w_planes, w_turned, w_mx = {}, {}, {}, {}, {}
         y_turned, y_mx, x_mixed, x_mx, dh, dh_mx = {}, {}, {}, {}, {}, {}
-        bank, first_term, second_term = {}, {}, {}
+        bank, first_term, first_pair, second_pair = {}, {}, {}, {}
 
         def quantise(name, bufs, source):
             words = source.shape[1] // PACK
@@ -137,28 +142,43 @@ def tile_shard_weight_grad_s7_kernel(tc, x, dy, w2_bytes, w2_scale, g, c, out):
         def turn(ps, row, gi, u):
             nc.tensor.transpose(ps, row.bitcast(F32)[:, PAIR * gi + u : PAIR * (gi + 1) : 2], ident[:])
 
-        def turn_row(row, turned):
+        def split_row(row):
+            halves = work.tile([P, 2, PAIR], F32, name="split", bufs=SPLITS, align_bytes=64)
+            nc.scalar.copy(out=halves[:], in_=row.bitcast(F32).rearrange("p (w u) -> p u w", u=2))
+            return halves
+
+        def turn_row(row, turned, halves=None):
             ps = psum_bank([P, 2, 2, P])
             for gi in range(2):
                 for u in range(2):
-                    turn(ps[:, gi, u, :], row, gi, u)
+                    if halves is None:
+                        turn(ps[:, gi, u, :], row, gi, u)
+                    else:
+                        nc.tensor.transpose(ps[:, gi, u, :], halves[:, u, P * gi : P * (gi + 1)], ident[:])
             nc.scalar.copy(out=turned, in_=ps[:].rearrange("p g u m -> p g m u"))
 
-        def y_slot(a, tp):
-            return "y_turned%d" % ((2 * a + tp) % Y_SLOTS)
+        free_stages = list(range(STAGES))
+        stage_of = {}
+
+        def stage(key, shape, dtype, newest=False):
+            stage_of[key] = free_stages.pop(-1 if newest else 0)
+            return work.tile(shape, dtype, name="stage%d" % stage_of[key], bufs=1, align_bytes=64)
+
+        def leave(key):
+            free_stages.append(stage_of[key])
 
         def turn_y(a, t):
-            tp = t // 2
-            if (a, tp) not in y_turned:
-                y_turned[a, tp] = work.tile([P, 2, 2, P, 2], F32, name=y_slot(a, tp), bufs=1, align_bytes=64)
-            turn_row(y_raw[a, tp][:, t % 2, :], y_turned[a, tp][:, t % 2])
+            if a not in y_turned:
+                y_turned[a] = stage(("y", a), [P, PACK, 2, P, 2], F32)
+            turn_row(y_raw[a, t // 2][:, t % 2, :], y_turned[a][:, t])
 
-        def quantise_y(a, tp):
-            source = y_turned[a, tp][:].rearrange("p r g m u -> p (r g m u)").bitcast(BF16)
-            y_mx[a, tp] = quantise("y", 2 * GROUPS, source)
+        def quantise_y(a):
+            source = y_turned[a][:].rearrange("p r g m u -> p (r g m u)").bitcast(BF16)
+            y_mx[a] = quantise("y", GROUPS, source)
+            leave(("y", a))
 
         def wide_tile(b):
-            w_wide[b] = work.tile([P, N], BF16, name="w_wide", bufs=6, align_bytes=64)
+            w_wide[b] = work.tile([P, N], BF16, name="w_wide", bufs=4, align_bytes=64)
             return w_wide[b]
 
         def pair_tile(j):
@@ -178,16 +198,32 @@ def tile_shard_weight_grad_s7_kernel(tc, x, dy, w2_bytes, w2_scale, g, c, out):
                 )
 
         def turn_strip(b):
-            turn_row(w_wide[b][:], pair_tile(b // 2)[:, :, b % 2])
+            turn_row(w_wide[b][:], pair_tile(b // 2)[:, :, b % 2], w_split.get(b))
 
-        def widen_pair(j):
+        def split_strip(b):
+            w_split[b] = split_row(w_wide[b][:])
+
+        def split_tiles(j):
+            both = stage(("w", j), [P, 2, 2, PAIR], F32, newest=True)
             for i in range(2):
-                nc.scalar.copy(out=wide_tile(2 * j + i)[:], in_=w_raw[j][:, i, :].bitcast(FP8))
+                w_split[2 * j + i] = both[:, i]
 
-        def split_pair(j):
-            for b in (2 * j, 2 * j + 1):
-                w_split[b] = work.tile([P, 2, PAIR], F32, name="w_split", bufs=2, align_bytes=64)
-                nc.scalar.copy(out=w_split[b][:], in_=w_wide[b][:].bitcast(F32).rearrange("p (w u) -> p u w", u=2))
+        def scale_split(engine, b, n0, n1):
+            ws = slice(n0 // PACK, n1 // PACK)
+            engine.tensor_tensor(
+                out=w_split[b].bitcast(BF16).rearrange("p u (w e) -> p u w e", e=2)[:, :, ws, :],
+                in0=w_wide[b][:].rearrange("p (w u e) -> p u w e", u=2, e=2)[:, :, ws, :],
+                in1=scale_all[:].rearrange("p g j (u e) -> p u (g j) e", u=2)[:, :, ws, :],
+                op=MULT,
+            )
+
+        def scale_pair_gpsimd(j):
+            split_tiles(j)
+            for i in range(2):
+                scale_split(nc.gpsimd, 2 * j + i, 0, N)
+
+        def widen_strip(b):
+            nc.scalar.copy(out=wide_tile(b)[:], in_=w_raw[b // 2][:, b % 2, :].bitcast(FP8))
 
         def turn_pair(j, gi):
             ps = psum_bank([P, 2, 2, P])
@@ -200,7 +236,7 @@ def tile_shard_weight_grad_s7_kernel(tc, x, dy, w2_bytes, w2_scale, g, c, out):
             bank["pair", j, gi] = ps
 
         def scale_pair(j, gi):
-            w_planes[j, gi] = work.tile([P, PACK, PAIR], BF16, name="w_planes", bufs=4, align_bytes=64)
+            w_planes[j, gi] = work.tile([P, PACK, PAIR], BF16, name="w_planes", bufs=2, align_bytes=64)
             for t in range(PACK):
                 u, e = divmod(t, 2)
                 elements = bank["pair", j, gi][:, u].rearrange("p i f -> p (i f)").bitcast(BF16)
@@ -210,11 +246,6 @@ def tile_shard_weight_grad_s7_kernel(tc, x, dy, w2_bytes, w2_scale, g, c, out):
                     func=COPY,
                     scale=scale_col[:, gi, t : t + 1],
                 )
-
-        def turn_and_scale_pair(j):
-            for gi in range(2):
-                turn_pair(j, gi)
-                scale_pair(j, gi)
 
         def mix_pair(j):
             for gi in range(2):
@@ -227,13 +258,11 @@ def tile_shard_weight_grad_s7_kernel(tc, x, dy, w2_bytes, w2_scale, g, c, out):
             source = w_turned[j][:].rearrange("p g i f u -> p (g i f u)").bitcast(BF16)
             w_mx[j] = quantise("w", PAIRS, source)
 
-        def slot_after(k):
-            return "dh%d" % (k % DH_SLOTS)
-
-        def mix_x_gpsimd(a, slot):
-            x_mixed[a] = work.tile([P, K, PACK], BF16, name=slot, bufs=1, align_bytes=64)
+        def mix_x_gpsimd(a):
+            if a // 2 not in x_mixed:
+                x_mixed[a // 2] = stage(("x", a // 2), [P, 2, K, PACK], BF16, newest=True)
             nc.gpsimd.tensor_scalar(
-                out=x_mixed[a][:, 0:X_GPSIMD, :],
+                out=x_mixed[a // 2][:, a % 2, 0:X_GPSIMD, :],
                 in0=x_raw[a][:, :, 0:X_GPSIMD].rearrange("p t k -> p k t"),
                 scalar1=1.0,
                 scalar2=0.0,
@@ -242,30 +271,40 @@ def tile_shard_weight_grad_s7_kernel(tc, x, dy, w2_bytes, w2_scale, g, c, out):
             )
 
         def mix_x_scalar(a):
-            nc.scalar.copy(out=mixed_runs(x_mixed[a][:, X_GPSIMD:K, :]), in_=in_runs(x_raw[a][:, :, X_GPSIMD:K]))
+            nc.scalar.copy(
+                out=mixed_runs(x_mixed[a // 2][:, a % 2, X_GPSIMD:K, :]), in_=in_runs(x_raw[a][:, :, X_GPSIMD:K])
+            )
 
-        def quantise_x(a):
-            x_mx[a] = quantise("x", GROUPS, x_mixed[a][:].rearrange("p k t -> p (k t)"))
+        def quantise_x(d):
+            x_mx[d] = quantise("x", D, x_mixed[d][:].rearrange("p q k t -> p (q k t)"))
+            leave(("x", d))
 
         units = [(a, b) for a in range(GROUPS) for b in range(BEAT)]
         units = units + [(a, 2 * j + i) for j in range(2, PAIRS) for a in range(GROUPS) for i in range(2)]
         units = units[:-BEAT] + [(a, 2 * (PAIRS - 1) + i) for i in range(2) for a in range(GROUPS - 2, GROUPS)]
         place = {u: n for n, u in enumerate(units)}
         last_beat = len(units) // BEAT - 1
+        chunks = [BAR] * BARS + [BEAT] * (len(units) // BEAT - 2 * BARS)
+        chunk_of = [(k, i) for k in range(len(chunks)) for i in range(chunks[k])]
 
         def unit(n):
             a, b = units[n]
-            k, i = divmod(n, BEAT)
             ps = psum_bank([P, PACK, P])
+            bank["unit", n] = ps
             for t in range(PACK):
                 for gi in range(2):
-                    y0 = PAIR * (t % 2) + P * gi
+                    y0 = PAIR * t + P * gi
                     w0 = PAIR * gi + P * (b % 2)
                     multiply(
-                        ps[:, t, :], y_mx[a, t // 2], slice(y0, y0 + P), w_mx[b // 2], slice(w0, w0 + P), gi == 0, gi == 1
+                        ps[:, t, :], y_mx[a], slice(y0, y0 + P), w_mx[b // 2], slice(w0, w0 + P), gi == 0, gi == 1
                     )
+
+        def read_unit(n):
+            a, b = units[n]
+            k, i = chunk_of[n]
+            ps = bank["unit", n]
             if k not in dh:
-                dh[k] = work.tile([P, BEAT * P, PACK], BF16, name=slot_after(k), bufs=1, align_bytes=64)
+                dh[k] = stage(("dh", k), [P, chunks[k] * P, PACK], BF16)
             f0 = P * (b % BEAT)
             nc.vector.tensor_tensor(
                 out=mixed_runs(dh[k][:, P * i : P * (i + 1), :]),
@@ -275,14 +314,23 @@ def tile_shard_weight_grad_s7_kernel(tc, x, dy, w2_bytes, w2_scale, g, c, out):
             )
 
         def beat(k):
-            for n in range(BEAT * k, BEAT * (k + 1)):
-                unit(n)
+            for n in range(BEAT * k, BEAT * (k + 1), READS):
+                unit_run(n, READS)
 
-        def quantise_dh(k, first=0, count=BEAT):
+        def unit_run(n, count):
+            for m in range(n, n + count):
+                unit(m)
+            for m in reversed(range(n, n + count)):
+                read_unit(m)
+
+        def quantise_dh(k, first=0, count=None):
+            count = count or chunks[k]
             source = dh[k][:, P * first : P * (first + count), :].rearrange("p f t -> p (f t)")
-            quantised = quantise("dh", 6, source)
+            quantised = quantise("dh", 4, source)
             for i in range(count):
-                dh_mx[BEAT * k + first + i] = (quantised, P * i)
+                dh_mx[sum(chunks[:k]) + first + i] = (quantised, P * i)
+            if first + count == chunks[k]:
+                leave(("dh", k))
 
         def half(d, j, h, strip=0, width=PAIR):
             ps = psum_bank([P, 2, width])
@@ -291,15 +339,17 @@ def tile_shard_weight_grad_s7_kernel(tc, x, dy, w2_bytes, w2_scale, g, c, out):
                 for q in range(2):
                     quantised, f0 = dh_mx[place[2 * d + q, 2 * j + strip]]
                     multiply(
-                        ps[:, k2, :], x_mx[2 * d + q], slice(k0, k0 + P), quantised, slice(f0, f0 + width), q == 0, q == 1
+                        ps[:, k2, :], x_mx[d], slice(K * q + k0, K * q + k0 + P), quantised, slice(f0, f0 + width), q == 0, q == 1
                     )
             bank["half", d, j, h, strip] = ps
 
-        def shard0(j):
-            for h in range(2):
+        def shard0(j, hs=(0, 1)):
+            for h in hs:
                 half(0, j, h)
-                first_term[j, h] = work.tile([P, 2, PAIR], F32, name="first_term", bufs=8)
-                nc.scalar.activation(out=first_term[j, h][:], in_=bank["half", 0, j, h, 0][:], func=COPY, scale=c_all[:, 0:1])
+                if h == 0:
+                    first_pair[j] = work.tile([P, 2, 2, PAIR], F32, name="first_term", bufs=4)
+                first_term[j, h] = first_pair[j][:, h]
+                nc.scalar.activation(out=first_term[j, h], in_=bank["half", 0, j, h, 0][:], func=COPY, scale=c_all[:, 0:1])
 
         def sum_on_vector(j, h, strip=0, width=PAIR):
             total = first_term[j, h][:, :, P * strip : P * strip + width]
@@ -309,130 +359,154 @@ def tile_shard_weight_grad_s7_kernel(tc, x, dy, w2_bytes, w2_scale, g, c, out):
             f0 = PAIR * j + P * strip
             nc.sync.dma_start(out=out_view[h][:, :, f0 : f0 + width], in_=total)
 
-        def shard1_on_scalar(j, h):
-            half(1, j, h)
-            second_term[j, h] = work.tile([P, 2, PAIR], F32, name="second_term", bufs=4)
-            nc.scalar.activation(out=second_term[j, h][:], in_=bank["half", 1, j, h, 0][:], func=COPY, scale=c_all[:, 1:2])
+        def shard1_pair(j, hs=(0, 1)):
+            second_pair[j] = work.tile([P, 2, 2, PAIR], F32, name="second_term", bufs=3)
+            for h in hs:
+                half(1, j, h)
+                nc.scalar.activation(
+                    out=second_pair[j][:, h], in_=bank["half", 1, j, h, 0][:], func=COPY, scale=c_all[:, 1:2]
+                )
 
-        def sum_on_gpsimd(j, h, k):
-            total = work.tile([P, 2, PAIR], F32, name=slot_after(k), bufs=1, align_bytes=64)
-            nc.gpsimd.tensor_tensor(out=total[:], in0=first_term[j, h][:], in1=second_term[j, h][:], op=ADD)
-            nc.sync.dma_start(out=out_view[h][:, :, PAIR * j : PAIR * (j + 1)], in_=total[:])
+        def sums_on_gpsimd(pairs=(), halves=()):
+            total = stage("total", [P, BEAT, 2, PAIR], F32, newest=True)
+            i = 0
+            for j in pairs:
+                nc.gpsimd.tensor_tensor(out=total[:, i : i + 2], in0=first_pair[j][:], in1=second_pair[j][:], op=ADD)
+                for h in range(2):
+                    nc.sync.dma_start(out=out_view[h][:, :, PAIR * j : PAIR * (j + 1)], in_=total[:, i + h])
+                i = i + 2
+            for j, h in halves:
+                nc.gpsimd.tensor_tensor(out=total[:, i], in0=first_term[j, h], in1=second_pair[j][:, h], op=ADD)
+                nc.sync.dma_start(out=out_view[h][:, :, PAIR * j : PAIR * (j + 1)], in_=total[:, i])
+                i = i + 1
+            leave("total")
 
-        for t in range(PACK - 1):
+        for t in range(PACK):
             turn_y(0, t)
         for b in range(BEAT):
             scale_strip(b, parts=2 if b == 0 else 1)
             turn_strip(b)
-            if b == 0:
-                turn_y(0, PACK - 1)
-            if b == 1:
-                turn_y(1, 0)
-        quantise_y(0, 0)
-        quantise_y(0, 1)
-        for t in range(1, PACK):
-            turn_y(1, t)
-        quantise_w(0)
-        quantise_w(1)
-        scale_strip(BEAT)
-        quantise_y(1, 0)
-        mix_x_gpsimd(0, y_slot(1, 0))
-        widen_pair(VECTOR_PAIRS)
-        mix_x_scalar(0)
-        nc.scalar.copy(out=c_all[:], in_=c_bf[:])
+            if b > 0:
+                turn_y(1, b - 1)
+        quantise_y(0)
+        turn_y(1, PACK - 1)
+        turn_y(2, 0)
+        load_w(3)
         load_y_group(3)
         load_g(2, 0)
         load_w(4)
         load_x(2)
         load_g(3, 0)
+        quantise_w(0)
+        scale_strip(4)
+        quantise_w(1)
+        scale_strip(5)
+        quantise_y(1)
+        mix_x_gpsimd(0)
+        mix_x_gpsimd(1)
+        mix_x_scalar(0)
+        nc.scalar.copy(out=c_all[:], in_=c_bf[:])
+        split_strip(4)
+        split_strip(5)
         load_x(3)
+        load_g(0, 1)
+        load_g(1, 1)
+        load_g(2, 1)
+        load_g(3, 1)
         load_w(5)
-        for a in range(GROUPS):
-            load_g(a, 1)
-
-        last_pair = PAIRS - 1
-
-        def on_road(k, lead):
-            j, odd = divmod(k + lead, 2)
-            return j if not odd and VECTOR_PAIRS <= j < PAIRS else None
-
-        for k in range(GROUPS):
-            for n in range(BEAT * k, BEAT * (k + 1)):
-                if k == 1 and n % BEAT == BEAT - 1:
-                    turn_strip(BEAT)
-                    turn_strip(BEAT + 1)
-                unit(n)
-            if k == 0:
-                quantise_y(1, 1)
-                scale_strip(BEAT + 1)
-            elif k + 1 < GROUPS:
-                quantise_y(k + 1, 0)
-                quantise_y(k + 1, 1)
-            if k == 2:
-                quantise_w(VECTOR_PAIRS - 1)
-            quantise_x(k)
-            quantise_dh(k)
-            if k + 1 < GROUPS:
-                mix_x_gpsimd(k + 1, slot_after(k))
-            if k + 2 < GROUPS:
-                for t in range(PACK):
-                    turn_y(k + 2, t)
-            if k == 0:
-                split_pair(VECTOR_PAIRS)
-            if on_road(k, 4):
-                turn_and_scale_pair(on_road(k, 4))
-            if on_road(k, 3):
-                mix_pair(on_road(k, 3))
-            if k >= 2:
-                shard0(k - 2)
-            if on_road(k, 7):
-                widen_pair(on_road(k, 7))
-            if k + 1 < GROUPS:
-                mix_x_scalar(k + 1)
-            load_g(k, 2)
-
-        for k in range(GROUPS, last_beat):
-            j, d = divmod(k, 2)
-            beat(k)
-            if on_road(k, 2):
-                quantise_w(on_road(k, 2))
-            if j == 2:
-                half(1, d, 0)
-                half(1, d, 1)
-                sum_on_vector(d, 0)
-                quantise_dh(k)
-                sum_on_vector(d, 1)
-            elif d == 1:
-                quantise_dh(k)
-                sum_on_gpsimd(j - 1, 1, k)
-            elif j < last_pair:
-                quantise_dh(k)
-                shard1_on_scalar(j - 1, 0)
-                sum_on_gpsimd(j - 1, 0, k)
-                shard1_on_scalar(j - 1, 1)
-            else:
-                half(1, j - 1, 1)
-                sum_on_vector(j - 1, 1)
-                quantise_dh(k)
-                shard1_on_scalar(j - 1, 0)
-                sum_on_gpsimd(j - 1, 0, k)
-            if on_road(k, 3):
-                mix_pair(on_road(k, 3))
-            if d == 1:
-                shard0(j)
-            if on_road(k, 5) == last_pair:
-                split_pair(last_pair)
-            if on_road(k, 4):
-                turn_and_scale_pair(on_road(k, 4))
-
+        beat(0)
+        for t in range(1, PACK):
+            turn_y(2, t)
+        beat(1)
+        mix_x_scalar(1)
+        widen_strip(6)
+        turn_strip(4)
+        turn_strip(5)
+        for t in range(PACK):
+            turn_y(3, t)
+        quantise_y(2)
+        widen_strip(7)
+        quantise_x(0)
+        quantise_dh(0)
+        quantise_y(3)
+        mix_x_gpsimd(2)
+        mix_x_gpsimd(3)
+        load_g(0, 2)
+        load_g(1, 2)
+        mix_x_scalar(2)
+        widen_strip(8)
+        beat(2)
+        turn_pair(3, 0)
+        turn_pair(3, 1)
+        scale_pair(3, 0)
+        scale_pair(3, 1)
+        mix_x_scalar(3)
+        mix_pair(3)
+        beat(3)
+        shard0(0)
+        shard0(1)
+        widen_strip(9)
+        quantise_w(2)
+        quantise_x(1)
+        quantise_dh(1)
+        quantise_w(3)
+        scale_pair_gpsimd(4)
+        load_g(2, 2)
+        load_g(3, 2)
+        widen_strip(10)
+        beat(4)
+        widen_strip(11)
+        beat(5)
+        shard1_pair(0, (0,))
+        half(1, 0, 1)
+        shard1_pair(1)
+        sum_on_vector(0, 1)
+        quantise_dh(2)
+        sums_on_gpsimd(halves=((0, 0),))
+        split_strip(10)
+        split_strip(11)
+        beat(6)
+        quantise_dh(3)
+        sums_on_gpsimd(pairs=(1,))
+        turn_strip(8)
+        turn_strip(9)
+        leave(("w", 4))
+        turn_pair(5, 0)
+        turn_pair(5, 1)
+        shard0(2)
+        scale_pair(5, 0)
+        scale_pair(5, 1)
+        beat(7)
+        quantise_w(4)
+        quantise_dh(4)
+        shard1_pair(2)
+        sums_on_gpsimd(pairs=(2,))
+        shard0(3)
+        mix_pair(5)
+        beat(8)
+        quantise_w(5)
+        quantise_dh(5)
+        shard1_pair(3)
+        sums_on_gpsimd(halves=((3, 0),))
+        beat(9)
+        quantise_dh(6)
+        sums_on_gpsimd(halves=((3, 1),))
+        shard0(4)
+        beat(10)
+        quantise_dh(7)
+        shard1_pair(4, (1,))
+        half(1, 4, 0)
+        sums_on_gpsimd(halves=((4, 1),))
+        last_pair = 5
         first = BEAT * last_beat
         for n in range(first, first + BEAT - 1):
-            unit(n)
-        quantise_dh(last_beat, 0, 2)
-        unit(first + BEAT - 1)
+            unit_run(n, 1)
+        sum_on_vector(4, 0)
+        quantise_dh(8, 0, 2)
+        unit_run(first + BEAT - 1, 1)
         shard0(last_pair)
-        quantise_dh(last_beat, 2, 1)
-        quantise_dh(last_beat, 3, 1)
+        quantise_dh(8, 2, 1)
+        quantise_dh(8, 3, 1)
         for strip in range(2):
             for h in range(2):
                 half(1, last_pair, h, strip, P)

@@ -25,15 +25,23 @@ BEAT = 4
 G_COLS = BEAT * P
 RUN = 4
 VECTOR_PAIRS = 3
-X_GPSIMD = 384
+X_GPSIMD = 320
 BAR = 2 * BEAT
-BARS = 3
+BARS = 4
 STAGES = 5
 READS = 1
 BANKS = 8
-DH_SLOTS = 3
-SPLITS = 2
-Y_SLOTS = 4
+DH_SLOTS = 4
+SPLITS = 4
+FIRSTS = 4
+SECONDS = 4
+Y_RAW = 4
+X_RAW = 3
+G_RAW = 8
+W_RAW = 4
+WIDES = 4
+RUNS = (((0, 0), (0, 1), (0, 2), (0, 3), (1, 0), (1, 1), (1, 2), (1, 3)), ((0, 4), (0, 5), (1, 4), (1, 5), (0, 6), (0, 7), (1, 6), (1, 7)), ((2, 0), (2, 1), (2, 2), (2, 3), (3, 0), (3, 1), (3, 2), (3, 3)), ((2, 4), (2, 5), (2, 6), (2, 7), (3, 4), (3, 5), (3, 6), (3, 7)), ((0, 8), (0, 9), (1, 8), (1, 9)), ((2, 8), (2, 9), (3, 8), (3, 9)), ((0, 10), (0, 11), (1, 10), (1, 11)), ((2, 10), (3, 10), (2, 11), (3, 11)))
+STAGE_OF = {('w', 0): 0, ('dh', 0): 0, ('dh', 2): 0, ('w', 4): 0, ('total', 0): 0, ('w', 1): 1, ('w', 3): 1, ('x', 0): 1, ('x', 2): 1, ('w', 5): 1, ('total', 1): 1, ('y', 0): 2, ('y', 2): 2, ('x', 1): 2, ('x', 3): 2, ('dh', 4): 2, ('dh', 7): 2, ('y', 1): 3, ('split', 2, 0): 3, ('dh', 1): 3, ('dh', 6): 3, ('total', 3): 3, ('w', 2): 4, ('y', 3): 4, ('dh', 3): 4, ('dh', 5): 4}
 
 
 def tile_shard_weight_grad_s7_kernel(tc, x, dy, w2_bytes, w2_scale, g, c, out):
@@ -53,50 +61,38 @@ def tile_shard_weight_grad_s7_kernel(tc, x, dy, w2_bytes, w2_scale, g, c, out):
 
         def load_w(j, strips=(0, 1)):
             if j not in w_raw:
-                w_raw[j] = work.tile([P, 2, N], U8, name="w_raw", bufs=4)
+                w_raw[j] = work.tile([P, 2, N], U8, name="w_raw", bufs=W_RAW)
             part = slice(strips[0], strips[-1] + 1)
             nc.sync.dma_start(out=w_raw[j][:, part, :], in_=w_view[j][:, part, :])
 
         def load_y(a, rows):
-            tp = rows[0] // 2
-            if (a, tp) not in y_raw:
-                y_raw[a, tp] = work.tile([P, 2, N], BF16, name="y_raw", bufs=6, align_bytes=64)
-            nc.sync.dma_start(
-                out=y_raw[a, tp][:, rows[0] % 2 : rows[-1] % 2 + 1, :], in_=samples(dy, a)[:, rows[0] : rows[-1] + 1, :]
-            )
-
-        def load_y_group(a):
-            load_y(a, (0, 1))
-            load_y(a, (2, 3))
+            if len(rows) == 1:
+                tile = work.tile([P, 1, N], BF16, name="y_row", bufs=PACK, align_bytes=64)
+            else:
+                tile = work.tile([P, 2, N], BF16, name="y_raw", bufs=Y_RAW, align_bytes=64)
+            nc.sync.dma_start(out=tile[:], in_=samples(dy, a)[:, rows[0] : rows[-1] + 1, :])
+            for i, t in enumerate(rows):
+                y_raw[a, t] = tile[:, i, :]
 
         def load_x(a):
-            x_raw[a] = work.tile([P, PACK, K], BF16, name="x_raw", bufs=3, align_bytes=64)
+            x_raw[a] = work.tile([P, PACK, K], BF16, name="x_raw", bufs=X_RAW, align_bytes=64)
             nc.sync.dma_start(out=x_raw[a][:], in_=samples(x, a))
 
         def load_g(a, chunk):
-            g_raw[a, chunk] = work.tile([P, PACK, G_COLS], BF16, name="g_raw", bufs=2 * GROUPS, align_bytes=64)
+            g_raw[a, chunk] = work.tile([P, PACK, G_COLS], BF16, name="g_raw", bufs=G_RAW, align_bytes=64)
             nc.sync.dma_start(out=g_raw[a, chunk][:], in_=samples(g, a)[:, :, G_COLS * chunk : G_COLS * (chunk + 1)])
 
         scale_col = keep.tile([P, 2, PACK], F32, name="scale_col")
-        nc.sync.dma_start(out=scale_col[:], in_=w2_scale.rearrange("o (g p t) -> p (o g) t", p=P, t=PACK))
         c_bf = keep.tile([P, D], BF16, name="c_bf")
-        nc.scalar.dma_start(out=c_bf[:], in_=c.partition_broadcast(P))
 
-        load_y(0, (0,))
-        load_w(0, (0,))
-        load_y(0, (1,))
-        load_y(0, (2,))
-        load_w(0, (1,))
-        load_y(0, (3,))
-        load_w(1)
-        load_y_group(1)
-        load_w(2)
-        load_y(2, (0, 1))
-        load_x(0)
-        load_g(0, 0)
-        load_y(2, (2, 3))
-        load_x(1)
-        load_g(1, 0)
+        def load_scales():
+            nc.sync.dma_start(out=scale_col[:], in_=w2_scale.rearrange("o (g p t) -> p (o g) t", p=P, t=PACK))
+
+        def load_c():
+            nc.sync.dma_start(out=c_bf[:], in_=c.partition_broadcast(P))
+
+        def widen_c():
+            nc.scalar.copy(out=c_all[:], in_=c_bf[:])
 
         def psum_bank(shape):
             return psum.tile(shape, F32, name="bank", bufs=BANKS)
@@ -104,16 +100,12 @@ def tile_shard_weight_grad_s7_kernel(tc, x, dy, w2_bytes, w2_scale, g, c, out):
         ident = keep.tile([P, P], F32, name="ident", align_bytes=64)
         make_identity(nc, ident[:])
         c_all = keep.tile([P, D], F32, name="c_all")
-        scale_all = keep.tile([P, 2, P, PACK], F32, name="scale_all", align_bytes=64)
-        for gi in range(2):
-            ps = psum_bank([P, PACK, P])
-            for t in range(PACK):
-                nc.tensor.transpose(ps[:, t, :], scale_col[:, gi, t : t + 1].to_broadcast([P, P]), ident[:])
-            nc.scalar.copy(out=scale_all[:, gi], in_=ps[:].rearrange("p t j -> p j t"))
+        ident_bf = keep.tile([P, P], BF16, name="ident_bf", align_bytes=64)
+        nc.vector.tensor_copy(out=ident_bf[:], in_=ident[:])
 
-        w_wide, w_split, w_planes, w_turned, w_mx = {}, {}, {}, {}, {}
+        w_wide, y_split, w_planes, w_turned, w_mx = {}, {}, {}, {}, {}
         y_turned, y_mx, x_mixed, x_mx, dh, dh_mx = {}, {}, {}, {}, {}, {}
-        bank, first_term, first_pair, second_pair = {}, {}, {}, {}
+        bank, first_pair, second_term, result = {}, {}, {}, {}
 
         def quantise(name, bufs, source):
             words = source.shape[1] // PACK
@@ -143,11 +135,22 @@ def tile_shard_weight_grad_s7_kernel(tc, x, dy, w2_bytes, w2_scale, g, c, out):
             nc.tensor.transpose(ps, row.bitcast(F32)[:, PAIR * gi + u : PAIR * (gi + 1) : 2], ident[:])
 
         def split_row(row):
-            halves = work.tile([P, 2, PAIR], F32, name="split", bufs=SPLITS, align_bytes=64)
+            halves = work.tile([P, 2, PAIR], F32, name="y_row", bufs=PACK, align_bytes=64)
             nc.scalar.copy(out=halves[:], in_=row.bitcast(F32).rearrange("p (w u) -> p u w", u=2))
             return halves
 
-        def turn_row(row, turned, halves=None):
+        def split_row_gpsimd(row, halves):
+            nc.gpsimd.tensor_scalar(
+                out=halves[:].bitcast(BF16).rearrange("p u (w e) -> p u w e", e=2),
+                in0=row.rearrange("p (w u e) -> p u w e", u=2, e=2),
+                scalar1=1.0,
+                scalar2=0.0,
+                op0=MULT,
+                op1=ADD,
+            )
+            return halves
+
+        def turn_row(row, halves=None):
             ps = psum_bank([P, 2, 2, P])
             for gi in range(2):
                 for u in range(2):
@@ -155,114 +158,104 @@ def tile_shard_weight_grad_s7_kernel(tc, x, dy, w2_bytes, w2_scale, g, c, out):
                         turn(ps[:, gi, u, :], row, gi, u)
                     else:
                         nc.tensor.transpose(ps[:, gi, u, :], halves[:, u, P * gi : P * (gi + 1)], ident[:])
-            nc.scalar.copy(out=turned, in_=ps[:].rearrange("p g u m -> p g m u"))
+            return ps
 
-        free_stages = list(range(STAGES))
-        stage_of = {}
-
-        def stage(key, shape, dtype, newest=False):
-            stage_of[key] = free_stages.pop(-1 if newest else 0)
-            return work.tile(shape, dtype, name="stage%d" % stage_of[key], bufs=1, align_bytes=64)
-
-        def leave(key):
-            free_stages.append(stage_of[key])
+        def stage(key, shape, dtype):
+            return work.tile(shape, dtype, name="stage%d" % STAGE_OF[key], bufs=1, align_bytes=64)
 
         def turn_y(a, t):
+            bank["y", a, t] = turn_row(y_raw[a, t], y_split.get((a, t)))
+
+        def empty_y(a, t):
             if a not in y_turned:
                 y_turned[a] = stage(("y", a), [P, PACK, 2, P, 2], F32)
-            turn_row(y_raw[a, t // 2][:, t % 2, :], y_turned[a][:, t])
+            nc.scalar.copy(out=y_turned[a][:, t], in_=bank["y", a, t][:].rearrange("p g u m -> p g m u"))
+
+        def split_y(a, t):
+            y_split[a, t] = split_row(y_raw[a, t])
+
+        def split_y_gpsimd(a, t):
+            if ("split", a, t) in STAGE_OF:
+                halves = stage(("split", a, t), [P, 2, PAIR], F32)
+            else:
+                halves = work.tile([P, 2, PAIR], F32, name="y_row", bufs=PACK, align_bytes=64)
+            y_split[a, t] = split_row_gpsimd(y_raw[a, t], halves)
 
         def quantise_y(a):
             source = y_turned[a][:].rearrange("p r g m u -> p (r g m u)").bitcast(BF16)
             y_mx[a] = quantise("y", GROUPS, source)
-            leave(("y", a))
 
         def wide_tile(b):
-            w_wide[b] = work.tile([P, N], BF16, name="w_wide", bufs=4, align_bytes=64)
+            w_wide[b] = work.tile([P, N], BF16, name="w_wide", bufs=WIDES, align_bytes=64)
             return w_wide[b]
 
         def pair_tile(j):
             if j not in w_turned:
-                w_turned[j] = work.tile([P, 2, 2, P, 2], F32, name="w_turned", bufs=2, align_bytes=64)
+                w_turned[j] = stage(("w", j), [P, 2, 2, P, 2], F32)
             return w_turned[j]
 
-        def scale_strip(b, parts=1):
+        def widen_strip(b, parts=1):
             wide = wide_tile(b)
             for i in range(parts):
                 ns = slice(N // parts * i, N // parts * (i + 1))
+                nc.scalar.copy(out=wide[:, ns], in_=w_raw[b // 2][:, b % 2, ns].bitcast(FP8))
+
+        def turn_plane(ps, b, gi, t):
+            n0 = P * PACK * gi + t
+            nc.tensor.matmul(ps, lhsT=w_wide[b][:, n0 : P * PACK * (gi + 1) : PACK], rhs=ident_bf[:], start=True, stop=True)
+
+        def turn_strip(b, passes=(0, 1)):
+            for gi in passes:
+                ps = psum_bank([P, PACK, P])
+                for t in range(PACK):
+                    turn_plane(ps[:, t, :], b, gi, t)
+                bank["strip", b, gi] = ps
+
+        def scale_strip(b, passes=(0, 1)):
+            for gi in passes:
+                mixed = pair_tile(b // 2)[:, gi, b % 2].rearrange("p f u -> p (f u)").bitcast(BF16)
                 nc.vector.tensor_tensor(
-                    out=wide[:, ns],
-                    in0=w_raw[b // 2][:, b % 2, ns].bitcast(FP8),
-                    in1=scale_all[:].rearrange("p g j t -> p (g j t)")[:, ns],
+                    out=mixed.rearrange("p (f t) -> p f t", t=PACK),
+                    in0=bank["strip", b, gi][:].rearrange("p t f -> p f t"),
+                    in1=scale_col[:, gi, :].unsqueeze(1).to_broadcast([P, P, PACK]),
                     op=MULT,
                 )
 
-        def turn_strip(b):
-            turn_row(w_wide[b][:], pair_tile(b // 2)[:, :, b % 2], w_split.get(b))
-
-        def split_strip(b):
-            w_split[b] = split_row(w_wide[b][:])
-
-        def split_tiles(j):
-            both = stage(("w", j), [P, 2, 2, PAIR], F32, newest=True)
-            for i in range(2):
-                w_split[2 * j + i] = both[:, i]
-
-        def scale_split(engine, b, n0, n1):
-            ws = slice(n0 // PACK, n1 // PACK)
-            engine.tensor_tensor(
-                out=w_split[b].bitcast(BF16).rearrange("p u (w e) -> p u w e", e=2)[:, :, ws, :],
-                in0=w_wide[b][:].rearrange("p (w u e) -> p u w e", u=2, e=2)[:, :, ws, :],
-                in1=scale_all[:].rearrange("p g j (u e) -> p u (g j) e", u=2)[:, :, ws, :],
-                op=MULT,
-            )
-
-        def scale_pair_gpsimd(j):
-            split_tiles(j)
-            for i in range(2):
-                scale_split(nc.gpsimd, 2 * j + i, 0, N)
-
-        def widen_strip(b):
-            nc.scalar.copy(out=wide_tile(b)[:], in_=w_raw[b // 2][:, b % 2, :].bitcast(FP8))
-
         def turn_pair(j, gi):
-            ps = psum_bank([P, 2, 2, P])
             for u in range(2):
-                for i in range(2):
-                    if 2 * j + i in w_split:
-                        nc.tensor.transpose(ps[:, u, i, :], w_split[2 * j + i][:, u, P * gi : P * (gi + 1)], ident[:])
-                    else:
-                        turn(ps[:, u, i, :], w_wide[2 * j + i][:], gi, u)
-            bank["pair", j, gi] = ps
+                ps = psum_bank([P, 2, 2, P])
+                for e in range(2):
+                    for i in range(2):
+                        turn_plane(ps[:, e, i, :], 2 * j + i, gi, 2 * u + e)
+                bank["pair", j, gi, u] = ps
 
         def scale_pair(j, gi):
             w_planes[j, gi] = work.tile([P, PACK, PAIR], BF16, name="w_planes", bufs=2, align_bytes=64)
             for t in range(PACK):
                 u, e = divmod(t, 2)
-                elements = bank["pair", j, gi][:, u].rearrange("p i f -> p (i f)").bitcast(BF16)
                 nc.scalar.activation(
                     out=w_planes[j, gi][:, t, :],
-                    in_=elements[:, e : 2 * PAIR : 2],
+                    in_=bank["pair", j, gi, u][:, e].rearrange("p i f -> p (i f)"),
                     func=COPY,
                     scale=scale_col[:, gi, t : t + 1],
                 )
 
-        def mix_pair(j):
-            for gi in range(2):
-                mixed = pair_tile(j)[:, gi].rearrange("p i f u -> p (i f u)").bitcast(BF16)
-                nc.scalar.copy(
-                    out=mixed_runs(mixed.rearrange("p (f t) -> p f t", t=PACK)), in_=in_runs(w_planes[j, gi][:])
-                )
+        def mix_pair(j, gi):
+            mixed = pair_tile(j)[:, gi].rearrange("p i f u -> p (i f u)").bitcast(BF16)
+            nc.scalar.copy(out=mixed_runs(mixed.rearrange("p (f t) -> p f t", t=PACK)), in_=in_runs(w_planes[j, gi][:]))
 
         def quantise_w(j):
             source = w_turned[j][:].rearrange("p g i f u -> p (g i f u)").bitcast(BF16)
             w_mx[j] = quantise("w", PAIRS, source)
 
+        def mixed_x(a):
+            if a not in x_mixed:
+                x_mixed[a] = stage(("x", a), [P, K, PACK], BF16)
+            return x_mixed[a][:]
+
         def mix_x_gpsimd(a):
-            if a // 2 not in x_mixed:
-                x_mixed[a // 2] = stage(("x", a // 2), [P, 2, K, PACK], BF16, newest=True)
             nc.gpsimd.tensor_scalar(
-                out=x_mixed[a // 2][:, a % 2, 0:X_GPSIMD, :],
+                out=mixed_x(a)[:, 0:X_GPSIMD, :],
                 in0=x_raw[a][:, :, 0:X_GPSIMD].rearrange("p t k -> p k t"),
                 scalar1=1.0,
                 scalar2=0.0,
@@ -272,25 +265,17 @@ def tile_shard_weight_grad_s7_kernel(tc, x, dy, w2_bytes, w2_scale, g, c, out):
 
         def mix_x_scalar(a):
             nc.scalar.copy(
-                out=mixed_runs(x_mixed[a // 2][:, a % 2, X_GPSIMD:K, :]), in_=in_runs(x_raw[a][:, :, X_GPSIMD:K])
+                out=mixed_runs(mixed_x(a)[:, X_GPSIMD:K, :]), in_=in_runs(x_raw[a][:, :, X_GPSIMD:K])
             )
 
-        def quantise_x(d):
-            x_mx[d] = quantise("x", D, x_mixed[d][:].rearrange("p q k t -> p (q k t)"))
-            leave(("x", d))
+        def quantise_x(a):
+            x_mx[a] = quantise("x", GROUPS, x_mixed[a][:].rearrange("p k t -> p (k t)"))
 
-        units = [(a, b) for a in range(GROUPS) for b in range(BEAT)]
-        units = units + [(a, 2 * j + i) for j in range(2, PAIRS) for a in range(GROUPS) for i in range(2)]
-        units = units[:-BEAT] + [(a, 2 * (PAIRS - 1) + i) for i in range(2) for a in range(GROUPS - 2, GROUPS)]
-        place = {u: n for n, u in enumerate(units)}
-        last_beat = len(units) // BEAT - 1
-        chunks = [BAR] * BARS + [BEAT] * (len(units) // BEAT - 2 * BARS)
-        chunk_of = [(k, i) for k in range(len(chunks)) for i in range(chunks[k])]
+        run_of = {u: (k, i) for k, run in enumerate(RUNS) for i, u in enumerate(run)}
 
-        def unit(n):
-            a, b = units[n]
+        def unit(a, b):
             ps = psum_bank([P, PACK, P])
-            bank["unit", n] = ps
+            bank["unit", a, b] = ps
             for t in range(PACK):
                 for gi in range(2):
                     y0 = PAIR * t + P * gi
@@ -299,217 +284,374 @@ def tile_shard_weight_grad_s7_kernel(tc, x, dy, w2_bytes, w2_scale, g, c, out):
                         ps[:, t, :], y_mx[a], slice(y0, y0 + P), w_mx[b // 2], slice(w0, w0 + P), gi == 0, gi == 1
                     )
 
-        def read_unit(n):
-            a, b = units[n]
-            k, i = chunk_of[n]
-            ps = bank["unit", n]
+        def read_unit(a, b):
+            k, i = run_of[a, b]
             if k not in dh:
-                dh[k] = stage(("dh", k), [P, chunks[k] * P, PACK], BF16)
+                dh[k] = stage(("dh", k), [P, len(RUNS[k]) * P, PACK], BF16)
             f0 = P * (b % BEAT)
             nc.vector.tensor_tensor(
                 out=mixed_runs(dh[k][:, P * i : P * (i + 1), :]),
-                in0=in_runs(ps[:]),
+                in0=in_runs(bank["unit", a, b][:]),
                 in1=in_runs(g_raw[a, b // BEAT][:, :, f0 : f0 + P]),
                 op=MULT,
             )
 
-        def beat(k):
-            for n in range(BEAT * k, BEAT * (k + 1), READS):
-                unit_run(n, READS)
-
-        def unit_run(n, count):
-            for m in range(n, n + count):
-                unit(m)
-            for m in reversed(range(n, n + count)):
-                read_unit(m)
-
         def quantise_dh(k, first=0, count=None):
-            count = count or chunks[k]
+            count = count or len(RUNS[k])
             source = dh[k][:, P * first : P * (first + count), :].rearrange("p f t -> p (f t)")
-            quantised = quantise("dh", 4, source)
+            quantised = quantise("bar", BARS, source) if count == BAR else quantise("dh", DH_SLOTS, source)
             for i in range(count):
-                dh_mx[sum(chunks[:k]) + first + i] = (quantised, P * i)
-            if first + count == chunks[k]:
-                leave(("dh", k))
+                dh_mx[RUNS[k][first + i]] = (quantised, P * i)
 
         def half(d, j, h, strip=0, width=PAIR):
             ps = psum_bank([P, 2, width])
             for k2 in range(2):
                 k0 = P * (2 * h + k2)
                 for q in range(2):
-                    quantised, f0 = dh_mx[place[2 * d + q, 2 * j + strip]]
+                    quantised, f0 = dh_mx[2 * d + q, 2 * j + strip]
                     multiply(
-                        ps[:, k2, :], x_mx[d], slice(K * q + k0, K * q + k0 + P), quantised, slice(f0, f0 + width), q == 0, q == 1
+                        ps[:, k2, :], x_mx[2 * d + q], slice(k0, k0 + P), quantised, slice(f0, f0 + width), q == 0, q == 1
                     )
             bank["half", d, j, h, strip] = ps
 
-        def shard0(j, hs=(0, 1)):
-            for h in hs:
-                half(0, j, h)
-                if h == 0:
-                    first_pair[j] = work.tile([P, 2, 2, PAIR], F32, name="first_term", bufs=4)
-                first_term[j, h] = first_pair[j][:, h]
-                nc.scalar.activation(out=first_term[j, h], in_=bank["half", 0, j, h, 0][:], func=COPY, scale=c_all[:, 0:1])
+        def first(j, h):
+            if j not in first_pair:
+                first_pair[j] = work.tile([P, 2, 2, PAIR], F32, name="first_term", bufs=FIRSTS)
+            nc.scalar.activation(out=first_pair[j][:, h], in_=bank["half", 0, j, h, 0][:], func=COPY, scale=c_all[:, 0:1])
+
+        def second(j, h):
+            second_term[j, h] = work.tile([P, 2, PAIR], F32, name="second_term", bufs=SECONDS)
+            nc.scalar.activation(out=second_term[j, h][:], in_=bank["half", 1, j, h, 0][:], func=COPY, scale=c_all[:, 1:2])
 
         def sum_on_vector(j, h, strip=0, width=PAIR):
-            total = first_term[j, h][:, :, P * strip : P * strip + width]
+            total = first_pair[j][:, h, :, P * strip : P * strip + width]
             nc.vector.scalar_tensor_tensor(
                 out=total, in0=bank["half", 1, j, h, strip][:], scalar=c_all[:, 1:2], in1=total, op0=MULT, op1=ADD
             )
+            result[j, h, strip] = total
+
+        def sums_on_gpsimd(n, halves):
+            total = stage(("total", n), [P, BEAT, 2, PAIR], F32)
+            for i, (j, h) in enumerate(halves):
+                nc.gpsimd.tensor_tensor(out=total[:, i], in0=first_pair[j][:, h], in1=second_term[j, h][:], op=ADD)
+                result[j, h, 0] = total[:, i]
+
+        def store(j, h, strip=0, width=PAIR):
             f0 = PAIR * j + P * strip
-            nc.sync.dma_start(out=out_view[h][:, :, f0 : f0 + width], in_=total)
+            nc.sync.dma_start(out=out_view[h][:, :, f0 : f0 + width], in_=result[j, h, strip])
 
-        def shard1_pair(j, hs=(0, 1)):
-            second_pair[j] = work.tile([P, 2, 2, PAIR], F32, name="second_term", bufs=3)
-            for h in hs:
-                half(1, j, h)
-                nc.scalar.activation(
-                    out=second_pair[j][:, h], in_=bank["half", 1, j, h, 0][:], func=COPY, scale=c_all[:, 1:2]
-                )
-
-        def sums_on_gpsimd(pairs=(), halves=()):
-            total = stage("total", [P, BEAT, 2, PAIR], F32, newest=True)
-            i = 0
-            for j in pairs:
-                nc.gpsimd.tensor_tensor(out=total[:, i : i + 2], in0=first_pair[j][:], in1=second_pair[j][:], op=ADD)
-                for h in range(2):
-                    nc.sync.dma_start(out=out_view[h][:, :, PAIR * j : PAIR * (j + 1)], in_=total[:, i + h])
-                i = i + 2
-            for j, h in halves:
-                nc.gpsimd.tensor_tensor(out=total[:, i], in0=first_term[j, h], in1=second_pair[j][:, h], op=ADD)
-                nc.sync.dma_start(out=out_view[h][:, :, PAIR * j : PAIR * (j + 1)], in_=total[:, i])
-                i = i + 1
-            leave("total")
-
-        for t in range(PACK):
-            turn_y(0, t)
-        for b in range(BEAT):
-            scale_strip(b, parts=2 if b == 0 else 1)
-            turn_strip(b)
-            if b > 0:
-                turn_y(1, b - 1)
-        quantise_y(0)
-        turn_y(1, PACK - 1)
-        turn_y(2, 0)
-        load_w(3)
-        load_y_group(3)
-        load_g(2, 0)
-        load_w(4)
-        load_x(2)
-        load_g(3, 0)
+        load_w(0, (0,))
+        widen_strip(0, parts=2)
+        turn_strip(0)
+        load_scales()
+        scale_strip(0)
+        load_w(0, (1,))
+        widen_strip(1)
+        turn_strip(1)
+        scale_strip(1)
+        load_y(0, (0,))
+        load_w(1)
+        widen_strip(2)
+        turn_strip(2)
+        turn_y(0, 0)
+        scale_strip(2)
         quantise_w(0)
-        scale_strip(4)
+        widen_strip(3)
+        empty_y(0, 0)
+        load_y(0, (1,))
+        turn_y(0, 1)
+        empty_y(0, 1)
+        load_y(0, (2,))
+        turn_y(0, 2)
+        empty_y(0, 2)
+        load_y(0, (3,))
+        turn_y(0, 3)
+        turn_strip(3)
+        scale_strip(3)
+        empty_y(0, 3)
+        quantise_y(0)
         quantise_w(1)
-        scale_strip(5)
+        load_y(1, (0, 1))
+        turn_y(1, 0)
+        turn_y(1, 1)
+        empty_y(1, 0)
+        empty_y(1, 1)
+        load_y(1, (2, 3))
+        turn_y(1, 2)
+        turn_y(1, 3)
+        unit(0, 0)
+        unit(0, 1)
+        unit(0, 2)
+        unit(0, 3)
+        empty_y(1, 2)
+        empty_y(1, 3)
         quantise_y(1)
-        mix_x_gpsimd(0)
-        mix_x_gpsimd(1)
-        mix_x_scalar(0)
-        nc.scalar.copy(out=c_all[:], in_=c_bf[:])
-        split_strip(4)
-        split_strip(5)
-        load_x(3)
+        load_w(2)
+        widen_strip(4)
+        widen_strip(5)
+        turn_pair(2, 0)
+        turn_pair(2, 1)
+        load_w(3)
+        widen_strip(6)
+        widen_strip(7)
+        scale_pair(2, 0)
+        scale_pair(2, 1)
+        mix_pair(2, 0)
+        mix_pair(2, 1)
+        load_g(0, 0)
+        read_unit(0, 0)
+        unit(1, 0)
+        read_unit(0, 1)
+        unit(1, 1)
+        read_unit(0, 2)
+        unit(1, 2)
+        read_unit(0, 3)
+        unit(1, 3)
+        turn_strip(6)
+        turn_strip(7)
+        load_y(2, (0, 1))
+        split_y_gpsimd(2, 0)
+        split_y_gpsimd(2, 1)
+        load_g(1, 0)
+        read_unit(1, 0)
+        turn_y(2, 0)
+        read_unit(1, 1)
+        turn_y(2, 1)
+        read_unit(1, 2)
+        read_unit(1, 3)
+        scale_strip(6)
+        quantise_w(2)
+        scale_strip(7)
+        quantise_dh(0)
+        quantise_w(3)
+        empty_y(2, 0)
+        empty_y(2, 1)
+        load_y(2, (2, 3))
+        split_y_gpsimd(2, 2)
+        turn_y(2, 2)
+        empty_y(2, 2)
+        split_y_gpsimd(2, 3)
+        turn_y(2, 3)
+        unit(0, 4)
+        unit(0, 5)
+        unit(1, 4)
+        unit(1, 5)
+        unit(0, 6)
+        empty_y(2, 3)
         load_g(0, 1)
+        read_unit(0, 4)
+        read_unit(0, 5)
+        load_x(0)
+        mix_x_gpsimd(0)
         load_g(1, 1)
+        read_unit(1, 4)
+        read_unit(1, 5)
+        quantise_y(2)
+        read_unit(0, 6)
+        load_y(3, (0, 1))
+        split_y(3, 0)
+        turn_y(3, 0)
+        split_y(3, 1)
+        turn_y(3, 1)
+        load_y(3, (2, 3))
+        split_y(3, 2)
+        turn_y(3, 2)
+        split_y(3, 3)
+        turn_y(3, 3)
+        unit(0, 7)
+        unit(1, 6)
+        unit(1, 7)
+        unit(2, 0)
+        read_unit(0, 7)
+        read_unit(1, 6)
+        read_unit(1, 7)
+        mix_x_scalar(0)
+        empty_y(3, 0)
+        unit(2, 1)
+        empty_y(3, 1)
+        unit(2, 2)
+        empty_y(3, 2)
+        unit(2, 3)
+        empty_y(3, 3)
+        quantise_y(3)
+        unit(3, 0)
+        unit(3, 1)
+        unit(3, 2)
+        unit(3, 3)
+        quantise_x(0)
+        load_x(1)
+        mix_x_scalar(1)
+        mix_x_gpsimd(1)
+        quantise_x(1)
+        load_g(2, 0)
+        read_unit(2, 0)
+        half(0, 0, 0)
+        read_unit(2, 1)
+        half(0, 0, 1)
+        read_unit(2, 2)
+        half(0, 1, 0)
+        read_unit(2, 3)
+        half(0, 1, 1)
+        load_g(3, 0)
+        read_unit(3, 0)
+        unit(2, 4)
+        read_unit(3, 1)
+        unit(2, 5)
+        read_unit(3, 2)
+        unit(2, 6)
+        read_unit(3, 3)
+        unit(2, 7)
+        quantise_dh(1)
+        load_c()
+        widen_c()
+        load_x(2)
+        mix_x_gpsimd(2)
+        load_x(3)
+        mix_x_gpsimd(3)
+        load_w(4)
+        widen_strip(8)
+        widen_strip(9)
+        mix_x_scalar(2)
+        mix_x_scalar(3)
+        first(0, 0)
+        first(0, 1)
+        turn_pair(4, 0)
+        first(1, 0)
+        first(1, 1)
+        turn_pair(4, 1)
         load_g(2, 1)
+        read_unit(2, 4)
+        half(0, 2, 0)
+        read_unit(2, 5)
+        half(0, 2, 1)
+        read_unit(2, 6)
+        half(0, 3, 0)
+        read_unit(2, 7)
+        half(0, 3, 1)
+        quantise_dh(2)
+        quantise_x(2)
+        quantise_x(3)
         load_g(3, 1)
         load_w(5)
-        beat(0)
-        for t in range(1, PACK):
-            turn_y(2, t)
-        beat(1)
-        mix_x_scalar(1)
-        widen_strip(6)
-        turn_strip(4)
-        turn_strip(5)
-        for t in range(PACK):
-            turn_y(3, t)
-        quantise_y(2)
-        widen_strip(7)
-        quantise_x(0)
-        quantise_dh(0)
-        quantise_y(3)
-        mix_x_gpsimd(2)
-        mix_x_gpsimd(3)
-        load_g(0, 2)
-        load_g(1, 2)
-        mix_x_scalar(2)
-        widen_strip(8)
-        beat(2)
-        turn_pair(3, 0)
-        turn_pair(3, 1)
-        scale_pair(3, 0)
-        scale_pair(3, 1)
-        mix_x_scalar(3)
-        mix_pair(3)
-        beat(3)
-        shard0(0)
-        shard0(1)
-        widen_strip(9)
-        quantise_w(2)
-        quantise_x(1)
-        quantise_dh(1)
-        quantise_w(3)
-        scale_pair_gpsimd(4)
-        load_g(2, 2)
-        load_g(3, 2)
         widen_strip(10)
-        beat(4)
         widen_strip(11)
-        beat(5)
-        shard1_pair(0, (0,))
-        half(1, 0, 1)
-        shard1_pair(1)
-        sum_on_vector(0, 1)
-        quantise_dh(2)
-        sums_on_gpsimd(halves=((0, 0),))
-        split_strip(10)
-        split_strip(11)
-        beat(6)
+        scale_pair(4, 0)
+        unit(3, 4)
+        unit(3, 5)
+        read_unit(3, 4)
+        read_unit(3, 5)
+        scale_pair(4, 1)
+        unit(3, 6)
+        unit(3, 7)
+        read_unit(3, 6)
+        read_unit(3, 7)
+        first(2, 0)
+        half(1, 0, 0)
+        sum_on_vector(0, 0)
         quantise_dh(3)
-        sums_on_gpsimd(pairs=(1,))
-        turn_strip(8)
-        turn_strip(9)
-        leave(("w", 4))
+        first(2, 1)
+        half(1, 0, 1)
+        first(3, 0)
+        half(1, 1, 0)
+        first(3, 1)
+        half(1, 1, 1)
         turn_pair(5, 0)
         turn_pair(5, 1)
-        shard0(2)
-        scale_pair(5, 0)
-        scale_pair(5, 1)
-        beat(7)
+        mix_pair(4, 0)
+        mix_pair(4, 1)
         quantise_w(4)
+        unit(0, 8)
+        second(0, 1)
+        unit(0, 9)
+        second(1, 0)
+        unit(1, 8)
+        second(1, 1)
+        unit(1, 9)
+        scale_pair(5, 0)
+        half(1, 2, 0)
+        half(1, 2, 1)
+        scale_pair(5, 1)
+        half(1, 3, 0)
+        half(1, 3, 1)
+        mix_pair(5, 0)
+        mix_pair(5, 1)
+        second(3, 0)
+        sums_on_gpsimd(0, ((0, 1), (1, 0), (1, 1)))
+        second(3, 1)
+        load_g(0, 2)
+        read_unit(0, 8)
+        unit(2, 8)
+        read_unit(0, 9)
+        unit(2, 9)
+        load_g(1, 2)
+        read_unit(1, 8)
+        unit(3, 8)
+        read_unit(1, 9)
+        unit(3, 9)
+        sum_on_vector(2, 0)
+        sum_on_vector(2, 1)
         quantise_dh(4)
-        shard1_pair(2)
-        sums_on_gpsimd(pairs=(2,))
-        shard0(3)
-        mix_pair(5)
-        beat(8)
+        half(0, 4, 0)
+        half(0, 4, 1)
         quantise_w(5)
+        unit(0, 10)
+        unit(0, 11)
+        sums_on_gpsimd(1, ((3, 0), (3, 1)))
+        load_g(2, 2)
+        read_unit(2, 8)
+        unit(1, 10)
+        read_unit(2, 9)
+        unit(1, 11)
+        load_g(3, 2)
+        read_unit(3, 8)
+        read_unit(3, 9)
         quantise_dh(5)
-        shard1_pair(3)
-        sums_on_gpsimd(halves=((3, 0),))
-        beat(9)
-        quantise_dh(6)
-        sums_on_gpsimd(halves=((3, 1),))
-        shard0(4)
-        beat(10)
-        quantise_dh(7)
-        shard1_pair(4, (1,))
         half(1, 4, 0)
-        sums_on_gpsimd(halves=((4, 1),))
-        last_pair = 5
-        first = BEAT * last_beat
-        for n in range(first, first + BEAT - 1):
-            unit_run(n, 1)
+        half(1, 4, 1)
+        read_unit(0, 10)
+        read_unit(0, 11)
+        read_unit(1, 10)
+        read_unit(1, 11)
+        store(0, 0)
+        first(4, 0)
+        unit(2, 10)
         sum_on_vector(4, 0)
-        quantise_dh(8, 0, 2)
-        unit_run(first + BEAT - 1, 1)
-        shard0(last_pair)
-        quantise_dh(8, 2, 1)
-        quantise_dh(8, 3, 1)
-        for strip in range(2):
-            for h in range(2):
-                half(1, last_pair, h, strip, P)
-        for strip in range(2):
-            for h in range(2):
-                sum_on_vector(last_pair, h, strip, P)
+        quantise_dh(6)
+        read_unit(2, 10)
+        first(4, 1)
+        unit(3, 10)
+        unit(2, 11)
+        unit(3, 11)
+        half(0, 5, 0)
+        half(0, 5, 1)
+        read_unit(3, 10)
+        read_unit(2, 11)
+        quantise_dh(7, 0, 2)
+        half(1, 5, 0, 0, 128)
+        read_unit(3, 11)
+        quantise_dh(7, 2, 1)
+        quantise_dh(7, 3, 1)
+        second(4, 1)
+        half(1, 5, 1, 0, 128)
+        half(1, 5, 0, 1, 128)
+        half(1, 5, 1, 1, 128)
+        first(5, 0)
+        sum_on_vector(5, 0, 0, 128)
+        first(5, 1)
+        sum_on_vector(5, 1, 0, 128)
+        sum_on_vector(5, 0, 1, 128)
+        sum_on_vector(5, 1, 1, 128)
+        sums_on_gpsimd(3, ((4, 1),))
+        store(0, 1)
+        store(1, 0)
+        store(1, 1)
+        store(2, 0)
+        store(2, 1)
+        store(3, 0)
+        store(3, 1)
+        store(4, 0)
+        store(4, 1)
+        store(5, 0, 0, 128)
+        store(5, 1, 0, 128)
+        store(5, 0, 1, 128)
+        store(5, 1, 1, 128)

@@ -25,7 +25,7 @@ BEAT = 4
 G_COLS = BEAT * P
 RUN = 4
 VECTOR_PAIRS = 3
-X_GPSIMD = 320
+X_GPSIMD = 352
 BAR = 2 * BEAT
 BARS = 4
 STAGES = 5
@@ -41,7 +41,7 @@ G_RAW = 8
 W_RAW = 4
 WIDES = 4
 RUNS = (((0, 0), (0, 1), (0, 2), (0, 3), (1, 0), (1, 1), (1, 2), (1, 3)), ((0, 4), (0, 5), (1, 4), (1, 5), (0, 6), (0, 7), (1, 6), (1, 7)), ((2, 0), (2, 1), (2, 2), (2, 3), (3, 0), (3, 1), (3, 2), (3, 3)), ((2, 4), (2, 5), (2, 6), (2, 7), (3, 4), (3, 5), (3, 6), (3, 7)), ((0, 8), (0, 9), (1, 8), (1, 9)), ((2, 8), (2, 9), (3, 8), (3, 9)), ((0, 10), (0, 11), (1, 10), (1, 11)), ((2, 10), (3, 10), (2, 11), (3, 11)))
-STAGE_OF = {('w', 0): 0, ('dh', 0): 0, ('dh', 2): 0, ('w', 4): 0, ('total', 0): 0, ('w', 1): 1, ('w', 3): 1, ('x', 0): 1, ('x', 2): 1, ('w', 5): 1, ('total', 1): 1, ('y', 0): 2, ('y', 2): 2, ('x', 1): 2, ('x', 3): 2, ('dh', 4): 2, ('dh', 7): 2, ('y', 1): 3, ('split', 2, 0): 3, ('dh', 1): 3, ('dh', 6): 3, ('total', 3): 3, ('w', 2): 4, ('y', 3): 4, ('dh', 3): 4, ('dh', 5): 4}
+STAGE_OF = {('w', 0): 0, ('dh', 0): 0, ('dh', 2): 0, ('dh', 5): 0, ('total', 2): 0, ('w', 1): 1, ('w', 3): 1, ('x', 0): 1, ('x', 2): 1, ('w', 5): 1, ('dh', 6): 1, ('total', 3): 1, ('y', 0): 2, ('y', 2): 2, ('x', 1): 2, ('x', 3): 2, ('dh', 4): 2, ('total', 1): 2, ('y', 1): 3, ('split', 2, 0): 3, ('dh', 1): 3, ('w', 4): 3, ('dh', 7): 3, ('w', 2): 4, ('y', 3): 4, ('dh', 3): 4, ('total', 0): 4}
 
 
 def tile_shard_weight_grad_s7_kernel(tc, x, dy, w2_bytes, w2_scale, g, c, out):
@@ -103,7 +103,7 @@ def tile_shard_weight_grad_s7_kernel(tc, x, dy, w2_bytes, w2_scale, g, c, out):
         ident_bf = keep.tile([P, P], BF16, name="ident_bf", align_bytes=64)
         nc.vector.tensor_copy(out=ident_bf[:], in_=ident[:])
 
-        w_wide, y_split, w_planes, w_turned, w_mx = {}, {}, {}, {}, {}
+        w_wide, w_split, y_split, w_planes, w_turned, w_mx = {}, {}, {}, {}, {}, {}
         y_turned, y_mx, x_mixed, x_mx, dh, dh_mx = {}, {}, {}, {}, {}, {}
         bank, first_pair, second_term, result = {}, {}, {}, {}
 
@@ -215,11 +215,24 @@ def tile_shard_weight_grad_s7_kernel(tc, x, dy, w2_bytes, w2_scale, g, c, out):
             for gi in passes:
                 mixed = pair_tile(b // 2)[:, gi, b % 2].rearrange("p f u -> p (f u)").bitcast(BF16)
                 nc.vector.tensor_tensor(
-                    out=mixed.rearrange("p (f t) -> p f t", t=PACK),
-                    in0=bank["strip", b, gi][:].rearrange("p t f -> p f t"),
-                    in1=scale_col[:, gi, :].unsqueeze(1).to_broadcast([P, P, PACK]),
+                    out=mixed_runs(mixed.rearrange("p (f t) -> p f t", t=PACK)),
+                    in0=in_runs(bank["strip", b, gi][:]),
+                    in1=in_runs(scale_col[:, gi, :].unsqueeze(2).to_broadcast([P, PACK, P])),
                     op=MULT,
                 )
+
+        def turn_words(b):
+            bank["words", b] = turn_row(w_wide[b][:], w_split.get(b))
+
+        def empty_words(b):
+            nc.scalar.copy(out=pair_tile(b // 2)[:, :, b % 2], in_=bank["words", b][:].rearrange("p g u m -> p g m u"))
+
+        def scale_gpsimd(b):
+            values = pair_tile(b // 2)[:, :, b % 2].rearrange("p g f u -> p g (f u)").bitcast(BF16)
+            values = values.rearrange("p g (f t) -> p g f t", t=PACK)
+            nc.gpsimd.tensor_tensor(
+                out=values, in0=values, in1=scale_col[:].unsqueeze(2).to_broadcast([P, 2, P, PACK]), op=MULT
+            )
 
         def turn_pair(j, gi):
             for u in range(2):
@@ -240,6 +253,38 @@ def tile_shard_weight_grad_s7_kernel(tc, x, dy, w2_bytes, w2_scale, g, c, out):
                     scale=scale_col[:, gi, t : t + 1],
                 )
 
+        def split_strip(b):
+            w_split[b] = split_row(w_wide[b][:])
+
+        def turn_pair_words(j, gi):
+            ps = psum_bank([P, 2, 2, P])
+            for u in range(2):
+                for i in range(2):
+                    nc.tensor.transpose(ps[:, u, i, :], w_split[2 * j + i][:, u, P * gi : P * (gi + 1)], ident[:])
+            bank["pair", j, gi] = ps
+
+        def scale_pair_words(j, gi):
+            w_planes[j, gi] = work.tile([P, PACK, PAIR], BF16, name="w_planes", bufs=2, align_bytes=64)
+            for t in range(PACK):
+                u, e = divmod(t, 2)
+                elements = bank["pair", j, gi][:, u].rearrange("p i f -> p (i f)").bitcast(BF16)
+                nc.scalar.activation(
+                    out=w_planes[j, gi][:, t, :],
+                    in_=elements[:, e : 2 * PAIR : 2],
+                    func=COPY,
+                    scale=scale_col[:, gi, t : t + 1],
+                )
+
+        def scale_pair_vector(j, gi):
+            mixed = pair_tile(j)[:, gi].rearrange("p i f u -> p (i f u)").bitcast(BF16)
+            elements = bank["pair", j, gi][:].rearrange("p u i f -> p u (i f)").bitcast(BF16)
+            nc.vector.tensor_tensor(
+                out=mixed.rearrange("p (f u e) -> p f u e", u=2, e=2),
+                in0=elements.rearrange("p u (f e) -> p f u e", e=2),
+                in1=scale_col[:, gi, :].rearrange("p (u e) -> p u e", e=2).unsqueeze(1).to_broadcast([P, PAIR, 2, 2]),
+                op=MULT,
+            )
+
         def mix_pair(j, gi):
             mixed = pair_tile(j)[:, gi].rearrange("p i f u -> p (i f u)").bitcast(BF16)
             nc.scalar.copy(out=mixed_runs(mixed.rearrange("p (f t) -> p f t", t=PACK)), in_=in_runs(w_planes[j, gi][:]))
@@ -253,20 +298,18 @@ def tile_shard_weight_grad_s7_kernel(tc, x, dy, w2_bytes, w2_scale, g, c, out):
                 x_mixed[a] = stage(("x", a), [P, K, PACK], BF16)
             return x_mixed[a][:]
 
-        def mix_x_gpsimd(a):
+        def mix_x_gpsimd(a, k0=X_GPSIMD):
             nc.gpsimd.tensor_scalar(
-                out=mixed_x(a)[:, 0:X_GPSIMD, :],
-                in0=x_raw[a][:, :, 0:X_GPSIMD].rearrange("p t k -> p k t"),
+                out=mixed_x(a)[:, 0:k0, :],
+                in0=x_raw[a][:, :, 0:k0].rearrange("p t k -> p k t"),
                 scalar1=1.0,
                 scalar2=0.0,
                 op0=MULT,
                 op1=ADD,
             )
 
-        def mix_x_scalar(a):
-            nc.scalar.copy(
-                out=mixed_runs(mixed_x(a)[:, X_GPSIMD:K, :]), in_=in_runs(x_raw[a][:, :, X_GPSIMD:K])
-            )
+        def mix_x_scalar(a, k0=X_GPSIMD):
+            nc.scalar.copy(out=mixed_runs(mixed_x(a)[:, k0:K, :]), in_=in_runs(x_raw[a][:, :, k0:K]))
 
         def quantise_x(a):
             x_mx[a] = quantise("x", GROUPS, x_mixed[a][:].rearrange("p k t -> p (k t)"))
@@ -357,9 +400,12 @@ def tile_shard_weight_grad_s7_kernel(tc, x, dy, w2_bytes, w2_scale, g, c, out):
         scale_strip(2)
         quantise_w(0)
         widen_strip(3)
-        empty_y(0, 0)
         load_y(0, (1,))
         turn_y(0, 1)
+        load_w(2)
+        widen_strip(4)
+        widen_strip(5)
+        empty_y(0, 0)
         empty_y(0, 1)
         load_y(0, (2,))
         turn_y(0, 2)
@@ -379,109 +425,104 @@ def tile_shard_weight_grad_s7_kernel(tc, x, dy, w2_bytes, w2_scale, g, c, out):
         load_y(1, (2, 3))
         turn_y(1, 2)
         turn_y(1, 3)
-        unit(0, 0)
-        unit(0, 1)
-        unit(0, 2)
-        unit(0, 3)
-        empty_y(1, 2)
-        empty_y(1, 3)
-        quantise_y(1)
-        load_w(2)
-        widen_strip(4)
-        widen_strip(5)
         turn_pair(2, 0)
         turn_pair(2, 1)
-        load_w(3)
-        widen_strip(6)
-        widen_strip(7)
+        unit(0, 0)
+        unit(0, 1)
+        empty_y(1, 2)
+        unit(0, 2)
+        empty_y(1, 3)
+        unit(0, 3)
+        quantise_y(1)
         scale_pair(2, 0)
+        unit(1, 0)
+        unit(1, 1)
         scale_pair(2, 1)
-        mix_pair(2, 0)
-        mix_pair(2, 1)
+        unit(1, 2)
+        unit(1, 3)
         load_g(0, 0)
         read_unit(0, 0)
-        unit(1, 0)
         read_unit(0, 1)
-        unit(1, 1)
         read_unit(0, 2)
-        unit(1, 2)
         read_unit(0, 3)
-        unit(1, 3)
-        turn_strip(6)
-        turn_strip(7)
         load_y(2, (0, 1))
         split_y_gpsimd(2, 0)
         split_y_gpsimd(2, 1)
         load_g(1, 0)
         read_unit(1, 0)
-        turn_y(2, 0)
         read_unit(1, 1)
-        turn_y(2, 1)
         read_unit(1, 2)
         read_unit(1, 3)
-        scale_strip(6)
+        load_w(3)
+        widen_strip(6)
+        turn_strip(6)
+        widen_strip(7)
+        turn_strip(7)
+        turn_y(2, 0)
+        turn_y(2, 1)
+        mix_pair(2, 0)
+        mix_pair(2, 1)
         quantise_w(2)
+        scale_strip(6)
         scale_strip(7)
-        quantise_dh(0)
-        quantise_w(3)
         empty_y(2, 0)
         empty_y(2, 1)
         load_y(2, (2, 3))
         split_y_gpsimd(2, 2)
         turn_y(2, 2)
-        empty_y(2, 2)
-        split_y_gpsimd(2, 3)
         turn_y(2, 3)
         unit(0, 4)
         unit(0, 5)
         unit(1, 4)
         unit(1, 5)
-        unit(0, 6)
+        empty_y(2, 2)
         empty_y(2, 3)
         load_g(0, 1)
         read_unit(0, 4)
+        quantise_w(3)
+        unit(0, 6)
+        unit(0, 7)
         read_unit(0, 5)
         load_x(0)
         mix_x_gpsimd(0)
-        load_g(1, 1)
-        read_unit(1, 4)
-        read_unit(1, 5)
-        quantise_y(2)
-        read_unit(0, 6)
         load_y(3, (0, 1))
         split_y(3, 0)
         turn_y(3, 0)
         split_y(3, 1)
         turn_y(3, 1)
+        load_g(1, 1)
+        read_unit(1, 4)
+        read_unit(1, 5)
+        read_unit(0, 6)
+        read_unit(0, 7)
+        quantise_y(2)
         load_y(3, (2, 3))
         split_y(3, 2)
         turn_y(3, 2)
         split_y(3, 3)
         turn_y(3, 3)
-        unit(0, 7)
         unit(1, 6)
         unit(1, 7)
         unit(2, 0)
-        read_unit(0, 7)
+        unit(2, 1)
         read_unit(1, 6)
         read_unit(1, 7)
         mix_x_scalar(0)
         empty_y(3, 0)
-        unit(2, 1)
-        empty_y(3, 1)
         unit(2, 2)
-        empty_y(3, 2)
+        empty_y(3, 1)
         unit(2, 3)
+        empty_y(3, 2)
         empty_y(3, 3)
         quantise_y(3)
         unit(3, 0)
         unit(3, 1)
         unit(3, 2)
         unit(3, 3)
+        quantise_dh(0)
         quantise_x(0)
         load_x(1)
-        mix_x_scalar(1)
-        mix_x_gpsimd(1)
+        mix_x_scalar(1, 0)
         quantise_x(1)
         load_g(2, 0)
         read_unit(2, 0)
@@ -511,72 +552,74 @@ def tile_shard_weight_grad_s7_kernel(tc, x, dy, w2_bytes, w2_scale, g, c, out):
         load_w(4)
         widen_strip(8)
         widen_strip(9)
-        mix_x_scalar(2)
-        mix_x_scalar(3)
+        split_strip(8)
+        split_strip(9)
         first(0, 0)
+        half(0, 2, 0)
         first(0, 1)
-        turn_pair(4, 0)
+        half(0, 2, 1)
         first(1, 0)
+        half(0, 3, 0)
         first(1, 1)
-        turn_pair(4, 1)
+        half(0, 3, 1)
         load_g(2, 1)
         read_unit(2, 4)
-        half(0, 2, 0)
+        turn_pair_words(4, 0)
         read_unit(2, 5)
-        half(0, 2, 1)
+        turn_pair_words(4, 1)
         read_unit(2, 6)
-        half(0, 3, 0)
         read_unit(2, 7)
-        half(0, 3, 1)
         quantise_dh(2)
-        quantise_x(2)
-        quantise_x(3)
         load_g(3, 1)
         load_w(5)
         widen_strip(10)
         widen_strip(11)
-        scale_pair(4, 0)
-        unit(3, 4)
-        unit(3, 5)
-        read_unit(3, 4)
-        read_unit(3, 5)
-        scale_pair(4, 1)
-        unit(3, 6)
-        unit(3, 7)
-        read_unit(3, 6)
-        read_unit(3, 7)
+        split_strip(10)
+        split_strip(11)
+        turn_pair_words(5, 0)
+        turn_pair_words(5, 1)
+        mix_x_scalar(2)
+        quantise_x(2)
+        mix_x_scalar(3)
+        quantise_x(3)
+        scale_pair_vector(4, 0)
+        scale_pair_vector(4, 1)
         first(2, 0)
+        unit(3, 4)
+        read_unit(3, 4)
+        quantise_w(4)
+        first(2, 1)
+        unit(3, 5)
+        read_unit(3, 5)
+        first(3, 0)
+        unit(3, 6)
+        read_unit(3, 6)
+        first(3, 1)
+        unit(3, 7)
         half(1, 0, 0)
+        half(1, 0, 1)
+        read_unit(3, 7)
         sum_on_vector(0, 0)
         quantise_dh(3)
-        first(2, 1)
-        half(1, 0, 1)
-        first(3, 0)
+        scale_pair_words(5, 0)
         half(1, 1, 0)
-        first(3, 1)
+        scale_pair_words(5, 1)
         half(1, 1, 1)
-        turn_pair(5, 0)
-        turn_pair(5, 1)
-        mix_pair(4, 0)
-        mix_pair(4, 1)
-        quantise_w(4)
         unit(0, 8)
-        second(0, 1)
         unit(0, 9)
-        second(1, 0)
         unit(1, 8)
-        second(1, 1)
         unit(1, 9)
-        scale_pair(5, 0)
         half(1, 2, 0)
+        second(0, 1)
         half(1, 2, 1)
-        scale_pair(5, 1)
+        second(1, 0)
         half(1, 3, 0)
+        second(1, 1)
         half(1, 3, 1)
         mix_pair(5, 0)
         mix_pair(5, 1)
         second(3, 0)
-        sums_on_gpsimd(0, ((0, 1), (1, 0), (1, 1)))
+        sums_on_gpsimd(0, ((0, 1), (1, 0)))
         second(3, 1)
         load_g(0, 2)
         read_unit(0, 8)
@@ -590,13 +633,13 @@ def tile_shard_weight_grad_s7_kernel(tc, x, dy, w2_bytes, w2_scale, g, c, out):
         unit(3, 9)
         sum_on_vector(2, 0)
         sum_on_vector(2, 1)
+        quantise_w(5)
         quantise_dh(4)
         half(0, 4, 0)
         half(0, 4, 1)
-        quantise_w(5)
         unit(0, 10)
         unit(0, 11)
-        sums_on_gpsimd(1, ((3, 0), (3, 1)))
+        sums_on_gpsimd(1, ((1, 1),))
         load_g(2, 2)
         read_unit(2, 8)
         unit(1, 10)
@@ -612,6 +655,7 @@ def tile_shard_weight_grad_s7_kernel(tc, x, dy, w2_bytes, w2_scale, g, c, out):
         read_unit(0, 11)
         read_unit(1, 10)
         read_unit(1, 11)
+        sums_on_gpsimd(2, ((3, 0), (3, 1)))
         store(0, 0)
         first(4, 0)
         unit(2, 10)
@@ -644,9 +688,9 @@ def tile_shard_weight_grad_s7_kernel(tc, x, dy, w2_bytes, w2_scale, g, c, out):
         sums_on_gpsimd(3, ((4, 1),))
         store(0, 1)
         store(1, 0)
-        store(1, 1)
         store(2, 0)
         store(2, 1)
+        store(1, 1)
         store(3, 0)
         store(3, 1)
         store(4, 0)

@@ -41,7 +41,7 @@ G_RAW = 8
 W_RAW = 4
 WIDES = 4
 RUNS = (((0, 0), (0, 1), (0, 2), (0, 3), (1, 0), (1, 1), (1, 2), (1, 3)), ((0, 4), (0, 5), (1, 4), (1, 5), (0, 6), (0, 7), (1, 6), (1, 7)), ((2, 0), (2, 1), (2, 2), (2, 3), (3, 0), (3, 1), (3, 2), (3, 3)), ((2, 4), (2, 5), (2, 6), (2, 7), (3, 4), (3, 5), (3, 6), (3, 7)), ((0, 8), (0, 9), (1, 8), (1, 9)), ((2, 8), (2, 9), (3, 8), (3, 9)), ((0, 10), (0, 11), (1, 10), (1, 11)), ((2, 10), (3, 10), (2, 11), (3, 11)))
-STAGE_OF = {('w', 0): 0, ('dh', 0): 0, ('dh', 2): 0, ('dh', 5): 0, ('total', 2): 0, ('w', 1): 1, ('w', 3): 1, ('x', 0): 1, ('x', 2): 1, ('w', 5): 1, ('dh', 6): 1, ('total', 3): 1, ('y', 0): 2, ('y', 2): 2, ('x', 1): 2, ('x', 3): 2, ('dh', 4): 2, ('total', 1): 2, ('y', 1): 3, ('split', 2, 0): 3, ('dh', 1): 3, ('w', 4): 3, ('dh', 7): 3, ('w', 2): 4, ('y', 3): 4, ('dh', 3): 4, ('total', 0): 4}
+STAGE_OF = {('w', 0): 0, ('dh', 0): 0, ('dh', 2): 0, ('dh', 5): 0, ('total', 2): 0, ('w', 1): 1, ('w', 3): 1, ('x', 0): 1, ('x', 1): 1, ('w', 5): 1, ('dh', 6): 1, ('total', 3): 1, ('y', 0): 2, ('y', 2): 2, ('w', 4): 2, ('dh', 4): 2, ('total', 1): 2, ('y', 1): 3, ('split', 2, 0): 3, ('dh', 1): 3, ('dh', 7): 3, ('w', 2): 4, ('y', 3): 4, ('dh', 3): 4, ('total', 0): 4}
 
 
 def tile_shard_weight_grad_s7_kernel(tc, x, dy, w2_bytes, w2_scale, g, c, out):
@@ -294,9 +294,9 @@ def tile_shard_weight_grad_s7_kernel(tc, x, dy, w2_bytes, w2_scale, g, c, out):
             w_mx[j] = quantise("w", PAIRS, source)
 
         def mixed_x(a):
-            if a not in x_mixed:
-                x_mixed[a] = stage(("x", a), [P, K, PACK], BF16)
-            return x_mixed[a][:]
+            if a // 2 not in x_mixed:
+                x_mixed[a // 2] = stage(("x", a // 2), [P, 2, K, PACK], BF16)
+            return x_mixed[a // 2][:, a % 2]
 
         def mix_x_gpsimd(a, k0=X_GPSIMD):
             nc.gpsimd.tensor_scalar(
@@ -311,8 +311,8 @@ def tile_shard_weight_grad_s7_kernel(tc, x, dy, w2_bytes, w2_scale, g, c, out):
         def mix_x_scalar(a, k0=X_GPSIMD):
             nc.scalar.copy(out=mixed_runs(mixed_x(a)[:, k0:K, :]), in_=in_runs(x_raw[a][:, :, k0:K]))
 
-        def quantise_x(a):
-            x_mx[a] = quantise("x", GROUPS, x_mixed[a][:].rearrange("p k t -> p (k t)"))
+        def quantise_x(d):
+            x_mx[d] = quantise("x", D, x_mixed[d][:].rearrange("p q k t -> p (q k t)"))
 
         run_of = {u: (k, i) for k, run in enumerate(RUNS) for i, u in enumerate(run)}
 
@@ -353,7 +353,7 @@ def tile_shard_weight_grad_s7_kernel(tc, x, dy, w2_bytes, w2_scale, g, c, out):
                 for q in range(2):
                     quantised, f0 = dh_mx[2 * d + q, 2 * j + strip]
                     multiply(
-                        ps[:, k2, :], x_mx[2 * d + q], slice(k0, k0 + P), quantised, slice(f0, f0 + width), q == 0, q == 1
+                        ps[:, k2, :], x_mx[d], slice(K * q + k0, K * q + k0 + P), quantised, slice(f0, f0 + width), q == 0, q == 1
                     )
             bank["half", d, j, h, strip] = ps
 
@@ -448,20 +448,20 @@ def tile_shard_weight_grad_s7_kernel(tc, x, dy, w2_bytes, w2_scale, g, c, out):
         load_y(2, (0, 1))
         split_y_gpsimd(2, 0)
         split_y_gpsimd(2, 1)
-        load_g(1, 0)
-        read_unit(1, 0)
-        read_unit(1, 1)
-        read_unit(1, 2)
-        read_unit(1, 3)
         load_w(3)
         widen_strip(6)
         turn_strip(6)
         widen_strip(7)
         turn_strip(7)
-        turn_y(2, 0)
-        turn_y(2, 1)
         mix_pair(2, 0)
         mix_pair(2, 1)
+        load_g(1, 0)
+        read_unit(1, 0)
+        turn_y(2, 0)
+        read_unit(1, 1)
+        turn_y(2, 1)
+        read_unit(1, 2)
+        read_unit(1, 3)
         quantise_w(2)
         scale_strip(6)
         scale_strip(7)
@@ -520,101 +520,101 @@ def tile_shard_weight_grad_s7_kernel(tc, x, dy, w2_bytes, w2_scale, g, c, out):
         unit(3, 2)
         unit(3, 3)
         quantise_dh(0)
-        quantise_x(0)
         load_x(1)
         mix_x_scalar(1, 0)
-        quantise_x(1)
+        quantise_x(0)
         load_g(2, 0)
         read_unit(2, 0)
         half(0, 0, 0)
         read_unit(2, 1)
         half(0, 0, 1)
         read_unit(2, 2)
-        half(0, 1, 0)
         read_unit(2, 3)
-        half(0, 1, 1)
         load_g(3, 0)
         read_unit(3, 0)
-        unit(2, 4)
         read_unit(3, 1)
-        unit(2, 5)
         read_unit(3, 2)
-        unit(2, 6)
         read_unit(3, 3)
-        unit(2, 7)
         quantise_dh(1)
         load_c()
         widen_c()
-        load_x(2)
-        mix_x_gpsimd(2)
-        load_x(3)
-        mix_x_gpsimd(3)
         load_w(4)
         widen_strip(8)
         widen_strip(9)
         split_strip(8)
         split_strip(9)
+        turn_pair_words(4, 0)
+        turn_pair_words(4, 1)
+        half(0, 1, 0)
+        half(0, 1, 1)
+        unit(2, 4)
+        unit(2, 5)
+        load_x(2)
+        mix_x_gpsimd(2)
+        load_w(5)
+        widen_strip(10)
+        widen_strip(11)
+        split_strip(10)
         first(0, 0)
-        half(0, 2, 0)
+        unit(2, 6)
         first(0, 1)
+        unit(2, 7)
+        scale_pair_words(4, 0)
+        half(0, 2, 0)
+        scale_pair_words(4, 1)
         half(0, 2, 1)
         first(1, 0)
         half(0, 3, 0)
         first(1, 1)
         half(0, 3, 1)
+        mix_x_scalar(2)
+        load_x(3)
+        mix_x_scalar(3)
+        mix_pair(4, 0)
+        mix_pair(4, 1)
+        first(2, 0)
+        first(2, 1)
+        first(3, 0)
+        first(3, 1)
+        split_strip(11)
+        mix_x_gpsimd(3)
         load_g(2, 1)
         read_unit(2, 4)
-        turn_pair_words(4, 0)
-        read_unit(2, 5)
-        turn_pair_words(4, 1)
-        read_unit(2, 6)
-        read_unit(2, 7)
-        quantise_dh(2)
-        load_g(3, 1)
-        load_w(5)
-        widen_strip(10)
-        widen_strip(11)
-        split_strip(10)
-        split_strip(11)
-        turn_pair_words(5, 0)
-        turn_pair_words(5, 1)
-        mix_x_scalar(2)
-        quantise_x(2)
-        mix_x_scalar(3)
-        quantise_x(3)
-        scale_pair_vector(4, 0)
-        scale_pair_vector(4, 1)
-        first(2, 0)
         unit(3, 4)
-        read_unit(3, 4)
-        quantise_w(4)
-        first(2, 1)
+        read_unit(2, 5)
         unit(3, 5)
-        read_unit(3, 5)
-        first(3, 0)
+        read_unit(2, 6)
         unit(3, 6)
-        read_unit(3, 6)
-        first(3, 1)
+        read_unit(2, 7)
         unit(3, 7)
+        quantise_dh(2)
+        quantise_x(1)
         half(1, 0, 0)
         half(1, 0, 1)
-        read_unit(3, 7)
-        sum_on_vector(0, 0)
-        quantise_dh(3)
-        scale_pair_words(5, 0)
         half(1, 1, 0)
-        scale_pair_words(5, 1)
         half(1, 1, 1)
+        quantise_w(4)
+        second(0, 1)
+        second(1, 0)
+        second(1, 1)
+        load_g(3, 1)
+        read_unit(3, 4)
+        turn_pair_words(5, 0)
+        read_unit(3, 5)
+        turn_pair_words(5, 1)
+        read_unit(3, 6)
         unit(0, 8)
+        read_unit(3, 7)
         unit(0, 9)
+        sum_on_vector(0, 0)
         unit(1, 8)
         unit(1, 9)
+        quantise_dh(3)
         half(1, 2, 0)
-        second(0, 1)
         half(1, 2, 1)
-        second(1, 0)
+        scale_pair_words(5, 0)
         half(1, 3, 0)
-        second(1, 1)
+        scale_pair_words(5, 1)
         half(1, 3, 1)
         mix_pair(5, 0)
         mix_pair(5, 1)
@@ -633,17 +633,17 @@ def tile_shard_weight_grad_s7_kernel(tc, x, dy, w2_bytes, w2_scale, g, c, out):
         unit(3, 9)
         sum_on_vector(2, 0)
         sum_on_vector(2, 1)
-        quantise_w(5)
         quantise_dh(4)
         half(0, 4, 0)
         half(0, 4, 1)
-        unit(0, 10)
-        unit(0, 11)
         sums_on_gpsimd(1, ((1, 1),))
         load_g(2, 2)
         read_unit(2, 8)
-        unit(1, 10)
         read_unit(2, 9)
+        quantise_w(5)
+        unit(0, 10)
+        unit(0, 11)
+        unit(1, 10)
         unit(1, 11)
         load_g(3, 2)
         read_unit(3, 8)

@@ -25,7 +25,7 @@ BEAT = 4
 G_COLS = BEAT * P
 RUN = 4
 VECTOR_PAIRS = 3
-X_GPSIMD = 352
+X_GPSIMD = 368
 BAR = 2 * BEAT
 BARS = 4
 STAGES = 5
@@ -41,7 +41,7 @@ G_RAW = 8
 W_RAW = 4
 WIDES = 4
 RUNS = (((0, 0), (0, 1), (0, 2), (0, 3), (1, 0), (1, 1), (1, 2), (1, 3)), ((0, 4), (0, 5), (1, 4), (1, 5), (0, 6), (0, 7), (1, 6), (1, 7)), ((2, 0), (2, 1), (2, 2), (2, 3), (3, 0), (3, 1), (3, 2), (3, 3)), ((2, 4), (2, 5), (2, 6), (2, 7), (3, 4), (3, 5), (3, 6), (3, 7)), ((0, 8), (0, 9), (1, 8), (1, 9)), ((2, 8), (2, 9), (3, 8), (3, 9)), ((0, 10), (0, 11), (1, 10), (1, 11)), ((2, 10), (3, 10), (2, 11), (3, 11)))
-STAGE_OF = {('w', 0): 0, ('dh', 0): 0, ('dh', 2): 0, ('dh', 5): 0, ('total', 2): 0, ('w', 1): 1, ('w', 3): 1, ('x', 0): 1, ('x', 1): 1, ('w', 5): 1, ('dh', 6): 1, ('total', 3): 1, ('y', 0): 2, ('y', 2): 2, ('w', 4): 2, ('dh', 4): 2, ('total', 1): 2, ('y', 1): 3, ('split', 2, 0): 3, ('dh', 1): 3, ('dh', 7): 3, ('w', 2): 4, ('y', 3): 4, ('dh', 3): 4, ('total', 0): 4}
+STAGE_OF = {('w', 0): 0, ('dh', 0): 0, ('dh', 2): 0, ('dh', 5): 0, ('total', 2): 0, ('w', 1): 1, ('w', 3): 1, ('x', 0): 1, ('x', 1): 1, ('w', 5): 1, ('dh', 6): 1, ('total', 3): 1, ('y', 0): 2, ('y', 2): 2, ('w', 4): 2, ('dh', 4): 2, ('total', 1): 2, ('y', 1): 3, ('dh', 1): 3, ('dh', 7): 3, ('w', 2): 4, ('split', 2, 2): 4, ('y', 3): 4, ('dh', 3): 4, ('total', 0): 4}
 
 
 def tile_shard_weight_grad_s7_kernel(tc, x, dy, w2_bytes, w2_scale, g, c, out):
@@ -97,6 +97,8 @@ def tile_shard_weight_grad_s7_kernel(tc, x, dy, w2_bytes, w2_scale, g, c, out):
         def psum_bank(shape):
             return psum.tile(shape, F32, name="bank", bufs=BANKS)
 
+        warm = keep.tile([P, PACK * P], BF16, name="warm", align_bytes=64)
+        nc.vector.memset(warm[:], 1.0)
         ident = keep.tile([P, P], F32, name="ident", align_bytes=64)
         make_identity(nc, ident[:])
         c_all = keep.tile([P, D], F32, name="c_all")
@@ -105,7 +107,7 @@ def tile_shard_weight_grad_s7_kernel(tc, x, dy, w2_bytes, w2_scale, g, c, out):
 
         w_wide, w_split, y_split, w_planes, w_turned, w_mx = {}, {}, {}, {}, {}, {}
         y_turned, y_mx, x_mixed, x_mx, dh, dh_mx = {}, {}, {}, {}, {}, {}
-        bank, first_pair, second_term, result = {}, {}, {}, {}
+        bank, first_pair, second_term, result, w_loose, w_single, strip_mx = {}, {}, {}, {}, {}, {}, {}
 
         def quantise(name, bufs, source):
             words = source.shape[1] // PACK
@@ -221,18 +223,39 @@ def tile_shard_weight_grad_s7_kernel(tc, x, dy, w2_bytes, w2_scale, g, c, out):
                     op=MULT,
                 )
 
+        def empty_strip(b):
+            for gi in range(2):
+                mixed = pair_tile(b // 2)[:, gi, b % 2].rearrange("p f u -> p (f u)").bitcast(BF16)
+                nc.scalar.copy(
+                    out=mixed_runs(mixed.rearrange("p (f t) -> p f t", t=PACK)), in_=in_runs(bank["strip", b, gi][:])
+                )
+
         def turn_words(b):
             bank["words", b] = turn_row(w_wide[b][:], w_split.get(b))
 
         def empty_words(b):
-            nc.scalar.copy(out=pair_tile(b // 2)[:, :, b % 2], in_=bank["words", b][:].rearrange("p g u m -> p g m u"))
+            w_loose[b] = work.tile([P, 2, P, 2], F32, name="y_row", bufs=PACK, align_bytes=64)
+            nc.scalar.copy(out=w_loose[b][:], in_=bank["words", b][:].rearrange("p g u m -> p g m u"))
 
         def scale_gpsimd(b):
-            values = pair_tile(b // 2)[:, :, b % 2].rearrange("p g f u -> p g (f u)").bitcast(BF16)
+            if b in w_loose:
+                w_single[b] = stage(("strip", b), [P, 2, P, 2], F32)
+                words = w_single[b][:]
+            else:
+                words = pair_tile(b // 2)[:, :, b % 2]
+            values = words.rearrange("p g f u -> p g (f u)").bitcast(BF16)
             values = values.rearrange("p g (f t) -> p g f t", t=PACK)
+            source = values
+            if b in w_loose:
+                source = w_loose[b][:].rearrange("p g f u -> p g (f u)").bitcast(BF16).rearrange("p g (f t) -> p g f t", t=PACK)
             nc.gpsimd.tensor_tensor(
-                out=values, in0=values, in1=scale_col[:].unsqueeze(2).to_broadcast([P, 2, P, PACK]), op=MULT
+                out=values, in0=source, in1=scale_col[:].unsqueeze(2).to_broadcast([P, 2, P, PACK]), op=MULT
             )
+
+        def warm_up(count):
+            ps = psum_bank([P, PACK * P])
+            for i in range(count):
+                nc.tensor.matmul(ps[:], lhsT=warm[:, 0:P], rhs=warm[:], start=True, stop=True)
 
         def turn_pair(j, gi):
             for u in range(2):
@@ -260,7 +283,10 @@ def tile_shard_weight_grad_s7_kernel(tc, x, dy, w2_bytes, w2_scale, g, c, out):
             ps = psum_bank([P, 2, 2, P])
             for u in range(2):
                 for i in range(2):
-                    nc.tensor.transpose(ps[:, u, i, :], w_split[2 * j + i][:, u, P * gi : P * (gi + 1)], ident[:])
+                    if 2 * j + i in w_split:
+                        nc.tensor.transpose(ps[:, u, i, :], w_split[2 * j + i][:, u, P * gi : P * (gi + 1)], ident[:])
+                    else:
+                        turn(ps[:, u, i, :], w_wide[2 * j + i][:], gi, u)
             bank["pair", j, gi] = ps
 
         def scale_pair_words(j, gi):
@@ -291,7 +317,13 @@ def tile_shard_weight_grad_s7_kernel(tc, x, dy, w2_bytes, w2_scale, g, c, out):
 
         def quantise_w(j):
             source = w_turned[j][:].rearrange("p g i f u -> p (g i f u)").bitcast(BF16)
-            w_mx[j] = quantise("w", PAIRS, source)
+            w_mx[j] = quantise("w", PAIRS - 1, source)
+            for i in range(2):
+                strip_mx[2 * j + i] = (w_mx[j], PAIR, P * i)
+
+        def quantise_strip(b):
+            source = w_single[b][:].rearrange("p g f u -> p (g f u)").bitcast(BF16)
+            strip_mx[b] = (quantise("strip", 2, source), P, 0)
 
         def mixed_x(a):
             if a // 2 not in x_mixed:
@@ -322,10 +354,9 @@ def tile_shard_weight_grad_s7_kernel(tc, x, dy, w2_bytes, w2_scale, g, c, out):
             for t in range(PACK):
                 for gi in range(2):
                     y0 = PAIR * t + P * gi
-                    w0 = PAIR * gi + P * (b % 2)
-                    multiply(
-                        ps[:, t, :], y_mx[a], slice(y0, y0 + P), w_mx[b // 2], slice(w0, w0 + P), gi == 0, gi == 1
-                    )
+                    codes, per_pass, f0 = strip_mx[b]
+                    w0 = per_pass * gi + f0
+                    multiply(ps[:, t, :], y_mx[a], slice(y0, y0 + P), codes, slice(w0, w0 + P), gi == 0, gi == 1)
 
         def read_unit(a, b):
             k, i = run_of[a, b]
@@ -357,6 +388,18 @@ def tile_shard_weight_grad_s7_kernel(tc, x, dy, w2_bytes, w2_scale, g, c, out):
                     )
             bank["half", d, j, h, strip] = ps
 
+        def last_passes(q, h):
+            j, strip = PAIRS - 1, 1
+            if q == 0:
+                bank["half", 1, j, h, strip] = psum_bank([P, 2, P])
+            quantised, f0 = dh_mx[2 + q, 2 * j + strip]
+            for k2 in range(2):
+                k0 = K * q + P * (2 * h + k2)
+                multiply(
+                    bank["half", 1, j, h, strip][:, k2, :], x_mx[1], slice(k0, k0 + P), quantised, slice(f0, f0 + P),
+                    q == 0 and k2 == 0, q == 1 and k2 == 1,
+                )
+
         def first(j, h):
             if j not in first_pair:
                 first_pair[j] = work.tile([P, 2, 2, PAIR], F32, name="first_term", bufs=FIRSTS)
@@ -383,6 +426,7 @@ def tile_shard_weight_grad_s7_kernel(tc, x, dy, w2_bytes, w2_scale, g, c, out):
             f0 = PAIR * j + P * strip
             nc.sync.dma_start(out=out_view[h][:, :, f0 : f0 + width], in_=result[j, h, strip])
 
+        warm_up(5)
         load_w(0, (0,))
         widen_strip(0, parts=2)
         turn_strip(0)
@@ -392,31 +436,35 @@ def tile_shard_weight_grad_s7_kernel(tc, x, dy, w2_bytes, w2_scale, g, c, out):
         widen_strip(1)
         turn_strip(1)
         scale_strip(1)
+        quantise_w(0)
         load_y(0, (0,))
+        turn_y(0, 0)
         load_w(1)
         widen_strip(2)
-        turn_strip(2)
-        turn_y(0, 0)
-        scale_strip(2)
-        quantise_w(0)
         widen_strip(3)
+        empty_y(0, 0)
         load_y(0, (1,))
         turn_y(0, 1)
+        turn_strip(2)
+        turn_strip(3)
+        scale_strip(2)
+        scale_strip(3)
+        empty_y(0, 1)
         load_w(2)
         widen_strip(4)
         widen_strip(5)
-        empty_y(0, 0)
-        empty_y(0, 1)
         load_y(0, (2,))
         turn_y(0, 2)
         empty_y(0, 2)
         load_y(0, (3,))
         turn_y(0, 3)
-        turn_strip(3)
-        scale_strip(3)
+        turn_strip(4)
+        turn_strip(5)
+        scale_strip(4)
         empty_y(0, 3)
         quantise_y(0)
         quantise_w(1)
+        scale_strip(5)
         load_y(1, (0, 1))
         turn_y(1, 0)
         turn_y(1, 1)
@@ -425,71 +473,71 @@ def tile_shard_weight_grad_s7_kernel(tc, x, dy, w2_bytes, w2_scale, g, c, out):
         load_y(1, (2, 3))
         turn_y(1, 2)
         turn_y(1, 3)
-        turn_pair(2, 0)
-        turn_pair(2, 1)
         unit(0, 0)
         unit(0, 1)
-        empty_y(1, 2)
         unit(0, 2)
-        empty_y(1, 3)
         unit(0, 3)
+        empty_y(1, 2)
+        empty_y(1, 3)
         quantise_y(1)
-        scale_pair(2, 0)
-        unit(1, 0)
-        unit(1, 1)
-        scale_pair(2, 1)
-        unit(1, 2)
-        unit(1, 3)
         load_g(0, 0)
         read_unit(0, 0)
+        quantise_w(2)
         read_unit(0, 1)
         read_unit(0, 2)
         read_unit(0, 3)
-        load_y(2, (0, 1))
-        split_y_gpsimd(2, 0)
-        split_y_gpsimd(2, 1)
         load_w(3)
         widen_strip(6)
-        turn_strip(6)
         widen_strip(7)
-        turn_strip(7)
-        mix_pair(2, 0)
-        mix_pair(2, 1)
-        load_g(1, 0)
-        read_unit(1, 0)
+        turn_pair(3, 0)
+        turn_pair(3, 1)
+        unit(1, 0)
+        unit(1, 1)
+        unit(1, 2)
+        unit(1, 3)
+        load_y(2, (0, 1))
+        split_y(2, 0)
+        split_y(2, 1)
+        scale_pair(3, 0)
         turn_y(2, 0)
-        read_unit(1, 1)
         turn_y(2, 1)
-        read_unit(1, 2)
-        read_unit(1, 3)
-        quantise_w(2)
-        scale_strip(6)
-        scale_strip(7)
+        scale_pair(3, 1)
+        mix_pair(3, 0)
+        mix_pair(3, 1)
         empty_y(2, 0)
         empty_y(2, 1)
         load_y(2, (2, 3))
         split_y_gpsimd(2, 2)
         turn_y(2, 2)
-        turn_y(2, 3)
-        unit(0, 4)
-        unit(0, 5)
-        unit(1, 4)
-        unit(1, 5)
         empty_y(2, 2)
+        split_y_gpsimd(2, 3)
+        turn_y(2, 3)
         empty_y(2, 3)
-        load_g(0, 1)
-        read_unit(0, 4)
+        load_g(1, 0)
+        read_unit(1, 0)
+        unit(0, 4)
+        read_unit(1, 1)
+        unit(0, 5)
+        read_unit(1, 2)
+        unit(1, 4)
+        read_unit(1, 3)
+        unit(1, 5)
+        quantise_dh(0)
         quantise_w(3)
         unit(0, 6)
         unit(0, 7)
+        load_g(0, 1)
+        read_unit(0, 4)
         read_unit(0, 5)
         load_x(0)
-        mix_x_gpsimd(0)
+        mix_x_gpsimd(0, 512)
         load_y(3, (0, 1))
         split_y(3, 0)
         turn_y(3, 0)
         split_y(3, 1)
         turn_y(3, 1)
+        empty_y(3, 0)
+        empty_y(3, 1)
         load_g(1, 1)
         read_unit(1, 4)
         read_unit(1, 5)
@@ -497,21 +545,16 @@ def tile_shard_weight_grad_s7_kernel(tc, x, dy, w2_bytes, w2_scale, g, c, out):
         read_unit(0, 7)
         quantise_y(2)
         load_y(3, (2, 3))
-        split_y(3, 2)
         turn_y(3, 2)
-        split_y(3, 3)
         turn_y(3, 3)
         unit(1, 6)
         unit(1, 7)
         unit(2, 0)
         unit(2, 1)
+        unit(2, 2)
+        unit(2, 3)
         read_unit(1, 6)
         read_unit(1, 7)
-        mix_x_scalar(0)
-        empty_y(3, 0)
-        unit(2, 2)
-        empty_y(3, 1)
-        unit(2, 3)
         empty_y(3, 2)
         empty_y(3, 3)
         quantise_y(3)
@@ -519,7 +562,6 @@ def tile_shard_weight_grad_s7_kernel(tc, x, dy, w2_bytes, w2_scale, g, c, out):
         unit(3, 1)
         unit(3, 2)
         unit(3, 3)
-        quantise_dh(0)
         load_x(1)
         mix_x_scalar(1, 0)
         quantise_x(0)
@@ -530,12 +572,6 @@ def tile_shard_weight_grad_s7_kernel(tc, x, dy, w2_bytes, w2_scale, g, c, out):
         half(0, 0, 1)
         read_unit(2, 2)
         read_unit(2, 3)
-        load_g(3, 0)
-        read_unit(3, 0)
-        read_unit(3, 1)
-        read_unit(3, 2)
-        read_unit(3, 3)
-        quantise_dh(1)
         load_c()
         widen_c()
         load_w(4)
@@ -545,10 +581,16 @@ def tile_shard_weight_grad_s7_kernel(tc, x, dy, w2_bytes, w2_scale, g, c, out):
         split_strip(9)
         turn_pair_words(4, 0)
         turn_pair_words(4, 1)
+        load_g(3, 0)
+        read_unit(3, 0)
         half(0, 1, 0)
+        read_unit(3, 1)
         half(0, 1, 1)
+        read_unit(3, 2)
         unit(2, 4)
+        read_unit(3, 3)
         unit(2, 5)
+        quantise_dh(1)
         load_x(2)
         mix_x_gpsimd(2)
         load_w(5)
@@ -570,12 +612,12 @@ def tile_shard_weight_grad_s7_kernel(tc, x, dy, w2_bytes, w2_scale, g, c, out):
         mix_x_scalar(2)
         load_x(3)
         mix_x_scalar(3)
-        mix_pair(4, 0)
-        mix_pair(4, 1)
         first(2, 0)
         first(2, 1)
+        mix_pair(4, 0)
         first(3, 0)
         first(3, 1)
+        mix_pair(4, 1)
         split_strip(11)
         mix_x_gpsimd(3)
         load_g(2, 1)
@@ -593,7 +635,6 @@ def tile_shard_weight_grad_s7_kernel(tc, x, dy, w2_bytes, w2_scale, g, c, out):
         half(1, 0, 1)
         half(1, 1, 0)
         half(1, 1, 1)
-        quantise_w(4)
         second(0, 1)
         second(1, 0)
         second(1, 1)
@@ -603,10 +644,11 @@ def tile_shard_weight_grad_s7_kernel(tc, x, dy, w2_bytes, w2_scale, g, c, out):
         read_unit(3, 5)
         turn_pair_words(5, 1)
         read_unit(3, 6)
-        unit(0, 8)
         read_unit(3, 7)
-        unit(0, 9)
         sum_on_vector(0, 0)
+        quantise_w(4)
+        unit(0, 8)
+        unit(0, 9)
         unit(1, 8)
         unit(1, 9)
         quantise_dh(3)
@@ -677,8 +719,10 @@ def tile_shard_weight_grad_s7_kernel(tc, x, dy, w2_bytes, w2_scale, g, c, out):
         quantise_dh(7, 3, 1)
         second(4, 1)
         half(1, 5, 1, 0, 128)
-        half(1, 5, 0, 1, 128)
-        half(1, 5, 1, 1, 128)
+        last_passes(0, 0)
+        last_passes(0, 1)
+        last_passes(1, 0)
+        last_passes(1, 1)
         first(5, 0)
         sum_on_vector(5, 0, 0, 128)
         first(5, 1)

@@ -41,7 +41,7 @@ G_RAW = 8
 W_RAW = 4
 WIDES = 4
 RUNS = (((0, 0), (0, 1), (0, 2), (0, 3), (1, 0), (1, 1), (1, 2), (1, 3)), ((0, 4), (0, 5), (1, 4), (1, 5), (0, 6), (0, 7), (1, 6), (1, 7)), ((2, 0), (2, 1), (2, 2), (2, 3), (3, 0), (3, 1), (3, 2), (3, 3)), ((2, 4), (2, 5), (2, 6), (2, 7), (3, 4), (3, 5), (3, 6), (3, 7)), ((0, 8), (0, 9), (1, 8), (1, 9)), ((2, 8), (2, 9), (3, 8), (3, 9)), ((0, 10), (0, 11), (1, 10), (1, 11)), ((2, 10), (3, 10), (2, 11), (3, 11)))
-STAGE_OF = {('w', 0): 0, ('dh', 0): 0, ('dh', 2): 0, ('dh', 5): 0, ('total', 2): 0, ('w', 1): 1, ('w', 3): 1, ('x', 0): 1, ('x', 1): 1, ('w', 5): 1, ('dh', 6): 1, ('total', 3): 1, ('y', 0): 2, ('y', 2): 2, ('w', 4): 2, ('dh', 4): 2, ('total', 1): 2, ('y', 1): 3, ('dh', 1): 3, ('dh', 7): 3, ('w', 2): 4, ('split', 2, 2): 4, ('y', 3): 4, ('dh', 3): 4, ('total', 0): 4}
+STAGE_OF = {('w', 0): 0, ('dh', 0): 0, ('dh', 2): 0, ('dh', 5): 0, ('total', 2): 0, ('w', 1): 1, ('w', 3): 1, ('x', 0): 1, ('x', 1): 1, ('w', 5): 1, ('dh', 6): 1, ('total', 3): 1, ('y', 0): 2, ('y', 2): 2, ('w', 4): 2, ('dh', 4): 2, ('total', 1): 2, ('y', 1): 3, ('strip', 4): 3, ('dh', 1): 3, ('dh', 7): 3, ('strip', 5): 4, ('y', 3): 4, ('dh', 3): 4, ('total', 0): 4}
 
 
 def tile_shard_weight_grad_s7_kernel(tc, x, dy, w2_bytes, w2_scale, g, c, out):
@@ -83,10 +83,14 @@ def tile_shard_weight_grad_s7_kernel(tc, x, dy, w2_bytes, w2_scale, g, c, out):
             nc.sync.dma_start(out=g_raw[a, chunk][:], in_=samples(g, a)[:, :, G_COLS * chunk : G_COLS * (chunk + 1)])
 
         scale_col = keep.tile([P, 2, PACK], F32, name="scale_col")
+        scale_run = keep.tile([P, 2, PACK, RUN], F32, name="scale_run", align_bytes=64)
         c_bf = keep.tile([P, D], BF16, name="c_bf")
 
         def load_scales():
             nc.sync.dma_start(out=scale_col[:], in_=w2_scale.rearrange("o (g p t) -> p (o g) t", p=P, t=PACK))
+
+        def repeat_scales():
+            nc.vector.tensor_copy(out=scale_run[:], in_=scale_col[:].unsqueeze(3).to_broadcast([P, 2, PACK, RUN]))
 
         def load_c():
             nc.sync.dma_start(out=c_bf[:], in_=c.partition_broadcast(P))
@@ -97,8 +101,6 @@ def tile_shard_weight_grad_s7_kernel(tc, x, dy, w2_bytes, w2_scale, g, c, out):
         def psum_bank(shape):
             return psum.tile(shape, F32, name="bank", bufs=BANKS)
 
-        warm = keep.tile([P, PACK * P], BF16, name="warm", align_bytes=64)
-        nc.vector.memset(warm[:], 1.0)
         ident = keep.tile([P, P], F32, name="ident", align_bytes=64)
         make_identity(nc, ident[:])
         c_all = keep.tile([P, D], F32, name="c_all")
@@ -196,6 +198,13 @@ def tile_shard_weight_grad_s7_kernel(tc, x, dy, w2_bytes, w2_scale, g, c, out):
                 w_turned[j] = stage(("w", j), [P, 2, 2, P, 2], F32)
             return w_turned[j]
 
+        def strip_tile(b):
+            if ("strip", b) not in STAGE_OF:
+                return pair_tile(b // 2)[:, :, b % 2]
+            if b not in w_single:
+                w_single[b] = stage(("strip", b), [P, 2, P, 2], F32)
+            return w_single[b][:]
+
         def widen_strip(b, parts=1):
             wide = wide_tile(b)
             for i in range(parts):
@@ -215,17 +224,18 @@ def tile_shard_weight_grad_s7_kernel(tc, x, dy, w2_bytes, w2_scale, g, c, out):
 
         def scale_strip(b, passes=(0, 1)):
             for gi in passes:
-                mixed = pair_tile(b // 2)[:, gi, b % 2].rearrange("p f u -> p (f u)").bitcast(BF16)
+                mixed = strip_tile(b)[:, gi].rearrange("p f u -> p (f u)").bitcast(BF16)
                 nc.vector.tensor_tensor(
                     out=mixed_runs(mixed.rearrange("p (f t) -> p f t", t=PACK)),
                     in0=in_runs(bank["strip", b, gi][:]),
-                    in1=in_runs(scale_col[:, gi, :].unsqueeze(2).to_broadcast([P, PACK, P])),
+                    in1=scale_run[:, gi].unsqueeze(1).to_broadcast([P, P // RUN, PACK, RUN]),
                     op=MULT,
                 )
 
         def empty_strip(b):
+            w_loose[b] = work.tile([P, 2, P, 2], F32, name="loose", bufs=1, align_bytes=64)
             for gi in range(2):
-                mixed = pair_tile(b // 2)[:, gi, b % 2].rearrange("p f u -> p (f u)").bitcast(BF16)
+                mixed = w_loose[b][:, gi].rearrange("p f u -> p (f u)").bitcast(BF16)
                 nc.scalar.copy(
                     out=mixed_runs(mixed.rearrange("p (f t) -> p f t", t=PACK)), in_=in_runs(bank["strip", b, gi][:])
                 )
@@ -238,11 +248,7 @@ def tile_shard_weight_grad_s7_kernel(tc, x, dy, w2_bytes, w2_scale, g, c, out):
             nc.scalar.copy(out=w_loose[b][:], in_=bank["words", b][:].rearrange("p g u m -> p g m u"))
 
         def scale_gpsimd(b):
-            if b in w_loose:
-                w_single[b] = stage(("strip", b), [P, 2, P, 2], F32)
-                words = w_single[b][:]
-            else:
-                words = pair_tile(b // 2)[:, :, b % 2]
+            words = strip_tile(b)
             values = words.rearrange("p g f u -> p g (f u)").bitcast(BF16)
             values = values.rearrange("p g (f t) -> p g f t", t=PACK)
             source = values
@@ -251,11 +257,6 @@ def tile_shard_weight_grad_s7_kernel(tc, x, dy, w2_bytes, w2_scale, g, c, out):
             nc.gpsimd.tensor_tensor(
                 out=values, in0=source, in1=scale_col[:].unsqueeze(2).to_broadcast([P, 2, P, PACK]), op=MULT
             )
-
-        def warm_up(count):
-            ps = psum_bank([P, PACK * P])
-            for i in range(count):
-                nc.tensor.matmul(ps[:], lhsT=warm[:, 0:P], rhs=warm[:], start=True, stop=True)
 
         def turn_pair(j, gi):
             for u in range(2):
@@ -426,11 +427,11 @@ def tile_shard_weight_grad_s7_kernel(tc, x, dy, w2_bytes, w2_scale, g, c, out):
             f0 = PAIR * j + P * strip
             nc.sync.dma_start(out=out_view[h][:, :, f0 : f0 + width], in_=result[j, h, strip])
 
-        warm_up(5)
         load_w(0, (0,))
         widen_strip(0, parts=2)
         turn_strip(0)
         load_scales()
+        repeat_scales()
         scale_strip(0)
         load_w(0, (1,))
         widen_strip(1)
@@ -460,11 +461,11 @@ def tile_shard_weight_grad_s7_kernel(tc, x, dy, w2_bytes, w2_scale, g, c, out):
         turn_y(0, 3)
         turn_strip(4)
         turn_strip(5)
-        scale_strip(4)
         empty_y(0, 3)
         quantise_y(0)
         quantise_w(1)
         scale_strip(5)
+        empty_strip(4)
         load_y(1, (0, 1))
         turn_y(1, 0)
         turn_y(1, 1)
@@ -480,9 +481,9 @@ def tile_shard_weight_grad_s7_kernel(tc, x, dy, w2_bytes, w2_scale, g, c, out):
         empty_y(1, 2)
         empty_y(1, 3)
         quantise_y(1)
+        scale_gpsimd(4)
         load_g(0, 0)
         read_unit(0, 0)
-        quantise_w(2)
         read_unit(0, 1)
         read_unit(0, 2)
         read_unit(0, 3)
@@ -507,7 +508,6 @@ def tile_shard_weight_grad_s7_kernel(tc, x, dy, w2_bytes, w2_scale, g, c, out):
         empty_y(2, 0)
         empty_y(2, 1)
         load_y(2, (2, 3))
-        split_y_gpsimd(2, 2)
         turn_y(2, 2)
         empty_y(2, 2)
         split_y_gpsimd(2, 3)
@@ -515,12 +515,14 @@ def tile_shard_weight_grad_s7_kernel(tc, x, dy, w2_bytes, w2_scale, g, c, out):
         empty_y(2, 3)
         load_g(1, 0)
         read_unit(1, 0)
-        unit(0, 4)
         read_unit(1, 1)
-        unit(0, 5)
         read_unit(1, 2)
-        unit(1, 4)
         read_unit(1, 3)
+        quantise_strip(4)
+        unit(0, 4)
+        quantise_strip(5)
+        unit(0, 5)
+        unit(1, 4)
         unit(1, 5)
         quantise_dh(0)
         quantise_w(3)

@@ -21,27 +21,38 @@ PACK = 4
 GROUPS = D * T // (P * PACK)
 PAIR = 2 * P
 PAIRS = F // PAIR
-BEAT = 4
-G_COLS = BEAT * P
+LAST = PAIRS - 1
+CHUNK = 4
 RUN = 4
-VECTOR_PAIRS = 3
-X_GPSIMD = 368
-BAR = 2 * BEAT
-BARS = 4
-STAGES = 5
-READS = 1
 BANKS = 8
-DH_SLOTS = 4
-SPLITS = 4
-FIRSTS = 4
-SECONDS = 4
-Y_RAW = 4
-X_RAW = 3
-G_RAW = 8
-W_RAW = 4
-WIDES = 4
-RUNS = (((0, 0), (0, 1), (0, 2), (0, 3), (1, 0), (1, 1), (1, 2), (1, 3)), ((0, 4), (0, 5), (1, 4), (1, 5), (0, 6), (0, 7), (1, 6), (1, 7)), ((2, 0), (2, 1), (2, 2), (2, 3), (3, 0), (3, 1), (3, 2), (3, 3)), ((2, 4), (2, 5), (2, 6), (2, 7), (3, 4), (3, 5), (3, 6), (3, 7)), ((0, 8), (0, 9), (1, 8), (1, 9)), ((2, 8), (2, 9), (3, 8), (3, 9)), ((0, 10), (0, 11), (1, 10), (1, 11)), ((2, 10), (3, 10), (2, 11), (3, 11)))
-STAGE_OF = {('w', 0): 0, ('dh', 0): 0, ('dh', 2): 0, ('dh', 5): 0, ('total', 2): 0, ('w', 1): 1, ('w', 3): 1, ('x', 0): 1, ('x', 1): 1, ('w', 5): 1, ('dh', 6): 1, ('total', 3): 1, ('y', 0): 2, ('y', 2): 2, ('w', 4): 2, ('dh', 4): 2, ('total', 1): 2, ('y', 1): 3, ('strip', 4): 3, ('dh', 1): 3, ('dh', 7): 3, ('strip', 5): 4, ('y', 3): 4, ('dh', 3): 4, ('total', 0): 4}
+X_GPSIMD = 368
+WARM_UPS = 4
+
+
+def units_of(groups, pairs):
+    return [(a, 2 * j + i) for a in groups for j in pairs for i in range(2)]
+
+
+BATCHES = [
+    units_of((0, 1), (0, 1)),
+    units_of((0, 1), (2,)) + units_of((0, 1), (3,)),
+    units_of((2, 3), (0, 1)),
+    units_of((2, 3), (2, 3)),
+    units_of((0, 1), (4,)),
+    units_of((2, 3), (4,)),
+    units_of((0, 1), (5,)),
+    [(a, 2 * LAST + i) for i in range(2) for a in (2, 3)],
+]
+WIDE = 8
+
+SLOTS = [
+    [("w", 0), ("dh", 0), ("dh", 2), ("dh", 5), ("total", 2)],
+    [("w", 1), ("w", 3), ("x", 0), ("x", 1), ("w", 5), ("dh", 6), ("total", 3)],
+    [("y", 0), ("y", 2), ("w", 4), ("dh", 4), ("total", 1)],
+    [("y", 1), ("strip", 4), ("dh", 1), ("dh", 7)],
+    [("strip", 5), ("y", 3), ("dh", 3), ("total", 0)],
+]
+SLOT_OF = {tenant: i for i, tenants in enumerate(SLOTS) for tenant in tenants}
 
 
 def tile_shard_weight_grad_s7_kernel(tc, x, dy, w2_bytes, w2_scale, g, c, out):
@@ -52,69 +63,64 @@ def tile_shard_weight_grad_s7_kernel(tc, x, dy, w2_bytes, w2_scale, g, c, out):
         psum = ctx.enter_context(tc.psum_pool(name="psum", bufs=2))
         ctx.enter_context(tc.manual_schedule())
 
-        w_raw, y_raw, x_raw, g_raw = {}, {}, {}, {}
         w_view = w2_bytes.rearrange("(j i p) n -> j p i n", i=2, p=P)
         out_view = out.rearrange("(h k2 p) f -> h p k2 f", k2=2, p=P)
+        w_raw, y_raw, x_raw, g_raw = {}, {}, {}, {}
+        w_wide, w_split, w_planes, w_turned, w_single, strip_mx = {}, {}, {}, {}, {}, {}
+        y_split, y_turned, y_mx, x_mixed, x_mx, dh, dh_mx = {}, {}, {}, {}, {}, {}, {}
+        bank, first_pair, second_term, result = {}, {}, {}, {}
+
+        def psum_bank(shape):
+            return psum.tile(shape, F32, name="bank", bufs=BANKS)
+
+        def slot(tenant, shape, dtype):
+            return work.tile(shape, dtype, name="slot%d" % SLOT_OF[tenant], bufs=1, align_bytes=64)
+
+        def row_tile(shape, dtype):
+            return work.tile(shape, dtype, name="row", bufs=PACK, align_bytes=64)
 
         def samples(tensor, a):
             return tensor[a // 2].rearrange("(q p t) n -> q p t n", q=2, t=PACK)[a % 2]
 
         def load_w(j, strips=(0, 1)):
             if j not in w_raw:
-                w_raw[j] = work.tile([P, 2, N], U8, name="w_raw", bufs=W_RAW)
+                w_raw[j] = work.tile([P, 2, N], U8, name="w_raw", bufs=4)
             part = slice(strips[0], strips[-1] + 1)
             nc.sync.dma_start(out=w_raw[j][:, part, :], in_=w_view[j][:, part, :])
 
         def load_y(a, rows):
             if len(rows) == 1:
-                tile = work.tile([P, 1, N], BF16, name="y_row", bufs=PACK, align_bytes=64)
+                tile = row_tile([P, 1, N], BF16)
             else:
-                tile = work.tile([P, 2, N], BF16, name="y_raw", bufs=Y_RAW, align_bytes=64)
+                tile = work.tile([P, 2, N], BF16, name="y_raw", bufs=4, align_bytes=64)
             nc.sync.dma_start(out=tile[:], in_=samples(dy, a)[:, rows[0] : rows[-1] + 1, :])
             for i, t in enumerate(rows):
                 y_raw[a, t] = tile[:, i, :]
 
         def load_x(a):
-            x_raw[a] = work.tile([P, PACK, K], BF16, name="x_raw", bufs=X_RAW, align_bytes=64)
+            x_raw[a] = work.tile([P, PACK, K], BF16, name="x_raw", bufs=3, align_bytes=64)
             nc.sync.dma_start(out=x_raw[a][:], in_=samples(x, a))
 
         def load_g(a, chunk):
-            g_raw[a, chunk] = work.tile([P, PACK, G_COLS], BF16, name="g_raw", bufs=G_RAW, align_bytes=64)
-            nc.sync.dma_start(out=g_raw[a, chunk][:], in_=samples(g, a)[:, :, G_COLS * chunk : G_COLS * (chunk + 1)])
+            cols = slice(CHUNK * P * chunk, CHUNK * P * (chunk + 1))
+            g_raw[a, chunk] = work.tile([P, PACK, CHUNK * P], BF16, name="g_raw", bufs=2 * GROUPS, align_bytes=64)
+            nc.sync.dma_start(out=g_raw[a, chunk][:], in_=samples(g, a)[:, :, cols])
 
         scale_col = keep.tile([P, 2, PACK], F32, name="scale_col")
         scale_run = keep.tile([P, 2, PACK, RUN], F32, name="scale_run", align_bytes=64)
         c_bf = keep.tile([P, D], BF16, name="c_bf")
-
-        def load_scales():
-            nc.sync.dma_start(out=scale_col[:], in_=w2_scale.rearrange("o (g p t) -> p (o g) t", p=P, t=PACK))
-
-        def repeat_scales():
-            nc.vector.tensor_copy(out=scale_run[:], in_=scale_col[:].unsqueeze(3).to_broadcast([P, 2, PACK, RUN]))
-
-        def load_c():
-            nc.sync.dma_start(out=c_bf[:], in_=c.partition_broadcast(P))
-
-        def widen_c():
-            nc.scalar.copy(out=c_all[:], in_=c_bf[:])
-
-        def psum_bank(shape):
-            return psum.tile(shape, F32, name="bank", bufs=BANKS)
-
+        c_all = keep.tile([P, D], F32, name="c_all")
+        warm = keep.tile([P, PACK * P], BF16, name="warm", align_bytes=64)
+        nc.vector.memset(warm[:], 1.0)
         ident = keep.tile([P, P], F32, name="ident", align_bytes=64)
         make_identity(nc, ident[:])
-        c_all = keep.tile([P, D], F32, name="c_all")
         ident_bf = keep.tile([P, P], BF16, name="ident_bf", align_bytes=64)
         nc.vector.tensor_copy(out=ident_bf[:], in_=ident[:])
 
-        w_wide, w_split, y_split, w_planes, w_turned, w_mx = {}, {}, {}, {}, {}, {}
-        y_turned, y_mx, x_mixed, x_mx, dh, dh_mx = {}, {}, {}, {}, {}, {}
-        bank, first_pair, second_term, result, w_loose, w_single, strip_mx = {}, {}, {}, {}, {}, {}, {}
-
         def quantise(name, bufs, source):
-            words = source.shape[1] // PACK
-            codes = work.tile([P, words], U32, name=name + "_codes", bufs=bufs, align_bytes=64)
-            scales = work.tile([P, words], U8, name=name + "_scales", bufs=bufs, align_bytes=64)
+            columns = source.shape[1] // PACK
+            codes = work.tile([P, columns], U32, name=name + "_codes", bufs=bufs, align_bytes=64)
+            scales = work.tile([P, columns], U8, name=name + "_scales", bufs=bufs, align_bytes=64)
             nc.vector.quantize_mx(out=codes[:].bitcast(FP8X4), scales=scales[:], in_=source)
             return codes, scales
 
@@ -135,15 +141,23 @@ def tile_shard_weight_grad_s7_kernel(tc, x, dy, w2_bytes, w2_scale, g, c, out):
         def mixed_runs(mixed):
             return mixed.rearrange("p (c i) t -> p c t i", i=RUN)
 
-        def turn(ps, row, gi, u):
-            nc.tensor.transpose(ps, row.bitcast(F32)[:, PAIR * gi + u : PAIR * (gi + 1) : 2], ident[:])
+        def as_mixed(words):
+            return words.rearrange("p f u -> p (f u)").bitcast(BF16).rearrange("p (f t) -> p f t", t=PACK)
 
-        def split_row(row):
-            halves = work.tile([P, 2, PAIR], F32, name="y_row", bufs=PACK, align_bytes=64)
+        def turn(ps, row, halves, gi, u):
+            if halves is None:
+                words = row.bitcast(F32)[:, PAIR * gi + u : PAIR * (gi + 1) : 2]
+            else:
+                words = halves[:, u, P * gi : P * (gi + 1)]
+            nc.tensor.transpose(ps, words, ident[:])
+
+        def split_on_scalar(row):
+            halves = row_tile([P, 2, PAIR], F32)
             nc.scalar.copy(out=halves[:], in_=row.bitcast(F32).rearrange("p (w u) -> p u w", u=2))
             return halves
 
-        def split_row_gpsimd(row, halves):
+        def split_on_gpsimd(row):
+            halves = row_tile([P, 2, PAIR], F32)
             nc.gpsimd.tensor_scalar(
                 out=halves[:].bitcast(BF16).rearrange("p u (w e) -> p u w e", e=2),
                 in0=row.rearrange("p (w u e) -> p u w e", u=2, e=2),
@@ -154,173 +168,130 @@ def tile_shard_weight_grad_s7_kernel(tc, x, dy, w2_bytes, w2_scale, g, c, out):
             )
             return halves
 
-        def turn_row(row, halves=None):
-            ps = psum_bank([P, 2, 2, P])
-            for gi in range(2):
-                for u in range(2):
-                    if halves is None:
-                        turn(ps[:, gi, u, :], row, gi, u)
-                    else:
-                        nc.tensor.transpose(ps[:, gi, u, :], halves[:, u, P * gi : P * (gi + 1)], ident[:])
-            return ps
+        def split_y(a, tiles, split):
+            for t in tiles:
+                y_split[a, t] = split(y_raw[a, t])
 
-        def stage(key, shape, dtype):
-            return work.tile(shape, dtype, name="stage%d" % STAGE_OF[key], bufs=1, align_bytes=64)
+        def turn_y(a, tiles):
+            for t in tiles:
+                ps = psum_bank([P, 2, 2, P])
+                for gi in range(2):
+                    for u in range(2):
+                        turn(ps[:, gi, u, :], y_raw[a, t], y_split.get((a, t)), gi, u)
+                bank["y", a, t] = ps
 
-        def turn_y(a, t):
-            bank["y", a, t] = turn_row(y_raw[a, t], y_split.get((a, t)))
-
-        def empty_y(a, t):
+        def empty_y(a, tiles):
             if a not in y_turned:
-                y_turned[a] = stage(("y", a), [P, PACK, 2, P, 2], F32)
-            nc.scalar.copy(out=y_turned[a][:, t], in_=bank["y", a, t][:].rearrange("p g u m -> p g m u"))
-
-        def split_y(a, t):
-            y_split[a, t] = split_row(y_raw[a, t])
-
-        def split_y_gpsimd(a, t):
-            if ("split", a, t) in STAGE_OF:
-                halves = stage(("split", a, t), [P, 2, PAIR], F32)
-            else:
-                halves = work.tile([P, 2, PAIR], F32, name="y_row", bufs=PACK, align_bytes=64)
-            y_split[a, t] = split_row_gpsimd(y_raw[a, t], halves)
+                y_turned[a] = slot(("y", a), [P, PACK, 2, P, 2], F32)
+            for t in tiles:
+                nc.scalar.copy(out=y_turned[a][:, t], in_=bank["y", a, t][:].rearrange("p g u m -> p g m u"))
 
         def quantise_y(a):
-            source = y_turned[a][:].rearrange("p r g m u -> p (r g m u)").bitcast(BF16)
-            y_mx[a] = quantise("y", GROUPS, source)
+            y_mx[a] = quantise("y", GROUPS, y_turned[a][:].rearrange("p r g m u -> p (r g m u)").bitcast(BF16))
 
-        def wide_tile(b):
-            w_wide[b] = work.tile([P, N], BF16, name="w_wide", bufs=WIDES, align_bytes=64)
-            return w_wide[b]
+        def widen(strips, parts=1):
+            for b in strips:
+                w_wide[b] = work.tile([P, N], BF16, name="w_wide", bufs=4, align_bytes=64)
+                for i in range(parts):
+                    ns = slice(N // parts * i, N // parts * (i + 1))
+                    nc.scalar.copy(out=w_wide[b][:, ns], in_=w_raw[b // 2][:, b % 2, ns].bitcast(FP8))
 
         def pair_tile(j):
             if j not in w_turned:
-                w_turned[j] = stage(("w", j), [P, 2, 2, P, 2], F32)
+                w_turned[j] = slot(("w", j), [P, 2, 2, P, 2], F32)
             return w_turned[j]
 
         def strip_tile(b):
-            if ("strip", b) not in STAGE_OF:
+            if ("strip", b) not in SLOT_OF:
                 return pair_tile(b // 2)[:, :, b % 2]
             if b not in w_single:
-                w_single[b] = stage(("strip", b), [P, 2, P, 2], F32)
+                w_single[b] = slot(("strip", b), [P, 2, P, 2], F32)
             return w_single[b][:]
 
-        def widen_strip(b, parts=1):
-            wide = wide_tile(b)
-            for i in range(parts):
-                ns = slice(N // parts * i, N // parts * (i + 1))
-                nc.scalar.copy(out=wide[:, ns], in_=w_raw[b // 2][:, b % 2, ns].bitcast(FP8))
-
         def turn_plane(ps, b, gi, t):
-            n0 = P * PACK * gi + t
-            nc.tensor.matmul(ps, lhsT=w_wide[b][:, n0 : P * PACK * (gi + 1) : PACK], rhs=ident_bf[:], start=True, stop=True)
+            columns = w_wide[b][:, P * PACK * gi + t : P * PACK * (gi + 1) : PACK]
+            nc.tensor.matmul(ps, lhsT=columns, rhs=ident_bf[:], start=True, stop=True)
 
-        def turn_strip(b, passes=(0, 1)):
-            for gi in passes:
-                ps = psum_bank([P, PACK, P])
-                for t in range(PACK):
-                    turn_plane(ps[:, t, :], b, gi, t)
-                bank["strip", b, gi] = ps
+        def turn_strips(strips):
+            for b in strips:
+                for gi in range(2):
+                    ps = psum_bank([P, PACK, P])
+                    for t in range(PACK):
+                        turn_plane(ps[:, t, :], b, gi, t)
+                    bank["strip", b, gi] = ps
 
-        def scale_strip(b, passes=(0, 1)):
-            for gi in passes:
-                mixed = strip_tile(b)[:, gi].rearrange("p f u -> p (f u)").bitcast(BF16)
-                nc.vector.tensor_tensor(
-                    out=mixed_runs(mixed.rearrange("p (f t) -> p f t", t=PACK)),
-                    in0=in_runs(bank["strip", b, gi][:]),
-                    in1=scale_run[:, gi].unsqueeze(1).to_broadcast([P, P // RUN, PACK, RUN]),
-                    op=MULT,
-                )
+        def scale_on_vector(strips):
+            for b in strips:
+                for gi in range(2):
+                    nc.vector.tensor_tensor(
+                        out=mixed_runs(as_mixed(strip_tile(b)[:, gi])),
+                        in0=in_runs(bank["strip", b, gi][:]),
+                        in1=scale_run[:, gi].unsqueeze(1).to_broadcast([P, P // RUN, PACK, RUN]),
+                        op=MULT,
+                    )
 
         def empty_strip(b):
-            w_loose[b] = work.tile([P, 2, P, 2], F32, name="loose", bufs=1, align_bytes=64)
+            unscaled = work.tile([P, 2, P, 2], F32, name="unscaled", bufs=1, align_bytes=64)
             for gi in range(2):
-                mixed = w_loose[b][:, gi].rearrange("p f u -> p (f u)").bitcast(BF16)
-                nc.scalar.copy(
-                    out=mixed_runs(mixed.rearrange("p (f t) -> p f t", t=PACK)), in_=in_runs(bank["strip", b, gi][:])
-                )
+                nc.scalar.copy(out=mixed_runs(as_mixed(unscaled[:, gi])), in_=in_runs(bank["strip", b, gi][:]))
+            return unscaled
 
-        def turn_words(b):
-            bank["words", b] = turn_row(w_wide[b][:], w_split.get(b))
+        def scale_on_gpsimd(b, unscaled):
+            def values(words):
+                return words.rearrange("p g f u -> p g (f u)").bitcast(BF16).rearrange("p g (f t) -> p g f t", t=PACK)
 
-        def empty_words(b):
-            w_loose[b] = work.tile([P, 2, P, 2], F32, name="y_row", bufs=PACK, align_bytes=64)
-            nc.scalar.copy(out=w_loose[b][:], in_=bank["words", b][:].rearrange("p g u m -> p g m u"))
-
-        def scale_gpsimd(b):
-            words = strip_tile(b)
-            values = words.rearrange("p g f u -> p g (f u)").bitcast(BF16)
-            values = values.rearrange("p g (f t) -> p g f t", t=PACK)
-            source = values
-            if b in w_loose:
-                source = w_loose[b][:].rearrange("p g f u -> p g (f u)").bitcast(BF16).rearrange("p g (f t) -> p g f t", t=PACK)
             nc.gpsimd.tensor_tensor(
-                out=values, in0=source, in1=scale_col[:].unsqueeze(2).to_broadcast([P, 2, P, PACK]), op=MULT
-            )
-
-        def turn_pair(j, gi):
-            for u in range(2):
-                ps = psum_bank([P, 2, 2, P])
-                for e in range(2):
-                    for i in range(2):
-                        turn_plane(ps[:, e, i, :], 2 * j + i, gi, 2 * u + e)
-                bank["pair", j, gi, u] = ps
-
-        def scale_pair(j, gi):
-            w_planes[j, gi] = work.tile([P, PACK, PAIR], BF16, name="w_planes", bufs=2, align_bytes=64)
-            for t in range(PACK):
-                u, e = divmod(t, 2)
-                nc.scalar.activation(
-                    out=w_planes[j, gi][:, t, :],
-                    in_=bank["pair", j, gi, u][:, e].rearrange("p i f -> p (i f)"),
-                    func=COPY,
-                    scale=scale_col[:, gi, t : t + 1],
-                )
-
-        def split_strip(b):
-            w_split[b] = split_row(w_wide[b][:])
-
-        def turn_pair_words(j, gi):
-            ps = psum_bank([P, 2, 2, P])
-            for u in range(2):
-                for i in range(2):
-                    if 2 * j + i in w_split:
-                        nc.tensor.transpose(ps[:, u, i, :], w_split[2 * j + i][:, u, P * gi : P * (gi + 1)], ident[:])
-                    else:
-                        turn(ps[:, u, i, :], w_wide[2 * j + i][:], gi, u)
-            bank["pair", j, gi] = ps
-
-        def scale_pair_words(j, gi):
-            w_planes[j, gi] = work.tile([P, PACK, PAIR], BF16, name="w_planes", bufs=2, align_bytes=64)
-            for t in range(PACK):
-                u, e = divmod(t, 2)
-                elements = bank["pair", j, gi][:, u].rearrange("p i f -> p (i f)").bitcast(BF16)
-                nc.scalar.activation(
-                    out=w_planes[j, gi][:, t, :],
-                    in_=elements[:, e : 2 * PAIR : 2],
-                    func=COPY,
-                    scale=scale_col[:, gi, t : t + 1],
-                )
-
-        def scale_pair_vector(j, gi):
-            mixed = pair_tile(j)[:, gi].rearrange("p i f u -> p (i f u)").bitcast(BF16)
-            elements = bank["pair", j, gi][:].rearrange("p u i f -> p u (i f)").bitcast(BF16)
-            nc.vector.tensor_tensor(
-                out=mixed.rearrange("p (f u e) -> p f u e", u=2, e=2),
-                in0=elements.rearrange("p u (f e) -> p f u e", e=2),
-                in1=scale_col[:, gi, :].rearrange("p (u e) -> p u e", e=2).unsqueeze(1).to_broadcast([P, PAIR, 2, 2]),
+                out=values(strip_tile(b)),
+                in0=values(unscaled[:]),
+                in1=scale_col[:].unsqueeze(2).to_broadcast([P, 2, P, PACK]),
                 op=MULT,
             )
 
-        def mix_pair(j, gi):
-            mixed = pair_tile(j)[:, gi].rearrange("p i f u -> p (i f u)").bitcast(BF16)
-            nc.scalar.copy(out=mixed_runs(mixed.rearrange("p (f t) -> p f t", t=PACK)), in_=in_runs(w_planes[j, gi][:]))
+        def turn_pair_planes(j):
+            for gi in range(2):
+                for u in range(2):
+                    ps = psum_bank([P, 2, 2, P])
+                    for e in range(2):
+                        for i in range(2):
+                            turn_plane(ps[:, e, i, :], 2 * j + i, gi, 2 * u + e)
+                    for e in range(2):
+                        bank["plane", j, gi, 2 * u + e] = ps[:, e].rearrange("p i f -> p (i f)")
 
-        def quantise_w(j):
+        def turn_pair_words(j):
+            for gi in range(2):
+                ps = psum_bank([P, 2, 2, P])
+                for u in range(2):
+                    for i in range(2):
+                        turn(ps[:, u, i, :], w_wide[2 * j + i][:], w_split.get(2 * j + i), gi, u)
+                    elements = ps[:, u].rearrange("p i f -> p (i f)").bitcast(BF16)
+                    for e in range(2):
+                        bank["plane", j, gi, 2 * u + e] = elements[:, e : 2 * PAIR : 2]
+
+        def split_strips(strips):
+            for b in strips:
+                w_split[b] = split_on_scalar(w_wide[b][:])
+
+        def scale_on_scalar(j):
+            for gi in range(2):
+                w_planes[j, gi] = work.tile([P, PACK, PAIR], BF16, name="w_planes", bufs=2, align_bytes=64)
+                for t in range(PACK):
+                    nc.scalar.activation(
+                        out=w_planes[j, gi][:, t, :],
+                        in_=bank["plane", j, gi, t],
+                        func=COPY,
+                        scale=scale_col[:, gi, t : t + 1],
+                    )
+
+        def mix_pair(j, passes=(0, 1)):
+            for gi in passes:
+                words = pair_tile(j)[:, gi].rearrange("p i f u -> p (i f) u")
+                nc.scalar.copy(out=mixed_runs(as_mixed(words)), in_=in_runs(w_planes[j, gi][:]))
+
+        def quantise_pair(j):
             source = w_turned[j][:].rearrange("p g i f u -> p (g i f u)").bitcast(BF16)
-            w_mx[j] = quantise("w", PAIRS - 1, source)
+            codes = quantise("w", PAIRS - 1, source)
             for i in range(2):
-                strip_mx[2 * j + i] = (w_mx[j], PAIR, P * i)
+                strip_mx[2 * j + i] = (codes, PAIR, P * i)
 
         def quantise_strip(b):
             source = w_single[b][:].rearrange("p g f u -> p (g f u)").bitcast(BF16)
@@ -328,87 +299,93 @@ def tile_shard_weight_grad_s7_kernel(tc, x, dy, w2_bytes, w2_scale, g, c, out):
 
         def mixed_x(a):
             if a // 2 not in x_mixed:
-                x_mixed[a // 2] = stage(("x", a // 2), [P, 2, K, PACK], BF16)
+                x_mixed[a // 2] = slot(("x", a // 2), [P, 2, K, PACK], BF16)
             return x_mixed[a // 2][:, a % 2]
 
-        def mix_x_gpsimd(a, k0=X_GPSIMD):
+        def mix_x_gpsimd(a, k1):
             nc.gpsimd.tensor_scalar(
-                out=mixed_x(a)[:, 0:k0, :],
-                in0=x_raw[a][:, :, 0:k0].rearrange("p t k -> p k t"),
+                out=mixed_x(a)[:, 0:k1, :],
+                in0=x_raw[a][:, :, 0:k1].rearrange("p t k -> p k t"),
                 scalar1=1.0,
                 scalar2=0.0,
                 op0=MULT,
                 op1=ADD,
             )
 
-        def mix_x_scalar(a, k0=X_GPSIMD):
+        def mix_x_scalar(a, k0):
             nc.scalar.copy(out=mixed_runs(mixed_x(a)[:, k0:K, :]), in_=in_runs(x_raw[a][:, :, k0:K]))
 
         def quantise_x(d):
             x_mx[d] = quantise("x", D, x_mixed[d][:].rearrange("p q k t -> p (q k t)"))
 
-        run_of = {u: (k, i) for k, run in enumerate(RUNS) for i, u in enumerate(run)}
+        place = {u: (k, i) for k, batch in enumerate(BATCHES) for i, u in enumerate(batch)}
 
-        def unit(a, b):
-            ps = psum_bank([P, PACK, P])
-            bank["unit", a, b] = ps
-            for t in range(PACK):
-                for gi in range(2):
-                    y0 = PAIR * t + P * gi
-                    codes, per_pass, f0 = strip_mx[b]
-                    w0 = per_pass * gi + f0
-                    multiply(ps[:, t, :], y_mx[a], slice(y0, y0 + P), codes, slice(w0, w0 + P), gi == 0, gi == 1)
+        def units(some):
+            for a, b in some:
+                ps = psum_bank([P, PACK, P])
+                codes, per_pass, f0 = strip_mx[b]
+                for t in range(PACK):
+                    for gi in range(2):
+                        y0 = PAIR * t + P * gi
+                        w0 = per_pass * gi + f0
+                        multiply(ps[:, t, :], y_mx[a], slice(y0, y0 + P), codes, slice(w0, w0 + P), gi == 0, gi == 1)
+                bank["unit", a, b] = ps
 
-        def read_unit(a, b):
-            k, i = run_of[a, b]
-            if k not in dh:
-                dh[k] = stage(("dh", k), [P, len(RUNS[k]) * P, PACK], BF16)
-            f0 = P * (b % BEAT)
-            nc.vector.tensor_tensor(
-                out=mixed_runs(dh[k][:, P * i : P * (i + 1), :]),
-                in0=in_runs(bank["unit", a, b][:]),
-                in1=in_runs(g_raw[a, b // BEAT][:, :, f0 : f0 + P]),
-                op=MULT,
-            )
-
-        def quantise_dh(k, first=0, count=None):
-            count = count or len(RUNS[k])
-            source = dh[k][:, P * first : P * (first + count), :].rearrange("p f t -> p (f t)")
-            quantised = quantise("bar", BARS, source) if count == BAR else quantise("dh", DH_SLOTS, source)
-            for i in range(count):
-                dh_mx[RUNS[k][first + i]] = (quantised, P * i)
-
-        def half(d, j, h, strip=0, width=PAIR):
-            ps = psum_bank([P, 2, width])
-            for k2 in range(2):
-                k0 = P * (2 * h + k2)
-                for q in range(2):
-                    quantised, f0 = dh_mx[2 * d + q, 2 * j + strip]
-                    multiply(
-                        ps[:, k2, :], x_mx[d], slice(K * q + k0, K * q + k0 + P), quantised, slice(f0, f0 + width), q == 0, q == 1
-                    )
-            bank["half", d, j, h, strip] = ps
-
-        def last_passes(q, h):
-            j, strip = PAIRS - 1, 1
-            if q == 0:
-                bank["half", 1, j, h, strip] = psum_bank([P, 2, P])
-            quantised, f0 = dh_mx[2 + q, 2 * j + strip]
-            for k2 in range(2):
-                k0 = K * q + P * (2 * h + k2)
-                multiply(
-                    bank["half", 1, j, h, strip][:, k2, :], x_mx[1], slice(k0, k0 + P), quantised, slice(f0, f0 + P),
-                    q == 0 and k2 == 0, q == 1 and k2 == 1,
+        def reads(some):
+            for a, b in some:
+                k, i = place[a, b]
+                if k not in dh:
+                    dh[k] = slot(("dh", k), [P, len(BATCHES[k]) * P, PACK], BF16)
+                f0 = P * (b % CHUNK)
+                nc.vector.tensor_tensor(
+                    out=mixed_runs(dh[k][:, P * i : P * (i + 1), :]),
+                    in0=in_runs(bank["unit", a, b][:]),
+                    in1=in_runs(g_raw[a, b // CHUNK][:, :, f0 : f0 + P]),
+                    op=MULT,
                 )
 
-        def first(j, h):
-            if j not in first_pair:
-                first_pair[j] = work.tile([P, 2, 2, PAIR], F32, name="first_term", bufs=FIRSTS)
-            nc.scalar.activation(out=first_pair[j][:, h], in_=bank["half", 0, j, h, 0][:], func=COPY, scale=c_all[:, 0:1])
+        def quantise_dh(k, first=0, count=None):
+            count = count or len(BATCHES[k])
+            source = dh[k][:, P * first : P * (first + count), :].rearrange("p f t -> p (f t)")
+            codes = quantise("dh_wide" if count == WIDE else "dh", 4, source)
+            for i in range(count):
+                dh_mx[BATCHES[k][first + i]] = (codes, P * i)
 
-        def second(j, h):
-            second_term[j, h] = work.tile([P, 2, PAIR], F32, name="second_term", bufs=SECONDS)
-            nc.scalar.activation(out=second_term[j, h][:], in_=bank["half", 1, j, h, 0][:], func=COPY, scale=c_all[:, 1:2])
+        def second_pass(ps, d, q, k2, h, b, width, start, stop):
+            k0 = K * q + P * (2 * h + k2)
+            codes, f0 = dh_mx[2 * d + q, b]
+            multiply(ps[:, k2, :], x_mx[d], slice(k0, k0 + P), codes, slice(f0, f0 + width), start, stop)
+
+        def halves(d, j, width=PAIR):
+            for h in range(2):
+                ps = psum_bank([P, 2, width])
+                for k2 in range(2):
+                    for q in range(2):
+                        second_pass(ps, d, q, k2, h, 2 * j, width, q == 0, q == 1)
+                bank["half", d, j, h, 0] = ps
+
+        def last_strip():
+            for q in range(2):
+                for h in range(2):
+                    if q == 0:
+                        bank["half", 1, LAST, h, 1] = psum_bank([P, 2, P])
+                    for k2 in range(2):
+                        start, stop = q == 0 and k2 == 0, q == 1 and k2 == 1
+                        second_pass(bank["half", 1, LAST, h, 1], 1, q, k2, h, 2 * LAST + 1, P, start, stop)
+
+        def firsts(j):
+            first_pair[j] = work.tile([P, 2, 2, PAIR], F32, name="first_term", bufs=4)
+            for h in range(2):
+                nc.scalar.activation(
+                    out=first_pair[j][:, h], in_=bank["half", 0, j, h, 0][:], func=COPY, scale=c_all[:, 0:1]
+                )
+
+        def seconds(some):
+            for j, h in some:
+                second_term[j, h] = work.tile([P, 2, PAIR], F32, name="second_term", bufs=4)
+                nc.scalar.activation(
+                    out=second_term[j, h][:], in_=bank["half", 1, j, h, 0][:], func=COPY, scale=c_all[:, 1:2]
+                )
 
         def sum_on_vector(j, h, strip=0, width=PAIR):
             total = first_pair[j][:, h, :, P * strip : P * strip + width]
@@ -417,9 +394,9 @@ def tile_shard_weight_grad_s7_kernel(tc, x, dy, w2_bytes, w2_scale, g, c, out):
             )
             result[j, h, strip] = total
 
-        def sums_on_gpsimd(n, halves):
-            total = stage(("total", n), [P, BEAT, 2, PAIR], F32)
-            for i, (j, h) in enumerate(halves):
+        def sums_on_gpsimd(n, some):
+            total = slot(("total", n), [P, len(some), 2, PAIR], F32)
+            for i, (j, h) in enumerate(some):
                 nc.gpsimd.tensor_tensor(out=total[:, i], in0=first_pair[j][:, h], in1=second_term[j, h][:], op=ADD)
                 result[j, h, 0] = total[:, i]
 
@@ -427,321 +404,188 @@ def tile_shard_weight_grad_s7_kernel(tc, x, dy, w2_bytes, w2_scale, g, c, out):
             f0 = PAIR * j + P * strip
             nc.sync.dma_start(out=out_view[h][:, :, f0 : f0 + width], in_=result[j, h, strip])
 
+        b0, b1, b2, b3, b4, b5, b6, b7 = BATCHES
+
         load_w(0, (0,))
-        widen_strip(0, parts=2)
-        turn_strip(0)
-        load_scales()
-        repeat_scales()
-        scale_strip(0)
+        nc.sync.dma_start(out=scale_col[:], in_=w2_scale.rearrange("o (g p t) -> p (o g) t", p=P, t=PACK))
         load_w(0, (1,))
-        widen_strip(1)
-        turn_strip(1)
-        scale_strip(1)
-        quantise_w(0)
         load_y(0, (0,))
-        turn_y(0, 0)
         load_w(1)
-        widen_strip(2)
-        widen_strip(3)
-        empty_y(0, 0)
         load_y(0, (1,))
-        turn_y(0, 1)
-        turn_strip(2)
-        turn_strip(3)
-        scale_strip(2)
-        scale_strip(3)
-        empty_y(0, 1)
         load_w(2)
-        widen_strip(4)
-        widen_strip(5)
         load_y(0, (2,))
-        turn_y(0, 2)
-        empty_y(0, 2)
         load_y(0, (3,))
-        turn_y(0, 3)
-        turn_strip(4)
-        turn_strip(5)
-        empty_y(0, 3)
-        quantise_y(0)
-        quantise_w(1)
-        scale_strip(5)
-        empty_strip(4)
         load_y(1, (0, 1))
-        turn_y(1, 0)
-        turn_y(1, 1)
-        empty_y(1, 0)
-        empty_y(1, 1)
         load_y(1, (2, 3))
-        turn_y(1, 2)
-        turn_y(1, 3)
-        unit(0, 0)
-        unit(0, 1)
-        unit(0, 2)
-        unit(0, 3)
-        empty_y(1, 2)
-        empty_y(1, 3)
-        quantise_y(1)
-        scale_gpsimd(4)
         load_g(0, 0)
-        read_unit(0, 0)
-        read_unit(0, 1)
-        read_unit(0, 2)
-        read_unit(0, 3)
         load_w(3)
-        widen_strip(6)
-        widen_strip(7)
-        turn_pair(3, 0)
-        turn_pair(3, 1)
-        unit(1, 0)
-        unit(1, 1)
-        unit(1, 2)
-        unit(1, 3)
         load_y(2, (0, 1))
-        split_y(2, 0)
-        split_y(2, 1)
-        scale_pair(3, 0)
-        turn_y(2, 0)
-        turn_y(2, 1)
-        scale_pair(3, 1)
-        mix_pair(3, 0)
-        mix_pair(3, 1)
-        empty_y(2, 0)
-        empty_y(2, 1)
         load_y(2, (2, 3))
-        turn_y(2, 2)
-        empty_y(2, 2)
-        split_y_gpsimd(2, 3)
-        turn_y(2, 3)
-        empty_y(2, 3)
         load_g(1, 0)
-        read_unit(1, 0)
-        read_unit(1, 1)
-        read_unit(1, 2)
-        read_unit(1, 3)
-        quantise_strip(4)
-        unit(0, 4)
-        quantise_strip(5)
-        unit(0, 5)
-        unit(1, 4)
-        unit(1, 5)
-        quantise_dh(0)
-        quantise_w(3)
-        unit(0, 6)
-        unit(0, 7)
         load_g(0, 1)
-        read_unit(0, 4)
-        read_unit(0, 5)
         load_x(0)
-        mix_x_gpsimd(0, 512)
+        warm_bank = psum_bank([P, PACK * P])
+        for i in range(WARM_UPS):
+            nc.tensor.matmul(warm_bank[:], lhsT=warm[:, 0:P], rhs=warm[:], start=True, stop=True)
+        nc.vector.tensor_copy(out=scale_run[:], in_=scale_col[:].unsqueeze(3).to_broadcast([P, 2, PACK, RUN]))
+        widen((0,), parts=2)
+        widen((1, 2, 3))
+        turn_strips((0, 1))
+        scale_on_vector((0, 1))
+        quantise_pair(0)
+        turn_y(0, (0, 1))
+        empty_y(0, (0, 1))
+        turn_strips((2, 3))
+        scale_on_vector((2, 3))
+        widen((4, 5))
+        turn_y(0, (2, 3))
+        empty_y(0, (2, 3))
+        quantise_y(0)
+        quantise_pair(1)
+        turn_strips((4,))
+        unscaled_strip = empty_strip(4)
+        turn_y(1, (0, 1))
+        turn_strips((5,))
+        scale_on_vector((5,))
+        turn_y(1, (2, 3))
+        empty_y(1, range(PACK))
+        quantise_y(1)
+
         load_y(3, (0, 1))
-        split_y(3, 0)
-        turn_y(3, 0)
-        split_y(3, 1)
-        turn_y(3, 1)
-        empty_y(3, 0)
-        empty_y(3, 1)
         load_g(1, 1)
-        read_unit(1, 4)
-        read_unit(1, 5)
-        read_unit(0, 6)
-        read_unit(0, 7)
-        quantise_y(2)
         load_y(3, (2, 3))
-        turn_y(3, 2)
-        turn_y(3, 3)
-        unit(1, 6)
-        unit(1, 7)
-        unit(2, 0)
-        unit(2, 1)
-        unit(2, 2)
-        unit(2, 3)
-        read_unit(1, 6)
-        read_unit(1, 7)
-        empty_y(3, 2)
-        empty_y(3, 3)
-        quantise_y(3)
-        unit(3, 0)
-        unit(3, 1)
-        unit(3, 2)
-        unit(3, 3)
         load_x(1)
-        mix_x_scalar(1, 0)
-        quantise_x(0)
         load_g(2, 0)
-        read_unit(2, 0)
-        half(0, 0, 0)
-        read_unit(2, 1)
-        half(0, 0, 1)
-        read_unit(2, 2)
-        read_unit(2, 3)
-        load_c()
-        widen_c()
+        nc.sync.dma_start(out=c_bf[:], in_=c.partition_broadcast(P))
         load_w(4)
-        widen_strip(8)
-        widen_strip(9)
-        split_strip(8)
-        split_strip(9)
-        turn_pair_words(4, 0)
-        turn_pair_words(4, 1)
         load_g(3, 0)
-        read_unit(3, 0)
-        half(0, 1, 0)
-        read_unit(3, 1)
-        half(0, 1, 1)
-        read_unit(3, 2)
-        unit(2, 4)
-        read_unit(3, 3)
-        unit(2, 5)
-        quantise_dh(1)
         load_x(2)
-        mix_x_gpsimd(2)
         load_w(5)
-        widen_strip(10)
-        widen_strip(11)
-        split_strip(10)
-        first(0, 0)
-        unit(2, 6)
-        first(0, 1)
-        unit(2, 7)
-        scale_pair_words(4, 0)
-        half(0, 2, 0)
-        scale_pair_words(4, 1)
-        half(0, 2, 1)
-        first(1, 0)
-        half(0, 3, 0)
-        first(1, 1)
-        half(0, 3, 1)
-        mix_x_scalar(2)
+        scale_on_gpsimd(4, unscaled_strip)
+        widen((6, 7))
+        split_y(2, (0, 1), split_on_scalar)
+        split_y(2, (3,), split_on_gpsimd)
+        units(b0[:4])
+        turn_pair_planes(3)
+        reads(b0[:4])
+        units(b0[4:])
+        scale_on_scalar(3)
+        mix_pair(3)
+        turn_y(2, range(PACK))
+        empty_y(2, range(PACK))
+        reads(b0[4:])
+        quantise_strip(4)
+        quantise_strip(5)
+        quantise_dh(0)
+        quantise_pair(3)
+
+        mix_x_gpsimd(0, K)
         load_x(3)
-        mix_x_scalar(3)
-        first(2, 0)
-        first(2, 1)
-        mix_pair(4, 0)
-        first(3, 0)
-        first(3, 1)
-        mix_pair(4, 1)
-        split_strip(11)
-        mix_x_gpsimd(3)
         load_g(2, 1)
-        read_unit(2, 4)
-        unit(3, 4)
-        read_unit(2, 5)
-        unit(3, 5)
-        read_unit(2, 6)
-        unit(3, 6)
-        read_unit(2, 7)
-        unit(3, 7)
+        load_g(3, 1)
+        load_g(0, 2)
+        load_g(1, 2)
+        split_y(3, (0, 1), split_on_scalar)
+        units(b1[:6])
+        reads(b1[:6])
+        turn_y(3, range(PACK))
+        empty_y(3, range(PACK))
+        mix_x_scalar(1, 0)
+        quantise_y(2)
+        units(b1[6:])
+        reads(b1[6:])
+        load_g(2, 2)
+        quantise_y(3)
+        quantise_x(0)
+
+        nc.scalar.copy(out=c_all[:], in_=c_bf[:])
+        widen((8, 9))
+        split_strips((8, 9))
+        widen((10, 11))
+        split_strips((10,))
+        mix_x_gpsimd(2, X_GPSIMD)
+        mix_x_gpsimd(3, X_GPSIMD)
+        units(b2)
+        reads(b2)
+        load_g(3, 2)
+        quantise_dh(1)
+        halves(0, 0)
+        firsts(0)
+        turn_pair_words(4)
+        scale_on_scalar(4)
+        halves(0, 1)
+        firsts(1)
+        mix_x_scalar(2, X_GPSIMD)
+        mix_x_scalar(3, X_GPSIMD)
+
+        units(b3[:4])
+        reads(b3[:4])
         quantise_dh(2)
         quantise_x(1)
-        half(1, 0, 0)
-        half(1, 0, 1)
-        half(1, 1, 0)
-        half(1, 1, 1)
-        second(0, 1)
-        second(1, 0)
-        second(1, 1)
-        load_g(3, 1)
-        read_unit(3, 4)
-        turn_pair_words(5, 0)
-        read_unit(3, 5)
-        turn_pair_words(5, 1)
-        read_unit(3, 6)
-        read_unit(3, 7)
+        halves(0, 2)
+        firsts(2)
+        mix_pair(4, (0,))
+        halves(0, 3)
+        firsts(3)
+        mix_pair(4, (1,))
+        units(b3[4:])
+        reads(b3[4:])
+        halves(1, 0)
+        halves(1, 1)
         sum_on_vector(0, 0)
-        quantise_w(4)
-        unit(0, 8)
-        unit(0, 9)
-        unit(1, 8)
-        unit(1, 9)
-        quantise_dh(3)
-        half(1, 2, 0)
-        half(1, 2, 1)
-        scale_pair_words(5, 0)
-        half(1, 3, 0)
-        scale_pair_words(5, 1)
-        half(1, 3, 1)
-        mix_pair(5, 0)
-        mix_pair(5, 1)
-        second(3, 0)
-        sums_on_gpsimd(0, ((0, 1), (1, 0)))
-        second(3, 1)
-        load_g(0, 2)
-        read_unit(0, 8)
-        unit(2, 8)
-        read_unit(0, 9)
-        unit(2, 9)
-        load_g(1, 2)
-        read_unit(1, 8)
-        unit(3, 8)
-        read_unit(1, 9)
-        unit(3, 9)
-        sum_on_vector(2, 0)
-        sum_on_vector(2, 1)
-        quantise_dh(4)
-        half(0, 4, 0)
-        half(0, 4, 1)
-        sums_on_gpsimd(1, ((1, 1),))
-        load_g(2, 2)
-        read_unit(2, 8)
-        read_unit(2, 9)
-        quantise_w(5)
-        unit(0, 10)
-        unit(0, 11)
-        unit(1, 10)
-        unit(1, 11)
-        load_g(3, 2)
-        read_unit(3, 8)
-        read_unit(3, 9)
-        quantise_dh(5)
-        half(1, 4, 0)
-        half(1, 4, 1)
-        read_unit(0, 10)
-        read_unit(0, 11)
-        read_unit(1, 10)
-        read_unit(1, 11)
-        sums_on_gpsimd(2, ((3, 0), (3, 1)))
         store(0, 0)
-        first(4, 0)
-        unit(2, 10)
-        sum_on_vector(4, 0)
-        quantise_dh(6)
-        read_unit(2, 10)
-        first(4, 1)
-        unit(3, 10)
-        unit(2, 11)
-        unit(3, 11)
-        half(0, 5, 0)
-        half(0, 5, 1)
-        read_unit(3, 10)
-        read_unit(2, 11)
-        quantise_dh(7, 0, 2)
-        half(1, 5, 0, 0, 128)
-        read_unit(3, 11)
-        quantise_dh(7, 2, 1)
-        quantise_dh(7, 3, 1)
-        second(4, 1)
-        half(1, 5, 1, 0, 128)
-        last_passes(0, 0)
-        last_passes(0, 1)
-        last_passes(1, 0)
-        last_passes(1, 1)
-        first(5, 0)
-        sum_on_vector(5, 0, 0, 128)
-        first(5, 1)
-        sum_on_vector(5, 1, 0, 128)
-        sum_on_vector(5, 0, 1, 128)
-        sum_on_vector(5, 1, 1, 128)
-        sums_on_gpsimd(3, ((4, 1),))
+        seconds(((0, 1), (1, 0), (1, 1)))
+        quantise_pair(4)
+        quantise_dh(3)
+
+        sums_on_gpsimd(0, ((0, 1), (1, 0)))
         store(0, 1)
         store(1, 0)
-        store(2, 0)
-        store(2, 1)
+        turn_pair_words(LAST)
+        scale_on_scalar(LAST)
+        mix_pair(LAST)
+        units(b4)
+        reads(b4)
+        halves(1, 2)
+        halves(1, 3)
+        for h in range(2):
+            sum_on_vector(2, h)
+            store(2, h)
+        seconds(((3, 0), (3, 1)))
+        quantise_dh(4)
+        sums_on_gpsimd(1, ((1, 1),))
         store(1, 1)
+        units(b5)
+        reads(b5[:2])
+        quantise_pair(LAST)
+        reads(b5[2:])
+        quantise_dh(5)
+        halves(0, 4)
+        firsts(4)
+
+        sums_on_gpsimd(2, ((3, 0), (3, 1)))
         store(3, 0)
         store(3, 1)
+        units(b6)
+        reads(b6)
+        halves(1, 4)
+        sum_on_vector(4, 0)
         store(4, 0)
+        seconds(((4, 1),))
+        quantise_dh(6)
+        sums_on_gpsimd(3, ((4, 1),))
         store(4, 1)
-        store(5, 0, 0, 128)
-        store(5, 1, 0, 128)
-        store(5, 0, 1, 128)
-        store(5, 1, 1, 128)
+        units(b7)
+        halves(0, LAST)
+        firsts(LAST)
+        reads(b7[:3])
+        quantise_dh(7, 0, 2)
+        reads(b7[3:])
+        quantise_dh(7, 2, 1)
+        quantise_dh(7, 3, 1)
+        halves(1, LAST, P)
+        last_strip()
+        for strip in range(2):
+            for h in range(2):
+                sum_on_vector(LAST, h, strip, P)
+                store(LAST, h, strip, P)

@@ -552,27 +552,27 @@ def tile_shard_weight_grad_s7_kernel(tc, x, dy, w2_bytes, w2_scale, g, c, out):
             sum_on_vector(2, h)
             store(2, h)
         seconds(((3, 0), (3, 1)))
-        quantise_dh(4)
-        sums_on_gpsimd(1, ((1, 1),))
-        store(1, 1)
-        units(b5)
-        reads(b5[:2])
         quantise_pair(LAST)
-        reads(b5[2:])
+        quantise_dh(4)
+        sums_on_gpsimd(1, ((1, 1), (3, 0)))
+        store(1, 1)
+        store(3, 0)
+        units(b5)
+        reads(b5)
+
+        units(b6)
+        reads(b6[:1])
         quantise_dh(5)
+        sums_on_gpsimd(2, ((3, 1),))
+        store(3, 1)
+        reads(b6[1:])
         halves(0, 4)
         firsts(4)
-
-        sums_on_gpsimd(2, ((3, 0), (3, 1)))
-        store(3, 0)
-        store(3, 1)
-        units(b6)
-        reads(b6)
         halves(1, 4)
-        sum_on_vector(4, 0)
-        store(4, 0)
         seconds(((4, 1),))
         quantise_dh(6)
+        sum_on_vector(4, 0)
+        store(4, 0)
         sums_on_gpsimd(3, ((4, 1),))
         store(4, 1)
         units(b7)

@@ -22,10 +22,8 @@ GROUPS = D * T // (P * PACK)
 PAIR = 2 * P
 PAIRS = F // PAIR
 LAST = PAIRS - 1
-CHUNK = 4
 RUN = 4
 BANKS = 8
-X_GPSIMD = 368
 WARM_UPS = 4
 
 
@@ -44,13 +42,14 @@ BATCHES = [
     [(a, 2 * LAST + i) for i in range(2) for a in (2, 3)],
 ]
 WIDE = 8
-
+ROWS, W_RAW, Y_RAW, X_RAW, G_RAW, W_WIDE, W_PLANES = 6, 3, 4, 3, 7, 4, 3
+Y_CODES, Y_PARTS, DH_WIDE, DH_NARROW, FIRSTS, SECONDS = 1, 8, 4, 4, 4, 4
 SLOTS = [
-    [("w", 0), ("dh", 0), ("dh", 2), ("dh", 5), ("total", 2)],
-    [("w", 1), ("w", 3), ("x", 0), ("x", 1), ("w", 5), ("dh", 6), ("total", 3)],
-    [("y", 0), ("y", 2), ("w", 4), ("dh", 4), ("total", 1)],
-    [("y", 1), ("strip", 4), ("dh", 1), ("dh", 7)],
-    [("strip", 5), ("y", 3), ("dh", 3), ("total", 0)],
+    [("y", 1), ("w", 2), ("w", 3), ("y", 3), ("x", 1), ("w", 4), ("dh", 4), ("total", 0), ("dh", 7)],
+    [("w", 0), ("dh", 0), ("x", 0), ("x", 2), ("w", 5), ("dh", 6), ("total", 2)],
+    [("w", 1), ("dh", 1), ("x", 3), ("dh", 5), ("total", 1)],
+    [("y", 0), ("y", 2), ("dh", 2)],
+    [("dh", 3)],
 ]
 SLOT_OF = {tenant: i for i, tenants in enumerate(SLOTS) for tenant in tenants}
 
@@ -66,45 +65,53 @@ def tile_shard_weight_grad_s7_kernel(tc, x, dy, w2_bytes, w2_scale, g, c, out):
         w_view = w2_bytes.rearrange("(j i p) n -> j p i n", i=2, p=P)
         out_view = out.rearrange("(h k2 p) f -> h p k2 f", k2=2, p=P)
         w_raw, y_raw, x_raw, g_raw = {}, {}, {}, {}
-        w_wide, w_split, w_planes, w_turned, w_single, strip_mx = {}, {}, {}, {}, {}, {}
+        w_wide, w_split, w_planes, w_turned, strip_mx = {}, {}, {}, {}, {}
         y_split, y_turned, y_mx, x_mixed, x_mx, dh, dh_mx = {}, {}, {}, {}, {}, {}, {}
         bank, first_pair, second_term, result = {}, {}, {}, {}
 
-        def psum_bank(shape):
-            return psum.tile(shape, F32, name="bank", bufs=BANKS)
+        def psum_bank(shape, dtype=F32):
+            return psum.tile(shape, dtype, name="bank", bufs=BANKS)
 
         def slot(tenant, shape, dtype):
             return work.tile(shape, dtype, name="slot%d" % SLOT_OF[tenant], bufs=1, align_bytes=64)
 
         def row_tile(shape, dtype):
-            return work.tile(shape, dtype, name="row", bufs=PACK, align_bytes=64)
+            return work.tile(shape, dtype, name="row", bufs=ROWS, align_bytes=64)
 
         def samples(tensor, a):
             return tensor[a // 2].rearrange("(q p t) n -> q p t n", q=2, t=PACK)[a % 2]
 
-        def load_w(j, strips=(0, 1)):
+        def load_w(j, strips=(0, 1), cols=slice(0, N)):
             if j not in w_raw:
-                w_raw[j] = work.tile([P, 2, N], U8, name="w_raw", bufs=4)
+                w_raw[j] = work.tile([P, 2, N], U8, name="w_raw", bufs=W_RAW)
             part = slice(strips[0], strips[-1] + 1)
-            nc.sync.dma_start(out=w_raw[j][:, part, :], in_=w_view[j][:, part, :])
+            nc.sync.dma_start(out=w_raw[j][:, part, cols], in_=w_view[j][:, part, cols])
 
         def load_y(a, rows):
             if len(rows) == 1:
                 tile = row_tile([P, 1, N], BF16)
             else:
-                tile = work.tile([P, 2, N], BF16, name="y_raw", bufs=4, align_bytes=64)
+                tile = work.tile([P, 2, N], BF16, name="y_raw", bufs=Y_RAW, align_bytes=64)
             nc.sync.dma_start(out=tile[:], in_=samples(dy, a)[:, rows[0] : rows[-1] + 1, :])
             for i, t in enumerate(rows):
                 y_raw[a, t] = tile[:, i, :]
 
         def load_x(a):
-            x_raw[a] = work.tile([P, PACK, K], BF16, name="x_raw", bufs=3, align_bytes=64)
+            x_raw[a] = work.tile([P, PACK, K], BF16, name="x_raw", bufs=X_RAW, align_bytes=64)
             nc.sync.dma_start(out=x_raw[a][:], in_=samples(x, a))
 
-        def load_g(a, chunk):
-            cols = slice(CHUNK * P * chunk, CHUNK * P * (chunk + 1))
-            g_raw[a, chunk] = work.tile([P, PACK, CHUNK * P], BF16, name="g_raw", bufs=2 * GROUPS, align_bytes=64)
-            nc.sync.dma_start(out=g_raw[a, chunk][:], in_=samples(g, a)[:, :, cols])
+        def load_g(a, first, last, name, bufs):
+            cols = slice(PAIR * first, PAIR * (last + 1))
+            tile = work.tile([P, PACK, PAIR * (last + 1 - first)], BF16, name=name, bufs=bufs, align_bytes=64)
+            nc.sync.dma_start(out=tile[:], in_=samples(g, a)[:, :, cols])
+            for b in range(2 * first, 2 * last + 2):
+                g_raw[a, b] = tile[:, :, P * (b - 2 * first) : P * (b - 2 * first + 1)]
+
+        def load_g_wide(a, first, last):
+            load_g(a, first, last, "g_wide", 2)
+
+        def load_g_narrow(a, first, last):
+            load_g(a, first, last, "g_narrow", 4)
 
         scale_col = keep.tile([P, 2, PACK], F32, name="scale_col")
         scale_run = keep.tile([P, 2, PACK, RUN], F32, name="scale_run", align_bytes=64)
@@ -156,6 +163,14 @@ def tile_shard_weight_grad_s7_kernel(tc, x, dy, w2_bytes, w2_scale, g, c, out):
             nc.scalar.copy(out=halves[:], in_=row.bitcast(F32).rearrange("p (w u) -> p u w", u=2))
             return halves
 
+        def split_on_vector(row):
+            halves = row_tile([P, 2, PAIR], F32)
+            nc.vector.tensor_copy(
+                out=halves[:].bitcast(BF16).rearrange("p u (w e) -> p u w e", e=2),
+                in_=row.rearrange("p (w u e) -> p u w e", u=2, e=2),
+            )
+            return halves
+
         def split_on_gpsimd(row):
             halves = row_tile([P, 2, PAIR], F32)
             nc.gpsimd.tensor_scalar(
@@ -186,76 +201,54 @@ def tile_shard_weight_grad_s7_kernel(tc, x, dy, w2_bytes, w2_scale, g, c, out):
             for t in tiles:
                 nc.scalar.copy(out=y_turned[a][:, t], in_=bank["y", a, t][:].rearrange("p g u m -> p g m u"))
 
-        def quantise_y(a):
-            y_mx[a] = quantise("y", GROUPS, y_turned[a][:].rearrange("p r g m u -> p (r g m u)").bitcast(BF16))
+        def quantise_y(a, first=0, count=PACK):
+            source = y_turned[a][:, first : first + count].rearrange("p r g m u -> p (r g m u)").bitcast(BF16)
+            codes = quantise("y" if count == PACK else "y_part", Y_CODES if count == PACK else Y_PARTS, source)
+            for i in range(count):
+                y_mx[a, first + i] = (codes, PAIR * i)
 
-        def widen(strips, parts=1):
+        def widen(strips, parts=1, copy=nc.scalar.copy):
             for b in strips:
-                w_wide[b] = work.tile([P, N], BF16, name="w_wide", bufs=4, align_bytes=64)
+                w_wide[b] = work.tile([P, N], BF16, name="w_wide", bufs=W_WIDE, align_bytes=64)
                 for i in range(parts):
                     ns = slice(N // parts * i, N // parts * (i + 1))
-                    nc.scalar.copy(out=w_wide[b][:, ns], in_=w_raw[b // 2][:, b % 2, ns].bitcast(FP8))
+                    copy(out=w_wide[b][:, ns], in_=w_raw[b // 2][:, b % 2, ns].bitcast(FP8))
 
         def pair_tile(j):
             if j not in w_turned:
                 w_turned[j] = slot(("w", j), [P, 2, 2, P, 2], F32)
             return w_turned[j]
 
-        def strip_tile(b):
-            if ("strip", b) not in SLOT_OF:
-                return pair_tile(b // 2)[:, :, b % 2]
-            if b not in w_single:
-                w_single[b] = slot(("strip", b), [P, 2, P, 2], F32)
-            return w_single[b][:]
-
         def turn_plane(ps, b, gi, t):
             columns = w_wide[b][:, P * PACK * gi + t : P * PACK * (gi + 1) : PACK]
             nc.tensor.matmul(ps, lhsT=columns, rhs=ident_bf[:], start=True, stop=True)
 
-        def turn_strips(strips):
+        def turn_strips(strips, passes=(0, 1)):
             for b in strips:
-                for gi in range(2):
+                for gi in passes:
                     ps = psum_bank([P, PACK, P])
                     for t in range(PACK):
                         turn_plane(ps[:, t, :], b, gi, t)
                     bank["strip", b, gi] = ps
 
-        def scale_on_vector(strips):
+        def scale_on_vector(strips, passes=(0, 1)):
             for b in strips:
-                for gi in range(2):
+                for gi in passes:
                     nc.vector.tensor_tensor(
-                        out=mixed_runs(as_mixed(strip_tile(b)[:, gi])),
+                        out=mixed_runs(as_mixed(pair_tile(b // 2)[:, gi, b % 2])),
                         in0=in_runs(bank["strip", b, gi][:]),
                         in1=scale_run[:, gi].unsqueeze(1).to_broadcast([P, P // RUN, PACK, RUN]),
                         op=MULT,
                     )
 
-        def empty_strip(b):
-            unscaled = work.tile([P, 2, P, 2], F32, name="unscaled", bufs=1, align_bytes=64)
-            for gi in range(2):
-                nc.scalar.copy(out=mixed_runs(as_mixed(unscaled[:, gi])), in_=in_runs(bank["strip", b, gi][:]))
-            return unscaled
-
-        def scale_on_gpsimd(b, unscaled):
-            def values(words):
-                return words.rearrange("p g f u -> p g (f u)").bitcast(BF16).rearrange("p g (f t) -> p g f t", t=PACK)
-
-            nc.gpsimd.tensor_tensor(
-                out=values(strip_tile(b)),
-                in0=values(unscaled[:]),
-                in1=scale_col[:].unsqueeze(2).to_broadcast([P, 2, P, PACK]),
-                op=MULT,
-            )
-
-        def turn_pair_planes(j):
-            for gi in range(2):
-                for u in range(2):
-                    ps = psum_bank([P, 2, 2, P])
-                    for e in range(2):
-                        for i in range(2):
-                            turn_plane(ps[:, e, i, :], 2 * j + i, gi, 2 * u + e)
-                    for e in range(2):
-                        bank["plane", j, gi, 2 * u + e] = ps[:, e].rearrange("p i f -> p (i f)")
+        def turn_planes(j, gi, ts=range(PACK)):
+            if ("pass", j, gi) not in bank:
+                bank["pass", j, gi] = psum_bank([P, PACK, 2, P], BF16)
+            ps = bank["pass", j, gi]
+            for t in ts:
+                for i in range(2):
+                    turn_plane(ps[:, t, i, :], 2 * j + i, gi, t)
+                bank["plane", j, gi, t] = ps[:, t].rearrange("p i f -> p (i f)")
 
         def turn_pair_words(j):
             for gi in range(2):
@@ -267,13 +260,13 @@ def tile_shard_weight_grad_s7_kernel(tc, x, dy, w2_bytes, w2_scale, g, c, out):
                     for e in range(2):
                         bank["plane", j, gi, 2 * u + e] = elements[:, e : 2 * PAIR : 2]
 
-        def split_strips(strips):
+        def split_strips(strips, split):
             for b in strips:
-                w_split[b] = split_on_scalar(w_wide[b][:])
+                w_split[b] = split(w_wide[b][:])
 
-        def scale_on_scalar(j):
-            for gi in range(2):
-                w_planes[j, gi] = work.tile([P, PACK, PAIR], BF16, name="w_planes", bufs=2, align_bytes=64)
+        def planes_on_scalar(j, passes=(0, 1)):
+            for gi in passes:
+                w_planes[j, gi] = work.tile([P, PACK, PAIR], BF16, name="w_planes", bufs=W_PLANES, align_bytes=64)
                 for t in range(PACK):
                     nc.scalar.activation(
                         out=w_planes[j, gi][:, t, :],
@@ -282,41 +275,62 @@ def tile_shard_weight_grad_s7_kernel(tc, x, dy, w2_bytes, w2_scale, g, c, out):
                         scale=scale_col[:, gi, t : t + 1],
                     )
 
-        def mix_pair(j, passes=(0, 1)):
+        def planes_on_vector(j, passes=(0, 1)):
             for gi in passes:
-                words = pair_tile(j)[:, gi].rearrange("p i f u -> p (i f) u")
-                nc.scalar.copy(out=mixed_runs(as_mixed(words)), in_=in_runs(w_planes[j, gi][:]))
+                w_planes[j, gi] = work.tile([P, PACK, PAIR], BF16, name="w_planes", bufs=W_PLANES, align_bytes=64)
+                for t in range(PACK):
+                    nc.vector.tensor_scalar(
+                        out=w_planes[j, gi][:, t, :],
+                        in0=bank["plane", j, gi, t],
+                        scalar1=scale_col[:, gi, t : t + 1],
+                        scalar2=None,
+                        op0=MULT,
+                    )
+
+        def pair_words(j, gi):
+            return as_mixed(pair_tile(j)[:, gi].rearrange("p i f u -> p (i f) u"))
+
+        def mix_pair_scalar(j, passes=(0, 1)):
+            for gi in passes:
+                nc.scalar.copy(out=mixed_runs(pair_words(j, gi)), in_=in_runs(w_planes[j, gi][:]))
+
+        def mix_pair_gpsimd(j, passes=(0, 1)):
+            for gi in passes:
+                nc.gpsimd.tensor_scalar(
+                    out=pair_words(j, gi),
+                    in0=w_planes[j, gi][:].rearrange("p t f -> p f t"),
+                    scalar1=1.0,
+                    scalar2=0.0,
+                    op0=MULT,
+                    op1=ADD,
+                )
 
         def quantise_pair(j):
             source = w_turned[j][:].rearrange("p g i f u -> p (g i f u)").bitcast(BF16)
-            codes = quantise("w", PAIRS - 1, source)
+            codes = quantise("w", PAIRS, source)
             for i in range(2):
                 strip_mx[2 * j + i] = (codes, PAIR, P * i)
 
-        def quantise_strip(b):
-            source = w_single[b][:].rearrange("p g f u -> p (g f u)").bitcast(BF16)
-            strip_mx[b] = (quantise("strip", 2, source), P, 0)
-
         def mixed_x(a):
-            if a // 2 not in x_mixed:
-                x_mixed[a // 2] = slot(("x", a // 2), [P, 2, K, PACK], BF16)
-            return x_mixed[a // 2][:, a % 2]
+            if a not in x_mixed:
+                x_mixed[a] = slot(("x", a), [P, K, PACK], BF16)
+            return x_mixed[a]
 
-        def mix_x_gpsimd(a, k1):
+        def mix_x_gpsimd(a, k0, k1):
             nc.gpsimd.tensor_scalar(
-                out=mixed_x(a)[:, 0:k1, :],
-                in0=x_raw[a][:, :, 0:k1].rearrange("p t k -> p k t"),
+                out=mixed_x(a)[:, k0:k1, :],
+                in0=x_raw[a][:, :, k0:k1].rearrange("p t k -> p k t"),
                 scalar1=1.0,
                 scalar2=0.0,
                 op0=MULT,
                 op1=ADD,
             )
 
-        def mix_x_scalar(a, k0):
-            nc.scalar.copy(out=mixed_runs(mixed_x(a)[:, k0:K, :]), in_=in_runs(x_raw[a][:, :, k0:K]))
+        def mix_x_scalar(a, k0, k1):
+            nc.scalar.copy(out=mixed_runs(mixed_x(a)[:, k0:k1, :]), in_=in_runs(x_raw[a][:, :, k0:k1]))
 
-        def quantise_x(d):
-            x_mx[d] = quantise("x", D, x_mixed[d][:].rearrange("p q k t -> p (q k t)"))
+        def quantise_x(a):
+            x_mx[a] = quantise("x", GROUPS, x_mixed[a][:].rearrange("p k t -> p (k t)"))
 
         place = {u: (k, i) for k, batch in enumerate(BATCHES) for i, u in enumerate(batch)}
 
@@ -325,10 +339,11 @@ def tile_shard_weight_grad_s7_kernel(tc, x, dy, w2_bytes, w2_scale, g, c, out):
                 ps = psum_bank([P, PACK, P])
                 codes, per_pass, f0 = strip_mx[b]
                 for t in range(PACK):
+                    y_codes, m0 = y_mx[a, t]
                     for gi in range(2):
-                        y0 = PAIR * t + P * gi
+                        y0 = m0 + P * gi
                         w0 = per_pass * gi + f0
-                        multiply(ps[:, t, :], y_mx[a], slice(y0, y0 + P), codes, slice(w0, w0 + P), gi == 0, gi == 1)
+                        multiply(ps[:, t, :], y_codes, slice(y0, y0 + P), codes, slice(w0, w0 + P), gi == 0, gi == 1)
                 bank["unit", a, b] = ps
 
         def reads(some):
@@ -336,28 +351,27 @@ def tile_shard_weight_grad_s7_kernel(tc, x, dy, w2_bytes, w2_scale, g, c, out):
                 k, i = place[a, b]
                 if k not in dh:
                     dh[k] = slot(("dh", k), [P, len(BATCHES[k]) * P, PACK], BF16)
-                f0 = P * (b % CHUNK)
                 nc.vector.tensor_tensor(
                     out=mixed_runs(dh[k][:, P * i : P * (i + 1), :]),
                     in0=in_runs(bank["unit", a, b][:]),
-                    in1=in_runs(g_raw[a, b // CHUNK][:, :, f0 : f0 + P]),
+                    in1=in_runs(g_raw[a, b]),
                     op=MULT,
                 )
 
         def quantise_dh(k, first=0, count=None):
             count = count or len(BATCHES[k])
             source = dh[k][:, P * first : P * (first + count), :].rearrange("p f t -> p (f t)")
-            codes = quantise("dh_wide" if count == WIDE else "dh", 4, source)
+            codes = quantise("dh_wide" if count == WIDE else "dh", DH_WIDE if count == WIDE else DH_NARROW, source)
             for i in range(count):
                 dh_mx[BATCHES[k][first + i]] = (codes, P * i)
 
         def second_pass(ps, d, q, k2, h, b, width, start, stop):
-            k0 = K * q + P * (2 * h + k2)
+            k0 = P * (2 * h + k2)
             codes, f0 = dh_mx[2 * d + q, b]
-            multiply(ps[:, k2, :], x_mx[d], slice(k0, k0 + P), codes, slice(f0, f0 + width), start, stop)
+            multiply(ps[:, k2, :], x_mx[2 * d + q], slice(k0, k0 + P), codes, slice(f0, f0 + width), start, stop)
 
-        def halves(d, j, width=PAIR):
-            for h in range(2):
+        def halves(d, j, width=PAIR, hs=(0, 1)):
+            for h in hs:
                 ps = psum_bank([P, 2, width])
                 for k2 in range(2):
                     for q in range(2):
@@ -373,16 +387,20 @@ def tile_shard_weight_grad_s7_kernel(tc, x, dy, w2_bytes, w2_scale, g, c, out):
                         start, stop = q == 0 and k2 == 0, q == 1 and k2 == 1
                         second_pass(bank["half", 1, LAST, h, 1], 1, q, k2, h, 2 * LAST + 1, P, start, stop)
 
-        def firsts(j):
-            first_pair[j] = work.tile([P, 2, 2, PAIR], F32, name="first_term", bufs=4)
+        def firsts(j, cols=slice(0, PAIR)):
+            if j not in first_pair:
+                first_pair[j] = work.tile([P, 2, 2, PAIR], F32, name="first_term", bufs=FIRSTS)
             for h in range(2):
                 nc.scalar.activation(
-                    out=first_pair[j][:, h], in_=bank["half", 0, j, h, 0][:], func=COPY, scale=c_all[:, 0:1]
+                    out=first_pair[j][:, h, :, cols],
+                    in_=bank["half", 0, j, h, 0][:, :, cols],
+                    func=COPY,
+                    scale=c_all[:, 0:1],
                 )
 
         def seconds(some):
             for j, h in some:
-                second_term[j, h] = work.tile([P, 2, PAIR], F32, name="second_term", bufs=4)
+                second_term[j, h] = work.tile([P, 2, PAIR], F32, name="second_term", bufs=SECONDS)
                 nc.scalar.activation(
                     out=second_term[j, h][:], in_=bank["half", 1, j, h, 0][:], func=COPY, scale=c_all[:, 1:2]
                 )
@@ -404,148 +422,173 @@ def tile_shard_weight_grad_s7_kernel(tc, x, dy, w2_bytes, w2_scale, g, c, out):
             f0 = PAIR * j + P * strip
             nc.sync.dma_start(out=out_view[h][:, :, f0 : f0 + width], in_=result[j, h, strip])
 
-        b0, b1, b2, b3, b4, b5, b6, b7 = BATCHES
+        def load_scales():
+            nc.sync.dma_start(out=scale_col[:], in_=w2_scale.rearrange("o (g p t) -> p (o g) t", p=P, t=PACK))
 
+        def load_c():
+            nc.sync.dma_start(out=c_bf[:], in_=c.partition_broadcast(P))
+
+        def warm_up():
+            warm_bank = psum_bank([P, PACK * P])
+            for i in range(WARM_UPS):
+                nc.tensor.matmul(warm_bank[:], lhsT=warm[:, 0:P], rhs=warm[:], start=True, stop=True)
+
+        b0, b1, b2, b3, b4, b5, b6, b7 = BATCHES
         load_w(0, (0,))
-        nc.sync.dma_start(out=scale_col[:], in_=w2_scale.rearrange("o (g p t) -> p (o g) t", p=P, t=PACK))
         load_w(0, (1,))
-        load_y(0, (0,))
+        load_scales()
         load_w(1)
+        load_y(0, (0,))
         load_y(0, (1,))
         load_w(2)
         load_y(0, (2,))
         load_y(0, (3,))
         load_y(1, (0, 1))
         load_y(1, (2, 3))
-        load_g(0, 0)
+        warm_up()
+        widen((0,), parts=2)
+        widen((1,), copy=nc.vector.tensor_copy)
+        nc.scalar.copy(out=scale_run[:], in_=scale_col[:].unsqueeze(3).to_broadcast([P, 2, PACK, RUN]))
+        widen((2,), parts=2)
+        widen((3,))
+        split_y(0, (1,), split_on_scalar)
         load_w(3)
+        load_g_wide(0, 0, 2)
+        load_w(4)
+        load_g_wide(1, 0, 2)
         load_y(2, (0, 1))
         load_y(2, (2, 3))
-        load_g(1, 0)
-        load_g(0, 1)
-        load_x(0)
-        warm_bank = psum_bank([P, PACK * P])
-        for i in range(WARM_UPS):
-            nc.tensor.matmul(warm_bank[:], lhsT=warm[:, 0:P], rhs=warm[:], start=True, stop=True)
-        nc.vector.tensor_copy(out=scale_run[:], in_=scale_col[:].unsqueeze(3).to_broadcast([P, 2, PACK, RUN]))
-        widen((0,), parts=2)
-        widen((1, 2, 3))
-        turn_strips((0, 1))
-        scale_on_vector((0, 1))
-        quantise_pair(0)
-        turn_y(0, (0, 1))
-        empty_y(0, (0, 1))
-        turn_strips((2, 3))
-        scale_on_vector((2, 3))
+        turn_strips((0, 1, 2))
+        scale_on_vector((0, 1, 2))
+        turn_y(0, (0,))
+        turn_strips((3,))
+        scale_on_vector((3,))
+        turn_y(0, (1, 2, 3))
         widen((4, 5))
-        turn_y(0, (2, 3))
+        empty_y(0, (0, 1))
+        split_y(1, (1,), split_on_scalar)
         empty_y(0, (2, 3))
-        quantise_y(0)
+        quantise_pair(0)
         quantise_pair(1)
-        turn_strips((4,))
-        unscaled_strip = empty_strip(4)
-        turn_y(1, (0, 1))
-        turn_strips((5,))
-        scale_on_vector((5,))
-        turn_y(1, (2, 3))
-        empty_y(1, range(PACK))
-        quantise_y(1)
-
+        quantise_y(0, 0, 2)
+        quantise_y(0, 2, 2)
+        turn_planes(2, 0)
+        turn_y(1, (0,))
+        turn_planes(2, 1, (0, 1))
+        turn_y(1, (1,))
         load_y(3, (0, 1))
-        load_g(1, 1)
-        load_y(3, (2, 3))
-        load_x(1)
-        load_g(2, 0)
-        nc.sync.dma_start(out=c_bf[:], in_=c.partition_broadcast(P))
-        load_w(4)
-        load_g(3, 0)
-        load_x(2)
-        load_w(5)
-        scale_on_gpsimd(4, unscaled_strip)
-        widen((6, 7))
-        split_y(2, (0, 1), split_on_scalar)
-        split_y(2, (3,), split_on_gpsimd)
+        load_x(0)
+        load_g_narrow(0, 3, 3)
+        turn_y(1, (2, 3))
+        turn_planes(2, 1, (2, 3))
+        empty_y(1, range(PACK))
+        planes_on_vector(2, (0,))
+        quantise_y(1, 0, 2)
+        planes_on_vector(2, (1,))
+        quantise_y(1, 2, 2)
+        widen((6, 7, 8))
+        mix_pair_gpsimd(2, (1,))
+        mix_pair_scalar(2, (0,))
         units(b0[:4])
-        turn_pair_planes(3)
+        turn_planes(3, 0)
+        turn_planes(3, 1)
         reads(b0[:4])
         units(b0[4:])
-        scale_on_scalar(3)
-        mix_pair(3)
-        turn_y(2, range(PACK))
-        empty_y(2, range(PACK))
+        planes_on_scalar(3)
+        widen((9,))
+        split_y(2, range(PACK), split_on_scalar)
+        load_y(3, (2, 3))
+        load_g_narrow(1, 3, 3)
+        load_x(1)
+        load_c()
+        quantise_pair(2)
+        mix_pair_gpsimd(3)
         reads(b0[4:])
-        quantise_strip(4)
-        quantise_strip(5)
-        quantise_dh(0)
+        units(b1[:4])
+        split_y(3, (0,), split_on_scalar)
+        turn_y(2, range(PACK))
+        reads(b1[:3])
+        empty_y(2, (0, 1))
+        split_y(3, (1,), split_on_scalar)
+        empty_y(2, (2, 3))
+        load_g_wide(2, 0, 1)
+        load_w(5)
         quantise_pair(3)
-
-        mix_x_gpsimd(0, K)
-        load_x(3)
-        load_g(2, 1)
-        load_g(3, 1)
-        load_g(0, 2)
-        load_g(1, 2)
-        split_y(3, (0, 1), split_on_scalar)
-        units(b1[:6])
-        reads(b1[:6])
+        quantise_dh(0)
+        mix_x_gpsimd(0, 0, 208)
+        reads(b1[3:4])
+        load_g_wide(3, 0, 1)
+        load_x(2)
+        load_g_narrow(2, 2, 3)
+        load_g_narrow(3, 2, 3)
+        split_y(3, (2, 3), split_on_scalar)
+        units(b1[4:])
+        reads(b1[4:6])
+        quantise_y(2, 0, 2)
+        quantise_y(2, 2, 2)
+        reads(b1[6:])
         turn_y(3, range(PACK))
         empty_y(3, range(PACK))
-        mix_x_scalar(1, 0)
-        quantise_y(2)
-        units(b1[6:])
-        reads(b1[6:])
-        load_g(2, 2)
-        quantise_y(3)
-        quantise_x(0)
-
+        quantise_y(3, 0, 2)
+        quantise_y(3, 2, 2)
+        units(b2[:4])
+        mix_x_gpsimd(1, 0, K)
         nc.scalar.copy(out=c_all[:], in_=c_bf[:])
-        widen((8, 9))
-        split_strips((8, 9))
+        split_strips((8, 9), split_on_scalar)
+        mix_x_scalar(0, 208, K)
+        load_x(3)
         widen((10, 11))
-        split_strips((10,))
-        mix_x_gpsimd(2, X_GPSIMD)
-        mix_x_gpsimd(3, X_GPSIMD)
-        units(b2)
+        split_strips((10, 11), split_on_scalar)
+        units(b2[4:])
         reads(b2)
-        load_g(3, 2)
-        quantise_dh(1)
+        load_g_wide(0, 4, 5)
+        load_g_wide(1, 4, 5)
+        load_g_narrow(2, 4, 5)
+        load_g_narrow(3, 4, 5)
+        turn_pair_words(4)
+        planes_on_scalar(4)
+        units(b3[:4])
+        quantise_x(0)
+        quantise_x(1)
+        mix_pair_gpsimd(4, (0,))
+        mix_pair_scalar(4, (1,))
+        reads(b3[:4])
         halves(0, 0)
         firsts(0)
-        turn_pair_words(4)
-        scale_on_scalar(4)
         halves(0, 1)
         firsts(1)
-        mix_x_scalar(2, X_GPSIMD)
-        mix_x_scalar(3, X_GPSIMD)
-
-        units(b3[:4])
-        reads(b3[:4])
-        quantise_dh(2)
-        quantise_x(1)
-        halves(0, 2)
-        firsts(2)
-        mix_pair(4, (0,))
-        halves(0, 3)
-        firsts(3)
-        mix_pair(4, (1,))
+        quantise_dh(1)
+        mix_x_gpsimd(3, 0, 384)
+        mix_x_scalar(2, 0, K)
+        mix_x_scalar(3, 384, K)
         units(b3[4:])
         reads(b3[4:])
-        halves(1, 0)
-        halves(1, 1)
-        sum_on_vector(0, 0)
-        store(0, 0)
-        seconds(((0, 1), (1, 0), (1, 1)))
+        halves(0, 2)
+        firsts(2)
+        halves(0, 3)
+        firsts(3)
         quantise_pair(4)
-        quantise_dh(3)
-
-        sums_on_gpsimd(0, ((0, 1), (1, 0)))
-        store(0, 1)
-        store(1, 0)
-        turn_pair_words(LAST)
-        scale_on_scalar(LAST)
-        mix_pair(LAST)
+        quantise_dh(2)
+        quantise_x(2)
+        quantise_x(3)
         units(b4)
         reads(b4)
+        turn_pair_words(LAST)
+        planes_on_scalar(LAST)
+        halves(1, 0)
+        halves(1, 1)
+        quantise_dh(3)
+        quantise_dh(4)
+        for h in range(2):
+            sum_on_vector(0, h)
+            store(0, h)
+        seconds(((1, 0), (1, 1)))
+        sums_on_gpsimd(0, ((1, 0), (1, 1)))
+        store(1, 0)
+        store(1, 1)
+        mix_pair_scalar(LAST)
+        units(b5)
+        reads(b5)
         halves(1, 2)
         halves(1, 3)
         for h in range(2):
@@ -553,31 +596,25 @@ def tile_shard_weight_grad_s7_kernel(tc, x, dy, w2_bytes, w2_scale, g, c, out):
             store(2, h)
         seconds(((3, 0), (3, 1)))
         quantise_pair(LAST)
-        quantise_dh(4)
-        sums_on_gpsimd(1, ((1, 1), (3, 0)))
-        store(1, 1)
-        store(3, 0)
-        units(b5)
-        reads(b5)
-
-        units(b6)
-        reads(b6[:1])
         quantise_dh(5)
-        sums_on_gpsimd(2, ((3, 1),))
-        store(3, 1)
-        reads(b6[1:])
         halves(0, 4)
         firsts(4)
+        sums_on_gpsimd(1, ((3, 0), (3, 1)))
+        store(3, 0)
+        store(3, 1)
+        units(b6)
+        reads(b6)
         halves(1, 4)
-        seconds(((4, 1),))
-        quantise_dh(6)
         sum_on_vector(4, 0)
         store(4, 0)
-        sums_on_gpsimd(3, ((4, 1),))
+        seconds(((4, 1),))
+        quantise_dh(6)
+        sums_on_gpsimd(2, ((4, 1),))
         store(4, 1)
         units(b7)
         halves(0, LAST)
-        firsts(LAST)
+        firsts(LAST, slice(0, P))
+        firsts(LAST, slice(P, PAIR))
         reads(b7[:3])
         quantise_dh(7, 0, 2)
         reads(b7[3:])

@@ -36,20 +36,20 @@ BATCHES = [
     units_of((0, 1), (2,)) + units_of((0, 1), (3,)),
     units_of((2, 3), (0, 1)),
     units_of((2, 3), (2, 3)),
-    units_of((0, 1), (4,)),
-    units_of((2, 3), (4,)),
+    units_of((0, 1, 2, 3), (4,)),
     units_of((0, 1), (5,)),
     [(a, 2 * LAST + i) for i in range(2) for a in (2, 3)],
 ]
 WIDE = 8
-ROWS, W_RAW, Y_RAW, X_RAW, G_RAW, W_WIDE, W_PLANES = 6, 3, 4, 3, 7, 4, 3
-Y_CODES, Y_PARTS, DH_WIDE, DH_NARROW, FIRSTS, SECONDS = 1, 8, 4, 4, 4, 4
+ROWS, W_RAW, Y_RAW, X_RAW, W_WIDE, W_PLANES = 6, 3, 4, 3, 4, 3
+Y_CODES, Y_PARTS, DH_WIDE, DH_NARROW, FIRSTS, SECONDS = 3, 2, 4, 4, 4, 4
 SLOTS = [
-    [("y", 1), ("w", 2), ("w", 3), ("y", 3), ("x", 1), ("w", 4), ("dh", 4), ("total", 0), ("dh", 7)],
-    [("w", 0), ("dh", 0), ("x", 0), ("x", 2), ("w", 5), ("dh", 6), ("total", 2)],
-    [("w", 1), ("dh", 1), ("x", 3), ("dh", 5), ("total", 1)],
-    [("y", 0), ("y", 2), ("dh", 2)],
-    [("dh", 3)],
+    [("y", 1), ("y", 3), ("x", 2), ("w", 5)],
+    [("w", 0), ("dh", 0), ("dh", 4), ("total", 1)],
+    [("w", 2), ("w", 3), ("x", 0), ("x", 3), ("dh", 5), ("total", 2)],
+    [("y", 0), ("y", 2), ("dh", 2), ("dh", 6)],
+    [("dh", 1), ("w", 4)],
+    [("dh", 3), ("total", 0)],
 ]
 SLOT_OF = {tenant: i for i, tenants in enumerate(SLOTS) for tenant in tenants}
 
@@ -69,8 +69,17 @@ def tile_shard_weight_grad_s7_kernel(tc, x, dy, w2_bytes, w2_scale, g, c, out):
         y_split, y_turned, y_mx, x_mixed, x_mx, dh, dh_mx = {}, {}, {}, {}, {}, {}, {}
         bank, first_pair, second_term, result = {}, {}, {}, {}
 
-        def psum_bank(shape, dtype=F32):
-            return psum.tile(shape, dtype, name="bank", bufs=BANKS)
+        free_banks = list(range(BANKS))
+        bank_of = {}
+
+        def psum_bank(key, shape, dtype=F32):
+            bank_of[key] = free_banks[0]
+            free_banks.remove(bank_of[key])
+            bank[key] = psum.tile(shape, dtype, name="bank%d" % bank_of[key], bufs=1)
+            return bank[key]
+
+        def emptied(key):
+            free_banks.append(bank_of[key])
 
         def slot(tenant, shape, dtype):
             return work.tile(shape, dtype, name="slot%d" % SLOT_OF[tenant], bufs=1, align_bytes=64)
@@ -111,7 +120,7 @@ def tile_shard_weight_grad_s7_kernel(tc, x, dy, w2_bytes, w2_scale, g, c, out):
             load_g(a, first, last, "g_wide", 2)
 
         def load_g_narrow(a, first, last):
-            load_g(a, first, last, "g_narrow", 4)
+            load_g(a, first, last, "g_narrow", 3)
 
         scale_col = keep.tile([P, 2, PACK], F32, name="scale_col")
         scale_run = keep.tile([P, 2, PACK, RUN], F32, name="scale_run", align_bytes=64)
@@ -189,17 +198,17 @@ def tile_shard_weight_grad_s7_kernel(tc, x, dy, w2_bytes, w2_scale, g, c, out):
 
         def turn_y(a, tiles):
             for t in tiles:
-                ps = psum_bank([P, 2, 2, P])
+                ps = psum_bank(("y", a, t), [P, 2, 2, P])
                 for gi in range(2):
                     for u in range(2):
                         turn(ps[:, gi, u, :], y_raw[a, t], y_split.get((a, t)), gi, u)
-                bank["y", a, t] = ps
 
         def empty_y(a, tiles):
             if a not in y_turned:
                 y_turned[a] = slot(("y", a), [P, PACK, 2, P, 2], F32)
             for t in tiles:
                 nc.scalar.copy(out=y_turned[a][:, t], in_=bank["y", a, t][:].rearrange("p g u m -> p g m u"))
+                emptied(("y", a, t))
 
         def quantise_y(a, first=0, count=PACK):
             source = y_turned[a][:, first : first + count].rearrange("p r g m u -> p (r g m u)").bitcast(BF16)
@@ -215,6 +224,10 @@ def tile_shard_weight_grad_s7_kernel(tc, x, dy, w2_bytes, w2_scale, g, c, out):
                     copy(out=w_wide[b][:, ns], in_=w_raw[b // 2][:, b % 2, ns].bitcast(FP8))
 
         def pair_tile(j):
+            if j < 2:
+                if "head" not in w_turned:
+                    w_turned["head"] = slot(("w", 0), [P, 2, 2, 2, P, 2], F32)
+                return w_turned["head"][:, j]
             if j not in w_turned:
                 w_turned[j] = slot(("w", j), [P, 2, 2, P, 2], F32)
             return w_turned[j]
@@ -226,10 +239,9 @@ def tile_shard_weight_grad_s7_kernel(tc, x, dy, w2_bytes, w2_scale, g, c, out):
         def turn_strips(strips, passes=(0, 1)):
             for b in strips:
                 for gi in passes:
-                    ps = psum_bank([P, PACK, P])
+                    ps = psum_bank(("strip", b, gi), [P, PACK, P])
                     for t in range(PACK):
                         turn_plane(ps[:, t, :], b, gi, t)
-                    bank["strip", b, gi] = ps
 
         def scale_on_vector(strips, passes=(0, 1)):
             for b in strips:
@@ -240,10 +252,11 @@ def tile_shard_weight_grad_s7_kernel(tc, x, dy, w2_bytes, w2_scale, g, c, out):
                         in1=scale_run[:, gi].unsqueeze(1).to_broadcast([P, P // RUN, PACK, RUN]),
                         op=MULT,
                     )
+                    emptied(("strip", b, gi))
 
         def turn_planes(j, gi, ts=range(PACK)):
             if ("pass", j, gi) not in bank:
-                bank["pass", j, gi] = psum_bank([P, PACK, 2, P], BF16)
+                psum_bank(("pass", j, gi), [P, PACK, 2, P], BF16)
             ps = bank["pass", j, gi]
             for t in ts:
                 for i in range(2):
@@ -252,7 +265,7 @@ def tile_shard_weight_grad_s7_kernel(tc, x, dy, w2_bytes, w2_scale, g, c, out):
 
         def turn_pair_words(j):
             for gi in range(2):
-                ps = psum_bank([P, 2, 2, P])
+                ps = psum_bank(("pass", j, gi), [P, 2, 2, P])
                 for u in range(2):
                     for i in range(2):
                         turn(ps[:, u, i, :], w_wide[2 * j + i][:], w_split.get(2 * j + i), gi, u)
@@ -274,6 +287,7 @@ def tile_shard_weight_grad_s7_kernel(tc, x, dy, w2_bytes, w2_scale, g, c, out):
                         func=COPY,
                         scale=scale_col[:, gi, t : t + 1],
                     )
+                emptied(("pass", j, gi))
 
         def planes_on_vector(j, passes=(0, 1)):
             for gi in passes:
@@ -286,19 +300,20 @@ def tile_shard_weight_grad_s7_kernel(tc, x, dy, w2_bytes, w2_scale, g, c, out):
                         scalar2=None,
                         op0=MULT,
                     )
+                emptied(("pass", j, gi))
 
         def pair_words(j, gi):
             return as_mixed(pair_tile(j)[:, gi].rearrange("p i f u -> p (i f) u"))
 
-        def mix_pair_scalar(j, passes=(0, 1)):
+        def mix_pair_scalar(j, passes=(0, 1), cols=slice(0, PAIR)):
             for gi in passes:
-                nc.scalar.copy(out=mixed_runs(pair_words(j, gi)), in_=in_runs(w_planes[j, gi][:]))
+                nc.scalar.copy(out=mixed_runs(pair_words(j, gi)[:, cols]), in_=in_runs(w_planes[j, gi][:, :, cols]))
 
-        def mix_pair_gpsimd(j, passes=(0, 1)):
+        def mix_pair_gpsimd(j, passes=(0, 1), cols=slice(0, PAIR)):
             for gi in passes:
                 nc.gpsimd.tensor_scalar(
-                    out=pair_words(j, gi),
-                    in0=w_planes[j, gi][:].rearrange("p t f -> p f t"),
+                    out=pair_words(j, gi)[:, cols],
+                    in0=w_planes[j, gi][:, :, cols].rearrange("p t f -> p f t"),
                     scalar1=1.0,
                     scalar2=0.0,
                     op0=MULT,
@@ -307,14 +322,24 @@ def tile_shard_weight_grad_s7_kernel(tc, x, dy, w2_bytes, w2_scale, g, c, out):
 
         def quantise_pair(j):
             source = w_turned[j][:].rearrange("p g i f u -> p (g i f u)").bitcast(BF16)
-            codes = quantise("w", PAIRS, source)
+            codes = quantise("w", PAIRS - 2, source)
             for i in range(2):
                 strip_mx[2 * j + i] = (codes, PAIR, P * i)
 
+        def quantise_head_pairs():
+            source = w_turned["head"][:].rearrange("p j g i f u -> p (j g i f u)").bitcast(BF16)
+            codes = quantise("w_head", 1, source)
+            for b in range(4):
+                strip_mx[b] = (codes, PAIR, 2 * PAIR * (b // 2) + P * (b % 2))
+
         def mixed_x(a):
-            if a not in x_mixed:
-                x_mixed[a] = slot(("x", a), [P, K, PACK], BF16)
-            return x_mixed[a]
+            if a >= 2:
+                if a not in x_mixed:
+                    x_mixed[a] = slot(("x", a), [P, K, PACK], BF16)
+                return x_mixed[a]
+            if 0 not in x_mixed:
+                x_mixed[0] = slot(("x", 0), [P, 2, K, PACK], BF16)
+            return x_mixed[0][:, a]
 
         def mix_x_gpsimd(a, k0, k1):
             nc.gpsimd.tensor_scalar(
@@ -330,21 +355,26 @@ def tile_shard_weight_grad_s7_kernel(tc, x, dy, w2_bytes, w2_scale, g, c, out):
             nc.scalar.copy(out=mixed_runs(mixed_x(a)[:, k0:k1, :]), in_=in_runs(x_raw[a][:, :, k0:k1]))
 
         def quantise_x(a):
-            x_mx[a] = quantise("x", GROUPS, x_mixed[a][:].rearrange("p k t -> p (k t)"))
+            if a >= 2:
+                x_mx[a] = (quantise("x_group", 2, x_mixed[a][:].rearrange("p k t -> p (k t)")), 0)
+            else:
+                codes = quantise("x_shard", 1, x_mixed[0][:].rearrange("p q k t -> p (q k t)"))
+                for q in range(2):
+                    x_mx[q] = (codes, K * q)
 
         place = {u: (k, i) for k, batch in enumerate(BATCHES) for i, u in enumerate(batch)}
 
-        def units(some):
+        def units(some, tiles=range(PACK)):
             for a, b in some:
-                ps = psum_bank([P, PACK, P])
+                if ("unit", a, b) not in bank:
+                    psum_bank(("unit", a, b), [P, PACK, P])
                 codes, per_pass, f0 = strip_mx[b]
-                for t in range(PACK):
+                for t in tiles:
                     y_codes, m0 = y_mx[a, t]
                     for gi in range(2):
-                        y0 = m0 + P * gi
-                        w0 = per_pass * gi + f0
-                        multiply(ps[:, t, :], y_codes, slice(y0, y0 + P), codes, slice(w0, w0 + P), gi == 0, gi == 1)
-                bank["unit", a, b] = ps
+                        y_cols = slice(m0 + P * gi, m0 + P * (gi + 1))
+                        w_cols = slice(per_pass * gi + f0, per_pass * gi + f0 + P)
+                        multiply(bank["unit", a, b][:, t, :], y_codes, y_cols, codes, w_cols, gi == 0, gi == 1)
 
         def reads(some):
             for a, b in some:
@@ -357,6 +387,7 @@ def tile_shard_weight_grad_s7_kernel(tc, x, dy, w2_bytes, w2_scale, g, c, out):
                     in1=in_runs(g_raw[a, b]),
                     op=MULT,
                 )
+                emptied(("unit", a, b))
 
         def quantise_dh(k, first=0, count=None):
             count = count or len(BATCHES[k])
@@ -366,23 +397,23 @@ def tile_shard_weight_grad_s7_kernel(tc, x, dy, w2_bytes, w2_scale, g, c, out):
                 dh_mx[BATCHES[k][first + i]] = (codes, P * i)
 
         def second_pass(ps, d, q, k2, h, b, width, start, stop):
-            k0 = P * (2 * h + k2)
+            x_codes, x0 = x_mx[2 * d + q]
+            k0 = x0 + P * (2 * h + k2)
             codes, f0 = dh_mx[2 * d + q, b]
-            multiply(ps[:, k2, :], x_mx[2 * d + q], slice(k0, k0 + P), codes, slice(f0, f0 + width), start, stop)
+            multiply(ps[:, k2, :], x_codes, slice(k0, k0 + P), codes, slice(f0, f0 + width), start, stop)
 
         def halves(d, j, width=PAIR, hs=(0, 1)):
             for h in hs:
-                ps = psum_bank([P, 2, width])
+                ps = psum_bank(("half", d, j, h, 0), [P, 2, width])
                 for k2 in range(2):
                     for q in range(2):
                         second_pass(ps, d, q, k2, h, 2 * j, width, q == 0, q == 1)
-                bank["half", d, j, h, 0] = ps
 
         def last_strip():
             for q in range(2):
                 for h in range(2):
                     if q == 0:
-                        bank["half", 1, LAST, h, 1] = psum_bank([P, 2, P])
+                        psum_bank(("half", 1, LAST, h, 1), [P, 2, P])
                     for k2 in range(2):
                         start, stop = q == 0 and k2 == 0, q == 1 and k2 == 1
                         second_pass(bank["half", 1, LAST, h, 1], 1, q, k2, h, 2 * LAST + 1, P, start, stop)
@@ -397,30 +428,41 @@ def tile_shard_weight_grad_s7_kernel(tc, x, dy, w2_bytes, w2_scale, g, c, out):
                     func=COPY,
                     scale=c_all[:, 0:1],
                 )
+                if cols.stop == PAIR:
+                    emptied(("half", 0, j, h, 0))
 
-        def seconds(some):
+        def seconds(some, rows=slice(0, 2)):
             for j, h in some:
                 second_term[j, h] = work.tile([P, 2, PAIR], F32, name="second_term", bufs=SECONDS)
                 nc.scalar.activation(
-                    out=second_term[j, h][:], in_=bank["half", 1, j, h, 0][:], func=COPY, scale=c_all[:, 1:2]
+                    out=second_term[j, h][:, rows],
+                    in_=bank["half", 1, j, h, 0][:, rows],
+                    func=COPY,
+                    scale=c_all[:, 1:2],
                 )
+                if rows.stop == 2:
+                    emptied(("half", 1, j, h, 0))
 
-        def sum_on_vector(j, h, strip=0, width=PAIR):
-            total = first_pair[j][:, h, :, P * strip : P * strip + width]
+        def sum_on_vector(j, h, strip=0, width=PAIR, rows=slice(0, 2)):
+            total = first_pair[j][:, h, rows, P * strip : P * strip + width]
             nc.vector.scalar_tensor_tensor(
-                out=total, in0=bank["half", 1, j, h, strip][:], scalar=c_all[:, 1:2], in1=total, op0=MULT, op1=ADD
+                out=total, in0=bank["half", 1, j, h, strip][:, rows], scalar=c_all[:, 1:2], in1=total, op0=MULT, op1=ADD
             )
-            result[j, h, strip] = total
+            emptied(("half", 1, j, h, strip))
+            f0 = PAIR * j + P * strip
+            nc.sync.dma_start(out=out_view[h][:, rows, f0 : f0 + width], in_=total)
 
         def sums_on_gpsimd(n, some):
             total = slot(("total", n), [P, len(some), 2, PAIR], F32)
-            for i, (j, h) in enumerate(some):
-                nc.gpsimd.tensor_tensor(out=total[:, i], in0=first_pair[j][:, h], in1=second_term[j, h][:], op=ADD)
-                result[j, h, 0] = total[:, i]
+            for i, (j, h, rows) in enumerate(some):
+                nc.gpsimd.tensor_tensor(
+                    out=total[:, i, rows], in0=first_pair[j][:, h, rows], in1=second_term[j, h][:, rows], op=ADD
+                )
+                result[j, h] = (total[:, i, rows], rows)
 
-        def store(j, h, strip=0, width=PAIR):
-            f0 = PAIR * j + P * strip
-            nc.sync.dma_start(out=out_view[h][:, :, f0 : f0 + width], in_=result[j, h, strip])
+        def store(j, h):
+            total, rows = result[j, h]
+            nc.sync.dma_start(out=out_view[h][:, rows, PAIR * j : PAIR * (j + 1)], in_=total)
 
         def load_scales():
             nc.sync.dma_start(out=scale_col[:], in_=w2_scale.rearrange("o (g p t) -> p (o g) t", p=P, t=PACK))
@@ -429,11 +471,13 @@ def tile_shard_weight_grad_s7_kernel(tc, x, dy, w2_bytes, w2_scale, g, c, out):
             nc.sync.dma_start(out=c_bf[:], in_=c.partition_broadcast(P))
 
         def warm_up():
-            warm_bank = psum_bank([P, PACK * P])
+            warm_bank = psum_bank("warm", [P, PACK * P])
+            emptied("warm")
             for i in range(WARM_UPS):
                 nc.tensor.matmul(warm_bank[:], lhsT=warm[:, 0:P], rhs=warm[:], start=True, stop=True)
 
-        b0, b1, b2, b3, b4, b5, b6, b7 = BATCHES
+        b0, b1, b2, b3, b4, b5, b6 = BATCHES
+        both, upper, lower = slice(0, 2), slice(0, 1), slice(1, 2)
         load_w(0, (0,))
         load_w(0, (1,))
         load_scales()
@@ -459,170 +503,170 @@ def tile_shard_weight_grad_s7_kernel(tc, x, dy, w2_bytes, w2_scale, g, c, out):
         load_y(2, (0, 1))
         load_y(2, (2, 3))
         turn_strips((0, 1, 2))
-        scale_on_vector((0, 1, 2))
+        scale_on_vector((0, 1))
         turn_y(0, (0,))
         turn_strips((3,))
-        scale_on_vector((3,))
+        scale_on_vector((2,))
         turn_y(0, (1, 2, 3))
+        scale_on_vector((3,))
         widen((4, 5))
-        empty_y(0, (0, 1))
-        split_y(1, (1,), split_on_scalar)
-        empty_y(0, (2, 3))
-        quantise_pair(0)
-        quantise_pair(1)
+        empty_y(0, range(PACK))
         quantise_y(0, 0, 2)
+        quantise_head_pairs()
         quantise_y(0, 2, 2)
         turn_planes(2, 0)
         turn_y(1, (0,))
         turn_planes(2, 1, (0, 1))
         turn_y(1, (1,))
-        load_y(3, (0, 1))
         load_x(0)
+        load_y(3, (0, 1))
         load_g_narrow(0, 3, 3)
         turn_y(1, (2, 3))
         turn_planes(2, 1, (2, 3))
         empty_y(1, range(PACK))
-        planes_on_vector(2, (0,))
-        quantise_y(1, 0, 2)
-        planes_on_vector(2, (1,))
-        quantise_y(1, 2, 2)
-        widen((6, 7, 8))
-        mix_pair_gpsimd(2, (1,))
+        planes_on_vector(2)
+        quantise_y(1)
+        widen((6, 7))
+        mix_pair_gpsimd(2, (1,), slice(0, 208))
         mix_pair_scalar(2, (0,))
-        units(b0[:4])
+        mix_pair_scalar(2, (1,), slice(208, PAIR))
+        widen((8,))
+        units(b0[:4], (0, 1))
+        units(b0[:4], (2, 3))
         turn_planes(3, 0)
         turn_planes(3, 1)
-        reads(b0[:4])
-        units(b0[4:])
+        reads(b0[:3])
         planes_on_scalar(3)
-        widen((9,))
-        split_y(2, range(PACK), split_on_scalar)
+        units(b0[4:])
+        quantise_pair(2)
+        mix_pair_gpsimd(3, (0,))
+        mix_pair_gpsimd(3, (1,), slice(0, 192))
+        split_y(2, (0,), split_on_scalar)
+        mix_pair_scalar(3, (1,), slice(192, PAIR))
+        split_y(2, (1, 2, 3), split_on_scalar)
         load_y(3, (2, 3))
         load_g_narrow(1, 3, 3)
         load_x(1)
         load_c()
-        quantise_pair(2)
-        mix_pair_gpsimd(3)
-        reads(b0[4:])
+        reads(b0[3:])
         units(b1[:4])
         split_y(3, (0,), split_on_scalar)
         turn_y(2, range(PACK))
-        reads(b1[:3])
+        reads(b1[:1])
+        quantise_pair(3)
+        mix_x_gpsimd(0, 0, 400)
+        reads(b1[1:4])
+        load_g_wide(2, 0, 3)
+        load_x(2)
+        load_w(5)
+        load_g_wide(3, 0, 3)
         empty_y(2, (0, 1))
         split_y(3, (1,), split_on_scalar)
         empty_y(2, (2, 3))
-        load_g_wide(2, 0, 1)
-        load_w(5)
-        quantise_pair(3)
-        quantise_dh(0)
-        mix_x_gpsimd(0, 0, 208)
-        reads(b1[3:4])
-        load_g_wide(3, 0, 1)
-        load_x(2)
-        load_g_narrow(2, 2, 3)
-        load_g_narrow(3, 2, 3)
-        split_y(3, (2, 3), split_on_scalar)
+        split_y(3, (2,), split_on_scalar)
         units(b1[4:])
         reads(b1[4:6])
-        quantise_y(2, 0, 2)
-        quantise_y(2, 2, 2)
-        reads(b1[6:])
+        quantise_y(2)
+        widen((9,))
         turn_y(3, range(PACK))
+        reads(b1[6:])
         empty_y(3, range(PACK))
-        quantise_y(3, 0, 2)
-        quantise_y(3, 2, 2)
-        units(b2[:4])
-        mix_x_gpsimd(1, 0, K)
+        quantise_dh(0)
+        quantise_y(3)
+        mix_x_gpsimd(2, 0, 432)
         nc.scalar.copy(out=c_all[:], in_=c_bf[:])
         split_strips((8, 9), split_on_scalar)
-        mix_x_scalar(0, 208, K)
+        mix_x_scalar(0, 400, K)
         load_x(3)
-        widen((10, 11))
-        split_strips((10, 11), split_on_scalar)
-        units(b2[4:])
-        reads(b2)
-        load_g_wide(0, 4, 5)
-        load_g_wide(1, 4, 5)
-        load_g_narrow(2, 4, 5)
-        load_g_narrow(3, 4, 5)
+        mix_x_scalar(1, 0, K)
+        units(b2[:4] + b3[:4])
+        reads(b2[:4] + b3[:1])
         turn_pair_words(4)
         planes_on_scalar(4)
-        units(b3[:4])
+        units(b2[4:7])
         quantise_x(0)
-        quantise_x(1)
-        mix_pair_gpsimd(4, (0,))
-        mix_pair_scalar(4, (1,))
-        reads(b3[:4])
+        mix_x_gpsimd(3, 0, 400)
+        mix_x_scalar(2, 432, K)
+        mix_x_scalar(3, 400, K)
+        widen((10,))
+        reads(b3[1:4])
+        load_g_wide(0, 4, 5)
+        load_g_narrow(1, 4, 5)
+        load_g_narrow(2, 4, 5)
+        load_g_narrow(3, 4, 5)
+        units(b2[7:])
         halves(0, 0)
-        firsts(0)
+        reads(b2[4:6])
         halves(0, 1)
+        firsts(0)
         firsts(1)
         quantise_dh(1)
-        mix_x_gpsimd(3, 0, 384)
-        mix_x_scalar(2, 0, K)
-        mix_x_scalar(3, 384, K)
+        mix_pair_gpsimd(4, (0,))
+        mix_pair_scalar(4, (1,))
+        widen((11,))
+        reads(b2[6:])
         units(b3[4:])
-        reads(b3[4:])
         halves(0, 2)
-        firsts(2)
         halves(0, 3)
+        reads(b3[4:6])
+        firsts(2)
         firsts(3)
+        turn_planes(LAST, 0)
+        turn_planes(LAST, 1)
         quantise_pair(4)
         quantise_dh(2)
         quantise_x(2)
+        units(b4[:4])
+        reads(b3[6:])
         quantise_x(3)
-        units(b4)
-        reads(b4)
-        turn_pair_words(LAST)
+        quantise_dh(3)
         planes_on_scalar(LAST)
         halves(1, 0)
         halves(1, 1)
-        quantise_dh(3)
-        quantise_dh(4)
-        for h in range(2):
-            sum_on_vector(0, h)
-            store(0, h)
-        seconds(((1, 0), (1, 1)))
-        sums_on_gpsimd(0, ((1, 0), (1, 1)))
+        mix_pair_scalar(LAST, (0,))
+        seconds(((0, 0), (0, 1), (1, 0), (1, 1)))
+        mix_pair_scalar(LAST, (1,))
+        sums_on_gpsimd(0, ((0, 0, both), (0, 1, both), (1, 0, both)))
+        store(0, 0)
+        store(0, 1)
         store(1, 0)
-        store(1, 1)
-        mix_pair_scalar(LAST)
-        units(b5)
-        reads(b5)
+        reads(b4[:4])
+        units(b4[4:])
+        reads(b4[4:])
         halves(1, 2)
         halves(1, 3)
-        for h in range(2):
-            sum_on_vector(2, h)
-            store(2, h)
-        seconds(((3, 0), (3, 1)))
+        sum_on_vector(2, 0)
+        seconds(((2, 1),))
+        seconds(((3, 0),), upper)
         quantise_pair(LAST)
-        quantise_dh(5)
+        quantise_dh(4)
+        sums_on_gpsimd(1, ((1, 1, both), (2, 1, both), (3, 0, upper)))
+        sum_on_vector(3, 0, rows=lower)
+        sum_on_vector(3, 1)
+        store(1, 1)
+        store(2, 1)
+        store(3, 0)
+        units(b5)
+        reads(b5)
         halves(0, 4)
         firsts(4)
-        sums_on_gpsimd(1, ((3, 0), (3, 1)))
-        store(3, 0)
-        store(3, 1)
-        units(b6)
-        reads(b6)
         halves(1, 4)
-        sum_on_vector(4, 0)
-        store(4, 0)
         seconds(((4, 1),))
-        quantise_dh(6)
-        sums_on_gpsimd(2, ((4, 1),))
+        sum_on_vector(4, 0)
+        quantise_dh(5)
+        sums_on_gpsimd(2, ((4, 1, both),))
         store(4, 1)
-        units(b7)
+        units(b6)
         halves(0, LAST)
+        reads(b6[:3])
         firsts(LAST, slice(0, P))
         firsts(LAST, slice(P, PAIR))
-        reads(b7[:3])
-        quantise_dh(7, 0, 2)
-        reads(b7[3:])
-        quantise_dh(7, 2, 1)
-        quantise_dh(7, 3, 1)
+        quantise_dh(6, 0, 2)
+        reads(b6[3:])
+        quantise_dh(6, 2, 1)
+        quantise_dh(6, 3, 1)
         halves(1, LAST, P)
         last_strip()
         for strip in range(2):
             for h in range(2):
                 sum_on_vector(LAST, h, strip, P)
-                store(LAST, h, strip, P)

from contextlib import ExitStack

import concourse.mybir as mybir
from concourse.masks import make_identity

D, T, K, N, F = 2, 1024, 512, 1024, 1536
FLOPS = 2 * D * T * N * F + 2 * D * T * K * F

F32 = mybir.dt.float32
BF16 = mybir.dt.bfloat16
U32 = mybir.dt.uint32
U8 = mybir.dt.uint8
FP8 = mybir.dt.float8_e4m3fn
FP8X4 = mybir.dt.float8_e4m3fn_x4
MULT = mybir.AluOpType.mult
ADD = mybir.AluOpType.add
COPY = mybir.ActivationFunctionType.Copy

P = 128
PACK = 4
GROUPS = D * T // (P * PACK)
PAIR = 2 * P
PAIRS = F // PAIR
LAST = PAIRS - 1
RUN = 4
BANKS = 8
WARM_UPS = 4


def units_of(groups, pairs):
    return [(a, 2 * j + i) for a in groups for j in pairs for i in range(2)]


BATCHES = [
    units_of((0, 1), (0, 1)),
    units_of((0, 1), (2,)) + units_of((0, 1), (3,)),
    units_of((2, 3), (0, 1)),
    units_of((2, 3), (2, 3)),
    units_of((0, 1, 2, 3), (4,)),
    units_of((0, 1), (5,)),
    [(a, 2 * LAST + i) for i in range(2) for a in (2, 3)],
]
WIDE = 8
ROWS, W_RAW, Y_RAW, X_RAW, W_WIDE, W_PLANES = 6, 3, 4, 3, 4, 3
Y_CODES, Y_PARTS, DH_WIDE, DH_NARROW, FIRSTS, SECONDS = 3, 2, 4, 4, 4, 4
SLOTS = [
    [("y", 1), ("y", 3), ("x", 2), ("w", 5)],
    [("w", 0), ("dh", 0), ("dh", 4), ("total", 1)],
    [("w", 2), ("w", 3), ("x", 0), ("x", 3), ("dh", 5), ("total", 2)],
    [("y", 0), ("y", 2), ("dh", 2), ("dh", 6)],
    [("dh", 1), ("w", 4)],
    [("dh", 3), ("total", 0)],
]
SLOT_OF = {tenant: i for i, tenants in enumerate(SLOTS) for tenant in tenants}


def tile_shard_weight_grad_s7_kernel(tc, x, dy, w2_bytes, w2_scale, g, c, out):
    nc = tc.nc
    with ExitStack() as ctx:
        keep = ctx.enter_context(tc.tile_pool(name="keep", bufs=1))
        work = ctx.enter_context(tc.tile_pool(name="work", bufs=2))
        psum = ctx.enter_context(tc.psum_pool(name="psum", bufs=2))
        ctx.enter_context(tc.manual_schedule())

        w_view = w2_bytes.rearrange("(j i p) n -> j p i n", i=2, p=P)
        out_view = out.rearrange("(h k2 p) f -> h p k2 f", k2=2, p=P)
        w_raw, y_raw, x_raw, g_raw = {}, {}, {}, {}
        w_wide, w_split, w_planes, w_turned, strip_mx = {}, {}, {}, {}, {}
        y_split, y_turned, y_mx, x_mixed, x_mx, dh, dh_mx = {}, {}, {}, {}, {}, {}, {}
        bank, first_pair, second_term, result = {}, {}, {}, {}

        free_banks = list(range(BANKS))
        bank_of = {}

        def psum_bank(key, shape, dtype=F32):
            bank_of[key] = free_banks[0]
            free_banks.remove(bank_of[key])
            bank[key] = psum.tile(shape, dtype, name="bank%d" % bank_of[key], bufs=1)
            return bank[key]

        def emptied(key):
            free_banks.append(bank_of[key])

        def slot(tenant, shape, dtype):
            return work.tile(shape, dtype, name="slot%d" % SLOT_OF[tenant], bufs=1, align_bytes=64)

        def row_tile(shape, dtype):
            return work.tile(shape, dtype, name="row", bufs=ROWS, align_bytes=64)

        def samples(tensor, a):
            return tensor[a // 2].rearrange("(q p t) n -> q p t n", q=2, t=PACK)[a % 2]

        def load_w(j, strips=(0, 1), cols=slice(0, N)):
            if j not in w_raw:
                w_raw[j] = work.tile([P, 2, N], U8, name="w_raw", bufs=W_RAW)
            part = slice(strips[0], strips[-1] + 1)
            nc.sync.dma_start(out=w_raw[j][:, part, cols], in_=w_view[j][:, part, cols])

        def load_y(a, rows):
            if len(rows) == 1:
                tile = row_tile([P, 1, N], BF16)
            else:
                tile = work.tile([P, 2, N], BF16, name="y_raw", bufs=Y_RAW, align_bytes=64)
            nc.sync.dma_start(out=tile[:], in_=samples(dy, a)[:, rows[0] : rows[-1] + 1, :])
            for i, t in enumerate(rows):
                y_raw[a, t] = tile[:, i, :]

        def load_x(a):
            x_raw[a] = work.tile([P, PACK, K], BF16, name="x_raw", bufs=X_RAW, align_bytes=64)
            nc.sync.dma_start(out=x_raw[a][:], in_=samples(x, a))

        def load_g(a, first, last, name, bufs):
            cols = slice(PAIR * first, PAIR * (last + 1))
            tile = work.tile([P, PACK, PAIR * (last + 1 - first)], BF16, name=name, bufs=bufs, align_bytes=64)
            nc.sync.dma_start(out=tile[:], in_=samples(g, a)[:, :, cols])
            for b in range(2 * first, 2 * last + 2):
                g_raw[a, b] = tile[:, :, P * (b - 2 * first) : P * (b - 2 * first + 1)]

        def load_g_wide(a, first, last):
            load_g(a, first, last, "g_wide", 2)

        def load_g_narrow(a, first, last):
            load_g(a, first, last, "g_narrow", 3)

        scale_col = keep.tile([P, 2, PACK], F32, name="scale_col")
        scale_run = keep.tile([P, 2, PACK, RUN], F32, name="scale_run", align_bytes=64)
        c_bf = keep.tile([P, D], BF16, name="c_bf")
        c_all = keep.tile([P, D], F32, name="c_all")
        warm = keep.tile([P, PACK * P], BF16, name="warm", align_bytes=64)
        nc.vector.memset(warm[:], 1.0)
        ident = keep.tile([P, P], F32, name="ident", align_bytes=64)
        make_identity(nc, ident[:])
        ident_bf = keep.tile([P, P], BF16, name="ident_bf", align_bytes=64)
        nc.vector.tensor_copy(out=ident_bf[:], in_=ident[:])

        def quantise(name, bufs, source):
            columns = source.shape[1] // PACK
            codes = work.tile([P, columns], U32, name=name + "_codes", bufs=bufs, align_bytes=64)
            scales = work.tile([P, columns], U8, name=name + "_scales", bufs=bufs, align_bytes=64)
            nc.vector.quantize_mx(out=codes[:].bitcast(FP8X4), scales=scales[:], in_=source)
            return codes, scales

        def multiply(ps, lhs, lhs_cols, rhs, rhs_cols, start, stop):
            nc.tensor.matmul_mx(
                out=ps,
                lhsT=lhs[0][:, lhs_cols].bitcast(FP8X4),
                lhsT_scale=lhs[1][:, lhs_cols],
                rhs=rhs[0][:, rhs_cols].bitcast(FP8X4),
                rhs_scale=rhs[1][:, rhs_cols],
                start=start,
                stop=stop,
            )

        def in_runs(rows):
            return rows.rearrange("p t (c i) -> p c t i", i=RUN)

        def mixed_runs(mixed):
            return mixed.rearrange("p (c i) t -> p c t i", i=RUN)

        def as_mixed(words):
            return words.rearrange("p f u -> p (f u)").bitcast(BF16).rearrange("p (f t) -> p f t", t=PACK)

        def turn(ps, row, halves, gi, u):
            if halves is None:
                words = row.bitcast(F32)[:, PAIR * gi + u : PAIR * (gi + 1) : 2]
            else:
                words = halves[:, u, P * gi : P * (gi + 1)]
            nc.tensor.transpose(ps, words, ident[:])

        def split_on_scalar(row):
            halves = row_tile([P, 2, PAIR], F32)
            nc.scalar.copy(out=halves[:], in_=row.bitcast(F32).rearrange("p (w u) -> p u w", u=2))
            return halves

        def split_on_vector(row):
            halves = row_tile([P, 2, PAIR], F32)
            nc.vector.tensor_copy(
                out=halves[:].bitcast(BF16).rearrange("p u (w e) -> p u w e", e=2),
                in_=row.rearrange("p (w u e) -> p u w e", u=2, e=2),
            )
            return halves

        def split_on_gpsimd(row):
            halves = row_tile([P, 2, PAIR], F32)
            nc.gpsimd.tensor_scalar(
                out=halves[:].bitcast(BF16).rearrange("p u (w e) -> p u w e", e=2),
                in0=row.rearrange("p (w u e) -> p u w e", u=2, e=2),
                scalar1=1.0,
                scalar2=0.0,
                op0=MULT,
                op1=ADD,
            )
            return halves

        def split_y(a, tiles, split):
            for t in tiles:
                y_split[a, t] = split(y_raw[a, t])

        def turn_y(a, tiles):
            for t in tiles:
                ps = psum_bank(("y", a, t), [P, 2, 2, P])
                for gi in range(2):
                    for u in range(2):
                        turn(ps[:, gi, u, :], y_raw[a, t], y_split.get((a, t)), gi, u)

        def empty_y(a, tiles):
            if a not in y_turned:
                y_turned[a] = slot(("y", a), [P, PACK, 2, P, 2], F32)
            for t in tiles:
                nc.scalar.copy(out=y_turned[a][:, t], in_=bank["y", a, t][:].rearrange("p g u m -> p g m u"))
                emptied(("y", a, t))

        def quantise_y(a, first=0, count=PACK):
            source = y_turned[a][:, first : first + count].rearrange("p r g m u -> p (r g m u)").bitcast(BF16)
            codes = quantise("y" if count == PACK else "y_part", Y_CODES if count == PACK else Y_PARTS, source)
            for i in range(count):
                y_mx[a, first + i] = (codes, PAIR * i)

        def widen(strips, parts=1, copy=nc.scalar.copy):
            for b in strips:
                w_wide[b] = work.tile([P, N], BF16, name="w_wide", bufs=W_WIDE, align_bytes=64)
                for i in range(parts):
                    ns = slice(N // parts * i, N // parts * (i + 1))
                    copy(out=w_wide[b][:, ns], in_=w_raw[b // 2][:, b % 2, ns].bitcast(FP8))

        def pair_tile(j):
            if j < 2:
                if "head" not in w_turned:
                    w_turned["head"] = slot(("w", 0), [P, 2, 2, 2, P, 2], F32)
                return w_turned["head"][:, j]
            if j not in w_turned:
                w_turned[j] = slot(("w", j), [P, 2, 2, P, 2], F32)
            return w_turned[j]

        def turn_plane(ps, b, gi, t):
            columns = w_wide[b][:, P * PACK * gi + t : P * PACK * (gi + 1) : PACK]
            nc.tensor.matmul(ps, lhsT=columns, rhs=ident_bf[:], start=True, stop=True)

        def turn_strips(strips, passes=(0, 1)):
            for b in strips:
                for gi in passes:
                    ps = psum_bank(("strip", b, gi), [P, PACK, P])
                    for t in range(PACK):
                        turn_plane(ps[:, t, :], b, gi, t)

        def scale_on_vector(strips, passes=(0, 1)):
            for b in strips:
                for gi in passes:
                    nc.vector.tensor_tensor(
                        out=mixed_runs(as_mixed(pair_tile(b // 2)[:, gi, b % 2])),
                        in0=in_runs(bank["strip", b, gi][:]),
                        in1=scale_run[:, gi].unsqueeze(1).to_broadcast([P, P // RUN, PACK, RUN]),
                        op=MULT,
                    )
                    emptied(("strip", b, gi))

        def turn_planes(j, gi, ts=range(PACK)):
            if ("pass", j, gi) not in bank:
                psum_bank(("pass", j, gi), [P, PACK, 2, P], BF16)
            ps = bank["pass", j, gi]
            for t in ts:
                for i in range(2):
                    turn_plane(ps[:, t, i, :], 2 * j + i, gi, t)
                bank["plane", j, gi, t] = ps[:, t].rearrange("p i f -> p (i f)")

        def turn_pair_words(j):
            for gi in range(2):
                ps = psum_bank(("pass", j, gi), [P, 2, 2, P])
                for u in range(2):
                    for i in range(2):
                        turn(ps[:, u, i, :], w_wide[2 * j + i][:], w_split.get(2 * j + i), gi, u)
                    elements = ps[:, u].rearrange("p i f -> p (i f)").bitcast(BF16)
                    for e in range(2):
                        bank["plane", j, gi, 2 * u + e] = elements[:, e : 2 * PAIR : 2]

        def split_strips(strips, split):
            for b in strips:
                w_split[b] = split(w_wide[b][:])

        def planes_on_scalar(j, passes=(0, 1)):
            for gi in passes:
                w_planes[j, gi] = work.tile([P, PACK, PAIR], BF16, name="w_planes", bufs=W_PLANES, align_bytes=64)
                for t in range(PACK):
                    nc.scalar.activation(
                        out=w_planes[j, gi][:, t, :],
                        in_=bank["plane", j, gi, t],
                        func=COPY,
                        scale=scale_col[:, gi, t : t + 1],
                    )
                emptied(("pass", j, gi))

        def planes_on_vector(j, passes=(0, 1)):
            for gi in passes:
                w_planes[j, gi] = work.tile([P, PACK, PAIR], BF16, name="w_planes", bufs=W_PLANES, align_bytes=64)
                for t in range(PACK):
                    nc.vector.tensor_scalar(
                        out=w_planes[j, gi][:, t, :],
                        in0=bank["plane", j, gi, t],
                        scalar1=scale_col[:, gi, t : t + 1],
                        scalar2=None,
                        op0=MULT,
                    )
                emptied(("pass", j, gi))

        def pair_words(j, gi):
            return as_mixed(pair_tile(j)[:, gi].rearrange("p i f u -> p (i f) u"))

        def mix_pair_scalar(j, passes=(0, 1), cols=slice(0, PAIR)):
            for gi in passes:
                nc.scalar.copy(out=mixed_runs(pair_words(j, gi)[:, cols]), in_=in_runs(w_planes[j, gi][:, :, cols]))

        def mix_pair_gpsimd(j, passes=(0, 1), cols=slice(0, PAIR)):
            for gi in passes:
                nc.gpsimd.tensor_scalar(
                    out=pair_words(j, gi)[:, cols],
                    in0=w_planes[j, gi][:, :, cols].rearrange("p t f -> p f t"),
                    scalar1=1.0,
                    scalar2=0.0,
                    op0=MULT,
                    op1=ADD,
                )

        def quantise_pair(j):
            source = w_turned[j][:].rearrange("p g i f u -> p (g i f u)").bitcast(BF16)
            codes = quantise("w", PAIRS - 2, source)
            for i in range(2):
                strip_mx[2 * j + i] = (codes, PAIR, P * i)

        def quantise_head_pairs():
            source = w_turned["head"][:].rearrange("p j g i f u -> p (j g i f u)").bitcast(BF16)
            codes = quantise("w_head", 1, source)
            for b in range(4):
                strip_mx[b] = (codes, PAIR, 2 * PAIR * (b // 2) + P * (b % 2))

        def mixed_x(a):
            if a >= 2:
                if a not in x_mixed:
                    x_mixed[a] = slot(("x", a), [P, K, PACK], BF16)
                return x_mixed[a]
            if 0 not in x_mixed:
                x_mixed[0] = slot(("x", 0), [P, 2, K, PACK], BF16)
            return x_mixed[0][:, a]

        def mix_x_gpsimd(a, k0, k1):
            nc.gpsimd.tensor_scalar(
                out=mixed_x(a)[:, k0:k1, :],
                in0=x_raw[a][:, :, k0:k1].rearrange("p t k -> p k t"),
                scalar1=1.0,
                scalar2=0.0,
                op0=MULT,
                op1=ADD,
            )

        def mix_x_scalar(a, k0, k1):
            nc.scalar.copy(out=mixed_runs(mixed_x(a)[:, k0:k1, :]), in_=in_runs(x_raw[a][:, :, k0:k1]))

        def quantise_x(a):
            if a >= 2:
                x_mx[a] = (quantise("x_group", 2, x_mixed[a][:].rearrange("p k t -> p (k t)")), 0)
            else:
                codes = quantise("x_shard", 1, x_mixed[0][:].rearrange("p q k t -> p (q k t)"))
                for q in range(2):
                    x_mx[q] = (codes, K * q)

        place = {u: (k, i) for k, batch in enumerate(BATCHES) for i, u in enumerate(batch)}

        def units(some, tiles=range(PACK)):
            for a, b in some:
                if ("unit", a, b) not in bank:
                    psum_bank(("unit", a, b), [P, PACK, P])
                codes, per_pass, f0 = strip_mx[b]
                for t in tiles:
                    y_codes, m0 = y_mx[a, t]
                    for gi in range(2):
                        y_cols = slice(m0 + P * gi, m0 + P * (gi + 1))
                        w_cols = slice(per_pass * gi + f0, per_pass * gi + f0 + P)
                        multiply(bank["unit", a, b][:, t, :], y_codes, y_cols, codes, w_cols, gi == 0, gi == 1)

        def reads(some):
            for a, b in some:
                k, i = place[a, b]
                if k not in dh:
                    dh[k] = slot(("dh", k), [P, len(BATCHES[k]) * P, PACK], BF16)
                nc.vector.tensor_tensor(
                    out=mixed_runs(dh[k][:, P * i : P * (i + 1), :]),
                    in0=in_runs(bank["unit", a, b][:]),
                    in1=in_runs(g_raw[a, b]),
                    op=MULT,
                )
                emptied(("unit", a, b))

        def quantise_dh(k, first=0, count=None):
            count = count or len(BATCHES[k])
            source = dh[k][:, P * first : P * (first + count), :].rearrange("p f t -> p (f t)")
            codes = quantise("dh_wide" if count == WIDE else "dh", DH_WIDE if count == WIDE else DH_NARROW, source)
            for i in range(count):
                dh_mx[BATCHES[k][first + i]] = (codes, P * i)

        def second_pass(ps, d, q, k2, h, b, width, start, stop):
            x_codes, x0 = x_mx[2 * d + q]
            k0 = x0 + P * (2 * h + k2)
            codes, f0 = dh_mx[2 * d + q, b]
            multiply(ps[:, k2, :], x_codes, slice(k0, k0 + P), codes, slice(f0, f0 + width), start, stop)

        def halves(d, j, width=PAIR, hs=(0, 1)):
            for h in hs:
                ps = psum_bank(("half", d, j, h, 0), [P, 2, width])
                for k2 in range(2):
                    for q in range(2):
                        second_pass(ps, d, q, k2, h, 2 * j, width, q == 0, q == 1)

        def last_strip():
            for q in range(2):
                for h in range(2):
                    if q == 0:
                        psum_bank(("half", 1, LAST, h, 1), [P, 2, P])
                    for k2 in range(2):
                        start, stop = q == 0 and k2 == 0, q == 1 and k2 == 1
                        second_pass(bank["half", 1, LAST, h, 1], 1, q, k2, h, 2 * LAST + 1, P, start, stop)

        def firsts(j, cols=slice(0, PAIR)):
            if j not in first_pair:
                first_pair[j] = work.tile([P, 2, 2, PAIR], F32, name="first_term", bufs=FIRSTS)
            for h in range(2):
                nc.scalar.activation(
                    out=first_pair[j][:, h, :, cols],
                    in_=bank["half", 0, j, h, 0][:, :, cols],
                    func=COPY,
                    scale=c_all[:, 0:1],
                )
                if cols.stop == PAIR:
                    emptied(("half", 0, j, h, 0))

        def seconds(some, rows=slice(0, 2)):
            for j, h in some:
                second_term[j, h] = work.tile([P, 2, PAIR], F32, name="second_term", bufs=SECONDS)
                nc.scalar.activation(
                    out=second_term[j, h][:, rows],
                    in_=bank["half", 1, j, h, 0][:, rows],
                    func=COPY,
                    scale=c_all[:, 1:2],
                )
                if rows.stop == 2:
                    emptied(("half", 1, j, h, 0))

        def sum_on_vector(j, h, strip=0, width=PAIR, rows=slice(0, 2)):
            total = first_pair[j][:, h, rows, P * strip : P * strip + width]
            nc.vector.scalar_tensor_tensor(
                out=total, in0=bank["half", 1, j, h, strip][:, rows], scalar=c_all[:, 1:2], in1=total, op0=MULT, op1=ADD
            )
            emptied(("half", 1, j, h, strip))
            f0 = PAIR * j + P * strip
            nc.sync.dma_start(out=out_view[h][:, rows, f0 : f0 + width], in_=total)

        def sums_on_gpsimd(n, some):
            total = slot(("total", n), [P, len(some), 2, PAIR], F32)
            for i, (j, h, rows) in enumerate(some):
                nc.gpsimd.tensor_tensor(
                    out=total[:, i, rows], in0=first_pair[j][:, h, rows], in1=second_term[j, h][:, rows], op=ADD
                )
                result[j, h] = (total[:, i, rows], rows)

        def store(j, h):
            total, rows = result[j, h]
            nc.sync.dma_start(out=out_view[h][:, rows, PAIR * j : PAIR * (j + 1)], in_=total)

        def load_scales():
            nc.sync.dma_start(out=scale_col[:], in_=w2_scale.rearrange("o (g p t) -> p (o g) t", p=P, t=PACK))

        def load_c():
            nc.sync.dma_start(out=c_bf[:], in_=c.partition_broadcast(P))

        def warm_up():
            warm_bank = psum_bank("warm", [P, PACK * P])
            emptied("warm")
            for i in range(WARM_UPS):
                nc.tensor.matmul(warm_bank[:], lhsT=warm[:, 0:P], rhs=warm[:], start=True, stop=True)

        b0, b1, b2, b3, b4, b5, b6 = BATCHES
        both, upper, lower = slice(0, 2), slice(0, 1), slice(1, 2)
        load_w(0, (0,))
        load_w(0, (1,))
        load_scales()
        load_w(1)
        load_y(0, (0,))
        load_y(0, (1,))
        load_w(2)
        load_y(0, (2,))
        load_y(0, (3,))
        load_y(1, (0, 1))
        load_y(1, (2, 3))
        warm_up()
        widen((0,), parts=2)
        widen((1,), copy=nc.vector.tensor_copy)
        nc.scalar.copy(out=scale_run[:], in_=scale_col[:].unsqueeze(3).to_broadcast([P, 2, PACK, RUN]))
        widen((2,), parts=2)
        widen((3,))
        split_y(0, (1,), split_on_scalar)
        load_w(3)
        load_g_wide(0, 0, 2)
        load_w(4)
        load_g_wide(1, 0, 2)
        load_y(2, (0, 1))
        load_y(2, (2, 3))
        turn_strips((0, 1, 2))
        scale_on_vector((0, 1))
        turn_y(0, (0,))
        turn_strips((3,))
        scale_on_vector((2,))
        turn_y(0, (1, 2, 3))
        scale_on_vector((3,))
        widen((4, 5))
        empty_y(0, range(PACK))
        quantise_y(0, 0, 2)
        quantise_head_pairs()
        quantise_y(0, 2, 2)
        turn_planes(2, 0)
        turn_y(1, (0,))
        turn_planes(2, 1, (0, 1))
        turn_y(1, (1,))
        load_x(0)
        load_y(3, (0, 1))
        load_g_narrow(0, 3, 3)
        turn_y(1, (2, 3))
        turn_planes(2, 1, (2, 3))
        empty_y(1, range(PACK))
        planes_on_vector(2)
        quantise_y(1)
        widen((6, 7))
        mix_pair_gpsimd(2, (1,), slice(0, 208))
        mix_pair_scalar(2, (0,))
        mix_pair_scalar(2, (1,), slice(208, PAIR))
        widen((8,))
        units(b0[:4], (0, 1))
        units(b0[:4], (2, 3))
        turn_planes(3, 0)
        turn_planes(3, 1)
        reads(b0[:3])
        planes_on_scalar(3)
        units(b0[4:])
        quantise_pair(2)
        mix_pair_gpsimd(3, (0,))
        mix_pair_gpsimd(3, (1,), slice(0, 192))
        split_y(2, (0,), split_on_scalar)
        mix_pair_scalar(3, (1,), slice(192, PAIR))
        split_y(2, (1, 2, 3), split_on_scalar)
        load_y(3, (2, 3))
        load_g_narrow(1, 3, 3)
        load_x(1)
        load_c()
        reads(b0[3:])
        units(b1[:4])
        split_y(3, (0,), split_on_scalar)
        turn_y(2, range(PACK))
        reads(b1[:1])
        quantise_pair(3)
        mix_x_gpsimd(0, 0, 400)
        reads(b1[1:4])
        load_g_wide(2, 0, 3)
        load_x(2)
        load_w(5)
        load_g_wide(3, 0, 3)
        empty_y(2, (0, 1))
        split_y(3, (1,), split_on_scalar)
        empty_y(2, (2, 3))
        split_y(3, (2,), split_on_scalar)
        units(b1[4:])
        reads(b1[4:6])
        quantise_y(2)
        widen((9,))
        turn_y(3, range(PACK))
        reads(b1[6:])
        empty_y(3, range(PACK))
        quantise_dh(0)
        quantise_y(3)
        mix_x_gpsimd(2, 0, 432)
        nc.scalar.copy(out=c_all[:], in_=c_bf[:])
        split_strips((8, 9), split_on_scalar)
        mix_x_scalar(0, 400, K)
        load_x(3)
        mix_x_scalar(1, 0, K)
        units(b2[:4] + b3[:4])
        reads(b2[:4] + b3[:1])
        turn_pair_words(4)
        planes_on_scalar(4)
        units(b2[4:7])
        quantise_x(0)
        mix_x_gpsimd(3, 0, 400)
        mix_x_scalar(2, 432, K)
        mix_x_scalar(3, 400, K)
        widen((10,))
        reads(b3[1:4])
        load_g_wide(0, 4, 5)
        load_g_narrow(1, 4, 5)
        load_g_narrow(2, 4, 5)
        load_g_narrow(3, 4, 5)
        units(b2[7:])
        halves(0, 0)
        reads(b2[4:6])
        halves(0, 1)
        firsts(0)
        firsts(1)
        quantise_dh(1)
        mix_pair_gpsimd(4, (0,))
        mix_pair_scalar(4, (1,))
        widen((11,))
        reads(b2[6:])
        units(b3[4:])
        halves(0, 2)
        halves(0, 3)
        reads(b3[4:6])
        firsts(2)
        firsts(3)
        turn_planes(LAST, 0)
        turn_planes(LAST, 1)
        quantise_pair(4)
        quantise_dh(2)
        quantise_x(2)
        units(b4[:4])
        reads(b3[6:])
        quantise_x(3)
        quantise_dh(3)
        planes_on_scalar(LAST)
        halves(1, 0)
        halves(1, 1)
        mix_pair_scalar(LAST, (0,))
        seconds(((0, 0), (0, 1), (1, 0), (1, 1)))
        mix_pair_scalar(LAST, (1,))
        sums_on_gpsimd(0, ((0, 0, both), (0, 1, both), (1, 0, both)))
        store(0, 0)
        store(0, 1)
        store(1, 0)
        reads(b4[:4])
        units(b4[4:])
        reads(b4[4:])
        halves(1, 2)
        halves(1, 3)
        sum_on_vector(2, 0)
        seconds(((2, 1),))
        seconds(((3, 0),), upper)
        quantise_pair(LAST)
        quantise_dh(4)
        sums_on_gpsimd(1, ((1, 1, both), (2, 1, both), (3, 0, upper)))
        sum_on_vector(3, 0, rows=lower)
        sum_on_vector(3, 1)
        store(1, 1)
        store(2, 1)
        store(3, 0)
        units(b5)
        reads(b5)
        halves(0, 4)
        firsts(4)
        halves(1, 4)
        seconds(((4, 1),))
        sum_on_vector(4, 0)
        quantise_dh(5)
        sums_on_gpsimd(2, ((4, 1, both),))
        store(4, 1)
        units(b6)
        halves(0, LAST)
        reads(b6[:3])
        firsts(LAST, slice(0, P))
        firsts(LAST, slice(P, PAIR))
        quantise_dh(6, 0, 2)
        reads(b6[3:])
        quantise_dh(6, 2, 1)
        quantise_dh(6, 3, 1)
        halves(1, LAST, P)
        last_strip()
        for strip in range(2):
            for h in range(2):
                sum_on_vector(LAST, h, strip, P)
